import numpy as np, ml_dtypes
CORES = [24,25,26,27,28,29,30,31]
N = 8
BF = ml_dtypes.bfloat16
def gentries(a):
    return np.ascontiguousarray(a.reshape(8, 16, -1).transpose(0, 2, 1)).reshape(8, -1)
def gtable(e):
    e = np.asarray(e); return np.ascontiguousarray(e.reshape(8, -1, 16).transpose(0, 2, 1)).reshape(128, -1).astype(np.int32)
V, E, G, K, A, S, R = 2336, 32, 1792, 256, 48, 3, 181
W = V + (N - 1) * E
def far(d, g):
    return (g, 7 - g, (8 - g) % 8)[d % 3]
def watch(rng, ins, nd, out, dens):
    co = np.full((16, W), -1)
    for i in range(16):
        o = rng.permutation(G)[:int(dens * G)]
        j = (rng.random(len(o)) * np.maximum(nd[o], 1)).astype(np.int64)
        c = np.where(nd[o] > 0, ins[j, o], out[rng.integers(0, G, len(o))])
        c, first = np.unique(c, return_index=True); co[i, c] = o[first]
    return co
def lively(rng, dens=None, pa=None, sk=1.5, p=None):
    if dens is None: dens = rng.choice(np.array([0.12, 0.2, 0.3]))
    if pa is None: pa = rng.choice(np.array([0.15, 0.4, 0.65, 0.9]))
    if p is None: p = rng.permutation(V)
    al = rng.choice(np.array([0.06, 0.15, 0.3]))
    out, rest = p[:G].copy(), p[G:]; Z, B, T, U = rest[:R], rest[R:2 * R], rest[2 * R:2 * R + 24], rest[2 * R + 24:]
    x = np.full((16, V), -1); x[:, Z] = 0
    x[:, B] = (rng.random((16, R)) * (1 + rng.integers(1, 16, R))).astype(np.int64)
    x[:, T[:16]] = 15; x[rng.integers(0, 16, 8), T[8:16]] = 14; x[:, T[16:]] = 0; x[rng.integers(0, 16, 8), T[16:]] = 1
    kind = rng.choice(6, G, p=np.array([0.2, 0.33, 0.08, al, 0.06, 0.33 - al]))
    nd = np.where((kind == 1) | (kind == 2), rng.integers(1, 4, G), 0); nd = np.where(kind == 3, 1, nd); nd = np.where(kind == 4, rng.integers(2, 16, G), nd)
    zi = Z[rng.integers(0, R, (15, G))]
    ins = np.where((rng.random((15, G)) < 0.5) | (kind == 3) | (kind == 5), zi, B[rng.integers(0, R, (15, G))])
    h = rng.random((15, G)); ui = U[rng.integers(0, len(U), (15, G))]
    dep = np.where(h < 0.65, out[(G * rng.random((15, G)) ** sk).astype(np.int64)], np.where(h < 0.85, rng.integers(V, W, (15, G)), ui))
    dep = np.where((kind == 4) & (rng.random((15, G)) < 0.7), ui, dep)
    ins = np.where(np.arange(15)[:, None] < nd, dep, ins)
    ins[14] = np.where(kind == 2, T[rng.integers(0, 16, G)], ins[14])
    k5 = np.flatnonzero(kind == 5)
    if len(k5) == 0: k5 = np.arange(G)
    i3 = kind == 3
    ins[13] = np.where(i3 & (rng.random(G) < 0.2), out[k5[rng.integers(0, len(k5), G)]], ins[13])
    ins[12] = np.where(i3 & (rng.random(G) < 0.08), T[rng.integers(16, 24, G)], ins[12])
    ins[0] = np.where(i3 & (rng.random(G) < 0.04), out, ins[0])
    ins[1] = np.where(i3 & (rng.random(G) < 0.06), ins[0], ins[1])
    co = watch(rng, ins, nd, out, dens)
    gv = np.concatenate([np.take_along_axis(ins, np.argsort(rng.random((15, G)), axis=0), 0), out[None]])
    b = np.flatnonzero(rng.random(G) < 0.03); x[:, out[b]] = rng.integers(0, 16, (16, len(b)))
    return x, gv, co, (rng.random(G) < pa).astype(np.int64), out, Z, B, T, U
def alias(rng, q, k, u):
    k = np.asarray(k); q[1][:15, k] = q[5][rng.integers(0, R, (15, len(k)))]; q[1][rng.integers(0, 15, len(k)), k] = u; q[0][:, q[4][k]] = -1
def ready(rng, q, k):
    k = np.asarray(k); n = (15, len(k))
    q[1][:15, k] = np.where(rng.random(n) < 0.5, q[5][rng.integers(0, R, n)], q[6][rng.integers(0, R, n)]); q[0][:, q[4][k]] = -1
def exports(rng, P):
    n = (N - 1) * E
    return np.stack([np.stack([np.where(rng.random(n) < 0.75, q[4][(G * rng.random(n) ** 2).astype(np.int64)], rng.integers(0, V, n)) for q in p]) for p in P])
def pack(P, ex):
    def whole(i): return np.stack([np.concatenate([q[i] for q in p]) for p in P])
    return {"x0": whole(0).astype(np.float32).astype(BF), "gv": whole(1).astype(np.int32), "co": whole(2).astype(np.int32),
            "aw": np.stack([np.stack([q[3] for q in p]) for p in P]).astype(np.int32), "ex": np.stack([gtable(a) for a in ex])}
def setup_inputs(rng):
    P = [[lively(rng) for g in range(8)] for r in range(N)]
    return pack(P, exports(rng, P))
def setup_inputs_spread(rng):
    P = []
    for r in range(N):
        P.append([])
        for g in range(8):
            q = lively(rng, dens=rng.choice(np.array([0.03, 0.4, 0.9])), pa=rng.choice(np.array([0.05, 0.5, 1.0])), sk=4.0)
            s = np.flatnonzero(rng.random(G) < 0.2); q[1][:15, s] = rng.integers(0, W, (15, len(s)))
            q[0][:, q[6]] = np.minimum(np.exp2(4 * rng.random(R)) * rng.random((16, R)), 15).astype(np.int64)
            P[r].append(q)
    return pack(P, exports(rng, P))
def setup_inputs_ends(rng):
    P = []
    for r in range(N):
        P.append([])
        for g in range(8):
            p = np.insert(np.insert(1 + rng.permutation(V - 2), G - 1, V - 1), G, 0)
            q = lively(rng, p=p, pa=(0.15, 0.6)[(g // 2 + r) % 2]); x, gv, co, aw, out, Z, B, T, U = q
            x[:, B] = 15 * rng.integers(0, 2, (16, R))
            t = rng.integers(0, 7, G); ins = np.zeros((15, G), np.int64); own = out[(G * rng.random(G) ** 1.5).astype(np.int64)]
            ins[:4] = np.where(t == 0, B[rng.integers(0, R, (4, G))], 0)
            ins[0] = np.where((t == 1) | (t == 2), W - 1, np.where((t == 3) | (t == 5), own, ins[0]))
            ins[1] = np.where(t == 2, W - 1, np.where(t == 5, T[rng.integers(0, 16, G)], ins[1])); ins[2] = np.where(t == 2, W - 1, ins[2])
            ins = np.where(t == 4, W - 1, ins)
            co[:] = watch(rng, ins, ((t > 0) & (t < 6)).astype(np.int64), out, 0.2)
            gv[:15] = np.take_along_axis(ins, np.argsort(rng.random((15, G)), axis=0), 0)
            co[co == G - 1] = -1
            if g % 2: co[:, W - 1] = G - 1
            else: co[np.arange(16), out[:16]] = G - 1
            aw[0] = 1; aw[G - 1] = 1
            if (g + r) % 2: x[:, V - 1] = 15 * rng.integers(0, 2, 16)
            else:
                x[:, V - 1] = -1; gv[:15, G - 1] = 0; gv[:4, G - 1] = B[rng.integers(0, R, 4)]
            P[r].append(q)
    ex = exports(rng, P)
    ex = np.where(rng.random(ex.shape) < 0.75, np.where(rng.random(ex.shape) < 0.5, 0, V - 1), ex); ex[..., -1] = V - 1
    return pack(P, ex)
def setup_inputs_corners(rng):
    P = []
    for r in range(N):
        P.append([])
        for g in range(8):
            c = (g + 3 * r) % 8
            q = lively(rng, dens=0.9 if c == 7 else None); x, gv, co, aw, out, Z, B, T, U = q
            if c == 0: aw[:] = 0
            elif c == 1:
                aw[:] = 0; aw[G - 1] = 1; ready(rng, q, [G - 1]); hs = rng.permutation(G - 1)[:16]
                co[np.isin(co, hs)] = -1; co[np.arange(16), out[G - 1]] = hs
            elif c < 5:
                m, n = K + c - 3, A + c - 3; ix = np.sort(rng.permutation(G)[:m]); aw[:] = 0; aw[ix] = 1
                ready(rng, q, ix); k = ix[np.sort(rng.permutation(K - 1)[:n])]; u = U[rng.permutation(len(U))[:n]]
                alias(rng, q, k, u); co[:, u] = -1
            elif c == 5: aw[:] = 1
            elif c == 6:
                aw[:] = 1; co[:] = -1; n = min(S, G // K); j = np.arange(A)
                for t in range(n):
                    u = out[(t + 1) * K + j] if t + 1 < n else U[:A]
                    alias(rng, q, t * K + j, u); hs = rng.permutation(G); co[t, out[t * K + j]] = hs[:A]
                    if t + 1 < n: co[t, u[A - 1]] = hs[A]
            else:
                hs = rng.permutation(G)[:24]; aw[:12] = 1; alias(rng, q, np.arange(12), U[:12])
                co[np.isin(co, hs)] = -1; co[:, U[:12]] = -1; co[:, out[:12]] = -1
                for j in range(12):
                    a, b = ((16, 16), (0, 0), (8, 7 + j % 4 // 2))[j // 4]
                    co[:a, out[j]] = hs[j]; co[b:, U[j]] = hs[12 + j]
            P[r].append(q)
    return pack(P, exports(rng, P))
def setup_inputs_crowd(rng):
    P = []; k7 = np.arange(7, G, K)
    for r in range(N):
        P.append([])
        for g in range(8):
            c = (g + r) % 8; q = lively(rng); x, gv, co, aw, out, Z, B, T, U = q
            if c < 6: aw[:] = 1; co[:] = -1
            if c < 2:
                alias(rng, q, np.arange(G), np.full(G, U[0])); co[0, out[0]] = 5; co[0, out[K]] = 6
                if c == 0: alias(rng, q, [K - 1], [U[2]])
                if c == 1: alias(rng, q, k7, np.full(len(k7), U[1])); alias(rng, q, [3], [out[K - 1]])
            elif c < 4:
                gv[:15] = out[0]; x[:, out] = -1; ready(rng, q, [0]); co[np.arange(16), out[0]] = G - 1 - np.arange(16)
                if c == 3: gv[3, k7] = U[0]
            elif c < 6:
                ready(rng, q, np.arange(G))
                for i in range(16): co[i, out[:K]] = rng.permutation(G)[:K]
                co[co == G - 1] = -1; co[np.arange(16), out[:16]] = G - 1
                if c == 5: co[0, out[0]] = -1; gv[14, K - 1] = U[0]
            elif c == 7 and r < 2:
                hs = rng.permutation(G)[:(N - 1) * E]; ready(rng, q, hs); aw[:] = 0; co[:] = -1; co[0, V:] = hs
            P[r].append(q)
    ex = exports(rng, P)
    for r in range(1, N, 2):
        for g in range(8): ex[r, g] = P[r][g][4][0]
    for r in range(2):
        for d in range(1, N):
            g = far(d, 7 - r); ex[r ^ d, g, (d - 1) * E:d * E] = P[r ^ d][g][6][rng.integers(0, R, E)]
    g = far(1, 6); ex[0, g, 0] = P[0][g][8][2]
    return pack(P, ex)
def relay(rng, q):
    x, gv, co, aw, out, Z, B, T, U = q; co[:] = -1; aw[:] = 0; m = G - 1
    p = 1 + rng.permutation(G - 2); b = p[:S]; k, j, c, h, v = p[S:S + 5]
    ready(rng, q, b); gv[rng.integers(0, 15, S - 1), b[1:]] = out[b[:-1]]; co[0, out[b[:-1]]] = b[1:]
    alias(rng, q, [k, m, j, c, v], [out[m], U[0], U[0], U[1], out[b[S - 2]]])
    aw[[b[0], k, c]] = 1; co[1, out[b[S - 3]]] = m; co[1, out[b[S - 2]]] = k; co[2, out[b[S - 2]]] = j
    co[5, out[c]] = 0; co[5, U[1]] = h
    if S > 3: co[3, out[b[S - 4]]] = v
    else: aw[v] = 1
    return [(0, B[0]), (1, out[b[S - 1]]), (2, out[v])]
def quiet(rng, q, idle):
    x, gv, co, aw, out, Z, B, T, U = q; co[:] = -1; aw[:] = 0; y = rng.permutation(G)[:2]
    if idle:
        alias(rng, q, y, [V, V + 1]); aw[y] = 1
        return [(slice(E - 2, None, E), out[y[0]]), (2 * E, out[y[1]])]
    ready(rng, q, y[:1]); co[3, V + 2] = y[0]
    return []
def setup_inputs_calm(rng):
    P = []; put = []
    for r in range(N):
        P.append([])
        for g in range(8):
            odd = (g + r) % 2 == 1; end = odd and g > 5
            q = lively(rng, p=np.insert(1 + rng.permutation(V - 1), G + 2 * R + 24, 0) if end else None); P[r].append(q)
            if end: put += [(r, g, s, v) for s, v in relay(rng, q)]
            elif odd and g < 2: put += [(r, g, s, v) for s, v in quiet(rng, q, r // 2 % 2 == 0)]
            if odd: continue
            x, gv, co, aw, out, Z, B, T, U = q; n = (g // 2 + r) % 4
            co[:] = -1; aw[:] = 0; p = rng.permutation(G); b = p[:S]; a = p[S:4 * S].reshape(3, S); e = p[4 * S:7 * S].reshape(3, S); w = p[7 * S:7 * S + 3]
            ready(rng, q, b); aw[b[0]] = 1; gv[rng.integers(0, 15, S - 1), b[1:]] = out[b[:-1]]
            last = S if n else 3
            co[0, out[b[:last - 1]]] = b[1:last]
            for j in range(n):
                alias(rng, q, a[j], np.concatenate([out[a[j, 1:]], np.array([U[j] if j < 2 else W - 1])]))
                aw[a[j, 0]] = 1; co[1 + j, out[b[:-1]]] = a[j, 1:]; co[8 + np.arange(S), out[a[j]]] = w[j]
            if n == 3:
                for j in range(3):
                    ready(rng, q, e[j]); gv[0, e[j, 1:]] = out[b[:-1]]; gv[1:1 + j, e[j]] = U[10 + j]; co[4 + j, out[b[:-1]]] = e[j, 1:]
    ex = exports(rng, P)
    for r, g, s, v in put: ex[r, g, s] = v
    return pack(P, ex)
def check_inputs(d):
    bad = []
    for k, lo, hi in (("x0", -1, 15), ("gv", 0, W - 1), ("co", -1, G - 1), ("aw", 0, 1), ("ex", 0, V - 1)):
        v = np.asarray(d[k]).astype(np.float64)
        if not (np.min(v) >= lo and np.max(v) <= hi): bad.append("range of " + k)
    v = np.asarray(d["x0"]).astype(np.float32).reshape(N, 8, 16, V)
    if not np.all(v == np.floor(v)): bad.append("x0 holds whole numbers")
    if np.any(np.any(v < 0, axis=2) != np.all(v < 0, axis=2)): bad.append("a column of x0 is -1 on all rows of a group or on none")
    o = np.sort(np.asarray(d["gv"]).reshape(N, 8, 16, G)[:, :, 15], axis=-1)
    if np.min(o) < 0 or np.max(o) >= V: bad.append("range of the outputs in gv")
    if np.any(o[..., 1:] == o[..., :-1]): bad.append("outputs in gv differ")
    c = np.sort(np.asarray(d["co"]), axis=-1)
    if np.any((c[..., 1:] == c[..., :-1]) & (c[..., 1:] >= 0)): bad.append("no goal twice in a row of co")
    return bad
def reference(x0, gv, co, aw, ex):
    X = np.full((N, 8, 16, W), -1, np.int64); X[..., :V] = np.asarray(x0).astype(np.float32).astype(np.int64).reshape(N, 8, 16, V)
    GV = gv.astype(np.int64).reshape(N, 8, 16, G); CO = co.astype(np.int64).reshape(N, 8, 16, W); awake = aw.astype(np.int64)
    EX = np.stack([gentries(a) for a in ex]).astype(np.int64); F = np.tile(np.arange(W), (N, 8, 1))
    for step in range(S):
        woken = np.zeros((N, 8, G), bool); sent = np.zeros((N, 8, 16, (N - 1) * E), np.int64)
        for r in range(N):
            for g in range(8):
                x, f, c = X[r, g], F[r, g], CO[r, g]
                k = np.flatnonzero(awake[r, g])[:K]; awake[r, g, k] = 0
                n = f[GV[r, g][:, k]]; o = n[15]; free = x[0, n[:15]] < 0
                cnt = np.add.reduce(free.astype(np.int64), axis=0); M = np.maximum(np.max(x[:, n[:15]], axis=1), 0)
                u = np.add.reduce(np.where(free, n[:15], 0), axis=0)
                todo = x[0, o] < 0
                binds = todo & ((cnt == 0) | np.all(M == 15, axis=0))
                wants = todo & ~binds & (cnt == 1) & np.all(M == 0, axis=0) & (u != o)
                cand = np.flatnonzero(wants)[:A]; a, b = o[cand], u[cand]
                first = np.zeros(len(cand), bool); first[np.unique(b, return_index=True)[1]] = True
                clash = np.any((c[:, a] >= 0) & (c[:, b] >= 0), axis=0)
                ok = first & ~np.isin(b, o[binds | wants]) & ~clash; a, b = a[ok], b[ok]
                x[:, o[binds]] = M[:, binds]
                hit = c[:, o[binds]].reshape(-1); woken[r, g, hit[hit >= 0]] = True
                c[:, b] = np.where(c[:, a] >= 0, c[:, a], c[:, b])
                f[a] = b; F[r, g] = f[f]
                sent[r, g] = x[:, F[r, g][EX[r, g]]]
        for r in range(N):
            for g in range(8):
                come = np.concatenate([sent[r ^ d, far(d, g)][:, (d - 1) * E:d * E] for d in range(1, N)], axis=1)
                new = V + np.flatnonzero((X[r, g, 0, V:] < 0) & (come[0] >= 0)); X[r, g, :, V:] = come
                hit = CO[r, g][:, new].reshape(-1); woken[r, g, hit[hit >= 0]] = True
        awake[woken] = 1
    return {"yx": X.reshape(N, 128, W).astype(np.float32).astype(BF), "yf": F.astype(np.float32), "yw": awake.astype(np.float32), "yc": np.add.reduce(CO, axis=2).astype(np.float32)}

@@ -1,0 +1,608 @@
+from concourse.bass import DstId, RemoteDMATransfer
+from concourse.mybir import AluOpType as A, AxisListType, ActivationFunctionType as AF
+
+V, W, G, NI = 2336, 2560, 1792, 224
+D = 304
+XW = D + W + 16
+WK = 257
+WW = 2064
+BIG = float(2 ** 21)
+MAGIC = 12582912.0
+AL = 65536.0
+LEV = (16, 64, 256)
+BIND_ACT, IMP_ACT = (13, 13, 14), (6, 6, 6)
+
+
+def sb(n, dt):
+    return ("sbuf", [128, n], dt)
+
+
+F32, BF, I32, U16 = "float32", "bfloat16", "int32", "uint16"
+SCRATCH = {
+    "awi": sb(112, I32), "awb": sb(112, BF), "aws": sb(128, BF),
+    "gvi": sb(2048, I32), "ci": sb(W, I32), "exi": sb(16, I32), "exu": sb(16, U16),
+    "XF": sb(XW, BF), "XT": sb(D + W, BF), "C": sb(XW, F32), "F": sb(D + W, F32),
+    "NC": sb(W, BF), "em": sb(V, BF), "et": sb(V, BF),
+    "AV": sb(WW, BF), "AS": sb(WW, F32), "lv": sb(256, BF), "ls": sb(256, F32),
+    "GG": sb(4096, BF), "S": sb(4096, BF), "SM": sb(1536, BF), "RM": sb(256, BF), "RO": sb(256, BF),
+    "pi": sb(8, I32), "co_": sb(32, F32), "xr": sb(256, F32), "mg": sb(128, F32),
+    "oh": sb(16, F32), "pw": sb(32, F32), "t16": sb(32, F32), "dg": sb(160, F32), "dgi": sb(160, I32),
+    "dg2": sb(160, I32), "Bn": sb(128, F32), "An": sb(32, F32),
+    "WE": sb(160, BF), "WO": sb(160, BF), "BO": sb(128, BF), "TRI": sb(128, BF), "ZS": sb(144, BF),
+    "ZSf": sb(144, F32), "Z0": sb(144, BF), "Ib": sb(128, BF), "If": sb(128, F32),
+    "I16": sb(128, BF), "I256": sb(128, BF), "MM": sb(1408, BF), "PM": sb(1152, BF),
+    "H0f": sb(144, F32), "H1f": sb(144, F32), "H0b": sb(144, BF), "H1b": sb(144, BF),
+    "ones": sb(224, BF), "jw": sb(16, F32), "jb": sb(16, BF), "jh": sb(16, F32), "jc": sb(16, F32),
+    "LC": sb(256, F32), "KJ": sb(256, F32), "CCb": sb(256, BF), "CCi": sb(224, BF),
+    "M192": sb(192, F32), "DL": sb(224, BF), "L0": sb(224, BF),
+    "P": sb(144, BF), "pre": sb(128, F32), "q": sb(112, F32), "rem": sb(112, BF), "remT": sb(224, F32),
+    "EQ": sb(1024, BF), "junk": sb(2064, BF), "acc": sb(16, F32), "bw": sb(16, U16), "bb": sb(16, BF),
+    "cmp": sb(256, BF), "eu": sb(16, U16), "gve": sb(256, U16),
+    "ZZ": sb(608, F32), "tt": sb(256, BF), "want": sb(304, BF), "rank": sb(304, BF), "o304": sb(304, BF),
+    "ob": sb(256, F32), "lat": sb(256, F32), "w16": sb(16, F32), "obu": sb(16, U16),
+    "tmn": sb(256, BF), "cg": sb(256, F32), "TT": sb(256, F32), "wl": sb(256, U16), "wi": sb(224, U16),
+    "ASb": sb(G, BF), "SW": sb(448, F32), "ca": sb(4, F32), "lz": sb(12, U16), "l2": sb(192, F32),
+    "uo": sb(12, F32), "lu": sb(4, U16), "lo": sb(12, U16), "lt": sb(12, U16),
+    "nco": sb(48, F32), "fl": sb(48, BF), "E": sb(1200, BF), "EO": sb(1200, BF), "gr": sb(4, F32),
+    "x48": sb(48, BF), "c48": sb(48, F32),
+    "xe": sb(224, BF), "re_": sb(224, BF), "t2": sb(224, BF), "snd": sb(672, BF), "land": sb(672, BF),
+    "ti": sb(224, BF), "nf": sb(224, BF), "qm": sb(224, F32),
+    "yw_": sb(112, F32), "yc_": sb(160, F32),
+    "pa": ("psum", [128, 512], F32), "pb": ("psum", [128, 512], F32), "pc": ("psum", [128, 512], F32),
+    "pd": ("psum", [128, 512], F32), "pe": ("psum", [128, 512], F32), "pf": ("psum", [128, 512], F32),
+    "pg": ("psum", [128, 512], F32), "ph": ("psum", [128, 512], F32),
+}
+DMAS = ["d_aw", "d_x0", "d_gv", "d_ex", "d_c0", "d_c1", "d_y0", "d_y1", "d_yf", "d_yw", "d_yc"]
+SEMAPHORES = ["sV", "sA", "sP", "sG", "snt", "arr0", "arr1", "arr2"] + DMAS
+PARTS = ("MM", "PM", "acca", "accv", "TT", "lt0", "lt1", "lt2", "NC0", "NC1", "NC2", "NC3", "NC4", "ZZd", "CCb",
+         "CCi", "Cd", "EO", "ca", "junk", "EQ", "want")
+PSUMS = ("pa", "pb", "pc", "pd", "pe", "pf", "pg", "ph")
+
+
+def rank_program(g, core, T, topo):
+    rank = T.rank_of(core)
+    if rank is None:
+        return
+    eng = {"V": g.vector, "A": g.scalar, "P": g.tensor, "G": g, "S": g.sync}
+    cnt = {"V": 0, "A": 0, "P": 0, "G": 0}
+    seen = {e: {} for e in eng}
+    lastw, readers, tops = {}, {}, {}
+
+    def need(e, tok):
+        if seen[e].get(tok[0], 0) < tok[1]:
+            eng[e].wait_ge(T.sem[tok[0]], tok[1])
+            seen[e][tok[0]] = tok[1]
+
+    def deps(e, r, w):
+        own = "s" + e
+        want = {}
+        toks = []
+        for n in r:
+            if n in lastw and not (e == "P" and lastw[n][0] == own):
+                toks.append(lastw[n])
+            if n in PSUMS:
+                toks += [t for t in readers.get(n, []) if t[0] != own]
+        for n in w:
+            part = n in PARTS
+            if n in lastw and not (lastw[n][0] == own and (part or e == "P")):
+                toks.append(lastw[n])
+            toks += [t for t in readers.get(n, []) if not (e == "P" and t[0] == own)]
+        for s, v in toks:
+            want[s] = max(want.get(s, 0), v)
+        for s in want:
+            need(e, (s, want[s]))
+
+    def done(tok, r, w):
+        tops[tok[0]] = tok[1]
+        for n in r:
+            readers.setdefault(n, []).append(tok)
+        for n in w:
+            lastw[n] = tok
+            readers[n] = []
+
+    def op(e, fn, r, w):
+        r, w = r.split(), w.split()
+        deps(e, r, w)
+        ins = fn()
+        cnt[e] += 1
+        ins.then_inc(T.sem["s" + e], 1)
+        done(("s" + e, cnt[e]), r, w)
+
+    def mm(lst, r, w):
+        def f():
+            ins = None
+            for o, l, x, s0, s1 in lst:
+                ins = g.tensor.matmul(o, l, x, s0, s1)
+            return ins
+        op("P", f, r, w)
+
+    def grp(o, terms):
+        return [(o, l, x, i == 0, i == len(terms) - 1) for i, (l, x) in enumerate(terms)]
+
+    def dma(sem, o, i, r, w, e="S"):
+        r, w = r.split(), w.split()
+        deps(e, r, w)
+        eng[e].dma_start(o, i).then_inc(T.sem[sem], 16)
+        done((sem, 16), r, w)
+
+    v = g.vector
+
+    def ts(o, i, s1, o0, r, w, s2=None, o1=None):
+        if o1 is None:
+            op("V", lambda: v.tensor_scalar(o, i, s1, None, o0), r, w)
+        else:
+            op("V", lambda: v.tensor_scalar(o, i, s1, s2, o0, o1), r, w)
+
+    def tt(o, a, b, o0, r, w):
+        op("V", lambda: v.tensor_tensor(o, a, b, o0), r, w)
+
+    def cp(o, i, r, w):
+        op("V", lambda: v.tensor_copy(o, i), r, w)
+
+    def ms(o, c, w):
+        op("V", lambda: v.memset(o, c), "", w)
+
+    def scan(o, a, b, init, o0, o1, r, w):
+        op("V", lambda: v.tensor_tensor_scan(o, a, b, init, o0, o1), r, w)
+
+    def act(o, i, f, r, w, **kw):
+        op("A", lambda: g.scalar.activation(o, i, f, **kw), r, w)
+
+    def iota(o, pat, base, cm, w, fl=True):
+        if fl:
+            op("G", lambda: g.iota(o, pat, base, cm, allow_small_or_imprecise_dtypes=True), "", w)
+        else:
+            op("G", lambda: g.iota(o, pat, base, cm), "", w)
+
+    def col(i):
+        return T.co_[:, i:i + 1]
+
+    def M(i):
+        return T.MM[:, 128 * i:128 * i + 128]
+
+    dma("d_aw", T.awi[:], T.aw[:], "", "awi")
+    dma("d_x0", T.XT[:, D:D + V], T.x0[:], "", "x0")
+    dma("d_gv", T.gvi[:, 0:G], T.gv[:], "", "gvi")
+    dma("d_ex", T.exi[:, 0:14], T.ex[:], "", "exi")
+    dma("d_c0", T.ci[:, 0:1280], T.co[:, 0:1280], "", "ci0")
+    dma("d_c1", T.ci[:, 1280:W], T.co[:, 1280:W], "", "ci1")
+
+    iota(T.pi[:, 0:1], [[0, 1]], 0, 1, "pi0", False)
+    iota(T.xr[:], [[1, 256]], 0, 0, "xr")
+    iota(T.mg[:], [[16, 8], [0, 16]], 0, 0, "mg")
+    iota(T.ones[:], [[0, 224]], 1, 0, "ones")
+    iota(T.aws[:, 112:128], [[0, 16]], 1, 0, "awsd")
+    iota(T.P[:, 0:16], [[0, 16]], 0, 0, "P0")
+    iota(T.EQ[:, 127::128], [[0, 8]], -1024, 0, "EQs")
+    ms(T.t16[:, 0:16], 4.0, "t16a")
+    ms(T.t16[:, 16:32], 0.0, "t16b")
+    ms(T.oh[:], 0.25, "oh")
+    for j, m in enumerate((15, 16, 1, 96)):
+        ts(T.pi[:, j + 1:j + 2], T.pi[:, 0:1], m, A.bitwise_and, "pi0", "pi%d" % (j + 1))
+    cp(T.co_[:, 0:5], T.pi[:, 0:5], "pi0 pi1 pi2 pi3 pi4", "c0")
+    scan(T.pw[:, 0:16], T.t16[:, 0:16], T.t16[:, 16:32], 0.25, A.mult, A.add, "t16a t16b", "pw0")
+    scan(T.pw[:, 16:32], T.oh[:], T.t16[:, 16:32], 4.0, A.mult, A.add, "oh t16b", "pw1")
+    ts(T.oh[:], T.xr[:, 0:16], col(1), A.is_equal, "xr c0 pw1", "oh")
+    ts(col(5), col(1), 4.0, A.is_lt, "c0", "c5")
+    ts(col(6), col(1), 6.5, A.is_lt, "c0", "c6")
+    tt(T.t16[:, 0:16], T.pw[:, 0:16], T.oh[:], A.mult, "pw0 oh", "t16a")
+    tt(T.t16[:, 16:32], T.pw[:, 16:32], T.oh[:], A.mult, "pw1 oh pw0", "t16b")
+    tt(col(7), col(6), col(5), A.subtract, "c5 c6", "c7")
+    op("V", lambda: v.tensor_reduce(col(8), T.t16[:, 0:16], AxisListType.X, A.add), "t16a", "c8")
+    op("V", lambda: v.tensor_reduce(col(9), T.t16[:, 16:32], AxisListType.X, A.add), "t16b", "c9")
+    tt(col(10), col(9), col(5), A.mult, "c9 c5", "c10")
+    ts(col(11), col(9), 256.0, A.mult, "c9 c7", "c11", col(7), A.mult)
+    ts(T.dg[:, 0:128], T.xr[:, 0:128], col(10), A.mult, "xr c10", "dga", -0.4921875, A.add)
+    ts(T.dg[:, 128:160], T.xr[:, 0:32], col(11), A.mult, "xr c11", "dgb", -0.4921875, A.add)
+    cp(T.dgi[:], T.dg[:], "dga dgb", "dgi")
+    ts(T.dg2[:], T.dgi[:], 3, A.bitwise_and, "dgi", "dg2")
+    ts(T.Bn[:], T.dg2[:, 0:128], -0.0625, A.mult, "dg2", "Bn", -15.0625, A.add)
+    ts(T.An[:], T.dg2[:, 128:160], -0.0625, A.mult, "dg2", "An")
+    for h in range(20):
+        act(T.NC[:, 128 * h:128 * h + 128], T.Bn[:], AF.Identity, "Bn An", "NC%d" % (h // 4), bias=T.An[:, h:h + 1])
+    ts(col(12), col(0), 16.0, A.add, "c0", "c12")
+    ts(col(13), col(2), 0.0, A.is_equal, "c0", "c13")
+    ts(col(14), col(2), 0.0, A.is_gt, "c0", "c14")
+    tt(col(15), col(0), col(1), A.subtract, "c0", "c15")
+    ts(T.WE[:], T.xr[:, 0:160], col(12), A.is_equal, "xr c12 c13", "WE", col(13), A.mult)
+    ts(T.WO[:], T.xr[:, 0:160], col(12), A.is_equal, "xr c12 c14", "WO", col(14), A.mult)
+    ts(col(16), col(15), 15.0, A.add, "c15", "c16")
+    ts(T.BO[:], T.mg[:], col(15), A.is_equal, "mg c15", "BO")
+    op("G", lambda: g.affine_select(T.TRI[:], T.BO[:], [[1, 128]], A.is_ge, 0.0, 0, -1), "BO", "TRI")
+    iota(T.gvi[:, G:2048], [[0, 256]], W, 0, "gvd", False)
+    iota(T.XF[:, 0:D], [[0, D]], 0, 0, "XFd")
+    iota(T.XF[:, D + W:XW], [[0, 16]], 0, 0, "XFz")
+    iota(T.M192[:, 0:144], [[-16, 3], [1, 48]], 0, 0, "M192")
+    iota(T.SM[:], [[0, 1536]], 1, 0, "SM")
+    iota(T.SM[:, 0::16], [[0, 96]], 0, 0, "SM")
+    iota(T.SM[:, 15::16], [[0, 96]], 0, 0, "SM")
+    iota(T.ZZ[:, 256:304], [[1, 48]], 256, 0, "ZZd")
+    iota(T.ZZ[:, 560:608], [[1, 48]], 256, 0, "ZZd")
+    iota(T.want[:, 256:304], [[0, 48]], 1, 0, "wantd")
+    iota(T.o304[:], [[0, 304]], 1, 0, "o304")
+    iota(T.C[:, 0:D], [[0, D]], -1, 0, "Cd")
+    iota(T.C[:, D + W:XW], [[0, 16]], -1, 0, "Cd")
+    iota(T.AS[:], [[0, WW]], 0, 0, "AS")
+    iota(T.M192[:, 144:192], [[0, 48]], 0, 0, "M192z")
+    iota(T.XT[:, 0:D], [[0, D]], 0, 0, "XTd")
+    cp(T.awb[:], T.awi[:], "awi", "awb")
+
+    def turn(src, r, bank):
+        lst = []
+        for t in range(7):
+            lst.append((T[bank][:, 32 * t:32 * t + 16], T.WE[:, 16:144], src(t), True, True))
+            lst.append((T[bank][:, 32 * t + 16:32 * t + 32], T.WO[:, 32:160], src(t), True, True))
+        mm(lst, r + " WE WO", bank)
+
+    turn(lambda t: T.awb[:, 16 * t:16 * t + 16], "awb", "pe")
+    ts(T.ZS[:], T.xr[:, 0:144], col(16), A.is_equal, "xr c16", "ZS")
+    ts(T.jw[:], T.xr[:, 0:16], 16.0, A.mult, "xr c0", "jw", col(1), A.add)
+    for t in range(7):
+        op("V", lambda: v.transpose(T.TT[:, t:t + 218:7], T.pe[:, 32 * t:32 * t + 32]), "pe", "TT")
+    cp(T.jb[:], T.jw[:], "jw", "jb")
+    ts(T.jh[:], T.jw[:], 0.5, A.add, "jw", "jh")
+    cp(T.aws[:, 0:112], T.TT[:, 0:112], "TT", "aws")
+    ts(T.I16[:], T.xr[:, 0:128], col(0), A.is_equal, "xr c0", "I16", 16.0, A.mult)
+    ts(T.Ib[:], T.xr[:, 0:128], col(0), A.is_equal, "xr c0", "Ib")
+
+    chunks = [(a, min(a + 512, V)) for a in range(0, V, 512)]
+
+    def enc_v(k):
+        a, b = chunks[k]
+        ts(T.em[:, a:b], T.XT[:, D + a:D + b], 0.0, A.min, "x0", "em%d" % k)
+        scan(T.et[:, a:b], T.NC[:, a:b], T.em[:, a:b], 0.0, A.min, A.mult, "em%d NC%d" % (k, k), "et%d" % k)
+
+    def enc_p(k):
+        a, b = chunks[k]
+        bk = ("pg", "ph")[k % 2]
+        mm(grp(T[bk][:, 0:b - a], [(T.Ib[:], T.XT[:, D + a:D + b]), (T.Ib[:], T.et[:, a:b])]), "x0 Ib et%d" % k, bk)
+        act(T.XF[:, D + a:D + b], T[bk][:, 0:b - a], AF.Copy, bk, "XFe%d" % k)
+
+    def consts2():
+        ts(col(17), col(1), 15.0, A.is_equal, "c0", "c17")
+        ts(col(18), col(7), 0.5, A.mult, "c7 c5", "c18", col(5), A.add)
+        ts(col(20), col(17), 16.0, A.mult, "c17", "c20", 64.0, A.add)
+        ts(col(19), col(18), 16.0, A.mult, "c18 c8", "c19", col(8), A.mult)
+        ts(M(3), T.BO[:], col(17), A.mult, "BO c17", "M3", 16.0, A.mult)
+        ts(M(8), T.BO[:], col(19), A.mult, "BO c19", "M8")
+        ts(M(1), T.BO[:], col(20), A.mult, "BO c20", "M1")
+
+    def consts2a():
+        for i, src, n, c in ((0, T.BO[:], "BO", -64.0), (2, M(3), "M3", -1.0), (4, T.BO[:], "BO", -2 * AL),
+                             (5, T.BO[:], "BO", 2 * AL), (6, M(3), "M3", AL / 16), (7, M(3), "M3", -AL / 16),
+                             (9, M(8), "M8", -1.0), (10, T.BO[:], "BO", AL)):
+            act(M(i), src, AF.Copy, n, "MM", scale=c)
+
+    def consts3():
+        ts(col(21), col(1), 1.0, A.add, "c0", "c21")
+        ts(col(22), col(1), 15.0, A.is_lt, "c0", "c22", BIG, A.mult)
+        ts(T.lat[:, 0:16], T.oh[:], -2 * BIG, A.mult, "oh", "lat")
+        ts(T.LC[:, 0:16], T.xr[:, 0:16], col(21), A.is_equal, "xr c21", "LC", BIG, A.mult)
+        ts(T.jc[:], T.jw[:], col(22), A.add, "jw c22", "jc")
+        tt(T.LC[:, 0:16], T.LC[:, 0:16], T.lat[:, 0:16], A.add, "LC lat", "LC")
+        ts(col(23), col(1), 2.0, A.mult, "c0", "c23", col(4), A.add)
+        ts(col(25), col(3), -128.0, A.mult, "c0", "c25", 256.0, A.add)
+        ts(col(26), col(3), -112.0, A.mult, "c0", "c26", 256.0, A.add)
+        ts(col(24), col(23), 1.0, A.add, "c23", "c24")
+        for n, c in (("H0", 13), ("H1", 14)):
+            ts(T[n + "f"][:], T.xr[:, 0:144], col(24), A.is_equal, "xr c24 c13 c14", n + "f", col(c), A.mult)
+        ts(col(27), col(15), -1.0, A.mult, "c15", "c27", 112.0, A.add)
+        ts(col(29), col(15), 0.0, A.is_gt, "c15", "c29", 128.0, A.mult)
+        ts(col(31), col(1), 0.0, A.is_equal, "c0", "c31")
+        ts(col(28), col(27), col(1), A.add, "c27 c0", "c28")
+        ts(col(30), col(29), col(15), A.subtract, "c29 c15 c0", "c30", col(1), A.add)
+        ts(T.M192[:, 0:144], T.M192[:, 0:144], col(1), A.is_ge, "M192 c0", "M192", 8192.0, A.mult)
+        ts(PMm(1, 2), T.xr[:, 0:128], col(28), A.is_equal, "xr c28", "PM1")
+        ts(PMm(2, 2), T.xr[:, 0:128], col(30), A.is_equal, "xr c30", "PM2")
+        cp(T.exu[:, 0:14], T.exi[:, 0:14], "exi", "exu")
+
+    def consts3a():
+        for n in (16, 32, 64, 128):
+            act(T.LC[:, n:2 * n], T.LC[:, 0:n], AF.Copy, "LC", "LC")
+        act(T.KJ[:], T.xr[:], AF.Identity, "xr", "KJ", bias=1.0 / 256 - 1.0, scale=1.0 / 256)
+        for n in ("H0", "H1"):
+            act(T[n + "b"][:], T[n + "f"][:], AF.Copy, n + "f", n + "b", scale=256.0)
+        for h in range(2):
+            act(T.CCb[:, 128 * h:128 * h + 128], T.xr[:, 0:128], AF.Identity, "xr c25", "CCb", bias=col(25), scale=-1.0)
+
+    def consts4a():
+        for h in range(2):
+            act(T.CCi[:, 112 * h:112 * h + 112], T.xr[:, 0:112], AF.Identity, "xr c26", "CCi", bias=col(26), scale=-1.0)
+        act(T.DL[:], T.NC[:, V:W], AF.Identity, "NC4", "DL", bias=-15.0, scale=-1.0)
+        act(T.L0[:], T.NC[:, V:W], AF.Identity, "NC4", "L0", bias=-1.0, scale=-1.0)
+        for k in range(3):
+            for j, c in enumerate((512.0, -512.0)):
+                act(PMm(k, j), PMm(k, 2), AF.Copy, "Ib PM1 PM2", "PM", scale=c)
+        act(T.If[:], T.Ib[:], AF.Copy, "Ib", "If")
+        act(T.I256[:], T.Ib[:], AF.Copy, "Ib", "I256", scale=256.0)
+        act(T.ZSf[:], T.ZS[:], AF.Copy, "ZS", "ZSf")
+        act(T.Z0[:], T.ZS[:], AF.Identity, "ZS c31", "Z0", scale=col(31))
+
+    def PMm(k, j):
+        if (k, j) == (0, 2):
+            return T.Ib[:]
+        a = 128 * (3 * k + j)
+        return T.PM[:, a:a + 128]
+
+    def sel(Z, p):
+        return Z[:, 15 - p:143 - p]
+
+    XFall = "XF XFd XFz XFi XFe0 XFe1 XFe2 XFe3 XFe4"
+    Call = "C Cd C0 C1"
+
+    def refresh(s):
+        for k in range(s, -1, -1):
+            cp(T.x48[:], T.XF[:].indirect(T.lt[:, 4 * k:4 * k + 3]), "XF lt%d" % k, "x48")
+            cp(T.XF[:].indirect(T.lo[:, 4 * k:4 * k + 3]), T.x48[:], "x48 lo%d" % k, "XF")
+
+    def shuffle(bank, n, terms, cc, r):
+        lst = []
+        for h in range(2):
+            tl = []
+            for nm, src in terms:
+                Wm = T["H%d%s" % (h, nm)]
+                tl += [(Wm[:, 1:129], src[:, 0:n]), (Wm[:, 0:128], src[:, n:2 * n])]
+            tl.append((T.Ib[:], cc[:, n * h:n * h + n]))
+            lst += grp(T[bank][:, n * h:n * h + n], tl)
+        mm(lst, r + " H0f H1f H0b H1b Ib", bank)
+
+    def lists(bank, k, out, name, add):
+        for s in range(k):
+            op("V", lambda: v.transpose(T.TT[:, s:32 * k:k], T[bank][:, s:32 * k:k]), bank, "TT")
+        ts(out[:, 0:32 * k], T.TT[:, 0:32 * k], add, A.add, "TT", name)
+
+    def scat_a(L, name, k, rows):
+        for r in rows:
+            act(T.AS[:].indirect(L[:, k * r:k * r + k]), T.ls[:, 0:16 * k], AF.Silu, name + " ls", "AS")
+
+    def scat_v(L, name, k, rows):
+        for r in rows:
+            cp(T.AV[:].indirect(L[:, k * r:k * r + k]), T.lv[:, 0:16 * k], name + " lv", "AV")
+
+    for s in range(3):
+        last = s == 2
+        mm([(T.pa[:, 0:128], T.TRI[:], T.aws[:], True, True), (T.pa[:, 128:256], T.BO[:], T.aws[:], True, True)],
+           "TRI BO aws awsd", "pa")
+        iota(T.ls[:], [[0, 256]], LEV[s], 0, "ls")
+        iota(T.lv[:], [[0, 256]], LEV[s], 0, "lv")
+        if s == 0:
+            iota(T.AV[:], [[0, WW]], 0, 0, "AV")
+        if s == 1:
+            iota(T.F[:], [[1, D + W]], -D, 0, "F")
+        scan(T.P[:, 1:129], T.ones[:, 0:128], T.pa[:, 128:256], 0.0, A.mult, A.add, "ones pa P0", "P")
+        for c in range(8, 16):
+            act(T.junk[:, 128 * c - 1024:128 * c - 897], T.P[:, 1:128], AF.Sign, "P jh", "junk acca",
+                bias=T.jh[:, c:c + 1], scale=-1.0, accum_out=T.acc[:, c:c + 1])
+        for c in range(8):
+            ts(T.EQ[:, 128 * c:128 * c + 127], T.P[:, 1:128], T.jb[:, c:c + 1], A.is_le, "P jb", "EQ")
+        tt(T.pre[:], T.pa[:, 0:128], T.P[:, 0:128], A.add, "pa P P0", "pre")
+        scan(T.EO[:, 0:1024], T.EQ[:], T.EQ[:], 0.0, A.add, A.max, "EQ EQs", "EO")
+        cp(T.bw[:, 0:8], T.EO[:, 126:1024:128], "EO", "bw0")
+        ts(T.bw[:, 8:16], T.acc[:, 8:16], 127.0, A.add, "acca", "bw1", 0.5, A.mult)
+        tt(T.cmp[:], T.pre[:].indirect(T.bw[:]), T.xr[:], A.is_le, "pre bw0 bw1 xr", "cmp")
+        cp(T.bb[:, 0:8], T.EO[:, 126:1024:128], "EO", "bb0")
+        ts(T.bb[:, 8:16], T.acc[:, 8:16], 127.0, A.add, "acca", "bb1", 0.5, A.mult)
+        mm([(T.pa[:, 256:272], sel(T.ZS, p), T.cmp[:, p::16], p == 0, False) for p in range(16)], "ZS cmp", "pa")
+        mm([(T.pa[:, 256:272], T.I16[:], T.bb[:], False, True)], "I16 bb0 bb1", "pa")
+        if s == 0:
+            consts2()
+            consts2a()
+            for k in range(2):
+                enc_v(k)
+                enc_p(k)
+        cp(T.eu[:], T.pa[:, 256:272], "pa", "eu")
+        if s == 0:
+            for k in range(2, 5):
+                enc_v(k)
+                enc_p(k)
+            act(T.XF[:, D + V:D + W], T.NC[:, V:W], AF.Identity, "NC4", "XFi", bias=-1.0, scale=-1.0)
+        cp(T.gve[:], T.gvi[:].indirect(T.eu[:]), "gvi gvd eu", "gve")
+        win = T.XF[:, D:XW]
+
+        def ga(a, b, n):
+            act(T.GG[:, 16 * a:16 * b], win.indirect(T.gve[:, a:b]), AF.Copy, XFall + " gve", n)
+
+        def sc(a, b, n):
+            scan(T.S[:, 16 * a:16 * b], T.SM[:, 0:16 * (b - a)], T.GG[:, 16 * a:16 * b], 0.0, A.mult, A.max,
+                 "SM G" + n, "S" + n)
+
+        def rnd(a, b, r, n):
+            ts(T.RM[:, a:b], T.S[:, 16 * a + 14:16 * b:16], MAGIC, A.add, r, "RM" + n, MAGIC, A.subtract)
+            ts(T.RO[:, a:b], T.S[:, 16 * a + 15:16 * b:16], MAGIC, A.add, r, "RO" + n, MAGIC, A.subtract)
+
+        MA = " MM M1 M3 M8"
+        zb = float(D - 623925)
+
+        def views(a, b):
+            return T.S[:, 16 * a + 14:16 * b:16], T.S[:, 16 * a + 15:16 * b:16], T.RM[:, a:b], T.RO[:, a:b]
+
+        def p_g(a, b, r, bk):
+            mm([(T[bk][:, a:b], M(0), T.GG[:, 16 * a + i:16 * b:16], i == 0, False) for i in range(15)], r + MA, bk)
+
+        def p_bind(a, b, r, n):
+            mx, go, rm, ro = views(a, b)
+            mm(grp(T.pe[:, a:b], [(M(8), go)]), r + MA, "pe")
+            act(T.ZZ[:, 304 + a:304 + b], T.pe[:, a:b], AF.Identity, "pe", "ZO" + n, bias=zb)
+            mm(grp(T.pc[:, a:b], [(M(4), mx), (M(6), go), (M(5), rm), (M(7), ro)]), r + " RM%s RO%s" % (n, n), "pc")
+
+        def p_want(a, b, r, n, bk):
+            mx, go, rm, ro = views(a, b)
+            o = T[bk][:, a:b]
+            mm([(o, M(1), mx, False, False), (o, M(3), go, False, False), (o, M(2), rm, False, False),
+                (o, M(2), ro, False, True)], r + " RM%s RO%s" % (n, n), bk)
+
+        Sall = "S0 S1 S2 S3"
+        if s == 0:
+            ga(0, 96, "G0")
+        ga(96, 160, "G1")
+        ga(160, 224, "G2")
+        if s == 0:
+            consts3()
+            cp(T.C[:, D:D + 1280], T.ci[:, 0:1280], "ci0", "C0")
+            cp(T.GG[:, 3584:4096], win.indirect(T.gve[:, 224:256]), XFall + " gve", "G3")
+        else:
+            ga(224, 256, "G3")
+            cp(T.GG[:, 0:1536], win.indirect(T.gve[:, 0:96]), XFall + " gve", "G0")
+        p_g(0, 160, "G0 G1", "pb")
+        sc(0, 96, "0")
+        sc(96, 160, "1")
+        rnd(0, 160, "S0 S1", "a")
+        p_bind(0, 160, "S0 S1", "a")
+        if s == 0:
+            cp(T.C[:, D + 1280:D + W], T.ci[:, 1280:W], "ci1", "C1")
+        p_g(160, 256, "G2 G3", "pg")
+        sc(160, 224, "2")
+        sc(224, 256, "3")
+        rnd(160, 256, "S2 S3", "b")
+        p_bind(160, 256, "S2 S3", "b")
+        mx, go = views(0, 256)[0:2]
+        mm(grp(T.pd[:, 0:256], [(M(8), mx), (M(9), go)]), Sall, "pd")
+        p_want(0, 160, "S0 S1", "a", "pb")
+        p_want(160, 256, "S2 S3", "b", "pg")
+        mm(grp(T.ph[:, 0:256], [(M(8), mx)]), Sall, "ph")
+        if s == 0:
+            consts3a()
+        tt(T.q[:], T.pre[:, 0:112], T.aws[:, 0:112], A.mult, "pre aws", "q")
+        tt(T.ob[:], T.pc[:, 0:256], T.ZZ[:, 304:560], A.min, "pc ZOa ZOb", "ob")
+        scan(T.lat[:], T.LC[:], T.ob[:], 0.0, A.add, A.max, "LC ob", "lat")
+        tt(T.w16[:], T.lat[:, 15::16], T.jc[:], A.max, "lat jc", "w16")
+        ts(T.rem[:], T.q[:], 256.5, A.is_gt, "q", "rem", float(LEV[s]), A.mult)
+        ts(T.obu[:], T.w16[:], col(22), A.subtract, "w16 c22", "obu")
+        act(T.cg[:], T.C[:].indirect(T.obu[:]), AF.Copy, Call + " obu", "cg")
+        act(T.ZZ[:, 0:256], T.ph[:, 0:256], AF.Identity, "ph", "ZU", bias=zb)
+        tt(T.tmn[:], T.C[:].indirect(T.obu[:]), T.KJ[:], A.min, Call + " obu KJ", "tmn")
+        shuffle("pf", 128, [("b", T.tmn), ("f", T.cg)], T.CCb, "tmn cg CCb")
+        ts(T.tt[:], T.pd[:, 0:256], 0.0, A.is_equal, "pd", "tt", 1.5, A.add)
+        tt(T.want[:, 0:160], T.pb[:, 0:160], T.tt[:, 0:160], A.is_gt, "pb tt", "want")
+        tt(T.want[:, 160:256], T.pg[:, 160:256], T.tt[:, 160:256], A.is_gt, "pg tt", "want")
+        scan(T.rank[:], T.o304[:], T.want[:], 0.0, A.mult, A.add, "o304 want wantd", "rank")
+        if s == 0:
+            consts4a()
+        for t in range(3):
+            act(T.junk[:, 1152 + 304 * t:1456 + 304 * t], T.rank[:], AF.Sign, "rank jh", "junk ca",
+                bias=T.jh[:, t:t + 1], scale=-1.0, accum_out=T.ca[:, t:t + 1])
+        mm(grp(T.pc[:, 0:256], [(M(4), mx), (M(6), go), (M(5), T.RM[:]), (M(7), T.RO[:]), (M(10), T.want[:, 0:256])]),
+           Sall + " RMa RMb ROa ROb want", "pc")
+        cp(T.XF[:].indirect(T.obu[:]), T.S[:, 14::16], Sall + " obu", XFall)
+        lists("pf", 8, T.wl, "wl", 256.0)
+        scat_a(T.wl, "wl", 16, range(BIND_ACT[s]))
+        for j in range(3):
+            ts(T.lz[:, 3 * j:3 * j + 3], T.ca[:, 0:3], 304.0, A.add, "ca", "lz%d" % j, 0.5, A.mult)
+        ts(T.lz[:, 9:12], T.ca[:, 0:3], 912.0, A.add, "ca", "lz3", 0.5, A.mult)
+        tt(T.SW[:, 256:448], T.ZZ[:].indirect(T.lz[:]), T.M192[:], A.add, "ZOa ZOb ZU ZZd lz0 lz1 lz2 lz3 M192 M192z", "SW1")
+        tt(T.SW[:, 0:256], T.pc[:, 0:256], T.ZZ[:, 304:560], A.min, "pc ZOa ZOb", "SW0")
+        scan(T.l2[:], T.LC[:, 0:192], T.SW[:, 256:448], 0.0, A.add, A.max, "LC SW1", "l2")
+        lo, lt = T.lo[:, 4 * s:4 * s + 3], T.lt[:, 4 * s:4 * s + 3]
+        ts(lo, T.l2[:, 159:192:16], col(22), A.subtract, "l2 c22", "lo%d" % s)
+        ts(T.lu[:, 0:3], T.l2[:, 15:144:64], col(22), A.subtract, "l2 c22", "lu", 8192.0, A.subtract)
+        ts(T.uo[:, 0:3], T.l2[:, 15:144:64], col(22), A.subtract, "l2 c22", "uo0", 8192.0, A.subtract)
+        ts(T.uo[:, 4:7], T.l2[:, 159:192:16], col(22), A.subtract, "l2 c22", "uo1")
+        ts(T.nco[:], T.C[:].indirect(lo), 0.0, A.is_lt, Call + " lo%d" % s, "nco", 8192.0, A.mult)
+        tt(T.fl[:], T.C[:].indirect(T.lu[:, 0:3]), T.nco[:], A.is_ge, Call + " lu nco", "fl")
+        mm(grp(T.pa[:, 288:291], [(sel(T.ZS, p), T.fl[:, p::16]) for p in range(16)]), "ZS fl", "pa")
+        for t in range(3):
+            n = 304 + 48 * t
+            ts(T.E[:, 400 * t:400 * t + n], T.SW[:, 0:n], T.uo[:, t:t + 1], A.is_equal, "SW0 SW1 uo0", "E%d" % t,
+               -1.0, A.mult)
+        for t in range(3):
+            n = 304 + 48 * t
+            Et = T.E[:, 400 * t:400 * t + n]
+            scan(T.EO[:, 400 * t + 400 - n:400 * t + 400], Et, Et, 0.0, A.min, A.min, "E%d" % t, "EO")
+        tt(T.uo[:, 8:11], T.uo[:, 0:3], T.uo[:, 4:7], A.subtract, "uo0 uo1", "uo2")
+        tt(T.gr[:, 0:3], T.pa[:, 288:291], T.EO[:, 399::400], A.is_equal, "pa EO", "gr")
+        for t in range(3):
+            ts(T.lt[:, 4 * s + t:4 * s + t + 1], T.gr[:, t:t + 1], T.uo[:, 8 + t:9 + t], A.mult, "gr uo1 uo2",
+               "lt%d" % s, T.uo[:, 4 + t:5 + t], A.add)
+        refresh(s)
+        cp(T.xe[:], win.indirect(T.exu[:, 0:14]), "XF exu", "xe")
+        ts(T.re_[:], T.xe[:], MAGIC, A.add, "xe", "re", MAGIC, A.subtract)
+        la, lb = [], []
+        for d in range(1, 8):
+            a, b = 32 * d - 32, 32 * d
+            la += grp(T.pg[:, a:b], [(PMm(d % 3, 0), T.xe[:, a:b]), (PMm(d % 3, 1), T.re_[:, a:b])])
+            lb += grp(T.ph[:, a:b], [(PMm(d % 3, 2), T.re_[:, a:b])])
+        mm(la, "PM xe re", "pg")
+        mm(lb, "PM1 PM2 Ib re", "ph")
+        cp(T.c48[:], T.C[:].indirect(lo), Call + " lo%d" % s, "c48")
+        tt(T.nco[:], T.C[:].indirect(lt), T.c48[:], A.max, Call + " lt%d c48" % s, "nco")
+        cp(T.C[:].indirect(lt), T.nco[:], "nco lt%d" % s, Call)
+        tt(T.t2[:], T.pg[:, 0:224], T.DL[:], A.min, "pg DL", "t2")
+        tt(T.snd[:, 224 * s:224 * s + 224], T.ph[:, 0:224], T.t2[:], A.add, "ph t2", "snd%d" % s)
+        deps("G", ["snd%d" % s], [])
+        trs = []
+        for d in range(1, 8):
+            peer = T.cores[rank ^ d]
+            en = topo.engines(core, peer)
+            n = len(en) // 8
+            mask = sum(1 << e for e in en[n * (d - 1):n * d])
+            rid, pid, _ = topo.addr(peer)
+            a = 224 * s + 32 * (d - 1)
+            trs.append(RemoteDMATransfer(dst_ids=[DstId(rid=rid, pnc=pid)], dma_engine_mask=mask,
+                                         remote_sem=T.sem["arr%d" % s], src=T.snd[:, a:a + 32], dst=T.land[:, a:a + 32]))
+            tops["snt"] = tops.get("snt", 0) + n
+            tops["arr%d" % s] = tops.get("arr%d" % s, 0) + n
+        g.remote_dma_fused(trs, local_sem=T.sem.snt)
+        lastw["land%d" % s] = ("arr%d" % s, tops["arr%d" % s])
+        tt(T.ti[:], T.C[:, D + V:D + W], T.KJ[:, 0:224], A.min, "C KJ", "ti")
+        mm(grp(T.pg[:, 0:224], [(T.If[:], T.C[:, D + V:D + W]), (T.I256[:], T.ones[:]), (T.Ib[:], T.ones[:]),
+                                (T.I256[:], T.ti[:])]), "I256 If Ib ones ti C", "pg")
+        if last:
+            turn(lambda t: T.rem[:, t:112:7], "rem", "pe")
+            for k in range(2, -1, -1):
+                cp(T.c48[:], T.F[:].indirect(T.lt[:, 4 * k:4 * k + 3]), "F lt%d" % k, "c48")
+                cp(T.F[:].indirect(T.lo[:, 4 * k:4 * k + 3]), T.c48[:], "c48 lo%d" % k, "F")
+            dma("d_yf", T.yf[:], T.F[0:128:16, D:D + W], "F", "")
+            op("V", lambda: v.transpose(T.remT[:], T.pe[:, 0:224]), "pe", "remT")
+        scat_v(T.wl, "wl", 16, range(BIND_ACT[s], 16))
+        Ln = T.land[:, 224 * s:224 * s + 224]
+        Lp, lpn = (T.L0[:], "L0") if s == 0 else (T.land[:, 224 * s - 224:224 * s], "land%d" % (s - 1))
+        tt(T.nf[:], Ln, Lp, A.not_equal, "land%d %s" % (s, lpn), "nf")
+        tt(T.qm[:], T.pg[:, 0:224], T.nf[:], A.mult, "pg nf", "qm")
+        shuffle("pf", 112, [("f", T.qm)], T.CCi, "qm CCi")
+        cp(T.XT[:, 0:D + V].indirect(T.obu[:]), T.S[:, 14::16], Sall + " obu XTd", "x0")
+        if last:
+            dma("d_y0", T.yx[:, 0:V], T.XT[:, D:D + V], "x0", "")
+            ts(T.re_[:], Ln, MAGIC, A.add, "land2", "re", MAGIC, A.subtract)
+            mm(grp(T.ph[:, 0:224], [(PMm(0, 2), Ln), (PMm(0, 1), Ln), (PMm(0, 0), T.re_[:])]), "PM Ib land2 re", "ph")
+        lists("pf", 7, T.wi, "wi", -1.0)
+        scat_a(T.wi, "wi", 14, range(IMP_ACT[s]))
+        for h in range(2):
+            act(T.ASb[:, 896 * h:896 * h + 896], T.AS[:, WK + 896 * h:WK + 896 * h + 896], AF.Copy, "AS", "ASb%d" % h)
+        if last:
+            ts(T.XT[:, D + V:D + W], T.ph[:, 0:224], -1.0, A.max, "ph", "XTi")
+            dma("d_y1", T.yx[:, V:W], T.XT[:, D + V:D + W], "XTi", "")
+            mm(grp(T.pc[:, 0:160], [(sel(T.ZSf, p), T.C[:, D + 160 * p:D + 160 * p + 160]) for p in range(16)]),
+               "ZSf " + Call, "pc")
+        scat_v(T.wi, "wi", 14, range(IMP_ACT[s], 16))
+        if last:
+            act(T.yc_[:], T.pc[:, 0:160], AF.Copy, "pc", "yc")
+            dma("d_yc", T.yc[:], T.yc_[:], "yc", "")
+
+            def piece(Wn, p):
+                return Wn[:, WK + 112 * p:WK + 112 * p + 112]
+        else:
+            def piece(Wn, p):
+                return Wn[:, WK + p:WK + p + G:16]
+        o = T.pd[:, 0:112]
+        if not last:
+            mm([(o, T.Ib[:], T.rem[:], True, False)], "rem Ib", "pd")
+        for h in range(2):
+            if last:
+                lst = [(o, sel(T.Z0, p), T.ASb[:, 112 * p:112 * p + 112], p == 0, False) for p in range(8 * h, 8 * h + 8)]
+            else:
+                lst = [(T.pd[:, 56 * h:56 * h + 56], sel(T.Z0, p), T.ASb[:, 896 * h + p:896 * h + 896:16], False, False)
+                       for p in range(16)]
+            mm(lst, "Z0 ASb%d" % h, "pd")
+        if last:
+            mm([(T.pd[:, 16 * t:16 * t + 16], T.If[:], T.remT[:, 32 * t:32 * t + 16], False, False) for t in range(7)],
+               "remT If", "pd")
+        mm([(o, sel(T.Z0, p), piece(T.AV, p), False, p == 15) for p in range(16)], "Z0 AV", "pd")
+        if last:
+            ts(T.yw_[:], o, 0.75 * LEV[s], A.is_gt, "pd", "yw")
+            dma("d_yw", T.yw[:], T.yw_[:], "yw", "")
+        else:
+            cp(T.XF[:, D + V:D + W], Ln, "land%d" % s, "XF")
+            refresh(s)
+            ts(T.aws[:, 0:112], o, 0.75 * LEV[s], A.is_gt, "pd", "aws")
+    for k in tops:
+        need("S", (k, tops[k]))

@@ -9,7 +9,8 @@ WW = 2064
 BIG = float(2 ** 21)
 MAGIC = 12582912.0
 AL = 65536.0
-LEV = (16, 64, 256)
+LEV = (16, 128, 1024)
+AV_FIRST = False
 BIND_ACT, IMP_ACT = (13, 13, 14), (6, 6, 6)
 
 
@@ -27,7 +28,8 @@ SCRATCH = {
     "GG": sb(4096, BF), "S": sb(4096, BF), "SM": sb(1536, BF), "RM": sb(256, BF), "RO": sb(256, BF),
     "pi": sb(8, I32), "co_": sb(32, F32), "xr": sb(256, F32), "mg": sb(128, F32),
     "oh": sb(16, F32), "pw": sb(32, F32), "t16": sb(32, F32), "dg": sb(160, F32), "dgi": sb(160, I32),
-    "dg2": sb(160, I32), "Bn": sb(128, F32), "An": sb(32, F32),
+    "Bn": sb(160, F32), "AS2": sb(WW, F32), "AV2": sb(WW, BF), "Z0f": sb(144, F32),
+    "H0h": sb(144, "float16"), "H1h": sb(144, "float16"),
     "WE": sb(160, BF), "WO": sb(160, BF), "BO": sb(128, BF), "TRI": sb(128, BF), "ZS": sb(144, BF),
     "ZSf": sb(144, F32), "Z0": sb(144, BF), "Ib": sb(128, BF), "If": sb(128, F32),
     "I16": sb(128, BF), "I256": sb(128, BF), "MM": sb(1408, BF), "PM": sb(1152, BF),
@@ -40,19 +42,20 @@ SCRATCH = {
     "cmp": sb(256, BF), "eu": sb(16, U16), "gve": sb(256, U16),
     "ZZ": sb(608, F32), "tt": sb(256, BF), "want": sb(304, BF), "rank": sb(304, BF), "o304": sb(304, BF),
     "ob": sb(256, F32), "lat": sb(256, F32), "w16": sb(16, F32), "obu": sb(16, U16),
-    "tmn": sb(256, BF), "cg": sb(256, F32), "TT": sb(256, F32), "wl": sb(256, U16), "wi": sb(224, U16),
+    "tmn": sb(256, BF), "cg": sb(256, "float16"), "TT": sb(256, F32), "wl": sb(256, U16), "wi": sb(224, U16),
     "ASb": sb(G, BF), "SW": sb(448, F32), "ca": sb(4, F32), "lz": sb(12, U16), "l2": sb(192, F32),
     "uo": sb(12, F32), "lu": sb(4, U16), "lo": sb(12, U16), "lt": sb(12, U16),
     "nco": sb(48, F32), "fl": sb(48, BF), "E": sb(1200, BF), "EO": sb(1200, BF), "gr": sb(4, F32),
     "x48": sb(48, BF), "c48": sb(48, F32),
     "xe": sb(224, BF), "re_": sb(224, BF), "t2": sb(224, BF), "snd": sb(672, BF), "land": sb(672, BF),
-    "ti": sb(224, BF), "nf": sb(224, BF), "qm": sb(224, F32),
+    "ti": sb(224, BF), "nf": sb(224, BF), "qm": sb(224, "float16"),
     "yw_": sb(112, F32), "yc_": sb(160, F32),
     "pa": ("psum", [128, 512], F32), "pb": ("psum", [128, 512], F32), "pc": ("psum", [128, 512], F32),
     "pd": ("psum", [128, 512], F32), "pe": ("psum", [128, 512], F32), "pf": ("psum", [128, 512], F32),
     "pg": ("psum", [128, 512], F32), "ph": ("psum", [128, 512], F32),
 }
-DMAS = ["d_aw", "d_x0", "d_gv", "d_ex", "d_c0", "d_c1", "d_y0", "d_y1", "d_yf", "d_yw", "d_yc"]
+DMAS = ["d_aw", "d_x0", "d_gv", "d_ex", "d_c0", "d_c1", "d_y0", "d_y1", "d_yf", "d_yw", "d_yc",
+        "d_zAS", "d_zAV", "d_zAV2", "d_zAV3"]
 SEMAPHORES = ["sV", "sA", "sP", "sG", "snt", "arr0", "arr1", "arr2"] + DMAS
 PARTS = ("MM", "PM", "acca", "accv", "TT", "lt0", "lt1", "lt2", "NC0", "NC1", "NC2", "NC3", "NC4", "ZZd", "CCb",
          "CCi", "Cd", "EO", "ca", "junk", "EQ", "want")
@@ -195,11 +198,12 @@ def rank_program(g, core, T, topo):
     ts(T.dg[:, 0:128], T.xr[:, 0:128], col(10), A.mult, "xr c10", "dga", -0.4921875, A.add)
     ts(T.dg[:, 128:160], T.xr[:, 0:32], col(11), A.mult, "xr c11", "dgb", -0.4921875, A.add)
     cp(T.dgi[:], T.dg[:], "dga dgb", "dgi")
-    ts(T.dg2[:], T.dgi[:], 3, A.bitwise_and, "dgi", "dg2")
-    ts(T.Bn[:], T.dg2[:, 0:128], -0.0625, A.mult, "dg2", "Bn", -15.0625, A.add)
-    ts(T.An[:], T.dg2[:, 128:160], -0.0625, A.mult, "dg2", "An")
+    ts(T.dgi[:], T.dgi[:], 3, A.bitwise_and, "dgi", "dgi")
+    ts(T.Bn[:, 0:128], T.dgi[:, 0:128], -0.0625, A.mult, "dgi", "Bn", -15.0625, A.add)
+    ts(T.Bn[:, 128:160], T.dgi[:, 128:160], -0.0625, A.mult, "dgi", "An")
     for h in range(20):
-        act(T.NC[:, 128 * h:128 * h + 128], T.Bn[:], AF.Identity, "Bn An", "NC%d" % (h // 4), bias=T.An[:, h:h + 1])
+        act(T.NC[:, 128 * h:128 * h + 128], T.Bn[:, 0:128], AF.Identity, "Bn An", "NC%d" % (h // 4),
+            bias=T.Bn[:, 128 + h:129 + h])
     ts(col(12), col(0), 16.0, A.add, "c0", "c12")
     ts(col(13), col(2), 0.0, A.is_equal, "c0", "c13")
     ts(col(14), col(2), 0.0, A.is_gt, "c0", "c14")
@@ -222,7 +226,13 @@ def rank_program(g, core, T, topo):
     iota(T.o304[:], [[0, 304]], 1, 0, "o304")
     iota(T.C[:, 0:D], [[0, D]], -1, 0, "Cd")
     iota(T.C[:, D + W:XW], [[0, 16]], -1, 0, "Cd")
-    iota(T.AS[:], [[0, WW]], 0, 0, "AS")
+    H = WW // 2
+    for n in ("AS", "AV"):
+        iota(T[n][:, 0:H], [[0, H]], 0, 0, n)
+        dma("d_z" + n, T[n][:, H:WW], T[n][:, 0:H], n, n + "z")
+    dma("d_zAV2", T.AV2[:, 0:H], T.AV[:, 0:H], "AV", "AV2")
+    dma("d_zAV3", T.AV2[:, H:WW], T.AV[:, 0:H], "AV", "AV2z")
+    iota(T.AS2[:], [[0, WW]], 0, 0, "AS2")
     iota(T.M192[:, 144:192], [[0, 48]], 0, 0, "M192z")
     iota(T.XT[:, 0:D], [[0, D]], 0, 0, "XTd")
     cp(T.awb[:], T.awi[:], "awi", "awb")
@@ -237,24 +247,28 @@ def rank_program(g, core, T, topo):
     turn(lambda t: T.awb[:, 16 * t:16 * t + 16], "awb", "pe")
     ts(T.ZS[:], T.xr[:, 0:144], col(16), A.is_equal, "xr c16", "ZS")
     ts(T.jw[:], T.xr[:, 0:16], 16.0, A.mult, "xr c0", "jw", col(1), A.add)
+    ts(col(21), col(1), 1.0, A.add, "c0", "c21")
+    ts(T.lat[:, 0:16], T.oh[:], -2 * BIG, A.mult, "oh", "lat")
+    ts(T.I16[:], T.xr[:, 0:128], col(0), A.is_equal, "xr c0", "I16", 16.0, A.mult)
+    ts(T.LC[:, 0:16], T.xr[:, 0:16], col(21), A.is_equal, "xr c21", "LC", BIG, A.mult)
+    ts(T.Ib[:], T.xr[:, 0:128], col(0), A.is_equal, "xr c0", "Ib")
+    tt(T.LC[:, 0:16], T.LC[:, 0:16], T.lat[:, 0:16], A.add, "LC lat", "LC")
     for t in range(7):
         op("V", lambda: v.transpose(T.TT[:, t:t + 218:7], T.pe[:, 32 * t:32 * t + 32]), "pe", "TT")
     cp(T.jb[:], T.jw[:], "jw", "jb")
     ts(T.jh[:], T.jw[:], 0.5, A.add, "jw", "jh")
     cp(T.aws[:, 0:112], T.TT[:, 0:112], "TT", "aws")
-    ts(T.I16[:], T.xr[:, 0:128], col(0), A.is_equal, "xr c0", "I16", 16.0, A.mult)
-    ts(T.Ib[:], T.xr[:, 0:128], col(0), A.is_equal, "xr c0", "Ib")
 
     chunks = [(a, min(a + 512, V)) for a in range(0, V, 512)]
 
-    def enc_v(k):
+    def enc_m(k):
         a, b = chunks[k]
         ts(T.em[:, a:b], T.XT[:, D + a:D + b], 0.0, A.min, "x0", "em%d" % k)
-        scan(T.et[:, a:b], T.NC[:, a:b], T.em[:, a:b], 0.0, A.min, A.mult, "em%d NC%d" % (k, k), "et%d" % k)
 
     def enc_p(k):
         a, b = chunks[k]
-        bk = ("pg", "ph")[k % 2]
+        scan(T.et[:, a:b], T.NC[:, a:b], T.em[:, a:b], 0.0, A.min, A.mult, "em%d NC%d" % (k, k), "et%d" % k)
+        bk = ("pg", "ph", "pb", "pc", "pd")[k]
         mm(grp(T[bk][:, 0:b - a], [(T.Ib[:], T.XT[:, D + a:D + b]), (T.Ib[:], T.et[:, a:b])]), "x0 Ib et%d" % k, bk)
         act(T.XF[:, D + a:D + b], T[bk][:, 0:b - a], AF.Copy, bk, "XFe%d" % k)
 
@@ -267,6 +281,24 @@ def rank_program(g, core, T, topo):
         ts(M(8), T.BO[:], col(19), A.mult, "BO c19", "M8")
         ts(M(1), T.BO[:], col(20), A.mult, "BO c20", "M1")
 
+    def early_a():
+        for n in (16, 32, 64, 128):
+            act(T.LC[:, n:2 * n], T.LC[:, 0:n], AF.Copy, "LC", "LC")
+            if n == 16:
+                act(T.KJ[:], T.xr[:], AF.Identity, "xr", "KJ", bias=1.0 / 256 - 1.0, scale=1.0 / 256)
+            if n == 32:
+                act(T.XF[:, D + V:D + W], T.NC[:, V:W], AF.Identity, "NC4", "XFi", bias=-1.0, scale=-1.0)
+            if n == 64:
+                act(T.If[:], T.Ib[:], AF.Copy, "Ib", "If")
+
+    def late_a():
+        act(T.DL[:], T.NC[:, V:W], AF.Identity, "NC4", "DL", bias=-15.0, scale=-1.0)
+        act(T.L0[:], T.NC[:, V:W], AF.Identity, "NC4", "L0", bias=-1.0, scale=-1.0)
+        for j, c in enumerate((512.0, -512.0)):
+            act(PMm(0, j), T.Ib[:], AF.Copy, "Ib", "PM", scale=c)
+        act(T.I256[:], T.Ib[:], AF.Copy, "Ib", "I256", scale=256.0)
+        act(T.ZSf[:], T.ZS[:], AF.Copy, "ZS", "ZSf")
+
     def consts2a():
         for i, src, n, c in ((0, T.BO[:], "BO", -64.0), (2, M(3), "M3", -1.0), (4, T.BO[:], "BO", -2 * AL),
                              (5, T.BO[:], "BO", 2 * AL), (6, M(3), "M3", AL / 16), (7, M(3), "M3", -AL / 16),
@@ -274,18 +306,15 @@ def rank_program(g, core, T, topo):
             act(M(i), src, AF.Copy, n, "MM", scale=c)
 
     def consts3():
-        ts(col(21), col(1), 1.0, A.add, "c0", "c21")
         ts(col(22), col(1), 15.0, A.is_lt, "c0", "c22", BIG, A.mult)
-        ts(T.lat[:, 0:16], T.oh[:], -2 * BIG, A.mult, "oh", "lat")
-        ts(T.LC[:, 0:16], T.xr[:, 0:16], col(21), A.is_equal, "xr c21", "LC", BIG, A.mult)
-        ts(T.jc[:], T.jw[:], col(22), A.add, "jw c22", "jc")
-        tt(T.LC[:, 0:16], T.LC[:, 0:16], T.lat[:, 0:16], A.add, "LC lat", "LC")
         ts(col(23), col(1), 2.0, A.mult, "c0", "c23", col(4), A.add)
         ts(col(25), col(3), -128.0, A.mult, "c0", "c25", 256.0, A.add)
         ts(col(26), col(3), -112.0, A.mult, "c0", "c26", 256.0, A.add)
         ts(col(24), col(23), 1.0, A.add, "c23", "c24")
+        ts(T.jc[:], T.jw[:], col(22), A.add, "jw c22", "jc")
         for n, c in (("H0", 13), ("H1", 14)):
             ts(T[n + "f"][:], T.xr[:, 0:144], col(24), A.is_equal, "xr c24 c13 c14", n + "f", col(c), A.mult)
+            ts(T[n + "h"][:], T.xr[:, 0:144], col(24), A.is_equal, "xr c24 c13 c14", n + "h", col(c), A.mult)
         ts(col(27), col(15), -1.0, A.mult, "c15", "c27", 112.0, A.add)
         ts(col(29), col(15), 0.0, A.is_gt, "c15", "c29", 128.0, A.mult)
         ts(col(31), col(1), 0.0, A.is_equal, "c0", "c31")
@@ -297,25 +326,19 @@ def rank_program(g, core, T, topo):
         cp(T.exu[:, 0:14], T.exi[:, 0:14], "exi", "exu")
 
     def consts3a():
-        for n in (16, 32, 64, 128):
-            act(T.LC[:, n:2 * n], T.LC[:, 0:n], AF.Copy, "LC", "LC")
-        act(T.KJ[:], T.xr[:], AF.Identity, "xr", "KJ", bias=1.0 / 256 - 1.0, scale=1.0 / 256)
         for n in ("H0", "H1"):
             act(T[n + "b"][:], T[n + "f"][:], AF.Copy, n + "f", n + "b", scale=256.0)
         for h in range(2):
             act(T.CCb[:, 128 * h:128 * h + 128], T.xr[:, 0:128], AF.Identity, "xr c25", "CCb", bias=col(25), scale=-1.0)
+        late_a()
 
     def consts4a():
         for h in range(2):
             act(T.CCi[:, 112 * h:112 * h + 112], T.xr[:, 0:112], AF.Identity, "xr c26", "CCi", bias=col(26), scale=-1.0)
-        act(T.DL[:], T.NC[:, V:W], AF.Identity, "NC4", "DL", bias=-15.0, scale=-1.0)
-        act(T.L0[:], T.NC[:, V:W], AF.Identity, "NC4", "L0", bias=-1.0, scale=-1.0)
-        for k in range(3):
+        for k in range(1, 3):
             for j, c in enumerate((512.0, -512.0)):
-                act(PMm(k, j), PMm(k, 2), AF.Copy, "Ib PM1 PM2", "PM", scale=c)
-        act(T.If[:], T.Ib[:], AF.Copy, "Ib", "If")
-        act(T.I256[:], T.Ib[:], AF.Copy, "Ib", "I256", scale=256.0)
-        act(T.ZSf[:], T.ZS[:], AF.Copy, "ZS", "ZSf")
+                act(PMm(k, j), PMm(k, 2), AF.Copy, "PM1 PM2", "PM", scale=c)
+        act(T.Z0f[:], T.ZS[:], AF.Identity, "ZS c31", "Z0f", scale=col(31))
         act(T.Z0[:], T.ZS[:], AF.Identity, "ZS c31", "Z0", scale=col(31))
 
     def PMm(k, j):
@@ -331,9 +354,15 @@ def rank_program(g, core, T, topo):
     Call = "C Cd C0 C1"
 
     def refresh(s):
+        out = []
         for k in range(s, -1, -1):
-            cp(T.x48[:], T.XF[:].indirect(T.lt[:, 4 * k:4 * k + 3]), "XF lt%d" % k, "x48")
-            cp(T.XF[:].indirect(T.lo[:, 4 * k:4 * k + 3]), T.x48[:], "x48 lo%d" % k, "XF")
+            out.append(lambda k=k: cp(T.x48[:], T.XF[:].indirect(T.lt[:, 4 * k:4 * k + 3]), "XF lt%d" % k, "x48"))
+            out.append(lambda k=k: cp(T.XF[:].indirect(T.lo[:, 4 * k:4 * k + 3]), T.x48[:], "x48 lo%d" % k, "XF"))
+        return out
+
+    def ycm(a, b):
+        mm([(T.pc[:, 0:160], sel(T.ZSf, p), T.C[:, D + 160 * p:D + 160 * p + 160], p == 0, p == 15)
+            for p in range(a, b)], "ZSf " + Call, "pc")
 
     def shuffle(bank, n, terms, cc, r):
         lst = []
@@ -344,20 +373,26 @@ def rank_program(g, core, T, topo):
                 tl += [(Wm[:, 1:129], src[:, 0:n]), (Wm[:, 0:128], src[:, n:2 * n])]
             tl.append((T.Ib[:], cc[:, n * h:n * h + n]))
             lst += grp(T[bank][:, n * h:n * h + n], tl)
-        mm(lst, r + " H0f H1f H0b H1b Ib", bank)
+        mm(lst, r + " H0h H1h H0b H1b Ib", bank)
 
-    def lists(bank, k, out, name, add):
+    def lists(bank, k, out, name, add, between=None):
         for s in range(k):
             op("V", lambda: v.transpose(T.TT[:, s:32 * k:k], T[bank][:, s:32 * k:k]), bank, "TT")
+        if between:
+            between()
         ts(out[:, 0:32 * k], T.TT[:, 0:32 * k], add, A.add, "TT", name)
 
-    def scat_a(L, name, k, rows):
-        for r in rows:
-            act(T.AS[:].indirect(L[:, k * r:k * r + k]), T.ls[:, 0:16 * k], AF.Silu, name + " ls", "AS")
+    WN = {"AS": "AS ASz", "AS2": "AS2 AS2z", "AV": "AV AVz", "AV2": "AV2 AV2z"}
+
+    def scat_a(L, name, k, rows, two):
+        for j, r in enumerate(rows):
+            w = "AS2" if two and (len(rows) - j) % 2 == 1 else "AS"
+            act(T[w][:].indirect(L[:, k * r:k * r + k]), T.ls[:, 0:16 * k], AF.Silu, name + " ls", WN[w])
 
     def scat_v(L, name, k, rows):
         for r in rows:
-            cp(T.AV[:].indirect(L[:, k * r:k * r + k]), T.lv[:, 0:16 * k], name + " lv", "AV")
+            w = "AV2" if r % 2 == 1 and (k == 16 or r < 13) else "AV"
+            cp(T[w][:].indirect(L[:, k * r:k * r + k]), T.lv[:, 0:16 * k], name + " lv", WN[w])
 
     for s in range(3):
         last = s == 2
@@ -365,11 +400,14 @@ def rank_program(g, core, T, topo):
            "TRI BO aws awsd", "pa")
         iota(T.ls[:], [[0, 256]], LEV[s], 0, "ls")
         iota(T.lv[:], [[0, 256]], LEV[s], 0, "lv")
-        if s == 0:
-            iota(T.AV[:], [[0, WW]], 0, 0, "AV")
         if s == 1:
             iota(T.F[:], [[1, D + W]], -D, 0, "F")
+        if s == 0:
+            enc_m(0)
+            enc_m(1)
         scan(T.P[:, 1:129], T.ones[:, 0:128], T.pa[:, 128:256], 0.0, A.mult, A.add, "ones pa P0", "P")
+        if s == 0:
+            enc_m(2)
         for c in range(8, 16):
             act(T.junk[:, 128 * c - 1024:128 * c - 897], T.P[:, 1:128], AF.Sign, "P jh", "junk acca",
                 bias=T.jh[:, c:c + 1], scale=-1.0, accum_out=T.acc[:, c:c + 1])
@@ -377,25 +415,28 @@ def rank_program(g, core, T, topo):
             ts(T.EQ[:, 128 * c:128 * c + 127], T.P[:, 1:128], T.jb[:, c:c + 1], A.is_le, "P jb", "EQ")
         tt(T.pre[:], T.pa[:, 0:128], T.P[:, 0:128], A.add, "pa P P0", "pre")
         scan(T.EO[:, 0:1024], T.EQ[:], T.EQ[:], 0.0, A.add, A.max, "EQ EQs", "EO")
+        if s == 0:
+            early_a()
+            enc_p(0)
         cp(T.bw[:, 0:8], T.EO[:, 126:1024:128], "EO", "bw0")
         ts(T.bw[:, 8:16], T.acc[:, 8:16], 127.0, A.add, "acca", "bw1", 0.5, A.mult)
+        if s == 0:
+            enc_p(1)
         tt(T.cmp[:], T.pre[:].indirect(T.bw[:]), T.xr[:], A.is_le, "pre bw0 bw1 xr", "cmp")
         cp(T.bb[:, 0:8], T.EO[:, 126:1024:128], "EO", "bb0")
         ts(T.bb[:, 8:16], T.acc[:, 8:16], 127.0, A.add, "acca", "bb1", 0.5, A.mult)
         mm([(T.pa[:, 256:272], sel(T.ZS, p), T.cmp[:, p::16], p == 0, False) for p in range(16)], "ZS cmp", "pa")
         mm([(T.pa[:, 256:272], T.I16[:], T.bb[:], False, True)], "I16 bb0 bb1", "pa")
         if s == 0:
+            enc_m(3)
+            enc_m(4)
+            enc_p(2)
             consts2()
-            consts2a()
-            for k in range(2):
-                enc_v(k)
-                enc_p(k)
         cp(T.eu[:], T.pa[:, 256:272], "pa", "eu")
         if s == 0:
-            for k in range(2, 5):
-                enc_v(k)
-                enc_p(k)
-            act(T.XF[:, D + V:D + W], T.NC[:, V:W], AF.Identity, "NC4", "XFi", bias=-1.0, scale=-1.0)
+            enc_p(3)
+            enc_p(4)
+            consts2a()
         cp(T.gve[:], T.gvi[:].indirect(T.eu[:]), "gvi gvd eu", "gve")
         win = T.XF[:, D:XW]
 
@@ -464,33 +505,33 @@ def rank_program(g, core, T, topo):
             consts3a()
         tt(T.q[:], T.pre[:, 0:112], T.aws[:, 0:112], A.mult, "pre aws", "q")
         tt(T.ob[:], T.pc[:, 0:256], T.ZZ[:, 304:560], A.min, "pc ZOa ZOb", "ob")
-        scan(T.lat[:], T.LC[:], T.ob[:], 0.0, A.add, A.max, "LC ob", "lat")
-        tt(T.w16[:], T.lat[:, 15::16], T.jc[:], A.max, "lat jc", "w16")
         ts(T.rem[:], T.q[:], 256.5, A.is_gt, "q", "rem", float(LEV[s]), A.mult)
+        scan(T.lat[:], T.LC[:], T.ob[:], 0.0, A.add, A.max, "LC ob", "lat")
+        ts(T.tt[:], T.pd[:, 0:256], 0.0, A.is_equal, "pd", "tt", 1.5, A.add)
+        tt(T.w16[:], T.lat[:, 15::16], T.jc[:], A.max, "lat jc", "w16")
+        tt(T.want[:, 0:160], T.pb[:, 0:160], T.tt[:, 0:160], A.is_gt, "pb tt", "want")
         ts(T.obu[:], T.w16[:], col(22), A.subtract, "w16 c22", "obu")
+        tt(T.want[:, 160:256], T.pg[:, 160:256], T.tt[:, 160:256], A.is_gt, "pg tt", "want")
         act(T.cg[:], T.C[:].indirect(T.obu[:]), AF.Copy, Call + " obu", "cg")
         act(T.ZZ[:, 0:256], T.ph[:, 0:256], AF.Identity, "ph", "ZU", bias=zb)
         tt(T.tmn[:], T.C[:].indirect(T.obu[:]), T.KJ[:], A.min, Call + " obu KJ", "tmn")
-        shuffle("pf", 128, [("b", T.tmn), ("f", T.cg)], T.CCb, "tmn cg CCb")
-        ts(T.tt[:], T.pd[:, 0:256], 0.0, A.is_equal, "pd", "tt", 1.5, A.add)
-        tt(T.want[:, 0:160], T.pb[:, 0:160], T.tt[:, 0:160], A.is_gt, "pb tt", "want")
-        tt(T.want[:, 160:256], T.pg[:, 160:256], T.tt[:, 160:256], A.is_gt, "pg tt", "want")
+        shuffle("pf", 128, [("b", T.tmn), ("h", T.cg)], T.CCb, "tmn cg CCb")
         scan(T.rank[:], T.o304[:], T.want[:], 0.0, A.mult, A.add, "o304 want wantd", "rank")
-        if s == 0:
-            consts4a()
         for t in range(3):
             act(T.junk[:, 1152 + 304 * t:1456 + 304 * t], T.rank[:], AF.Sign, "rank jh", "junk ca",
                 bias=T.jh[:, t:t + 1], scale=-1.0, accum_out=T.ca[:, t:t + 1])
         mm(grp(T.pc[:, 0:256], [(M(4), mx), (M(6), go), (M(5), T.RM[:]), (M(7), T.RO[:]), (M(10), T.want[:, 0:256])]),
            Sall + " RMa RMb ROa ROb want", "pc")
         cp(T.XF[:].indirect(T.obu[:]), T.S[:, 14::16], Sall + " obu", XFall)
-        lists("pf", 8, T.wl, "wl", 256.0)
-        scat_a(T.wl, "wl", 16, range(BIND_ACT[s]))
+        lists("pf", 8, T.wl, "wl", 256.0, lambda: tt(T.SW[:, 0:256], T.pc[:, 0:256], T.ZZ[:, 304:560], A.min,
+                                                     "pc ZOa ZOb", "SW0"))
+        if s == 0:
+            consts4a()
+        scat_a(T.wl, "wl", 16, range(BIND_ACT[s]), True)
         for j in range(3):
             ts(T.lz[:, 3 * j:3 * j + 3], T.ca[:, 0:3], 304.0, A.add, "ca", "lz%d" % j, 0.5, A.mult)
         ts(T.lz[:, 9:12], T.ca[:, 0:3], 912.0, A.add, "ca", "lz3", 0.5, A.mult)
         tt(T.SW[:, 256:448], T.ZZ[:].indirect(T.lz[:]), T.M192[:], A.add, "ZOa ZOb ZU ZZd lz0 lz1 lz2 lz3 M192 M192z", "SW1")
-        tt(T.SW[:, 0:256], T.pc[:, 0:256], T.ZZ[:, 304:560], A.min, "pc ZOa ZOb", "SW0")
         scan(T.l2[:], T.LC[:, 0:192], T.SW[:, 256:448], 0.0, A.add, A.max, "LC SW1", "l2")
         lo, lt = T.lo[:, 4 * s:4 * s + 3], T.lt[:, 4 * s:4 * s + 3]
         ts(lo, T.l2[:, 159:192:16], col(22), A.subtract, "l2 c22", "lo%d" % s)
@@ -498,22 +539,31 @@ def rank_program(g, core, T, topo):
         ts(T.uo[:, 0:3], T.l2[:, 15:144:64], col(22), A.subtract, "l2 c22", "uo0", 8192.0, A.subtract)
         ts(T.uo[:, 4:7], T.l2[:, 159:192:16], col(22), A.subtract, "l2 c22", "uo1")
         ts(T.nco[:], T.C[:].indirect(lo), 0.0, A.is_lt, Call + " lo%d" % s, "nco", 8192.0, A.mult)
-        tt(T.fl[:], T.C[:].indirect(T.lu[:, 0:3]), T.nco[:], A.is_ge, Call + " lu nco", "fl")
-        mm(grp(T.pa[:, 288:291], [(sel(T.ZS, p), T.fl[:, p::16]) for p in range(16)]), "ZS fl", "pa")
         for t in range(3):
             n = 304 + 48 * t
             ts(T.E[:, 400 * t:400 * t + n], T.SW[:, 0:n], T.uo[:, t:t + 1], A.is_equal, "SW0 SW1 uo0", "E%d" % t,
                -1.0, A.mult)
+            if t == 0:
+                tt(T.fl[:], T.C[:].indirect(T.lu[:, 0:3]), T.nco[:], A.is_ge, Call + " lu nco", "fl")
+                mm(grp(T.pa[:, 288:291], [(sel(T.ZS, p), T.fl[:, p::16]) for p in range(16)]), "ZS fl", "pa")
         for t in range(3):
             n = 304 + 48 * t
             Et = T.E[:, 400 * t:400 * t + n]
             scan(T.EO[:, 400 * t + 400 - n:400 * t + 400], Et, Et, 0.0, A.min, A.min, "E%d" % t, "EO")
-        tt(T.uo[:, 8:11], T.uo[:, 0:3], T.uo[:, 4:7], A.subtract, "uo0 uo1", "uo2")
+        if last:
+            turn(lambda t: T.rem[:, t:112:7], "rem", "pe")
+        cp(T.c48[:], T.C[:].indirect(lo), Call + " lo%d" % s, "c48")
         tt(T.gr[:, 0:3], T.pa[:, 288:291], T.EO[:, 399::400], A.is_equal, "pa EO", "gr")
+        tt(T.uo[:, 8:11], T.uo[:, 0:3], T.uo[:, 4:7], A.subtract, "uo0 uo1", "uo2")
         for t in range(3):
             ts(T.lt[:, 4 * s + t:4 * s + t + 1], T.gr[:, t:t + 1], T.uo[:, 8 + t:9 + t], A.mult, "gr uo1 uo2",
                "lt%d" % s, T.uo[:, 4 + t:5 + t], A.add)
-        refresh(s)
+        move = [lambda: tt(T.nco[:], T.C[:].indirect(lt), T.c48[:], A.max, Call + " lt%d c48" % s, "nco"),
+                lambda: cp(T.C[:].indirect(lt), T.nco[:], "nco lt%d" % s, Call)]
+        for f in refresh(s):
+            f()
+            if move:
+                move.pop(0)()
         cp(T.xe[:], win.indirect(T.exu[:, 0:14]), "XF exu", "xe")
         ts(T.re_[:], T.xe[:], MAGIC, A.add, "xe", "re", MAGIC, A.subtract)
         la, lb = [], []
@@ -523,9 +573,9 @@ def rank_program(g, core, T, topo):
             lb += grp(T.ph[:, a:b], [(PMm(d % 3, 2), T.re_[:, a:b])])
         mm(la, "PM xe re", "pg")
         mm(lb, "PM1 PM2 Ib re", "ph")
-        cp(T.c48[:], T.C[:].indirect(lo), Call + " lo%d" % s, "c48")
-        tt(T.nco[:], T.C[:].indirect(lt), T.c48[:], A.max, Call + " lt%d c48" % s, "nco")
-        cp(T.C[:].indirect(lt), T.nco[:], "nco lt%d" % s, Call)
+        tt(T.ti[:], T.C[:, D + V:D + W], T.KJ[:, 0:224], A.min, "C KJ", "ti")
+        if last:
+            op("V", lambda: v.transpose(T.remT[:], T.pe[:, 0:224]), "pe", "remT")
         tt(T.t2[:], T.pg[:, 0:224], T.DL[:], A.min, "pg DL", "t2")
         tt(T.snd[:, 224 * s:224 * s + 224], T.ph[:, 0:224], T.t2[:], A.add, "ph t2", "snd%d" % s)
         deps("G", ["snd%d" % s], [])
@@ -543,41 +593,44 @@ def rank_program(g, core, T, topo):
             tops["arr%d" % s] = tops.get("arr%d" % s, 0) + n
         g.remote_dma_fused(trs, local_sem=T.sem.snt)
         lastw["land%d" % s] = ("arr%d" % s, tops["arr%d" % s])
-        tt(T.ti[:], T.C[:, D + V:D + W], T.KJ[:, 0:224], A.min, "C KJ", "ti")
         mm(grp(T.pg[:, 0:224], [(T.If[:], T.C[:, D + V:D + W]), (T.I256[:], T.ones[:]), (T.Ib[:], T.ones[:]),
                                 (T.I256[:], T.ti[:])]), "I256 If Ib ones ti C", "pg")
+        cp(T.XT[:, 0:D + V].indirect(T.obu[:]), T.S[:, 14::16], Sall + " obu XTd", "x0")
         if last:
-            turn(lambda t: T.rem[:, t:112:7], "rem", "pe")
-            for k in range(2, -1, -1):
-                cp(T.c48[:], T.F[:].indirect(T.lt[:, 4 * k:4 * k + 3]), "F lt%d" % k, "c48")
-                cp(T.F[:].indirect(T.lo[:, 4 * k:4 * k + 3]), T.c48[:], "c48 lo%d" % k, "F")
-            dma("d_yf", T.yf[:], T.F[0:128:16, D:D + W], "F", "")
-            op("V", lambda: v.transpose(T.remT[:], T.pe[:, 0:224]), "pe", "remT")
+            dma("d_y0", T.yx[:, 0:V], T.XT[:, D:D + V], "x0", "")
+            ycm(0, 8)
         scat_v(T.wl, "wl", 16, range(BIND_ACT[s], 16))
         Ln = T.land[:, 224 * s:224 * s + 224]
         Lp, lpn = (T.L0[:], "L0") if s == 0 else (T.land[:, 224 * s - 224:224 * s], "land%d" % (s - 1))
         tt(T.nf[:], Ln, Lp, A.not_equal, "land%d %s" % (s, lpn), "nf")
         tt(T.qm[:], T.pg[:, 0:224], T.nf[:], A.mult, "pg nf", "qm")
-        shuffle("pf", 112, [("f", T.qm)], T.CCi, "qm CCi")
-        cp(T.XT[:, 0:D + V].indirect(T.obu[:]), T.S[:, 14::16], Sall + " obu XTd", "x0")
+        shuffle("pf", 112, [("h", T.qm)], T.CCi, "qm CCi")
         if last:
-            dma("d_y0", T.yx[:, 0:V], T.XT[:, D:D + V], "x0", "")
             ts(T.re_[:], Ln, MAGIC, A.add, "land2", "re", MAGIC, A.subtract)
             mm(grp(T.ph[:, 0:224], [(PMm(0, 2), Ln), (PMm(0, 1), Ln), (PMm(0, 0), T.re_[:])]), "PM Ib land2 re", "ph")
         lists("pf", 7, T.wi, "wi", -1.0)
-        scat_a(T.wi, "wi", 14, range(IMP_ACT[s]))
+        scat_a(T.wi, "wi", 14, range(IMP_ACT[s]), False)
         for h in range(2):
             act(T.ASb[:, 896 * h:896 * h + 896], T.AS[:, WK + 896 * h:WK + 896 * h + 896], AF.Copy, "AS", "ASb%d" % h)
         if last:
             ts(T.XT[:, D + V:D + W], T.ph[:, 0:224], -1.0, A.max, "ph", "XTi")
             dma("d_y1", T.yx[:, V:W], T.XT[:, D + V:D + W], "XTi", "")
-            mm(grp(T.pc[:, 0:160], [(sel(T.ZSf, p), T.C[:, D + 160 * p:D + 160 * p + 160]) for p in range(16)]),
-               "ZSf " + Call, "pc")
-        scat_v(T.wi, "wi", 14, range(IMP_ACT[s], 16))
+        side = []
         if last:
-            act(T.yc_[:], T.pc[:, 0:160], AF.Copy, "pc", "yc")
-            dma("d_yc", T.yc[:], T.yc_[:], "yc", "")
-
+            for k in range(2, -1, -1):
+                side.append(lambda k=k: cp(T.c48[:], T.F[:].indirect(T.lt[:, 4 * k:4 * k + 3]), "F lt%d" % k, "c48"))
+                side.append(lambda k=k: cp(T.F[:].indirect(T.lo[:, 4 * k:4 * k + 3]), T.c48[:], "c48 lo%d" % k, "F"))
+            side.append(lambda: dma("d_yf", T.yf[:], T.F[0:128:16, D:D + W], "F", ""))
+        else:
+            side.append(lambda: cp(T.XF[:, D + V:D + W], Ln, "land%d" % s, "XF"))
+            side += refresh(s)[:-2]
+        for r in range(IMP_ACT[s], 16):
+            if side and len(side) >= 16 - r - 2 * last:
+                side.pop(0)()
+            scat_v(T.wi, "wi", 14, [r])
+        for f in side:
+            f()
+        if last:
             def piece(Wn, p):
                 return Wn[:, WK + 112 * p:WK + 112 * p + 112]
         else:
@@ -586,23 +639,32 @@ def rank_program(g, core, T, topo):
         o = T.pd[:, 0:112]
         if not last:
             mm([(o, T.Ib[:], T.rem[:], True, False)], "rem Ib", "pd")
+        mm([(o, sel(T.Z0f, p), piece(T.AS2, p), last and p == 0, False) for p in range(16)], "Z0f AS2", "pd")
+        if last:
+            ycm(8, 16)
+            mm([(T.pd[:, 16 * t:16 * t + 16], T.If[:], T.remT[:, 32 * t:32 * t + 16], False, False) for t in range(7)],
+               "remT If", "pd")
+            act(T.yc_[:], T.pc[:, 0:160], AF.Copy, "pc", "yc")
+            dma("d_yc", T.yc[:], T.yc_[:], "yc", "")
+        mm([(o, sel(T.Z0, p), piece(T.AV2, p), False, False) for p in range(16)], "Z0 AV2", "pd")
         for h in range(2):
             if last:
-                lst = [(o, sel(T.Z0, p), T.ASb[:, 112 * p:112 * p + 112], p == 0, False) for p in range(8 * h, 8 * h + 8)]
+                lst = [(o, sel(T.Z0, p), T.ASb[:, 112 * p:112 * p + 112], False, False) for p in range(8 * h, 8 * h + 8)]
             else:
                 lst = [(T.pd[:, 56 * h:56 * h + 56], sel(T.Z0, p), T.ASb[:, 896 * h + p:896 * h + 896:16], False, False)
                        for p in range(16)]
+            if h == 1 and AV_FIRST:
+                mm([(o, sel(T.Z0, p), piece(T.AV, p), False, False) for p in range(16)], "Z0 AV", "pd")
+                lst[-1] = lst[-1][0:4] + (True,)
             mm(lst, "Z0 ASb%d" % h, "pd")
-        if last:
-            mm([(T.pd[:, 16 * t:16 * t + 16], T.If[:], T.remT[:, 32 * t:32 * t + 16], False, False) for t in range(7)],
-               "remT If", "pd")
-        mm([(o, sel(T.Z0, p), piece(T.AV, p), False, p == 15) for p in range(16)], "Z0 AV", "pd")
+        if not AV_FIRST:
+            mm([(o, sel(T.Z0, p), piece(T.AV, p), False, p == 15) for p in range(16)], "Z0 AV", "pd")
         if last:
             ts(T.yw_[:], o, 0.75 * LEV[s], A.is_gt, "pd", "yw")
             dma("d_yw", T.yw[:], T.yw_[:], "yw", "")
         else:
-            cp(T.XF[:, D + V:D + W], Ln, "land%d" % s, "XF")
-            refresh(s)
+            for f in refresh(s)[-2:]:
+                f()
             ts(T.aws[:, 0:112], o, 0.75 * LEV[s], A.is_gt, "pd", "aws")
     for k in tops:
         need("S", (k, tops[k]))

@@ -1,65 +1,68 @@
 from concourse.bass import DstId, RemoteDMATransfer
 from concourse.mybir import AluOpType as A, AxisListType, ActivationFunctionType as AF
 
-V, W, G, NI = 2336, 2560, 1792, 224
+V, W, G = 2336, 2560, 1792
 D = 304
-XW = D + W + 16
-WK = 257
-WW = 2064
-BIG = float(2 ** 21)
+XW = D + W + 64
+WK = 256
+WW = WK + G
 MAGIC = 12582912.0
-AL = 65536.0
-LEV = (16, 128, 1024)
-AV_FIRST = False
-BIND_ACT, IMP_ACT = (13, 13, 14), (6, 6, 6)
+K1, K2 = 65536.0, 131072.0
+ZB = float(D - 623925)
+SH = 1024.0
+LEV = (16, 512, 16384)
+BIND_ACT = (24, 24, 24)
+IMP_ACT = (6, 6, 6)
+AV_ONLY = 3
+GA = 80
+EM_ACT = (1, 3)
 
 
 def sb(n, dt):
     return ("sbuf", [128, n], dt)
 
 
-F32, BF, I32, U16 = "float32", "bfloat16", "int32", "uint16"
+F32, BF, F16, I32, U16 = "float32", "bfloat16", "float16", "int32", "uint16"
 SCRATCH = {
-    "awi": sb(112, I32), "awb": sb(112, BF), "aws": sb(128, BF),
+    "awi": sb(112, I32), "awb": sb(112, BF), "aws": sb(128, BF), "sc1": sb(136, BF),
     "gvi": sb(2048, I32), "ci": sb(W, I32), "exi": sb(16, I32), "exu": sb(16, U16),
-    "XF": sb(XW, BF), "XT": sb(D + W, BF), "C": sb(XW, F32), "F": sb(D + W, F32),
-    "NC": sb(W, BF), "em": sb(V, BF), "et": sb(V, BF),
-    "AV": sb(WW, BF), "AS": sb(WW, F32), "lv": sb(256, BF), "ls": sb(256, F32),
-    "GG": sb(4096, BF), "S": sb(4096, BF), "SM": sb(1536, BF), "RM": sb(256, BF), "RO": sb(256, BF),
-    "pi": sb(8, I32), "co_": sb(32, F32), "xr": sb(256, F32), "mg": sb(128, F32),
+    "XF": sb(XW, BF), "XT": sb(D + W, BF), "C": sb(XW, F32), "F": sb(XW, F32),
+    "em": sb(V, BF), "et": sb(V, BF),
+    "AV": sb(WW, BF), "AV2": sb(WW, BF), "AS": sb(WW, F32), "AS2": sb(WW, F32), "ASb": sb(G, BF),
+    "ASc": sb(G, BF), "C16": sb(W, F16), "asn": sb(112, F32),
+    "lv": sb(224, BF), "ls": sb(224, F32),
+    "GG": sb(4096, BF), "S": sb(4864, BF), "SM": sb(2048, BF), "RM": sb(256, BF), "RO": sb(256, BF),
+    "pi": sb(8, I32), "co_": sb(48, F32), "xb": sb(256, BF), "mg": sb(512, BF), "JR": sb(512, BF),
     "oh": sb(16, F32), "pw": sb(32, F32), "t16": sb(32, F32), "dg": sb(160, F32), "dgi": sb(160, I32),
-    "Bn": sb(160, F32), "AS2": sb(WW, F32), "AV2": sb(WW, BF), "Z0f": sb(144, F32),
-    "H0h": sb(144, "float16"), "H1h": sb(144, "float16"),
-    "WE": sb(160, BF), "WO": sb(160, BF), "BO": sb(128, BF), "TRI": sb(128, BF), "ZS": sb(144, BF),
-    "ZSf": sb(144, F32), "Z0": sb(144, BF), "Ib": sb(128, BF), "If": sb(128, F32),
-    "I16": sb(128, BF), "I256": sb(128, BF), "MM": sb(1408, BF), "PM": sb(1152, BF),
-    "H0f": sb(144, F32), "H1f": sb(144, F32), "H0b": sb(144, BF), "H1b": sb(144, BF),
-    "ones": sb(224, BF), "jw": sb(16, F32), "jb": sb(16, BF), "jh": sb(16, F32), "jc": sb(16, F32),
-    "LC": sb(256, F32), "KJ": sb(256, F32), "CCb": sb(256, BF), "CCi": sb(224, BF),
-    "M192": sb(192, F32), "DL": sb(224, BF), "L0": sb(224, BF),
-    "P": sb(144, BF), "pre": sb(128, F32), "q": sb(112, F32), "rem": sb(112, BF), "remT": sb(224, F32),
-    "EQ": sb(1024, BF), "junk": sb(2064, BF), "acc": sb(16, F32), "bw": sb(16, U16), "bb": sb(16, BF),
-    "cmp": sb(256, BF), "eu": sb(16, U16), "gve": sb(256, U16),
-    "ZZ": sb(608, F32), "tt": sb(256, BF), "want": sb(304, BF), "rank": sb(304, BF), "o304": sb(304, BF),
-    "ob": sb(256, F32), "lat": sb(256, F32), "w16": sb(16, F32), "obu": sb(16, U16),
-    "tmn": sb(256, BF), "cg": sb(256, "float16"), "TT": sb(256, F32), "wl": sb(256, U16), "wi": sb(224, U16),
-    "ASb": sb(G, BF), "SW": sb(448, F32), "ca": sb(4, F32), "lz": sb(12, U16), "l2": sb(192, F32),
-    "uo": sb(12, F32), "lu": sb(4, U16), "lo": sb(12, U16), "lt": sb(12, U16),
-    "nco": sb(48, F32), "fl": sb(48, BF), "E": sb(1200, BF), "EO": sb(1200, BF), "gr": sb(4, F32),
-    "x48": sb(48, BF), "c48": sb(48, F32),
-    "xe": sb(224, BF), "re_": sb(224, BF), "t2": sb(224, BF), "snd": sb(672, BF), "land": sb(672, BF),
-    "ti": sb(224, BF), "nf": sb(224, BF), "qm": sb(224, "float16"),
+    "Bp": sb(512, BF), "An": sb(32, F32), "NC": sb(288, BF),
+    "WE": sb(160, BF), "WO": sb(160, BF), "BO": sb(512, BF), "TRI": sb(128, BF), "ZS": sb(144, BF), "Zd": sb(144, BF),
+    "ZSh": sb(144, F16), "Z8h": sb(144, F16), "Z0h": sb(144, F16), "Z0": sb(144, BF),
+    "If": sb(128, F32), "Ib": sb(128, BF), "IL": sb(128, BF), "ILf": sb(128, F32), "I8h": sb(256, F16),
+    "MM": sb(1408, BF), "PM": sb(1024, BF),
+    "H0h": sb(144, F16), "H1h": sb(144, F16), "H0b": sb(144, BF), "H1b": sb(144, BF),
+    "ones": sb(304, BF), "hv": sb(4, BF), "zr": sb(256, BF), "neg1": sb(224, BF), "k4": sb(224, BF),
+    "jh": sb(4, F32), "dd": sb(8, F32), "jr": sb(256, F32),
+    "KJ": sb(224, BF), "CCb": sb(128, BF), "CCi": sb(224, BF), "M192": sb(144, BF),
+    "EQ": sb(2048, BF), "pre": sb(128, F32), "sg": sb(112, BF), "remT": sb(224, F32),
+    "bw": sb(16, U16), "cmp": sb(256, BF), "eu": sb(16, U16), "gve": sb(256, U16),
+    "ob": sb(256, F16), "obu": sb(16, U16), "cg": sb(256, F16), "tm": sb(256, BF),
+    "TT": sb(256, F32), "TI": sb(224, F32), "wl": sb(256, U16), "wi": sb(224, U16),
+    "ab": sb(256, BF), "want": sb(304, BF), "rank": sb(304, BF), "ca": sb(4, F32),
+    "SW": sb(400, F16), "lz": sb(8, U16), "cs": sb(112, BF), "LU": sb(8, U16),
+    "cc": sb(112, F32), "mn": sb(48, F16), "mxc": sb(48, F32), "E": sb(1056, BF), "EO": sb(1056, F16),
+    "sel": sb(8, F32), "LT": sb(24, U16), "x48": sb(48, BF), "c48": sb(48, F32),
+    "snd": sb(672, BF), "land": sb(672, BF), "fn": sb(672, BF), "Cm": sb(224, F16), "ti": sb(224, BF), "wS": sb(224, BF),
     "yw_": sb(112, F32), "yc_": sb(160, F32),
-    "pa": ("psum", [128, 512], F32), "pb": ("psum", [128, 512], F32), "pc": ("psum", [128, 512], F32),
-    "pd": ("psum", [128, 512], F32), "pe": ("psum", [128, 512], F32), "pf": ("psum", [128, 512], F32),
-    "pg": ("psum", [128, 512], F32), "ph": ("psum", [128, 512], F32),
 }
-DMAS = ["d_aw", "d_x0", "d_gv", "d_ex", "d_c0", "d_c1", "d_y0", "d_y1", "d_yf", "d_yw", "d_yc",
-        "d_zAS", "d_zAV", "d_zAV2", "d_zAV3"]
-SEMAPHORES = ["sV", "sA", "sP", "sG", "snt", "arr0", "arr1", "arr2"] + DMAS
-PARTS = ("MM", "PM", "acca", "accv", "TT", "lt0", "lt1", "lt2", "NC0", "NC1", "NC2", "NC3", "NC4", "ZZd", "CCb",
-         "CCi", "Cd", "EO", "ca", "junk", "EQ", "want")
+PART = {}
+for _n in ("oh", "pw", "t16", "An", "jh", "dd", "ca", "sel"):
+    PART[_n] = (sum(x[1] for x in PART.values()), SCRATCH.pop(_n)[1][1])
+SCRATCH["fs"] = sb(sum(x[1] for x in PART.values()), F32)
 PSUMS = ("pa", "pb", "pc", "pd", "pe", "pf", "pg", "ph")
+for _b in PSUMS:
+    SCRATCH[_b] = ("psum", [128, 512], F32)
+DMAS = ["d_aw", "d_x0", "d_gv", "d_ex", "d_c0", "d_c1", "d_y0", "d_y1", "d_yf", "d_yw", "d_yc", "d_zS", "d_zV", "d_as"]
+SEMAPHORES = ["sV", "sA", "sP", "sG", "snt", "arr0", "arr1", "arr2"] + DMAS
 
 
 def rank_program(g, core, T, topo):
@@ -69,7 +72,24 @@ def rank_program(g, core, T, topo):
     eng = {"V": g.vector, "A": g.scalar, "P": g.tensor, "G": g, "S": g.sync}
     cnt = {"V": 0, "A": 0, "P": 0, "G": 0}
     seen = {e: {} for e in eng}
-    lastw, readers, tops = {}, {}, {}
+    uses, tops = {}, {}
+
+    def B(n, a=0, b=None, st=1):
+        if n in PART:
+            return B("fs", PART[n][0] + a, PART[n][0] + (PART[n][1] if b is None else b), st)
+        b = SCRATCH[n][1][1] if b is None else b
+        return (T[n][:, a:b:st] if st > 1 else T[n][:, a:b], n, a, b, st, None)
+
+    def rows(n, part, a, b):
+        return (T[n][part, a:b], n, a, b, 1, None)
+
+    def X(win, off):
+        return (win[0].indirect(off[0]),) + win[1:5] + (off,)
+
+    def meet(p, q):
+        if p[0] >= q[1] or q[0] >= p[1]:
+            return False
+        return p[2] != q[2] or (p[0] - q[0]) % p[2] == 0
 
     def need(e, tok):
         if seen[e].get(tok[0], 0) < tok[1]:
@@ -77,508 +97,510 @@ def rank_program(g, core, T, topo):
             seen[e][tok[0]] = tok[1]
 
     def deps(e, r, w):
-        own = "s" + e
-        want = {}
-        toks = []
-        for n in r:
-            if n in lastw and not (e == "P" and lastw[n][0] == own):
-                toks.append(lastw[n])
-            if n in PSUMS:
-                toks += [t for t in readers.get(n, []) if t[0] != own]
-        for n in w:
-            part = n in PARTS
-            if n in lastw and not (lastw[n][0] == own and (part or e == "P")):
-                toks.append(lastw[n])
-            toks += [t for t in readers.get(n, []) if not (e == "P" and t[0] == own)]
-        for s, v in toks:
-            want[s] = max(want.get(s, 0), v)
+        own, want = "s" + e, {}
+        for vs, wr in ((r, False), (w, True)):
+            for x in vs:
+                for (sem, w2, sp), n in uses.get(x[1], {}).items():
+                    if sem == own and e == "P":
+                        continue
+                    if (x[1] in PSUMS and sem != own) or ((wr or w2) and meet(sp, x[2:5])):
+                        want[sem] = max(want.get(sem, 0), n)
         for s in want:
             need(e, (s, want[s]))
 
     def done(tok, r, w):
         tops[tok[0]] = tok[1]
-        for n in r:
-            readers.setdefault(n, []).append(tok)
-        for n in w:
-            lastw[n] = tok
-            readers[n] = []
+        for vs, wr in ((r, False), (w, True)):
+            for x in vs:
+                uses.setdefault(x[1], {})[(tok[0], wr, x[2:5])] = tok[1]
+
+    def views(r, w):
+        r = [x for x in r if isinstance(x, tuple)]
+        return r + [x[5] for x in r + w if x[5]], w
 
     def op(e, fn, r, w):
-        r, w = r.split(), w.split()
+        r, w = views(r, w)
         deps(e, r, w)
         ins = fn()
         cnt[e] += 1
         ins.then_inc(T.sem["s" + e], 1)
         done(("s" + e, cnt[e]), r, w)
 
-    def mm(lst, r, w):
+    def ap(x):
+        return x[0] if isinstance(x, tuple) else x
+
+    def mm(lst):
         def f():
             ins = None
             for o, l, x, s0, s1 in lst:
-                ins = g.tensor.matmul(o, l, x, s0, s1)
+                ins = g.tensor.matmul(o[0], l[0], x[0], s0, s1)
             return ins
-        op("P", f, r, w)
+        op("P", f, [x for m in lst for x in m[1:3]], [m[0] for m in lst])
 
     def grp(o, terms):
         return [(o, l, x, i == 0, i == len(terms) - 1) for i, (l, x) in enumerate(terms)]
 
-    def dma(sem, o, i, r, w, e="S"):
-        r, w = r.split(), w.split()
+    def dma(sem, o, i, e="S"):
+        r, w = views([i], [o] if isinstance(o, tuple) else [])
         deps(e, r, w)
-        eng[e].dma_start(o, i).then_inc(T.sem[sem], 16)
+        eng[e].dma_start(ap(o), ap(i)).then_inc(T.sem[sem], 16)
         done((sem, 16), r, w)
 
     v = g.vector
 
-    def ts(o, i, s1, o0, r, w, s2=None, o1=None):
+    def ts(o, i, s1, o0, s2=None, o1=None):
         if o1 is None:
-            op("V", lambda: v.tensor_scalar(o, i, s1, None, o0), r, w)
+            op("V", lambda: v.tensor_scalar(o[0], i[0], ap(s1), None, o0), [i, s1], [o])
         else:
-            op("V", lambda: v.tensor_scalar(o, i, s1, s2, o0, o1), r, w)
+            op("V", lambda: v.tensor_scalar(o[0], i[0], ap(s1), ap(s2), o0, o1), [i, s1, s2], [o])
 
-    def tt(o, a, b, o0, r, w):
-        op("V", lambda: v.tensor_tensor(o, a, b, o0), r, w)
+    def tt(o, a, b, o0):
+        op("V", lambda: v.tensor_tensor(o[0], a[0], b[0], o0), [a, b], [o])
 
-    def cp(o, i, r, w):
-        op("V", lambda: v.tensor_copy(o, i), r, w)
+    def cp(o, i):
+        op("V", lambda: v.tensor_copy(o[0], i[0]), [i], [o])
 
-    def ms(o, c, w):
-        op("V", lambda: v.memset(o, c), "", w)
+    def ms(o, c):
+        op("V", lambda: v.memset(o[0], c), [], [o])
 
-    def scan(o, a, b, init, o0, o1, r, w):
-        op("V", lambda: v.tensor_tensor_scan(o, a, b, init, o0, o1), r, w)
+    def scan(o, a, b, init, o0, o1):
+        op("V", lambda: v.tensor_tensor_scan(o[0], a[0], b[0], init, o0, o1), [a, b], [o])
 
-    def act(o, i, f, r, w, **kw):
-        op("A", lambda: g.scalar.activation(o, i, f, **kw), r, w)
+    def vtr(o, i):
+        op("V", lambda: v.transpose(o[0], i[0]), [i], [o])
 
-    def iota(o, pat, base, cm, w, fl=True):
-        if fl:
-            op("G", lambda: g.iota(o, pat, base, cm, allow_small_or_imprecise_dtypes=True), "", w)
+    def red(o, i):
+        op("V", lambda: v.tensor_reduce(o[0], i[0], AxisListType.X, A.add), [i], [o])
+
+    def act(o, i, f, **kw):
+        acc = [kw["accum_out"]] if "accum_out" in kw else []
+        op("A", lambda: g.scalar.activation(o[0], i[0], f, **{k: ap(x) for k, x in kw.items()}),
+           [i] + [kw[k] for k in ("bias", "scale") if k in kw], [o] + acc)
+
+    def lin(o, i, scale, bias=0.0):
+        act(o, i, AF.Identity, scale=scale, bias=bias)
+
+    def iota(o, pat, base, cm=0):
+        if SCRATCH[o[1]][2] == I32:
+            op("G", lambda: g.iota(o[0], pat, base, cm), [], [o])
         else:
-            op("G", lambda: g.iota(o, pat, base, cm), "", w)
+            op("G", lambda: g.iota(o[0], pat, base, cm, allow_small_or_imprecise_dtypes=True), [], [o])
+
+    def fill(o, c):
+        iota(o, [[0, len(range(o[2], o[3], o[4]))]], c)
 
     def col(i):
-        return T.co_[:, i:i + 1]
+        return B("co_", i, i + 1)
 
     def M(i):
-        return T.MM[:, 128 * i:128 * i + 128]
+        return B("MM", 128 * i, 128 * i + 128)
 
-    dma("d_aw", T.awi[:], T.aw[:], "", "awi")
-    dma("d_x0", T.XT[:, D:D + V], T.x0[:], "", "x0")
-    dma("d_gv", T.gvi[:, 0:G], T.gv[:], "", "gvi")
-    dma("d_ex", T.exi[:, 0:14], T.ex[:], "", "exi")
-    dma("d_c0", T.ci[:, 0:1280], T.co[:, 0:1280], "", "ci0")
-    dma("d_c1", T.ci[:, 1280:W], T.co[:, 1280:W], "", "ci1")
+    def sel(n, p):
+        return B(n, 15 - p, 143 - p)
 
-    iota(T.pi[:, 0:1], [[0, 1]], 0, 1, "pi0", False)
-    iota(T.xr[:], [[1, 256]], 0, 0, "xr")
-    iota(T.mg[:], [[16, 8], [0, 16]], 0, 0, "mg")
-    iota(T.ones[:], [[0, 224]], 1, 0, "ones")
-    iota(T.aws[:, 112:128], [[0, 16]], 1, 0, "awsd")
-    iota(T.P[:, 0:16], [[0, 16]], 0, 0, "P0")
-    iota(T.EQ[:, 127::128], [[0, 8]], -1024, 0, "EQs")
-    ms(T.t16[:, 0:16], 4.0, "t16a")
-    ms(T.t16[:, 16:32], 0.0, "t16b")
-    ms(T.oh[:], 0.25, "oh")
+    Ib, BO, xb = B("Ib"), B("BO", 0, 128), B("xb", 0, 128)
+    x144, x160 = B("xb", 0, 144), B("xb", 0, 160)
+    I32x, MC = M(2), M(10)
+    EB = ("pa", "pc", "pd", "pe")
+
+    def PMm(kind, d):
+        k = d % 3
+        if (kind, k) == (0, 0):
+            return Ib
+        a = 128 * (3 * kind + k - 1)
+        return B("PM", a, a + 128)
+
+    dma("d_aw", B("awi"), T.aw[:])
+    dma("d_x0", B("XT", D, D + V), T.x0[:])
+    dma("d_gv", B("gvi", 0, G), T.gv[:])
+    dma("d_ex", B("exi", 0, 14), T.ex[:])
+    dma("d_c0", B("ci", 0, 1280), T.co[:, 0:1280])
+    dma("d_c1", B("ci", 1280, W), T.co[:, 1280:W])
+
+    iota(B("pi", 0, 1), [[0, 1]], 0, 1)
+    iota(B("xb"), [[1, 256]], 0)
+    iota(B("mg"), [[0, 4], [16, 8], [0, 16]], 0)
+    fill(B("ones"), 1)
+    iota(rows("JR", slice(0, 1), 0, 512), [[-16, 4], [0, 8], [-1, 16]], 0)
+    for k in range(7):
+        act(B("AS", WK + 256 * k, WK + 256 * k + 256), B("xb"), AF.Silu, scale=0.0)
+    dma("d_zS", B("AS2", WK, WW), B("AS", WK, WW))
+    ms(B("t16", 0, 16), 4.0)
+    ms(B("t16", 16, 32), 0.0)
+    ms(B("oh"), 0.25)
     for j, m in enumerate((15, 16, 1, 96)):
-        ts(T.pi[:, j + 1:j + 2], T.pi[:, 0:1], m, A.bitwise_and, "pi0", "pi%d" % (j + 1))
-    cp(T.co_[:, 0:5], T.pi[:, 0:5], "pi0 pi1 pi2 pi3 pi4", "c0")
-    scan(T.pw[:, 0:16], T.t16[:, 0:16], T.t16[:, 16:32], 0.25, A.mult, A.add, "t16a t16b", "pw0")
-    scan(T.pw[:, 16:32], T.oh[:], T.t16[:, 16:32], 4.0, A.mult, A.add, "oh t16b", "pw1")
-    ts(T.oh[:], T.xr[:, 0:16], col(1), A.is_equal, "xr c0 pw1", "oh")
-    ts(col(5), col(1), 4.0, A.is_lt, "c0", "c5")
-    ts(col(6), col(1), 6.5, A.is_lt, "c0", "c6")
-    tt(T.t16[:, 0:16], T.pw[:, 0:16], T.oh[:], A.mult, "pw0 oh", "t16a")
-    tt(T.t16[:, 16:32], T.pw[:, 16:32], T.oh[:], A.mult, "pw1 oh pw0", "t16b")
-    tt(col(7), col(6), col(5), A.subtract, "c5 c6", "c7")
-    op("V", lambda: v.tensor_reduce(col(8), T.t16[:, 0:16], AxisListType.X, A.add), "t16a", "c8")
-    op("V", lambda: v.tensor_reduce(col(9), T.t16[:, 16:32], AxisListType.X, A.add), "t16b", "c9")
-    tt(col(10), col(9), col(5), A.mult, "c9 c5", "c10")
-    ts(col(11), col(9), 256.0, A.mult, "c9 c7", "c11", col(7), A.mult)
-    ts(T.dg[:, 0:128], T.xr[:, 0:128], col(10), A.mult, "xr c10", "dga", -0.4921875, A.add)
-    ts(T.dg[:, 128:160], T.xr[:, 0:32], col(11), A.mult, "xr c11", "dgb", -0.4921875, A.add)
-    cp(T.dgi[:], T.dg[:], "dga dgb", "dgi")
-    ts(T.dgi[:], T.dgi[:], 3, A.bitwise_and, "dgi", "dgi")
-    ts(T.Bn[:, 0:128], T.dgi[:, 0:128], -0.0625, A.mult, "dgi", "Bn", -15.0625, A.add)
-    ts(T.Bn[:, 128:160], T.dgi[:, 128:160], -0.0625, A.mult, "dgi", "An")
-    for h in range(20):
-        act(T.NC[:, 128 * h:128 * h + 128], T.Bn[:, 0:128], AF.Identity, "Bn An", "NC%d" % (h // 4),
-            bias=T.Bn[:, 128 + h:129 + h])
-    ts(col(12), col(0), 16.0, A.add, "c0", "c12")
-    ts(col(13), col(2), 0.0, A.is_equal, "c0", "c13")
-    ts(col(14), col(2), 0.0, A.is_gt, "c0", "c14")
-    tt(col(15), col(0), col(1), A.subtract, "c0", "c15")
-    ts(T.WE[:], T.xr[:, 0:160], col(12), A.is_equal, "xr c12 c13", "WE", col(13), A.mult)
-    ts(T.WO[:], T.xr[:, 0:160], col(12), A.is_equal, "xr c12 c14", "WO", col(14), A.mult)
-    ts(col(16), col(15), 15.0, A.add, "c15", "c16")
-    ts(T.BO[:], T.mg[:], col(15), A.is_equal, "mg c15", "BO")
-    op("G", lambda: g.affine_select(T.TRI[:], T.BO[:], [[1, 128]], A.is_ge, 0.0, 0, -1), "BO", "TRI")
-    iota(T.gvi[:, G:2048], [[0, 256]], W, 0, "gvd", False)
-    iota(T.XF[:, 0:D], [[0, D]], 0, 0, "XFd")
-    iota(T.XF[:, D + W:XW], [[0, 16]], 0, 0, "XFz")
-    iota(T.M192[:, 0:144], [[-16, 3], [1, 48]], 0, 0, "M192")
-    iota(T.SM[:], [[0, 1536]], 1, 0, "SM")
-    iota(T.SM[:, 0::16], [[0, 96]], 0, 0, "SM")
-    iota(T.SM[:, 15::16], [[0, 96]], 0, 0, "SM")
-    iota(T.ZZ[:, 256:304], [[1, 48]], 256, 0, "ZZd")
-    iota(T.ZZ[:, 560:608], [[1, 48]], 256, 0, "ZZd")
-    iota(T.want[:, 256:304], [[0, 48]], 1, 0, "wantd")
-    iota(T.o304[:], [[0, 304]], 1, 0, "o304")
-    iota(T.C[:, 0:D], [[0, D]], -1, 0, "Cd")
-    iota(T.C[:, D + W:XW], [[0, 16]], -1, 0, "Cd")
-    H = WW // 2
-    for n in ("AS", "AV"):
-        iota(T[n][:, 0:H], [[0, H]], 0, 0, n)
-        dma("d_z" + n, T[n][:, H:WW], T[n][:, 0:H], n, n + "z")
-    dma("d_zAV2", T.AV2[:, 0:H], T.AV[:, 0:H], "AV", "AV2")
-    dma("d_zAV3", T.AV2[:, H:WW], T.AV[:, 0:H], "AV", "AV2z")
-    iota(T.AS2[:], [[0, WW]], 0, 0, "AS2")
-    iota(T.M192[:, 144:192], [[0, 48]], 0, 0, "M192z")
-    iota(T.XT[:, 0:D], [[0, D]], 0, 0, "XTd")
-    cp(T.awb[:], T.awi[:], "awi", "awb")
+        ts(B("pi", j + 1, j + 2), B("pi", 0, 1), m, A.bitwise_and)
+    scan(B("pw", 0, 16), B("t16", 0, 16), B("t16", 16, 32), 0.25, A.mult, A.add)
+    scan(B("pw", 16, 32), B("oh"), B("t16", 16, 32), 4.0, A.mult, A.add)
+    cp(B("co_", 0, 5), B("pi", 0, 5))
+    ms(B("aws", 112, 128), 1.0)
+    ms(B("sc1", 0, 1), 0.0)
+    ts(col(12), col(0), 16.0, A.add)
+    ts(col(13), col(2), 0.0, A.is_equal)
+    ts(col(14), col(2), 0.0, A.is_gt)
+    ts(B("oh"), B("xb", 0, 16), col(1), A.is_equal)
+    ts(col(5), col(1), 4.0, A.is_lt)
+    ts(col(6), col(1), 6.5, A.is_lt)
+    ts(B("WE"), x160, col(12), A.is_equal, col(13), A.mult)
+    ts(B("WO"), x160, col(12), A.is_equal, col(14), A.mult)
+    tt(B("t16", 16, 32), B("pw", 16, 32), B("oh"), A.mult)
+    tt(col(15), col(0), col(1), A.subtract)
+    tt(col(7), col(6), col(5), A.subtract)
+    red(col(9), B("t16", 16, 32))
+    cp(B("awb"), B("awi"))
 
-    def turn(src, r, bank):
+    def turn(terms, bank):
         lst = []
         for t in range(7):
-            lst.append((T[bank][:, 32 * t:32 * t + 16], T.WE[:, 16:144], src(t), True, True))
-            lst.append((T[bank][:, 32 * t + 16:32 * t + 32], T.WO[:, 32:160], src(t), True, True))
-        mm(lst, r + " WE WO", bank)
+            lst += grp(B(bank, 32 * t, 32 * t + 16), [(B("WE", 16, 144), f(t)) for f in terms])
+            lst += grp(B(bank, 32 * t + 16, 32 * t + 32), [(B("WO", 32, 160), f(t)) for f in terms])
+        mm(lst)
 
-    turn(lambda t: T.awb[:, 16 * t:16 * t + 16], "awb", "pe")
-    ts(T.ZS[:], T.xr[:, 0:144], col(16), A.is_equal, "xr c16", "ZS")
-    ts(T.jw[:], T.xr[:, 0:16], 16.0, A.mult, "xr c0", "jw", col(1), A.add)
-    ts(col(21), col(1), 1.0, A.add, "c0", "c21")
-    ts(T.lat[:, 0:16], T.oh[:], -2 * BIG, A.mult, "oh", "lat")
-    ts(T.I16[:], T.xr[:, 0:128], col(0), A.is_equal, "xr c0", "I16", 16.0, A.mult)
-    ts(T.LC[:, 0:16], T.xr[:, 0:16], col(21), A.is_equal, "xr c21", "LC", BIG, A.mult)
-    ts(T.Ib[:], T.xr[:, 0:128], col(0), A.is_equal, "xr c0", "Ib")
-    tt(T.LC[:, 0:16], T.LC[:, 0:16], T.lat[:, 0:16], A.add, "LC lat", "LC")
+    def open_counts():
+        mm([(B(b), rows("ones", slice(0, 1), 0, 128), rows("JR", slice(0, 1), 0, 512), True, False) for b in EB])
+
+    turn([lambda t: B("awb", 16 * t, 16 * t + 16)], "pf")
+    open_counts()
+    ts(B("BO"), B("mg"), col(15), A.is_equal)
+    op("G", lambda: g.affine_select(T.TRI[:], T.BO[:, 0:128], [[1, 128]], A.is_ge, 0.0, 0, -1), [BO], [B("TRI")])
+    for k, c in enumerate((1, 16)):
+        fill(B("hv", 2 * k, 2 * k + 1), c)
+    fill(B("zr"), 0)
+    fill(B("gvi", G, 2048), W)
+    fill(B("XF", D + W, XW), 0)
+    iota(B("jr"), [[1, 256]], -int(SH))
+    fill(B("C", 0, D), -1)
+    fill(B("C", D + W, XW), -1)
+    fill(B("ls"), LEV[0])
+    fill(B("XF", 0, D), 0)
+    fill(B("AV", WK, WW), 0)
+    dma("d_zV", B("AV2", WK, WW), B("AV", WK, WW))
+    fill(B("S", 4096, 4864), 0)
+    fill(B("want", 256, 304), 1)
+    iota(B("M192"), [[-16, 3], [1, 48]], 0)
+    fill(B("lv"), LEV[0])
+    tt(col(10), col(9), col(5), A.mult)
+    ts(col(11), col(9), 256.0, A.mult, col(7), A.mult)
+    ts(col(33), col(7), -14.0625 / 32, A.mult, -1.0 / 32, A.add)
+    ts(col(34), col(7), -14.0625, A.mult, 15.0625, A.add)
+    ts(B("dg", 0, 128), xb, col(10), A.mult, -0.4921875, A.add)
+    ts(B("dg", 128, 160), B("xb", 0, 32), col(11), A.mult, -0.4921875, A.add)
     for t in range(7):
-        op("V", lambda: v.transpose(T.TT[:, t:t + 218:7], T.pe[:, 32 * t:32 * t + 32]), "pe", "TT")
-    cp(T.jb[:], T.jw[:], "jw", "jb")
-    ts(T.jh[:], T.jw[:], 0.5, A.add, "jw", "jh")
-    cp(T.aws[:, 0:112], T.TT[:, 0:112], "TT", "aws")
+        vtr(B("TT", t, t + 218, 7), B("pf", 32 * t, 32 * t + 32))
+        if t == 3:
+            cp(B("dgi"), B("dg"))
+    ts(B("dgi"), B("dgi"), 3, A.bitwise_and)
+    cp(B("aws", 0, 112), B("TT", 0, 112))
 
-    chunks = [(a, min(a + 512, V)) for a in range(0, V, 512)]
+    def consts_0():
+        ts(B("An"), B("dgi", 128, 160), -0.0625 / 32, A.mult, col(33), A.add)
+        ts(B("Bp", 0, 128), B("dgi", 0, 128), 0.0625, A.mult, col(34), A.add)
+        ts(Ib, xb, col(0), A.is_equal)
+        ts(col(16), col(15), 15.0, A.add)
+        lin(B("hv", 1, 4, 2), B("hv", 0, 4, 2), 0.5)
+        for n in (128, 256):
+            lin(B("Bp", n, 2 * n), B("Bp", 0, n), 1.0)
+        lin(I32x, Ib, 32.0)
 
-    def enc_m(k):
-        a, b = chunks[k]
-        ts(T.em[:, a:b], T.XT[:, D + a:D + b], 0.0, A.min, "x0", "em%d" % k)
+    def mark(k, e):
+        for h in range(4 * k, min(4 * k + 4, 19)):
+            b = min(128 * h + 128, V)
+            if h % 4 in EM_ACT and e == "A":
+                act(B("em", 128 * h, b), B("XT", D + 128 * h, D + b), AF.Relu, scale=B("An", h, h + 1))
+            if h % 4 not in EM_ACT and e == "V":
+                ts(B("em", 128 * h, b), B("XT", D + 128 * h, D + b), B("An", h, h + 1), A.mult, 0.0, A.max)
 
-    def enc_p(k):
-        a, b = chunks[k]
-        scan(T.et[:, a:b], T.NC[:, a:b], T.em[:, a:b], 0.0, A.min, A.mult, "em%d NC%d" % (k, k), "et%d" % k)
-        bk = ("pg", "ph", "pb", "pc", "pd")[k]
-        mm(grp(T[bk][:, 0:b - a], [(T.Ib[:], T.XT[:, D + a:D + b]), (T.Ib[:], T.et[:, a:b])]), "x0 Ib et%d" % k, bk)
-        act(T.XF[:, D + a:D + b], T[bk][:, 0:b - a], AF.Copy, bk, "XFe%d" % k)
+    def enc(k):
+        a, b = 512 * k, min(512 * k + 512, V)
+        scan(B("et", a, b), B("Bp", 0, b - a), B("em", a, b), 0.0, A.max, A.mult)
+        bk = ("pb", "ph")[k % 2]
+        mm(grp(B(bk, 0, b - a), [(Ib, B("XT", D + a, D + b)), (I32x, B("et", a, b))]))
+        act(B("XF", D + a, D + b), B(bk, 0, b - a), AF.Copy)
 
-    def consts2():
-        ts(col(17), col(1), 15.0, A.is_equal, "c0", "c17")
-        ts(col(18), col(7), 0.5, A.mult, "c7 c5", "c18", col(5), A.add)
-        ts(col(20), col(17), 16.0, A.mult, "c17", "c20", 64.0, A.add)
-        ts(col(19), col(18), 16.0, A.mult, "c18 c8", "c19", col(8), A.mult)
-        ts(M(3), T.BO[:], col(17), A.mult, "BO c17", "M3", 16.0, A.mult)
-        ts(M(8), T.BO[:], col(19), A.mult, "BO c19", "M8")
-        ts(M(1), T.BO[:], col(20), A.mult, "BO c20", "M1")
+    def consts_a():
+        for a, b, lo, h in ((0, 96, 32, 18), (96, 224, 0, 19), (224, 288, 0, 20)):
+            ts(B("NC", a, b), B("Bp", lo, lo + b - a), B("An", h, h + 1), A.mult)
+        lin(B("XF", D + V, D + W), B("NC", 0, 224), -32.0, -1.0)
 
-    def early_a():
-        for n in (16, 32, 64, 128):
-            act(T.LC[:, n:2 * n], T.LC[:, 0:n], AF.Copy, "LC", "LC")
-            if n == 16:
-                act(T.KJ[:], T.xr[:], AF.Identity, "xr", "KJ", bias=1.0 / 256 - 1.0, scale=1.0 / 256)
-            if n == 32:
-                act(T.XF[:, D + V:D + W], T.NC[:, V:W], AF.Identity, "NC4", "XFi", bias=-1.0, scale=-1.0)
-            if n == 64:
-                act(T.If[:], T.Ib[:], AF.Copy, "Ib", "If")
+    def consts_b():
+        tt(B("t16", 0, 16), B("pw", 0, 16), B("oh"), A.mult)
+        ts(col(17), col(1), 15.0, A.is_equal)
+        ts(col(18), col(7), 8.0, A.mult)
+        ms(B("SM"), 1.0)
+        red(col(8), B("t16", 0, 16))
+        ts(col(18), col(5), 16.0, A.mult, col(18), A.add)
+        ts(col(38), B("oh", 0, 1), -655360.0, A.mult)
+        ms(B("SM", 0, 2048, 16), 0.0)
+        tt(col(19), col(18), col(8), A.mult)
+        ts(col(39), B("oh", 1, 2), -34816.0, A.mult, col(38), A.add)
+        ms(B("SM", 15, 2048, 16), 0.0)
+        ts(col(35), col(17), 16 * K1, A.mult, col(19), A.add)
+        ts(col(40), B("oh", 2, 3), -5.0, A.mult, col(39), A.add)
+        ts(M(0), BO, -64 * K1, A.mult)
 
-    def late_a():
-        act(T.DL[:], T.NC[:, V:W], AF.Identity, "NC4", "DL", bias=-15.0, scale=-1.0)
-        act(T.L0[:], T.NC[:, V:W], AF.Identity, "NC4", "L0", bias=-1.0, scale=-1.0)
-        for j, c in enumerate((512.0, -512.0)):
-            act(PMm(0, j), T.Ib[:], AF.Copy, "Ib", "PM", scale=c)
-        act(T.I256[:], T.Ib[:], AF.Copy, "Ib", "I256", scale=256.0)
-        act(T.ZSf[:], T.ZS[:], AF.Copy, "ZS", "ZSf")
-
-    def consts2a():
-        for i, src, n, c in ((0, T.BO[:], "BO", -64.0), (2, M(3), "M3", -1.0), (4, T.BO[:], "BO", -2 * AL),
-                             (5, T.BO[:], "BO", 2 * AL), (6, M(3), "M3", AL / 16), (7, M(3), "M3", -AL / 16),
-                             (9, M(8), "M8", -1.0), (10, T.BO[:], "BO", AL)):
-            act(M(i), src, AF.Copy, n, "MM", scale=c)
-
-    def consts3():
-        ts(col(22), col(1), 15.0, A.is_lt, "c0", "c22", BIG, A.mult)
-        ts(col(23), col(1), 2.0, A.mult, "c0", "c23", col(4), A.add)
-        ts(col(25), col(3), -128.0, A.mult, "c0", "c25", 256.0, A.add)
-        ts(col(26), col(3), -112.0, A.mult, "c0", "c26", 256.0, A.add)
-        ts(col(24), col(23), 1.0, A.add, "c23", "c24")
-        ts(T.jc[:], T.jw[:], col(22), A.add, "jw c22", "jc")
+    def consts_c():
+        ts(col(23), col(1), 2.0, A.mult, col(4), A.add)
+        ts(M(4), BO, -K2, A.mult)
+        ts(M(5), BO, K2, A.mult)
+        ts(col(24), col(23), 1.0, A.add)
+        ts(M(6), BO, col(35), A.mult)
+        ts(M(7), BO, col(17), A.mult, -16 * K1, A.mult)
+        ts(MC, BO, col(40), A.mult)
+        ts(B("Z0h"), B("ZS"), B("oh", 0, 1), A.mult)
+        ts(col(25), col(3), -64.0, A.mult, 256.0, A.add)
         for n, c in (("H0", 13), ("H1", 14)):
-            ts(T[n + "f"][:], T.xr[:, 0:144], col(24), A.is_equal, "xr c24 c13 c14", n + "f", col(c), A.mult)
-            ts(T[n + "h"][:], T.xr[:, 0:144], col(24), A.is_equal, "xr c24 c13 c14", n + "h", col(c), A.mult)
-        ts(col(27), col(15), -1.0, A.mult, "c15", "c27", 112.0, A.add)
-        ts(col(29), col(15), 0.0, A.is_gt, "c15", "c29", 128.0, A.mult)
-        ts(col(31), col(1), 0.0, A.is_equal, "c0", "c31")
-        ts(col(28), col(27), col(1), A.add, "c27 c0", "c28")
-        ts(col(30), col(29), col(15), A.subtract, "c29 c15 c0", "c30", col(1), A.add)
-        ts(T.M192[:, 0:144], T.M192[:, 0:144], col(1), A.is_ge, "M192 c0", "M192", 8192.0, A.mult)
-        ts(PMm(1, 2), T.xr[:, 0:128], col(28), A.is_equal, "xr c28", "PM1")
-        ts(PMm(2, 2), T.xr[:, 0:128], col(30), A.is_equal, "xr c30", "PM2")
-        cp(T.exu[:, 0:14], T.exi[:, 0:14], "exi", "exu")
+            ts(B(n + "h"), x144, col(24), A.is_equal, col(c), A.mult)
 
-    def consts3a():
+    def consts_ca():
+        lin(B("KJ"), B("xb", 0, 224), 1.0 / 256, 1.0 / 256 - 1.0)
+        for a in (0, 64):
+            lin(B("CCb", a, a + 64), B("xb", 0, 64), -1.0, col(25))
         for n in ("H0", "H1"):
-            act(T[n + "b"][:], T[n + "f"][:], AF.Copy, n + "f", n + "b", scale=256.0)
-        for h in range(2):
-            act(T.CCb[:, 128 * h:128 * h + 128], T.xr[:, 0:128], AF.Identity, "xr c25", "CCb", bias=col(25), scale=-1.0)
-        late_a()
+            lin(B(n + "b"), B(n + "h"), 256.0)
 
-    def consts4a():
-        for h in range(2):
-            act(T.CCi[:, 112 * h:112 * h + 112], T.xr[:, 0:112], AF.Identity, "xr c26", "CCi", bias=col(26), scale=-1.0)
-        for k in range(1, 3):
-            for j, c in enumerate((512.0, -512.0)):
-                act(PMm(k, j), PMm(k, 2), AF.Copy, "PM1 PM2", "PM", scale=c)
-        act(T.Z0f[:], T.ZS[:], AF.Identity, "ZS c31", "Z0f", scale=col(31))
-        act(T.Z0[:], T.ZS[:], AF.Identity, "ZS c31", "Z0", scale=col(31))
+    def consts_d():
+        ts(col(20), col(17), 16 * K1, A.mult, 64 * K1, A.add)
+        ts(M(8), BO, col(19), A.mult)
+        ts(M(9), BO, col(19), A.mult, -1.0, A.mult)
+        ts(M(3), BO, col(17), A.mult, 16 * K1, A.mult)
+        ts(M(1), BO, col(20), A.mult)
+        cp(B("exu", 0, 14), B("exi", 0, 14))
 
-    def PMm(k, j):
-        if (k, j) == (0, 2):
-            return T.Ib[:]
-        a = 128 * (3 * k + j)
-        return T.PM[:, a:a + 128]
+    def consts_da():
+        for i in (14, 15):
+            lin(B("S", 4096 + i, 4864, 16), B("NC", 240, 288), -32.0, -1.0)
+        lin(B("IL"), Ib, K1)
+        lin(B("jh", 0, 3), B("xb", 0, 48, 16), 1.0, col(41))
+        lin(B("Zd"), B("ZS"), col(19))
+        lin(B("Z8h"), B("ZS"), -8192.0)
+        for k in range(2):
+            lin(B("I8h", 128 * k, 128 * k + 128), Ib, 8192.0 * (2 * k - 1))
+            lin(B("dd", 4 * k, 4 * k + 4), B("xb", 0, 64, 16), 1.0, col(42))
 
-    def sel(Z, p):
-        return Z[:, 15 - p:143 - p]
+    def consts_e():
+        ts(col(27), col(15), -1.0, A.mult, 112.0, A.add)
+        ts(col(29), col(15), 0.0, A.is_gt, 128.0, A.mult)
+        ts(col(26), col(3), -112.0, A.mult, 256.0, A.add)
+        ms(B("lz", 3, 4), 4110)
+        tt(col(28), col(27), col(1), A.add)
+        tt(col(29), col(29), col(15), A.subtract)
+        ts(B("M192"), B("M192"), col(1), A.is_ge, 8192.0, A.mult)
+        ts(PMm(0, 1), xb, col(28), A.is_equal)
+        ts(PMm(0, 2), xb, col(1), A.subtract, col(29), A.is_equal)
+        for d, c in ((0, 15), (1, 27), (2, 29)):
+            ts(PMm(1, d), B("mg", 0, 128), col(c), A.is_equal, col(17), A.mult)
 
-    XFall = "XF XFd XFz XFi XFe0 XFe1 XFe2 XFe3 XFe4"
-    Call = "C Cd C0 C1"
+    def consts_ea():
+        for a in (0, 112):
+            lin(B("CCi", a, a + 112), B("xb", 0, 112), -1.0, col(26))
+        lin(B("Z0"), B("Z0h"), 1.0)
 
-    def refresh(s):
+    def refresh(ks, tab="XF", tmp="x48"):
         out = []
-        for k in range(s, -1, -1):
-            out.append(lambda k=k: cp(T.x48[:], T.XF[:].indirect(T.lt[:, 4 * k:4 * k + 3]), "XF lt%d" % k, "x48"))
-            out.append(lambda k=k: cp(T.XF[:].indirect(T.lo[:, 4 * k:4 * k + 3]), T.x48[:], "x48 lo%d" % k, "XF"))
+        for k in ks:
+            out.append(lambda k=k: cp(B(tmp), X(B(tab), B("LT", 8 * k + 4, 8 * k + 7))))
+            out.append(lambda k=k: cp(X(B(tab), B("LT", 8 * k, 8 * k + 3)), B(tmp)))
         return out
 
-    def ycm(a, b):
-        mm([(T.pc[:, 0:160], sel(T.ZSf, p), T.C[:, D + 160 * p:D + 160 * p + 160], p == 0, p == 15)
-            for p in range(a, b)], "ZSf " + Call, "pc")
+    def narrow(o, i):
+        op("G", lambda: g.affine_select(o[0], i[0], [[0, o[3] - o[2]]], A.is_ge, 0.0, 0, 0), [i], [o])
 
-    def shuffle(bank, n, terms, cc, r):
-        lst = []
-        for h in range(2):
-            tl = []
-            for nm, src in terms:
-                Wm = T["H%d%s" % (h, nm)]
-                tl += [(Wm[:, 1:129], src[:, 0:n]), (Wm[:, 0:128], src[:, n:2 * n])]
-            tl.append((T.Ib[:], cc[:, n * h:n * h + n]))
-            lst += grp(T[bank][:, n * h:n * h + n], tl)
-        mm(lst, r + " H0h H1h H0b H1b Ib", bank)
+    def shuffle(bank, n, nm, src, a=0):
+        if nm == "c":
+            mm([(B(bank, 0, 2 * n), Ib, B(src), True, False)])
+            return
+        mm([(B(bank, n * h, n * h + n), B("H%d%s" % (h, nm), 1 - k, 129 - k), B(src, a + n * k, a + n * k + n), False,
+             nm == "b" and h + k == 2) for h in range(2) for k in range(2)])
 
-    def lists(bank, k, out, name, add, between=None):
+    def lists(bank, k, tmp, a, out, between=None):
         for s in range(k):
-            op("V", lambda: v.transpose(T.TT[:, s:32 * k:k], T[bank][:, s:32 * k:k]), bank, "TT")
+            vtr(B(tmp, a + s, a + 32 * k, k), B(bank, s, 32 * k, k))
         if between:
             between()
-        ts(out[:, 0:32 * k], T.TT[:, 0:32 * k], add, A.add, "TT", name)
+        ts(B(out, a, a + 32 * k), B(tmp, a, a + 32 * k), WK - 1.0, A.add)
 
-    WN = {"AS": "AS ASz", "AS2": "AS2 AS2z", "AV": "AV AVz", "AV2": "AV2 AV2z"}
+    def scat_a(w, off):
+        act(X(B(w), off), B("ls", 0, 16 * (off[3] - off[2])), AF.Silu)
 
-    def scat_a(L, name, k, rows, two):
-        for j, r in enumerate(rows):
-            w = "AS2" if two and (len(rows) - j) % 2 == 1 else "AS"
-            act(T[w][:].indirect(L[:, k * r:k * r + k]), T.ls[:, 0:16 * k], AF.Silu, name + " ls", WN[w])
+    def scat_v(w, off):
+        cp(X(B(w), off), B("lv", 0, 16 * (off[3] - off[2])))
 
-    def scat_v(L, name, k, rows):
-        for r in rows:
-            w = "AV2" if r % 2 == 1 and (k == 16 or r < 13) else "AV"
-            cp(T[w][:].indirect(L[:, k * r:k * r + k]), T.lv[:, 0:16 * k], name + " lv", WN[w])
+    win = B("XF", D, XW)
+    later = []
+
+    def gap(n=1):
+        for _ in range(n):
+            if later:
+                later.pop(0)()
 
     for s in range(3):
-        last = s == 2
-        mm([(T.pa[:, 0:128], T.TRI[:], T.aws[:], True, True), (T.pa[:, 128:256], T.BO[:], T.aws[:], True, True)],
-           "TRI BO aws awsd", "pa")
-        iota(T.ls[:], [[0, 256]], LEV[s], 0, "ls")
-        iota(T.lv[:], [[0, 256]], LEV[s], 0, "lv")
+        first, last = s == 0, s == 2
+        scan(B("sc1", 1, 129), B("ones", 0, 128), B("aws"), 0.0, A.mult, A.add)
+        mm([(B("pb", 0, 128), B("TRI"), B("aws"), True, False)])
+        for b in range(4):
+            mm([(B(EB[b]), B("sc1", 1, 129), B("BO"), False, True)])
+            if b == 1:
+                mm([(B("pb", 0, 128), BO, B("sc1", 0, 128), False, True)])
+        if first:
+            consts_0()
+        gap()
+
+        def count(bank, h, k):
+            return [(B(bank, c, c + 1), B("EQ", 1024 * h + 128 * c, 1024 * h + 128 * c + 128),
+                     B("hv", k + c // 4, k + c // 4 + 1), k == 0, k == 0) for c in range(8)]
+
+        for h in range(2):
+            ts(B("EQ", 1024 * h, 1024 * h + 512), B(EB[2 * h]), 128.0 * h, A.is_le, 0.5, A.subtract)
+            act(B("EQ", 1024 * h + 512, 1024 * h + 1024), B(EB[2 * h + 1]), AF.Sign, bias=128.0 * h + 64.5, scale=-1.0)
+            if h == 0:
+                act(B("pre"), B("pb", 0, 128), AF.Copy)
+            mm(count(("pf", "pg")[h], h, 0))
+        if first:
+            ts(B("ZS"), x144, col(16), A.is_equal)
+            mark(0, "V")
+            mark(0, "A")
+            mark(1, "A")
+        for h in range(2):
+            ts(B("bw", 8 * h, 8 * h + 8), B(("pf", "pg")[h], 0, 8), 64.0, A.add)
+            o = B(("pa", "pc")[h], 0, 8)
+            mm([(o, BO, B("zr", 0, 8), True, False)] + count(("pa", "pc")[h], h, 2))
+            if first:
+                mark(1 + h, "V")
+            gap()
+            tt(B("cmp", 128 * h, 128 * h + 128), X(B("pre"), B("bw", 8 * h, 8 * h + 8)), B("xb", 128 * h, 128 * h + 128), A.is_le)
+            mm([(o, sel("ZS", p), B("cmp", 128 * h + p, 128 * h + 128, 16), False, p == 15) for p in range(16)])
+            if first:
+                enc(h)
+                mark(2 + h, "A")
+        if first:
+            mark(4, "A")
+            mark(3, "V")
+            enc(2)
+            mark(4, "V")
+            enc(3)
+            consts_a()
+            enc(4)
+        act(B("sg"), B("pre", 0, 112), AF.Sign, bias=-256.5)
         if s == 1:
-            iota(T.F[:], [[1, D + W]], -D, 0, "F")
-        if s == 0:
-            enc_m(0)
-            enc_m(1)
-        scan(T.P[:, 1:129], T.ones[:, 0:128], T.pa[:, 128:256], 0.0, A.mult, A.add, "ones pa P0", "P")
-        if s == 0:
-            enc_m(2)
-        for c in range(8, 16):
-            act(T.junk[:, 128 * c - 1024:128 * c - 897], T.P[:, 1:128], AF.Sign, "P jh", "junk acca",
-                bias=T.jh[:, c:c + 1], scale=-1.0, accum_out=T.acc[:, c:c + 1])
-        for c in range(8):
-            ts(T.EQ[:, 128 * c:128 * c + 127], T.P[:, 1:128], T.jb[:, c:c + 1], A.is_le, "P jb", "EQ")
-        tt(T.pre[:], T.pa[:, 0:128], T.P[:, 0:128], A.add, "pa P P0", "pre")
-        scan(T.EO[:, 0:1024], T.EQ[:], T.EQ[:], 0.0, A.add, A.max, "EQ EQs", "EO")
-        if s == 0:
-            early_a()
-            enc_p(0)
-        cp(T.bw[:, 0:8], T.EO[:, 126:1024:128], "EO", "bw0")
-        ts(T.bw[:, 8:16], T.acc[:, 8:16], 127.0, A.add, "acca", "bw1", 0.5, A.mult)
-        if s == 0:
-            enc_p(1)
-        tt(T.cmp[:], T.pre[:].indirect(T.bw[:]), T.xr[:], A.is_le, "pre bw0 bw1 xr", "cmp")
-        cp(T.bb[:, 0:8], T.EO[:, 126:1024:128], "EO", "bb0")
-        ts(T.bb[:, 8:16], T.acc[:, 8:16], 127.0, A.add, "acca", "bb1", 0.5, A.mult)
-        mm([(T.pa[:, 256:272], sel(T.ZS, p), T.cmp[:, p::16], p == 0, False) for p in range(16)], "ZS cmp", "pa")
-        mm([(T.pa[:, 256:272], T.I16[:], T.bb[:], False, True)], "I16 bb0 bb1", "pa")
-        if s == 0:
-            enc_m(3)
-            enc_m(4)
-            enc_p(2)
-            consts2()
-        cp(T.eu[:], T.pa[:, 256:272], "pa", "eu")
-        if s == 0:
-            enc_p(3)
-            enc_p(4)
-            consts2a()
-        cp(T.gve[:], T.gvi[:].indirect(T.eu[:]), "gvi gvd eu", "gve")
-        win = T.XF[:, D:XW]
+            for d in range(3):
+                lin(PMm(2, d), PMm(1, d), -1.0)
+            lin(B("ZSh"), B("ZS"), 1.0)
+            lin(B("If"), Ib, 1.0)
+            lin(B("ILf"), Ib, LEV[2] / 4)
+        for h in range(2):
+            ts(B("eu", 8 * h, 8 * h + 8), B(("pa", "pc")[h], 0, 8), 1024.0, A.add)
+            gap()
+            if first and h == 0:
+                consts_b()
+            cp(B("gve", 128 * h, 128 * h + 128), X(B("gvi"), B("eu", 8 * h, 8 * h + 8)))
+        if not first:
+            fill(B("ls"), LEV[s])
+            fill(B("lv"), LEV[s])
+        if s == 1:
+            iota(B("F"), [[1, XW]], -D)
 
-        def ga(a, b, n):
-            act(T.GG[:, 16 * a:16 * b], win.indirect(T.gve[:, a:b]), AF.Copy, XFall + " gve", n)
+        def ga(a, b):
+            act(B("GG", 16 * a, 16 * b), X(win, B("gve", a, b)), AF.Copy)
 
-        def sc(a, b, n):
-            scan(T.S[:, 16 * a:16 * b], T.SM[:, 0:16 * (b - a)], T.GG[:, 16 * a:16 * b], 0.0, A.mult, A.max,
-                 "SM G" + n, "S" + n)
+        def sc(a, b):
+            scan(B("S", 16 * a, 16 * b), B("SM", 0, 16 * (b - a)), B("GG", 16 * a, 16 * b), 0.0, A.mult, A.max)
 
-        def rnd(a, b, r, n):
-            ts(T.RM[:, a:b], T.S[:, 16 * a + 14:16 * b:16], MAGIC, A.add, r, "RM" + n, MAGIC, A.subtract)
-            ts(T.RO[:, a:b], T.S[:, 16 * a + 15:16 * b:16], MAGIC, A.add, r, "RO" + n, MAGIC, A.subtract)
+        def four(a, b):
+            return B("S", 16 * a + 14, 16 * b, 16), B("S", 16 * a + 15, 16 * b, 16), B("RM", a, b), B("RO", a, b)
 
-        MA = " MM M1 M3 M8"
-        zb = float(D - 623925)
+        def p_g(a, b, ins=range(15)):
+            mm([(B("ph", a, b), M(0), B("GG", 16 * a + i, 16 * b, 16), False, False) for i in ins])
 
-        def views(a, b):
-            return T.S[:, 16 * a + 14:16 * b:16], T.S[:, 16 * a + 15:16 * b:16], T.RM[:, a:b], T.RO[:, a:b]
+        def bind(h):
+            a, b = 128 * h, 128 * h + 128
+            mx, go, rm, ro = four(a, b)
+            ts(rm, mx, MAGIC, A.add, MAGIC, A.subtract)
+            ts(ro, go, MAGIC, A.add, MAGIC, A.subtract)
+            mm(grp(B(("pf", "pg")[h], 0, 128), [(M(4), mx), (M(5), rm), (M(7), ro), (M(6), go), (MC, B("ones", 0, 128))]))
 
-        def p_g(a, b, r, bk):
-            mm([(T[bk][:, a:b], M(0), T.GG[:, 16 * a + i:16 * b:16], i == 0, False) for i in range(15)], r + MA, bk)
+        def outs(h, between=None):
+            a, bk = 128 * h, ("pf", "pg")[h]
+            tt(B("ob", a, a + 128), B(bk, 0, 128), B("jr", a, a + 128), A.max)
+            mm(grp(B(bk, 128, 136), [(sel("Z0h", p), B("ob", a + p, a + 128, 16)) for p in range(16)]))
+            if between:
+                between()
+            ts(B("obu", 8 * h, 8 * h + 8), B(bk, 128, 136), SH, A.add)
 
-        def p_bind(a, b, r, n):
-            mx, go, rm, ro = views(a, b)
-            mm(grp(T.pe[:, a:b], [(M(8), go)]), r + MA, "pe")
-            act(T.ZZ[:, 304 + a:304 + b], T.pe[:, a:b], AF.Identity, "pe", "ZO" + n, bias=zb)
-            mm(grp(T.pc[:, a:b], [(M(4), mx), (M(6), go), (M(5), rm), (M(7), ro)]), r + " RM%s RO%s" % (n, n), "pc")
+        def waiters(h):
+            cp(B("cg", 128 * h, 128 * h + 128), X(B("C"), B("obu", 8 * h, 8 * h + 8)))
+            shuffle(("pb", "pc")[h], 64, "c", "CCb")
+            shuffle(("pb", "pc")[h], 64, "h", "cg", 128 * h)
 
-        def p_want(a, b, r, n, bk):
-            mx, go, rm, ro = views(a, b)
-            o = T[bk][:, a:b]
-            mm([(o, M(1), mx, False, False), (o, M(3), go, False, False), (o, M(2), rm, False, False),
-                (o, M(2), ro, False, True)], r + " RM%s RO%s" % (n, n), bk)
+        def marks(h):
+            a = 128 * h
+            scan(B("tm", a, a + 128), B("KJ", 0, 128), B("cg", a, a + 128), -1.0, A.max, A.min)
+            shuffle(("pb", "pc")[h], 64, "b", "tm", a)
 
-        Sall = "S0 S1 S2 S3"
-        if s == 0:
-            ga(0, 96, "G0")
-        ga(96, 160, "G1")
-        ga(160, 224, "G2")
-        if s == 0:
-            consts3()
-            cp(T.C[:, D:D + 1280], T.ci[:, 0:1280], "ci0", "C0")
-            cp(T.GG[:, 3584:4096], win.indirect(T.gve[:, 224:256]), XFall + " gve", "G3")
+        def half(i):
+            return B("wl", 8 * i, 8 * i + 8)
+
+        arows = list(range(BIND_ACT[s]))
+        vrows = list(range(BIND_ACT[s], 32))
+
+        def rows_a(n):
+            for _ in range(n):
+                if arows:
+                    scat_a(("AS", "AS2")[len(arows) % 2], half(arows.pop(0)))
+
+        def rows_v(n):
+            for _ in range(n):
+                if vrows:
+                    scat_v(("AV", "AV2")[len(vrows) % 2], half(vrows.pop(0)))
+
+        mm([(B("ph", 0, 256), BO, B("zr"), True, False)])
+        ga(0, GA)
+        if first:
+            ga(GA, 128)
+            consts_c()
+            cp(B("C", D, D + 1280), B("ci", 0, 1280))
+            cp(B("C", D + 1280, D + W), B("ci", 1280, W))
         else:
-            ga(224, 256, "G3")
-            cp(T.GG[:, 0:1536], win.indirect(T.gve[:, 0:96]), XFall + " gve", "G0")
-        p_g(0, 160, "G0 G1", "pb")
-        sc(0, 96, "0")
-        sc(96, 160, "1")
-        rnd(0, 160, "S0 S1", "a")
-        p_bind(0, 160, "S0 S1", "a")
-        if s == 0:
-            cp(T.C[:, D + 1280:D + W], T.ci[:, 1280:W], "ci1", "C1")
-        p_g(160, 256, "G2 G3", "pg")
-        sc(160, 224, "2")
-        sc(224, 256, "3")
-        rnd(160, 256, "S2 S3", "b")
-        p_bind(160, 256, "S2 S3", "b")
-        mx, go = views(0, 256)[0:2]
-        mm(grp(T.pd[:, 0:256], [(M(8), mx), (M(9), go)]), Sall, "pd")
-        p_want(0, 160, "S0 S1", "a", "pb")
-        p_want(160, 256, "S2 S3", "b", "pg")
-        mm(grp(T.ph[:, 0:256], [(M(8), mx)]), Sall, "ph")
-        if s == 0:
-            consts3a()
-        tt(T.q[:], T.pre[:, 0:112], T.aws[:, 0:112], A.mult, "pre aws", "q")
-        tt(T.ob[:], T.pc[:, 0:256], T.ZZ[:, 304:560], A.min, "pc ZOa ZOb", "ob")
-        ts(T.rem[:], T.q[:], 256.5, A.is_gt, "q", "rem", float(LEV[s]), A.mult)
-        scan(T.lat[:], T.LC[:], T.ob[:], 0.0, A.add, A.max, "LC ob", "lat")
-        ts(T.tt[:], T.pd[:, 0:256], 0.0, A.is_equal, "pd", "tt", 1.5, A.add)
-        tt(T.w16[:], T.lat[:, 15::16], T.jc[:], A.max, "lat jc", "w16")
-        tt(T.want[:, 0:160], T.pb[:, 0:160], T.tt[:, 0:160], A.is_gt, "pb tt", "want")
-        ts(T.obu[:], T.w16[:], col(22), A.subtract, "w16 c22", "obu")
-        tt(T.want[:, 160:256], T.pg[:, 160:256], T.tt[:, 160:256], A.is_gt, "pg tt", "want")
-        act(T.cg[:], T.C[:].indirect(T.obu[:]), AF.Copy, Call + " obu", "cg")
-        act(T.ZZ[:, 0:256], T.ph[:, 0:256], AF.Identity, "ph", "ZU", bias=zb)
-        tt(T.tmn[:], T.C[:].indirect(T.obu[:]), T.KJ[:], A.min, Call + " obu KJ", "tmn")
-        shuffle("pf", 128, [("b", T.tmn), ("h", T.cg)], T.CCb, "tmn cg CCb")
-        scan(T.rank[:], T.o304[:], T.want[:], 0.0, A.mult, A.add, "o304 want wantd", "rank")
-        for t in range(3):
-            act(T.junk[:, 1152 + 304 * t:1456 + 304 * t], T.rank[:], AF.Sign, "rank jh", "junk ca",
-                bias=T.jh[:, t:t + 1], scale=-1.0, accum_out=T.ca[:, t:t + 1])
-        mm(grp(T.pc[:, 0:256], [(M(4), mx), (M(6), go), (M(5), T.RM[:]), (M(7), T.RO[:]), (M(10), T.want[:, 0:256])]),
-           Sall + " RMa RMb ROa ROb want", "pc")
-        cp(T.XF[:].indirect(T.obu[:]), T.S[:, 14::16], Sall + " obu", XFall)
-        lists("pf", 8, T.wl, "wl", 256.0, lambda: tt(T.SW[:, 0:256], T.pc[:, 0:256], T.ZZ[:, 304:560], A.min,
-                                                     "pc ZOa ZOb", "SW0"))
-        if s == 0:
-            consts4a()
-        scat_a(T.wl, "wl", 16, range(BIND_ACT[s]), True)
-        for j in range(3):
-            ts(T.lz[:, 3 * j:3 * j + 3], T.ca[:, 0:3], 304.0, A.add, "ca", "lz%d" % j, 0.5, A.mult)
-        ts(T.lz[:, 9:12], T.ca[:, 0:3], 912.0, A.add, "ca", "lz3", 0.5, A.mult)
-        tt(T.SW[:, 256:448], T.ZZ[:].indirect(T.lz[:]), T.M192[:], A.add, "ZOa ZOb ZU ZZd lz0 lz1 lz2 lz3 M192 M192z", "SW1")
-        scan(T.l2[:], T.LC[:, 0:192], T.SW[:, 256:448], 0.0, A.add, A.max, "LC SW1", "l2")
-        lo, lt = T.lo[:, 4 * s:4 * s + 3], T.lt[:, 4 * s:4 * s + 3]
-        ts(lo, T.l2[:, 159:192:16], col(22), A.subtract, "l2 c22", "lo%d" % s)
-        ts(T.lu[:, 0:3], T.l2[:, 15:144:64], col(22), A.subtract, "l2 c22", "lu", 8192.0, A.subtract)
-        ts(T.uo[:, 0:3], T.l2[:, 15:144:64], col(22), A.subtract, "l2 c22", "uo0", 8192.0, A.subtract)
-        ts(T.uo[:, 4:7], T.l2[:, 159:192:16], col(22), A.subtract, "l2 c22", "uo1")
-        ts(T.nco[:], T.C[:].indirect(lo), 0.0, A.is_lt, Call + " lo%d" % s, "nco", 8192.0, A.mult)
-        for t in range(3):
-            n = 304 + 48 * t
-            ts(T.E[:, 400 * t:400 * t + n], T.SW[:, 0:n], T.uo[:, t:t + 1], A.is_equal, "SW0 SW1 uo0", "E%d" % t,
-               -1.0, A.mult)
-            if t == 0:
-                tt(T.fl[:], T.C[:].indirect(T.lu[:, 0:3]), T.nco[:], A.is_ge, Call + " lu nco", "fl")
-                mm(grp(T.pa[:, 288:291], [(sel(T.ZS, p), T.fl[:, p::16]) for p in range(16)]), "ZS fl", "pa")
-        for t in range(3):
-            n = 304 + 48 * t
-            Et = T.E[:, 400 * t:400 * t + n]
-            scan(T.EO[:, 400 * t + 400 - n:400 * t + 400], Et, Et, 0.0, A.min, A.min, "E%d" % t, "EO")
-        if last:
-            turn(lambda t: T.rem[:, t:112:7], "rem", "pe")
-        cp(T.c48[:], T.C[:].indirect(lo), Call + " lo%d" % s, "c48")
-        tt(T.gr[:, 0:3], T.pa[:, 288:291], T.EO[:, 399::400], A.is_equal, "pa EO", "gr")
-        tt(T.uo[:, 8:11], T.uo[:, 0:3], T.uo[:, 4:7], A.subtract, "uo0 uo1", "uo2")
-        for t in range(3):
-            ts(T.lt[:, 4 * s + t:4 * s + t + 1], T.gr[:, t:t + 1], T.uo[:, 8 + t:9 + t], A.mult, "gr uo1 uo2",
-               "lt%d" % s, T.uo[:, 4 + t:5 + t], A.add)
-        move = [lambda: tt(T.nco[:], T.C[:].indirect(lt), T.c48[:], A.max, Call + " lt%d c48" % s, "nco"),
-                lambda: cp(T.C[:].indirect(lt), T.nco[:], "nco lt%d" % s, Call)]
-        for f in refresh(s):
-            f()
-            if move:
-                move.pop(0)()
-        cp(T.xe[:], win.indirect(T.exu[:, 0:14]), "XF exu", "xe")
-        ts(T.re_[:], T.xe[:], MAGIC, A.add, "xe", "re", MAGIC, A.subtract)
-        la, lb = [], []
-        for d in range(1, 8):
-            a, b = 32 * d - 32, 32 * d
-            la += grp(T.pg[:, a:b], [(PMm(d % 3, 0), T.xe[:, a:b]), (PMm(d % 3, 1), T.re_[:, a:b])])
-            lb += grp(T.ph[:, a:b], [(PMm(d % 3, 2), T.re_[:, a:b])])
-        mm(la, "PM xe re", "pg")
-        mm(lb, "PM1 PM2 Ib re", "ph")
-        tt(T.ti[:], T.C[:, D + V:D + W], T.KJ[:, 0:224], A.min, "C KJ", "ti")
-        if last:
-            op("V", lambda: v.transpose(T.remT[:], T.pe[:, 0:224]), "pe", "remT")
-        tt(T.t2[:], T.pg[:, 0:224], T.DL[:], A.min, "pg DL", "t2")
-        tt(T.snd[:, 224 * s:224 * s + 224], T.ph[:, 0:224], T.t2[:], A.add, "ph t2", "snd%d" % s)
-        deps("G", ["snd%d" % s], [])
+            cp(B("GG", 16 * GA, 2048), X(win, B("gve", GA, 128)))
+        sc(0, 128)
+        ga(128, 192)
+        if first:
+            consts_ca()
+        ga(192, 256)
+        p_g(0, 128, range(10))
+        bind(0)
+        if first:
+            ts(col(41), col(1), 0.5, A.add)
+            ts(col(42), col(1), 256.0 + K2 - ZB, A.add)
+            consts_d()
+        outs(0, lambda: sc(128, 192))
+        p_g(0, 128, range(10, 15))
+        waiters(0)
+        marks(0)
+        p_g(128, 256, range(10))
+        sc(192, 256)
+        if first:
+            consts_da()
+        lists("pb", 4, "TT", 0, "wl", lambda: bind(1))
+        mx, go, rm, ro = four(0, 256)
+        outs(1)
+        mm(grp(B("pa", 0, 256), [(M(8), mx), (M(9), go)]))
+        p_g(128, 256, range(10, 15))
+        rows_a(3)
+        act(B("ab"), B("pa", 0, 256), AF.Abs, scale=0.0625)
+        waiters(1)
+        cp(X(B("XF"), B("obu")), mx)
+        old = refresh(range(s - 1, -1, -1))
+        marks(1)
+        o = B("ph", 0, 256)
+        mm([(o, M(1), mx, False, False), (o, M(3), go, False, False), (o, M(7), rm, False, False),
+            (o, M(7), ro, False, False), (o, Ib, B("ab"), False, True)])
+        for k in range(4):
+            if old:
+                old.pop(0)()
+            vtr(B("TT", 128 + k, 256, 4), B("pc", k, 128, 4))
+        snd = B("snd", 224 * s, 224 * s + 224)
+        cp(snd, X(win, B("exu", 0, 14)))
+        deps("G", [snd], [])
         trs = []
         for d in range(1, 8):
             peer = T.cores[rank ^ d]
@@ -592,79 +614,151 @@ def rank_program(g, core, T, topo):
             tops["snt"] = tops.get("snt", 0) + n
             tops["arr%d" % s] = tops.get("arr%d" % s, 0) + n
         g.remote_dma_fused(trs, local_sem=T.sem.snt)
-        lastw["land%d" % s] = ("arr%d" % s, tops["arr%d" % s])
-        mm(grp(T.pg[:, 0:224], [(T.If[:], T.C[:, D + V:D + W]), (T.I256[:], T.ones[:]), (T.Ib[:], T.ones[:]),
-                                (T.I256[:], T.ti[:])]), "I256 If Ib ones ti C", "pg")
-        cp(T.XT[:, 0:D + V].indirect(T.obu[:]), T.S[:, 14::16], Sall + " obu XTd", "x0")
+        Ln = B("land", 224 * s, 224 * s + 224)
+        done(("arr%d" % s, tops["arr%d" % s]), [], [Ln])
+        if first:
+            fill(B("neg1"), -1)
+            fill(B("k4"), 4096)
+            fill(B("XT", 0, D), 0)
+        ts(B("want", 0, 256), o, 2 * K1 + 1.0 / 32, A.is_gt)
+        ts(B("wl", 128, 256), B("TT", 128, 256), WK - 1.0, A.add)
+        mm(grp(B("pd", 0, 256), [(M(8), go), (B("IL"), B("want", 0, 256)), (MC, B("ones", 0, 256))]))
+        scan(B("rank"), B("ones"), B("want"), 0.0, A.mult, A.add)
+        rows_a(4)
+        for t in range(3):
+            act(B("EQ", 304 * t, 304 * t + 304), B("rank"), AF.Sign, bias=B("jh", t, t + 1), scale=-1.0,
+                accum_out=B("ca", t, t + 1))
+        rows_a(3)
+        tt(B("SW", 0, 256), B("pd", 0, 256), B("ob"), A.max)
+        if first:
+            consts_e()
         if last:
-            dma("d_y0", T.yx[:, 0:V], T.XT[:, D:D + V], "x0", "")
-            ycm(0, 8)
-        scat_v(T.wl, "wl", 16, range(BIND_ACT[s], 16))
-        Ln = T.land[:, 224 * s:224 * s + 224]
-        Lp, lpn = (T.L0[:], "L0") if s == 0 else (T.land[:, 224 * s - 224:224 * s], "land%d" % (s - 1))
-        tt(T.nf[:], Ln, Lp, A.not_equal, "land%d %s" % (s, lpn), "nf")
-        tt(T.qm[:], T.pg[:, 0:224], T.nf[:], A.mult, "pg nf", "qm")
-        shuffle("pf", 112, [("h", T.qm)], T.CCi, "qm CCi")
-        if last:
-            ts(T.re_[:], Ln, MAGIC, A.add, "land2", "re", MAGIC, A.subtract)
-            mm(grp(T.ph[:, 0:224], [(PMm(0, 2), Ln), (PMm(0, 1), Ln), (PMm(0, 0), T.re_[:])]), "PM Ib land2 re", "ph")
-        lists("pf", 7, T.wi, "wi", -1.0)
-        scat_a(T.wi, "wi", 14, range(IMP_ACT[s]), False)
-        for h in range(2):
-            act(T.ASb[:, 896 * h:896 * h + 896], T.AS[:, WK + 896 * h:WK + 896 * h + 896], AF.Copy, "AS", "ASb%d" % h)
-        if last:
-            ts(T.XT[:, D + V:D + W], T.ph[:, 0:224], -1.0, A.max, "ph", "XTi")
-            dma("d_y1", T.yx[:, V:W], T.XT[:, D + V:D + W], "XTi", "")
-        side = []
-        if last:
-            for k in range(2, -1, -1):
-                side.append(lambda k=k: cp(T.c48[:], T.F[:].indirect(T.lt[:, 4 * k:4 * k + 3]), "F lt%d" % k, "c48"))
-                side.append(lambda k=k: cp(T.F[:].indirect(T.lo[:, 4 * k:4 * k + 3]), T.c48[:], "c48 lo%d" % k, "F"))
-            side.append(lambda: dma("d_yf", T.yf[:], T.F[0:128:16, D:D + W], "F", ""))
+            cp(X(B("XT", 0, D + V), B("obu")), mx)
+            dma("d_y0", T.yx[:, 0:V], B("XT", D, D + V))
+            turn([lambda t: B("aws", t, 112, 7), lambda t: B("aws", t, 112, 7), lambda t: B("sg", t, 112, 7)], "pb")
         else:
-            side.append(lambda: cp(T.XF[:, D + V:D + W], Ln, "land%d" % s, "XF"))
-            side += refresh(s)[:-2]
+            rows_v(2 - first)
+        ts(B("lz", 0, 3), B("ca", 0, 3), 8.0, A.mult, 2447.0, A.add)
+        ts(B("lz", 4, 7), B("ca", 0, 3), 8.0, A.mult, 2446.0, A.add)
+        rows_v(1)
+        cp(B("cs"), X(B("S"), B("lz", 0, 7)))
+        dec = [(sel("Zd", p), B("cs", p, 112, 16)) for p in range(16)]
+        mm([m for t in range(3) for m in grp(B("pa", 48 * t, 48 * t + 48),
+                                             [(M(8), B("cs", 64, 112)), (Ib, B("M192", 48 * t, 48 * t + 48))])])
+        mm(grp(B("pe", 0, 7), dec))
+        mm([(B("pf", 0, 7), l, x, i == 0, False) for i, (l, x) in enumerate(dec)])
+        lin(B("SW", 256, 400), B("pa", 0, 144), 1.0, ZB - SH)
+        if first:
+            consts_ea()
+        rows_a(32)
+        rows_v(1)
+        ts(B("LU", 0, 7), B("pe", 0, 7), ZB, A.add)
+        ends = (0, 304, 656, 1056)
+
+        def equal(t):
+            ts(B("E", ends[t], ends[t + 1]), B("SW", 0, 304 + 48 * t), SH - ZB, A.add, B("pe", 4 + t, 5 + t), A.is_equal)
+
+        equal(0)
+        cp(B("cc"), X(B("C"), B("LU", 0, 7)))
+        equal(1)
+        tt(B("mn"), B("cc", 0, 48), B("cc", 64, 112), A.min)
+        mm([(B("pf", a, a + 3), sel("Z8h", p), B("mn", p, 48, 16), False, False) for a in (0, 4) for p in range(16)])
+        equal(2)
+        tt(B("mxc"), B("cc", 0, 48), B("cc", 64, 112), A.max)
+        scan(B("EO"), B("E"), B("E"), 0.0, A.add, A.max)
+        mm([(B("pf", a + t, a + t + 1), B("I8h", 128 * k, 128 * k + 128), B("EO", ends[t + 1 - k] - 1, ends[t + 1 - k]),
+             False, a + t + k == 7) for a in (0, 4) for t in range(3) for k in range(2) if t >= k])
+        fn = B("fn", 224 * s, 224 * s + 224)
+
+        def blk(n, d, k=0):
+            return B(n, 224 * k + 32 * d - 32, 224 * k + 32 * d)
+
+        lst = [(B("pg", 0, 224), Ib, B("neg1"), True, False)]
+        if first:
+            lst.append((B("pg", 0, 224), Ib, B("k4"), False, False))
+        else:
+            lst += [(blk("pg", d), PMm(2, d), blk("fn", d, s - 1), False, False) for d in range(1, 8)]
+        mm(lst)
+        if last:
+            vtr(B("remT"), B("pb", 0, 224))
+        shuffle("pb", 112, "c", "CCi")
+        ts(fn, Ln, 14.0625, A.is_equal, -4096.0, A.mult)
+        mm([(blk("pg", d), PMm(1, d), blk("fn", d, s), False, d == 7) for d in range(1, 8)])
+        tt(B("sel", 0, 7), B("pf", 0, 7), B("dd", 0, 7), A.max)
+        rows_v(1)
+        ts(B("LT", 8 * s, 8 * s + 7), B("sel", 0, 7), ZB - K2, A.add)
+        rows_v(1)
+        cp(X(B("C"), B("LT", 8 * s + 4, 8 * s + 7)), B("mxc"))
+        if last:
+            for a in (0, 1280):
+                narrow(B("C16", a, a + 1280), B("C", D + a, D + a + 1280))
+            dma("d_as", B("asn"), rows("AS2", slice(0, 128, 16), WK, WW))
+        else:
+            narrow(B("ASc"), B("AS2", WK, WW))
+        side = refresh(range(2, -1, -1), "F", "c48") if last else []
+        rows_v(1)
+        tt(B("Cm"), B("C", D + V, D + W), B("pg", 0, 224), A.min)
+        shuffle("pb", 112, "h", "Cm")
+        rows_v(1)
+        scan(B("ti"), B("KJ"), B("Cm"), -1.0, A.max, A.min)
+        shuffle("pb", 112, "b", "ti")
+        mm([m for d in range(1, 8) for m in grp(blk("pc", d), [(PMm(0, d), blk("land", d, s)), (PMm(1, d), blk("fn", d, s))])])
+        if not last:
+            mm([(B("pd", 0, 224), I32x, B("NC", 0, 224), True, False)]
+               + [(blk("pd", d), PMm(1, d), blk("fn", d, s), False, d == 7) for d in range(1, 8)])
+        rows_v(1)
+        lists("pb", 7, "TI", 0, "wi", lambda: rows_v(1))
+        if not last:
+            lin(B("wS"), B("pd", 0, 224), -1.0, -4097.0)
+            lin(B("ab", 0, 128), Ib, LEV[s] / 4)
+        for r in range(IMP_ACT[s]):
+            scat_a("AS", B("wi", 14 * r, 14 * r + 14))
+        for h in range(2):
+            act(B("ASb", 896 * h, 896 * h + 896), B("AS", WK + 896 * h, WK + 896 * h + 896), AF.Copy)
+        rows_v(32)
+        if last:
+            side.insert(0, lambda: ts(B("XT", D + V, D + W), B("pc", 0, 224), -1.0, A.max))
+            side.insert(1, lambda: dma("d_y1", T.yx[:, V:W], B("XT", D + V, D + W)))
+            side.append(lambda: dma("d_yf", T.yf[:], rows("F", slice(0, 128, 16), D, D + W)))
+        else:
+            side = [lambda: tt(B("XF", D + V, D + W), B("pc", 0, 224), B("wS"), A.max)]
         for r in range(IMP_ACT[s], 16):
-            if side and len(side) >= 16 - r - 2 * last:
+            scat_v("AV2" if r < 16 - AV_ONLY and r % 2 == AV_ONLY % 2 ^ 1 else "AV", B("wi", 14 * r, 14 * r + 14))
+            if side:
                 side.pop(0)()
-            scat_v(T.wi, "wi", 14, [r])
         for f in side:
             f()
+
+        def piece(n, p, a=WK):
+            return B(n, a + 112 * p, a + 112 * p + 112) if last else B(n, a + p, a + G, 16)
+
+        o = B("ph", 0, 112)
         if last:
-            def piece(Wn, p):
-                return Wn[:, WK + 112 * p:WK + 112 * p + 112]
+            mm([(o, B("If"), B("asn"), True, False)])
+            mm(grp(B("pe", 0, 160), [(sel("ZSh", p), B("C16", 160 * p, 160 * p + 160)) for p in range(16)]))
+            mm([(B("ph", 16 * t, 16 * t + 16), B("ILf"), B("remT", 32 * t, 32 * t + 16), False, False) for t in range(7)])
+            act(B("yc_"), B("pe", 0, 160), AF.Copy)
+            dma("d_yc", T.yc[:], B("yc_"))
         else:
-            def piece(Wn, p):
-                return Wn[:, WK + p:WK + p + G:16]
-        o = T.pd[:, 0:112]
-        if not last:
-            mm([(o, T.Ib[:], T.rem[:], True, False)], "rem Ib", "pd")
-        mm([(o, sel(T.Z0f, p), piece(T.AS2, p), last and p == 0, False) for p in range(16)], "Z0f AS2", "pd")
-        if last:
-            ycm(8, 16)
-            mm([(T.pd[:, 16 * t:16 * t + 16], T.If[:], T.remT[:, 32 * t:32 * t + 16], False, False) for t in range(7)],
-               "remT If", "pd")
-            act(T.yc_[:], T.pc[:, 0:160], AF.Copy, "pc", "yc")
-            dma("d_yc", T.yc[:], T.yc_[:], "yc", "")
-        mm([(o, sel(T.Z0, p), piece(T.AV2, p), False, False) for p in range(16)], "Z0 AV2", "pd")
+            il = B("ab", 0, 128)
+            mm([(o, il, B("aws", 0, 112), True, False), (o, il, B("aws", 0, 112), False, False),
+                (o, il, B("sg"), False, False)])
+            open_counts()
+            mm([(o, sel("Z0", p), piece("ASc", p, 0), False, False) for p in range(16)])
+        mm([(o, sel("Z0", p), piece("AV2", p), False, False) for p in range(16)])
         for h in range(2):
             if last:
-                lst = [(o, sel(T.Z0, p), T.ASb[:, 112 * p:112 * p + 112], False, False) for p in range(8 * h, 8 * h + 8)]
+                mm([(o, sel("Z0", p), piece("ASb", p, 0), False, False) for p in range(8 * h, 8 * h + 8)])
             else:
-                lst = [(T.pd[:, 56 * h:56 * h + 56], sel(T.Z0, p), T.ASb[:, 896 * h + p:896 * h + 896:16], False, False)
-                       for p in range(16)]
-            if h == 1 and AV_FIRST:
-                mm([(o, sel(T.Z0, p), piece(T.AV, p), False, False) for p in range(16)], "Z0 AV", "pd")
-                lst[-1] = lst[-1][0:4] + (True,)
-            mm(lst, "Z0 ASb%d" % h, "pd")
-        if not AV_FIRST:
-            mm([(o, sel(T.Z0, p), piece(T.AV, p), False, p == 15) for p in range(16)], "Z0 AV", "pd")
+                mm([(B("ph", 56 * h, 56 * h + 56), sel("Z0", p), B("ASb", 896 * h + p, 896 * h + 896, 16), False, False)
+                    for p in range(16)])
+        mm([(o, sel("Z0", p), piece("AV", p), False, p == 15) for p in range(16)])
         if last:
-            ts(T.yw_[:], o, 0.75 * LEV[s], A.is_gt, "pd", "yw")
-            dma("d_yw", T.yw[:], T.yw_[:], "yw", "")
+            ts(B("yw_"), o, 0.5 * LEV[s], A.is_gt)
+            dma("d_yw", T.yw[:], B("yw_"))
         else:
-            for f in refresh(s)[-2:]:
-                f()
-            ts(T.aws[:, 0:112], o, 0.75 * LEV[s], A.is_gt, "pd", "aws")
+            cp(X(B("XT", 0, D + V), B("obu")), mx)
+            ts(B("aws", 0, 112), o, 0.5 * LEV[s], A.is_gt)
+            later += refresh(range(s, -1, -1))
     for k in tops:
         need("S", (k, tops[k]))

@@ -11,11 +11,23 @@ K1, K2 = 65536.0, 131072.0
 ZB = float(D - 623925)
 SH = 1024.0
 LEV = (16, 512, 16384)
-BIND_ACT = (24, 24, 24)
-IMP_ACT = (6, 6, 6)
+HALVES = ((0, 128), (128, 256))
+BIND_VEC = ((2, 6), (2, 6), (2, 6))
+LATCH = (False, False)
+RO_ACT = (False, True)
+SW_ACT = False
+XT_PARTS = ((0, 256),)
+ROUNDS = 3
+SCAT_A = 2.8
+SND_ACT = False
+NARROW_G = 672
+IMP_ACT = (5, 6, 6)
 AV_ONLY = 3
-GA = 80
-EM_ACT = (1, 3)
+GATHER = ((0, 64, "A"), (64, 128, "V"), (128, 208, "A"), (208, 240, "A"), (240, 256, "V"))
+GATHER0 = GATHER
+SCANS = ((0, 64), (64, 128), (128, 208), (208, 256))
+EM_ACT = ()
+CY, CALL_V, CALL_A, HOP, GATH, SCAT, COL, FLY, OVER = 0.83, 66, 86, 160, 1.3, 2.8, 0.42, 2500, 150
 
 
 def sb(n, dt):
@@ -25,24 +37,24 @@ def sb(n, dt):
 F32, BF, F16, I32, U16 = "float32", "bfloat16", "float16", "int32", "uint16"
 SCRATCH = {
     "awi": sb(112, I32), "awb": sb(112, BF), "aws": sb(128, BF), "sc1": sb(136, BF),
-    "gvi": sb(2048, I32), "ci": sb(W, I32), "exi": sb(16, I32), "exu": sb(16, U16),
-    "XF": sb(XW, BF), "XT": sb(D + W, BF), "C": sb(XW, F32), "F": sb(XW, F32),
+    "gvi": sb(2048, I32), "exi": sb(16, I32), "exu": sb(16, U16),
+    "XF": sb(XW, BF), "XT": sb(D + W, BF), "C": sb(XW, I32), "F": sb(XW, F32),
     "em": sb(V, BF), "et": sb(V, BF),
     "AV": sb(WW, BF), "AV2": sb(WW, BF), "AS": sb(WW, F32), "AS2": sb(WW, F32), "ASb": sb(G, BF),
     "ASc": sb(G, BF), "C16": sb(W, F16), "asn": sb(112, F32),
-    "lv": sb(224, BF), "ls": sb(224, F32),
-    "GG": sb(4096, BF), "S": sb(4864, BF), "SM": sb(2048, BF), "RM": sb(256, BF), "RO": sb(256, BF),
+    "lv": sb(672, BF), "ls": sb(672, F32),
+    "GG": sb(4096, BF), "S": sb(4864, BF), "SM": sb(16 * max(b - a for a, b in SCANS), BF), "RM": sb(256, BF), "RO": sb(256, BF),
     "pi": sb(8, I32), "co_": sb(48, F32), "xb": sb(256, BF), "mg": sb(512, BF), "JR": sb(512, BF),
-    "oh": sb(16, F32), "pw": sb(32, F32), "t16": sb(32, F32), "dg": sb(160, F32), "dgi": sb(160, I32),
+    "oh": sb(16, F32), "pw": sb(32, F32), "t16": sb(64, F32), "dg": sb(160, F32), "dgi": sb(320, I32),
     "Bp": sb(512, BF), "An": sb(32, F32), "NC": sb(288, BF),
-    "WE": sb(160, BF), "WO": sb(160, BF), "BO": sb(512, BF), "TRI": sb(128, BF), "ZS": sb(144, BF), "Zd": sb(144, BF),
+    "J": sb(144, BF), "BO": sb(512, BF), "TRI": sb(128, BF), "ZS": sb(144, BF), "Zd": sb(144, BF),
     "ZSh": sb(144, F16), "Z8h": sb(144, F16), "Z0h": sb(144, F16), "Z0": sb(144, BF),
-    "If": sb(128, F32), "Ib": sb(128, BF), "IL": sb(128, BF), "ILf": sb(128, F32), "I8h": sb(256, F16),
+    "If": sb(128, F32), "IL": sb(384, BF), "ILf": sb(128, F32), "I8h": sb(256, F16),
     "MM": sb(1408, BF), "PM": sb(1024, BF),
     "H0h": sb(144, F16), "H1h": sb(144, F16), "H0b": sb(144, BF), "H1b": sb(144, BF),
     "ones": sb(304, BF), "hv": sb(4, BF), "zr": sb(256, BF), "neg1": sb(224, BF), "k4": sb(224, BF),
     "jh": sb(4, F32), "dd": sb(8, F32), "jr": sb(256, F32),
-    "KJ": sb(224, BF), "CCb": sb(128, BF), "CCi": sb(224, BF), "M192": sb(144, BF),
+    "KJ": sb(224, BF), "CCb": sb(256, BF), "LC": sb(256, BF), "lat": sb(256, F32), "CCi": sb(224, BF), "M192": sb(144, BF),
     "EQ": sb(2048, BF), "pre": sb(128, F32), "sg": sb(112, BF), "remT": sb(224, F32),
     "bw": sb(16, U16), "cmp": sb(256, BF), "eu": sb(16, U16), "gve": sb(256, U16),
     "ob": sb(256, F16), "obu": sb(16, U16), "cg": sb(256, F16), "tm": sb(256, BF),
@@ -61,8 +73,94 @@ SCRATCH["fs"] = sb(sum(x[1] for x in PART.values()), F32)
 PSUMS = ("pa", "pb", "pc", "pd", "pe", "pf", "pg", "ph")
 for _b in PSUMS:
     SCRATCH[_b] = ("psum", [128, 512], F32)
-DMAS = ["d_aw", "d_x0", "d_gv", "d_ex", "d_c0", "d_c1", "d_y0", "d_y1", "d_yf", "d_yw", "d_yc", "d_zS", "d_zV", "d_as"]
+DMAS = ["d_aw", "d_x0", "d_gv", "d_ex", "d_co", "d_y0", "d_y1", "d_yf", "d_yw", "d_yc", "d_zS", "d_zV", "d_as"]
 SEMAPHORES = ["sV", "sA", "sP", "sG", "snt", "arr0", "arr1", "arr2"] + DMAS
+
+
+def meet(p, q):
+    if p[0] >= q[1] or q[0] >= p[1]:
+        return False
+    return p[2] != q[2] or (p[0] - q[0]) % p[2] == 0
+
+
+def plan(calls):
+    n, uses = len(calls), {}
+    pre = [set(c["after"]) for c in calls]
+    for i, c in enumerate(calls):
+        for vs, wr in ((c["r"], False), (c["w"], True)):
+            for x in vs:
+                old, bank = uses.get(x[1], []), x[1] in PSUMS
+                for j, w2, sp in old:
+                    if j != i and not (c["mark"] and wr and w2 and calls[j]["mark"]):
+                        if (bank and (wr or w2 or calls[j]["e"] != c["e"])) or ((wr or w2) and meet(sp, x[2:5])):
+                            pre[i].add(j)
+                if wr and not c["mark"]:
+                    old = [u for u in old if not (bank or (x[4] == 1 and x[2] <= u[2][0] and u[2][1] <= x[3]))]
+                uses[x[1]] = old + [(i, wr, x[2:5])]
+    post = [[] for _ in calls]
+    for i in range(n):
+        for j in pre[i]:
+            post[j].append(i)
+
+    def hop(j, i):
+        if j in calls[i]["after"] or calls[j]["e"] == calls[i]["e"] == "P":
+            return 0
+        return HOP + calls[j]["late"]
+
+    chain = [0] * n
+    for j in range(n - 1, -1, -1):
+        chain[j] = calls[j]["ns"] + max([calls[j]["late"]] + [hop(j, i) + chain[i] for i in post[j]])
+    def place(order, back):
+        start, busy = [0] * n, {e: [] for e in "VAPGS"}
+        for i in order:
+            ns, line = calls[i]["ns"], busy[calls[i]["e"]]
+            if back:
+                t = max([calls[i]["late"]] + [start[j] + calls[j]["ns"] + hop(i, j) for j in post[i]])
+            else:
+                t = max([0] + [start[j] + calls[j]["ns"] + hop(j, i) for j in pre[i]])
+            k = 0
+            while k < len(line) and line[k][0] < t + ns:
+                t = max(t, line[k][1])
+                k += 1
+            line.insert(k, (t, t + ns))
+            start[i] = t
+        return start
+
+    def ends(start, back):
+        return [start[i] + calls[i]["ns"] + (0 if back else calls[i]["late"]) for i in range(n)]
+
+    left, ready, free = [len(p) for p in pre], [0] * n, {e: 0 for e in "VAPGS"}
+    cand = {e: [i for i in range(n) if calls[i]["e"] == e and not pre[i]] for e in free}
+    order = []
+    while len(order) < n:
+        best = None
+        for e in free:
+            if cand[e]:
+                pick = top = max(cand[e], key=lambda i: chain[i])
+                if ready[top] > free[e]:
+                    fit = [i for i in cand[e] if max(free[e], ready[i]) + calls[i]["ns"] <= ready[top] + OVER and i != top]
+                    pick = max(fit, key=lambda i: chain[i]) if fit else top
+                t = max(free[e], ready[pick])
+                if best is None or t < best[0]:
+                    best = (t, e, pick)
+        t, e, j = best
+        order.append(j)
+        cand[e].remove(j)
+        free[e] = t + calls[j]["ns"]
+        for i in post[j]:
+            ready[i] = max(ready[i], free[e] + hop(j, i))
+            left[i] -= 1
+            if not left[i]:
+                cand[calls[i]["e"]].append(i)
+    if not ROUNDS:
+        return order
+    best, start = None, place(order, False)
+    for _ in range(ROUNDS):
+        if best is None or max(ends(start, False)) < max(ends(best, False)):
+            best = start
+        for back in (True, False):
+            start = place(sorted(range(n), key=lambda i: -start[i] - calls[i]["ns"]), back)
+    return sorted(range(n), key=lambda i: best[i])
 
 
 def rank_program(g, core, T, topo):
@@ -70,9 +168,7 @@ def rank_program(g, core, T, topo):
     if rank is None:
         return
     eng = {"V": g.vector, "A": g.scalar, "P": g.tensor, "G": g, "S": g.sync}
-    cnt = {"V": 0, "A": 0, "P": 0, "G": 0}
-    seen = {e: {} for e in eng}
-    uses, tops = {}, {}
+    calls = []
 
     def B(n, a=0, b=None, st=1):
         if n in PART:
@@ -86,65 +182,42 @@ def rank_program(g, core, T, topo):
     def X(win, off):
         return (win[0].indirect(off[0]),) + win[1:5] + (off,)
 
-    def meet(p, q):
-        if p[0] >= q[1] or q[0] >= p[1]:
-            return False
-        return p[2] != q[2] or (p[0] - q[0]) % p[2] == 0
+    def size(x):
+        return 16 * size(x[5]) if x[5] else len(range(x[2], x[3], x[4]))
 
-    def need(e, tok):
-        if seen[e].get(tok[0], 0) < tok[1]:
-            eng[e].wait_ge(T.sem[tok[0]], tok[1])
-            seen[e][tok[0]] = tok[1]
-
-    def deps(e, r, w):
-        own, want = "s" + e, {}
-        for vs, wr in ((r, False), (w, True)):
-            for x in vs:
-                for (sem, w2, sp), n in uses.get(x[1], {}).items():
-                    if sem == own and e == "P":
-                        continue
-                    if (x[1] in PSUMS and sem != own) or ((wr or w2) and meet(sp, x[2:5])):
-                        want[sem] = max(want.get(sem, 0), n)
-        for s in want:
-            need(e, (s, want[s]))
-
-    def done(tok, r, w):
-        tops[tok[0]] = tok[1]
-        for vs, wr in ((r, False), (w, True)):
-            for x in vs:
-                uses.setdefault(x[1], {})[(tok[0], wr, x[2:5])] = tok[1]
-
-    def views(r, w):
+    def call(e, fn, r, w, ns, late=0, sem=None, mark=False, after=()):
         r = [x for x in r if isinstance(x, tuple)]
-        return r + [x[5] for x in r + w if x[5]], w
+        calls.append({"e": e, "fn": fn, "r": r + [x[5] for x in r + w if x[5]], "w": w, "ns": ns, "late": late,
+                      "sem": sem, "mark": mark, "after": list(after)})
+        return len(calls) - 1
 
-    def op(e, fn, r, w):
-        r, w = views(r, w)
-        deps(e, r, w)
-        ins = fn()
-        cnt[e] += 1
-        ins.then_inc(T.sem["s" + e], 1)
-        done(("s" + e, cnt[e]), r, w)
+    def op(e, fn, r, w, cycles=None):
+        o = w[0]
+        if o[5] or (r and r[0][5]):
+            ns = 55 + size(o) * (SCAT if o[5] else GATH)
+        else:
+            narrow = all(SCRATCH[x[1]][2] in (BF, F16, U16) for x in [o] + r if isinstance(x, tuple) and size(x) > 1)
+            ns = (CALL_A if e == "A" else CALL_V) + CY * size(o) * (cycles or (0.5 if narrow and e == "V" else 1))
+        return call(e, fn, r, w, ns)
 
     def ap(x):
         return x[0] if isinstance(x, tuple) else x
 
-    def mm(lst):
+    def mm(lst, mark=False):
         def f():
             ins = None
             for o, l, x, s0, s1 in lst:
                 ins = g.tensor.matmul(o[0], l[0], x[0], s0, s1)
             return ins
-        op("P", f, [x for m in lst for x in m[1:3]], [m[0] for m in lst])
+        ns = sum(max(64, size(m[2])) * COL * (4 if SCRATCH[m[2][1]][2] == F32 else 1) for m in lst)
+        call("P", f, [x for m in lst for x in m[1:3]], [m[0] for m in lst], ns, 60, mark=mark)
 
     def grp(o, terms):
         return [(o, l, x, i == 0, i == len(terms) - 1) for i, (l, x) in enumerate(terms)]
 
-    def dma(sem, o, i, e="S"):
-        r, w = views([i], [o] if isinstance(o, tuple) else [])
-        deps(e, r, w)
-        eng[e].dma_start(ap(o), ap(i)).then_inc(T.sem[sem], 16)
-        done((sem, 16), r, w)
+    def dma(sem, o, i, late, after=()):
+        return call("S", lambda: g.sync.dma_start(ap(o), ap(i)), [i], [o] if isinstance(o, tuple) else [], 50, late, sem,
+                    after=after)
 
     v = g.vector
 
@@ -155,7 +228,7 @@ def rank_program(g, core, T, topo):
             op("V", lambda: v.tensor_scalar(o[0], i[0], ap(s1), ap(s2), o0, o1), [i, s1, s2], [o])
 
     def tt(o, a, b, o0):
-        op("V", lambda: v.tensor_tensor(o[0], a[0], b[0], o0), [a, b], [o])
+        op("V", lambda: v.tensor_tensor(o[0], a[0], b[0], o0), [a, b], [o], 1 if a[1] in PSUMS or b[1] in PSUMS else 2)
 
     def cp(o, i):
         op("V", lambda: v.tensor_copy(o[0], i[0]), [i], [o])
@@ -170,7 +243,7 @@ def rank_program(g, core, T, topo):
         op("V", lambda: v.transpose(o[0], i[0]), [i], [o])
 
     def red(o, i):
-        op("V", lambda: v.tensor_reduce(o[0], i[0], AxisListType.X, A.add), [i], [o])
+        op("V", lambda: v.tensor_reduce(o[0], i[0], AxisListType.X, A.add), [i], [o], 16)
 
     def act(o, i, f, **kw):
         acc = [kw["accum_out"]] if "accum_out" in kw else []
@@ -181,13 +254,14 @@ def rank_program(g, core, T, topo):
         act(o, i, AF.Identity, scale=scale, bias=bias)
 
     def iota(o, pat, base, cm=0):
-        if SCRATCH[o[1]][2] == I32:
-            op("G", lambda: g.iota(o[0], pat, base, cm), [], [o])
-        else:
-            op("G", lambda: g.iota(o[0], pat, base, cm, allow_small_or_imprecise_dtypes=True), [], [o])
+        kw = {} if SCRATCH[o[1]][2] == I32 else {"allow_small_or_imprecise_dtypes": True}
+        call("G", lambda: g.iota(o[0], pat, base, cm, **kw), [], [o], 130 + 2 * CY * size(o))
 
     def fill(o, c):
-        iota(o, [[0, len(range(o[2], o[3], o[4]))]], c)
+        iota(o, [[0, size(o)]], c)
+
+    def select(o, i, pat, cm, test=A.is_ge):
+        call("G", lambda: g.affine_select(o[0], i[0], pat, test, 0.0, 0, cm), [i], [o], 170 + 2 * CY * size(o))
 
     def col(i):
         return B("co_", i, i + 1)
@@ -198,9 +272,9 @@ def rank_program(g, core, T, topo):
     def sel(n, p):
         return B(n, 15 - p, 143 - p)
 
-    Ib, BO, xb = B("Ib"), B("BO", 0, 128), B("xb", 0, 128)
-    x144, x160 = B("xb", 0, 144), B("xb", 0, 160)
-    I32x, MC = M(2), M(10)
+    Ib, BO, xb = B("J", 0, 128), B("BO", 0, 128), B("xb", 0, 128)
+    x144 = B("xb", 0, 144)
+    I32x, MC, IK = M(2), M(10), B("IL", 256, 384)
     EB = ("pa", "pc", "pd", "pe")
 
     def PMm(kind, d):
@@ -210,240 +284,220 @@ def rank_program(g, core, T, topo):
         a = 128 * (3 * kind + k - 1)
         return B("PM", a, a + 128)
 
-    dma("d_aw", B("awi"), T.aw[:])
-    dma("d_x0", B("XT", D, D + V), T.x0[:])
-    dma("d_gv", B("gvi", 0, G), T.gv[:])
-    dma("d_ex", B("exi", 0, 14), T.ex[:])
-    dma("d_c0", B("ci", 0, 1280), T.co[:, 0:1280])
-    dma("d_c1", B("ci", 1280, W), T.co[:, 1280:W])
+    k = []
+    for sem, o, i, late in (("d_aw", B("awi"), T.aw[:], 1100), ("d_x0", B("XT", D, D + V), T.x0[:], 3100),
+                            ("d_gv", B("gvi", 0, G), T.gv[:], 6200), ("d_ex", B("exi", 0, 14), T.ex[:], 6200),
+                            ("d_co", B("C", D, D + W), T.co[:], 10600)):
+        k = [dma(sem, o, i, late, k)]
 
     iota(B("pi", 0, 1), [[0, 1]], 0, 1)
     iota(B("xb"), [[1, 256]], 0)
     iota(B("mg"), [[0, 4], [16, 8], [0, 16]], 0)
     fill(B("ones"), 1)
     iota(rows("JR", slice(0, 1), 0, 512), [[-16, 4], [0, 8], [-1, 16]], 0)
-    for k in range(7):
-        act(B("AS", WK + 256 * k, WK + 256 * k + 256), B("xb"), AF.Silu, scale=0.0)
-    dma("d_zS", B("AS2", WK, WW), B("AS", WK, WW))
-    ms(B("t16", 0, 16), 4.0)
-    ms(B("t16", 16, 32), 0.0)
-    ms(B("oh"), 0.25)
     for j, m in enumerate((15, 16, 1, 96)):
         ts(B("pi", j + 1, j + 2), B("pi", 0, 1), m, A.bitwise_and)
-    scan(B("pw", 0, 16), B("t16", 0, 16), B("t16", 16, 32), 0.25, A.mult, A.add)
-    scan(B("pw", 16, 32), B("oh"), B("t16", 16, 32), 4.0, A.mult, A.add)
     cp(B("co_", 0, 5), B("pi", 0, 5))
-    ms(B("aws", 112, 128), 1.0)
-    ms(B("sc1", 0, 1), 0.0)
-    ts(col(12), col(0), 16.0, A.add)
     ts(col(13), col(2), 0.0, A.is_equal)
     ts(col(14), col(2), 0.0, A.is_gt)
+    tt(col(15), col(0), col(1), A.subtract)
+    ts(col(16), col(15), 15.0, A.add)
+    ts(col(17), col(1), 15.0, A.is_equal)
     ts(B("oh"), B("xb", 0, 16), col(1), A.is_equal)
+    for j in range(7):
+        act(B("AS", WK + 256 * j, WK + 256 * j + 256), B("xb"), AF.Silu, scale=0.0)
+        calls[-1]["ns"] += 1300 * (j == 0)
+    dma("d_zS", B("AS2", WK, WW), B("AS", WK, WW), 4000, k)
+    fill(B("AV", WK, WW), 0)
+    dma("d_zV", B("AV2", WK, WW), B("AV", WK, WW), 2500, k)
+    ms(B("t16", 0, 16), 4.0)
+    ms(B("t16", 16, 32), 0.0)
+    ms(B("t16", 32, 48), 0.25)
+    scan(B("pw", 0, 16), B("t16", 0, 16), B("t16", 16, 32), 0.25, A.mult, A.add)
+    scan(B("pw", 16, 32), B("t16", 32, 48), B("t16", 16, 32), 4.0, A.mult, A.add)
     ts(col(5), col(1), 4.0, A.is_lt)
     ts(col(6), col(1), 6.5, A.is_lt)
-    ts(B("WE"), x160, col(12), A.is_equal, col(13), A.mult)
-    ts(B("WO"), x160, col(12), A.is_equal, col(14), A.mult)
-    tt(B("t16", 16, 32), B("pw", 16, 32), B("oh"), A.mult)
-    tt(col(15), col(0), col(1), A.subtract)
     tt(col(7), col(6), col(5), A.subtract)
-    red(col(9), B("t16", 16, 32))
-    cp(B("awb"), B("awi"))
-
-    def turn(terms, bank):
-        lst = []
-        for t in range(7):
-            lst += grp(B(bank, 32 * t, 32 * t + 16), [(B("WE", 16, 144), f(t)) for f in terms])
-            lst += grp(B(bank, 32 * t + 16, 32 * t + 32), [(B("WO", 32, 160), f(t)) for f in terms])
-        mm(lst)
-
-    def open_counts():
-        mm([(B(b), rows("ones", slice(0, 1), 0, 128), rows("JR", slice(0, 1), 0, 512), True, False) for b in EB])
-
-    turn([lambda t: B("awb", 16 * t, 16 * t + 16)], "pf")
-    open_counts()
-    ts(B("BO"), B("mg"), col(15), A.is_equal)
-    op("G", lambda: g.affine_select(T.TRI[:], T.BO[:, 0:128], [[1, 128]], A.is_ge, 0.0, 0, -1), [BO], [B("TRI")])
-    for k, c in enumerate((1, 16)):
-        fill(B("hv", 2 * k, 2 * k + 1), c)
-    fill(B("zr"), 0)
-    fill(B("gvi", G, 2048), W)
-    fill(B("XF", D + W, XW), 0)
-    iota(B("jr"), [[1, 256]], -int(SH))
-    fill(B("C", 0, D), -1)
-    fill(B("C", D + W, XW), -1)
-    fill(B("ls"), LEV[0])
-    fill(B("XF", 0, D), 0)
-    fill(B("AV", WK, WW), 0)
-    dma("d_zV", B("AV2", WK, WW), B("AV", WK, WW))
-    fill(B("S", 4096, 4864), 0)
-    fill(B("want", 256, 304), 1)
-    iota(B("M192"), [[-16, 3], [1, 48]], 0)
-    fill(B("lv"), LEV[0])
+    tt(B("t16", 48, 64), B("pw", 16, 32), B("oh"), A.mult)
+    red(col(9), B("t16", 48, 64))
     tt(col(10), col(9), col(5), A.mult)
     ts(col(11), col(9), 256.0, A.mult, col(7), A.mult)
     ts(col(33), col(7), -14.0625 / 32, A.mult, -1.0 / 32, A.add)
     ts(col(34), col(7), -14.0625, A.mult, 15.0625, A.add)
-    ts(B("dg", 0, 128), xb, col(10), A.mult, -0.4921875, A.add)
-    ts(B("dg", 128, 160), B("xb", 0, 32), col(11), A.mult, -0.4921875, A.add)
+    ts(B("dgi", 0, 128), xb, col(10), A.mult, -0.4921875, A.add)
+    ts(B("dgi", 128, 160), B("xb", 0, 32), col(11), A.mult, -0.4921875, A.add)
+    ts(B("dgi", 160, 320), B("dgi", 0, 160), 3, A.bitwise_and)
+    ts(B("An"), B("dgi", 288, 320), -0.0625 / 32, A.mult, col(33), A.add)
+    ts(B("Bp", 0, 128), B("dgi", 160, 288), 0.0625, A.mult, col(34), A.add)
+    for n in (128, 256):
+        lin(B("Bp", n, 2 * n), B("Bp", 0, n), 1.0)
+    for a, b, lo, h in ((0, 96, 32, 18), (96, 224, 0, 19), (224, 288, 0, 20)):
+        ts(B("NC", a, b), B("Bp", lo, lo + b - a), B("An", h, h + 1), A.mult)
+    lin(B("XF", D + V, D + W), B("NC", 0, 224), -32.0, -1.0)
+    fill(B("S", 4096, 4864), 0)
+    for i in (14, 15):
+        lin(B("S", 4096 + i, 4864, 16), B("NC", 240, 288), -32.0, -1.0)
+    tt(B("t16", 0, 16), B("pw", 0, 16), B("oh"), A.mult)
+    red(col(8), B("t16", 0, 16))
+    ts(col(43), col(7), 8.0, A.mult)
+    ts(col(18), col(5), 16.0, A.mult, col(43), A.add)
+    tt(col(19), col(18), col(8), A.mult)
+    select(B("J"), B("ones", 0, 144), [[1, 144]], -1, A.is_equal)
+    ts(B("BO"), B("mg"), col(15), A.is_equal)
+    select(B("TRI"), BO, [[1, 128]], -1)
+    ts(B("ZS"), x144, col(16), A.is_equal)
+    for j, c in enumerate((1, 16)):
+        fill(B("hv", 2 * j, 2 * j + 1), c)
+    lin(B("hv", 1, 4, 2), B("hv", 0, 4, 2), 0.5)
+    lin(I32x, Ib, 32.0)
+    lin(col(38), B("oh", 0, 1), -622592.0)
+    lin(col(39), B("oh", 1, 2), -2048.0, col(38))
+    lin(col(40), B("oh", 2, 3), -5.0, col(39))
+    lin(col(35), col(17), -K1, col(40))
+    lin(col(20), col(17), 16 * K1, 64 * K1)
+    ts(M(0), BO, -64 * K1, A.mult)
+    ts(M(1), BO, col(20), A.mult)
+    lin(M(3), BO, col(35))
+    ts(M(4), BO, -K2, A.mult)
+    ts(M(5), BO, K2, A.mult)
+    ts(M(7), BO, col(17), A.mult, -16 * K1, A.mult)
+    ts(M(8), BO, col(19), A.mult)
+    ts(M(9), BO, col(19), A.mult, -1.0, A.mult)
+    ts(MC, BO, col(40), A.mult)
+    lin(IK, Ib, K1)
+    lin(B("Z0h"), B("ZS"), B("oh", 0, 1))
+    lin(B("Z0"), B("ZS"), B("oh", 0, 1))
+    lin(B("Zd"), B("ZS"), col(19))
+    lin(B("Z8h"), B("ZS"), -8192.0)
+    lin(B("ZSh"), B("ZS"), 1.0)
+    lin(B("If"), Ib, 1.0)
+    lin(B("ILf"), Ib, LEV[2] / 4)
+    for j in range(2):
+        lin(B("IL", 128 * j, 128 * j + 128), Ib, LEV[j] / 4)
+        lin(B("I8h", 128 * j, 128 * j + 128), Ib, 8192.0 * (2 * j - 1))
+    lin(col(23), col(1), 2.0, col(4))
+    lin(col(24), col(23), 1.0, 1.0)
+    for n, c in (("H0", 13), ("H1", 14)):
+        ts(B(n + "h"), x144, col(24), A.is_equal, col(c), A.mult)
+        lin(B(n + "b"), B(n + "h"), 256.0)
+    lin(col(27), col(15), -1.0, 112.0)
+    ts(col(44), col(15), 0.0, A.is_gt, 128.0, A.mult)
+    lin(col(28), col(27), 1.0, col(1))
+    lin(col(29), col(15), -1.0, col(44))
+    ts(PMm(0, 1), xb, col(28), A.is_equal)
+    ts(PMm(0, 2), xb, col(1), A.subtract, col(29), A.is_equal)
+    for d, c in ((0, 15), (1, 27), (2, 29)):
+        ts(PMm(1, d), B("mg", 0, 128), col(c), A.is_equal, col(17), A.mult)
+        lin(PMm(2, d), PMm(1, d), -1.0)
+    lin(B("KJ"), B("xb", 0, 224), 1.0 / 256, 1.0 / 256 - 1.0)
+    for n, c, a, b in [("CCb", 45 + h) + x for h, x in enumerate(HALVES)] + [("CCi", 26, 0, 224)]:
+        k = (b - a) // 2
+        lin(col(c), col(3), -1.0 * k, 256.0)
+        for j in (a, a + k):
+            lin(B(n, j, j + k), B("xb", 0, k), -1.0, col(c))
+    if True in LATCH:
+        ts(col(22), col(1), 15.0, A.is_lt, 4096.0, A.mult)
+        ts(B("lat", 0, 16), B("xb", 0, 16), 1.0, A.subtract, col(1), A.is_equal)
+        ts(B("lat", 16, 32), B("oh"), -2.0, A.mult)
+        tt(B("lat", 32, 48), B("lat", 0, 16), B("lat", 16, 32), A.add)
+        lin(B("LC", 0, 16), B("lat", 32, 48), 4096.0)
+        lin(col(22), col(22), 1.0, -SH)
+        for n in (16, 32, 64, 128):
+            lin(B("LC", n, 2 * n), B("LC", 0, n), 1.0)
+    lin(col(41), col(1), 1.0, 0.5)
+    lin(col(42), col(1), 1.0, 256.0 + K2 - ZB)
+    lin(B("jh", 0, 3), B("xb", 0, 48, 16), 1.0, col(41))
+    lin(B("dd", 0, 3), B("xb", 0, 48, 16), 1.0, col(42))
+    ms(B("aws", 112, 128), 1.0)
+    ms(B("sc1", 0, 1), 0.0)
+    ms(B("SM"), 1.0)
+    ms(B("SM", 0, None, 16), 0.0)
+    ms(B("SM", 15, None, 16), 0.0)
+    ms(B("lz", 3, 4), 4110)
+    iota(B("M192"), [[-16, 3], [1, 48]], 0)
+    ts(B("M192"), B("M192"), col(1), A.is_ge, 8192.0, A.mult)
+    iota(B("jr"), [[1, 256]], -int(SH))
+    for o, c in ((B("zr"), 0), (B("gvi", G, 2048), W), (B("XF", D + W, XW), 0), (B("C", 0, D), -1), (B("C", D + W, XW), -1),
+                 (B("XF", 0, D), 0), (B("want", 256, 304), 1), (B("neg1"), -1), (B("k4"), 4096), (B("XT", 0, D), 0)):
+        fill(o, c)
+    for s in range(3):
+        fill(B("ls", 224 * s, 224 * s + 224), LEV[s])
+        fill(B("lv", 224 * s, 224 * s + 224), LEV[s])
+    for a in range(0, XW, 488):
+        iota(B("F", a, a + 488), [[1, 488]], a - D)
+
+    def turn(terms, bank):
+        lst = []
+        for t in range(7):
+            for a in (0, 16):
+                lst += grp(B(bank, 32 * t + a, 32 * t + a + 16), [(B("J", a, a + 128), f(t)) for f in terms])
+        mm(lst)
+
+    cp(B("awb"), B("awi"))
+    turn([lambda t: B("awb", 16 * t, 16 * t + 16)], "pf")
     for t in range(7):
         vtr(B("TT", t, t + 218, 7), B("pf", 32 * t, 32 * t + 32))
-        if t == 3:
-            cp(B("dgi"), B("dg"))
-    ts(B("dgi"), B("dgi"), 3, A.bitwise_and)
     cp(B("aws", 0, 112), B("TT", 0, 112))
+    cp(B("exu", 0, 14), B("exi", 0, 14))
 
-    def consts_0():
-        ts(B("An"), B("dgi", 128, 160), -0.0625 / 32, A.mult, col(33), A.add)
-        ts(B("Bp", 0, 128), B("dgi", 0, 128), 0.0625, A.mult, col(34), A.add)
-        ts(Ib, xb, col(0), A.is_equal)
-        ts(col(16), col(15), 15.0, A.add)
-        lin(B("hv", 1, 4, 2), B("hv", 0, 4, 2), 0.5)
-        for n in (128, 256):
-            lin(B("Bp", n, 2 * n), B("Bp", 0, n), 1.0)
-        lin(I32x, Ib, 32.0)
-
-    def mark(k, e):
-        for h in range(4 * k, min(4 * k + 4, 19)):
+    def encode():
+        for h in range(19):
             b = min(128 * h + 128, V)
-            if h % 4 in EM_ACT and e == "A":
+            if h % 4 in EM_ACT:
                 act(B("em", 128 * h, b), B("XT", D + 128 * h, D + b), AF.Relu, scale=B("An", h, h + 1))
-            if h % 4 not in EM_ACT and e == "V":
+            else:
                 ts(B("em", 128 * h, b), B("XT", D + 128 * h, D + b), B("An", h, h + 1), A.mult, 0.0, A.max)
-
-    def enc(k):
-        a, b = 512 * k, min(512 * k + 512, V)
-        scan(B("et", a, b), B("Bp", 0, b - a), B("em", a, b), 0.0, A.max, A.mult)
-        bk = ("pb", "ph")[k % 2]
-        mm(grp(B(bk, 0, b - a), [(Ib, B("XT", D + a, D + b)), (I32x, B("et", a, b))]))
-        act(B("XF", D + a, D + b), B(bk, 0, b - a), AF.Copy)
-
-    def consts_a():
-        for a, b, lo, h in ((0, 96, 32, 18), (96, 224, 0, 19), (224, 288, 0, 20)):
-            ts(B("NC", a, b), B("Bp", lo, lo + b - a), B("An", h, h + 1), A.mult)
-        lin(B("XF", D + V, D + W), B("NC", 0, 224), -32.0, -1.0)
-
-    def consts_b():
-        tt(B("t16", 0, 16), B("pw", 0, 16), B("oh"), A.mult)
-        ts(col(17), col(1), 15.0, A.is_equal)
-        ts(col(18), col(7), 8.0, A.mult)
-        ms(B("SM"), 1.0)
-        red(col(8), B("t16", 0, 16))
-        ts(col(18), col(5), 16.0, A.mult, col(18), A.add)
-        ts(col(38), B("oh", 0, 1), -655360.0, A.mult)
-        ms(B("SM", 0, 2048, 16), 0.0)
-        tt(col(19), col(18), col(8), A.mult)
-        ts(col(39), B("oh", 1, 2), -34816.0, A.mult, col(38), A.add)
-        ms(B("SM", 15, 2048, 16), 0.0)
-        ts(col(35), col(17), 16 * K1, A.mult, col(19), A.add)
-        ts(col(40), B("oh", 2, 3), -5.0, A.mult, col(39), A.add)
-        ts(M(0), BO, -64 * K1, A.mult)
-
-    def consts_c():
-        ts(col(23), col(1), 2.0, A.mult, col(4), A.add)
-        ts(M(4), BO, -K2, A.mult)
-        ts(M(5), BO, K2, A.mult)
-        ts(col(24), col(23), 1.0, A.add)
-        ts(M(6), BO, col(35), A.mult)
-        ts(M(7), BO, col(17), A.mult, -16 * K1, A.mult)
-        ts(MC, BO, col(40), A.mult)
-        ts(B("Z0h"), B("ZS"), B("oh", 0, 1), A.mult)
-        ts(col(25), col(3), -64.0, A.mult, 256.0, A.add)
-        for n, c in (("H0", 13), ("H1", 14)):
-            ts(B(n + "h"), x144, col(24), A.is_equal, col(c), A.mult)
-
-    def consts_ca():
-        lin(B("KJ"), B("xb", 0, 224), 1.0 / 256, 1.0 / 256 - 1.0)
-        for a in (0, 64):
-            lin(B("CCb", a, a + 64), B("xb", 0, 64), -1.0, col(25))
-        for n in ("H0", "H1"):
-            lin(B(n + "b"), B(n + "h"), 256.0)
-
-    def consts_d():
-        ts(col(20), col(17), 16 * K1, A.mult, 64 * K1, A.add)
-        ts(M(8), BO, col(19), A.mult)
-        ts(M(9), BO, col(19), A.mult, -1.0, A.mult)
-        ts(M(3), BO, col(17), A.mult, 16 * K1, A.mult)
-        ts(M(1), BO, col(20), A.mult)
-        cp(B("exu", 0, 14), B("exi", 0, 14))
-
-    def consts_da():
-        for i in (14, 15):
-            lin(B("S", 4096 + i, 4864, 16), B("NC", 240, 288), -32.0, -1.0)
-        lin(B("IL"), Ib, K1)
-        lin(B("jh", 0, 3), B("xb", 0, 48, 16), 1.0, col(41))
-        lin(B("Zd"), B("ZS"), col(19))
-        lin(B("Z8h"), B("ZS"), -8192.0)
-        for k in range(2):
-            lin(B("I8h", 128 * k, 128 * k + 128), Ib, 8192.0 * (2 * k - 1))
-            lin(B("dd", 4 * k, 4 * k + 4), B("xb", 0, 64, 16), 1.0, col(42))
-
-    def consts_e():
-        ts(col(27), col(15), -1.0, A.mult, 112.0, A.add)
-        ts(col(29), col(15), 0.0, A.is_gt, 128.0, A.mult)
-        ts(col(26), col(3), -112.0, A.mult, 256.0, A.add)
-        ms(B("lz", 3, 4), 4110)
-        tt(col(28), col(27), col(1), A.add)
-        tt(col(29), col(29), col(15), A.subtract)
-        ts(B("M192"), B("M192"), col(1), A.is_ge, 8192.0, A.mult)
-        ts(PMm(0, 1), xb, col(28), A.is_equal)
-        ts(PMm(0, 2), xb, col(1), A.subtract, col(29), A.is_equal)
-        for d, c in ((0, 15), (1, 27), (2, 29)):
-            ts(PMm(1, d), B("mg", 0, 128), col(c), A.is_equal, col(17), A.mult)
-
-    def consts_ea():
-        for a in (0, 112):
-            lin(B("CCi", a, a + 112), B("xb", 0, 112), -1.0, col(26))
-        lin(B("Z0"), B("Z0h"), 1.0)
+        for k in range(5):
+            a, b = 512 * k, min(512 * k + 512, V)
+            scan(B("et", a, b), B("Bp", 0, b - a), B("em", a, b), 0.0, A.max, A.mult)
+            bk = ("ph", "pb")[k % 2]
+            mm(grp(B(bk, 0, b - a), [(Ib, B("XT", D + a, D + b)), (I32x, B("et", a, b))]))
+            act(B("XF", D + a, D + b), B(bk, 0, b - a), AF.Copy)
 
     def refresh(ks, tab="XF", tmp="x48"):
-        out = []
         for k in ks:
-            out.append(lambda k=k: cp(B(tmp), X(B(tab), B("LT", 8 * k + 4, 8 * k + 7))))
-            out.append(lambda k=k: cp(X(B(tab), B("LT", 8 * k, 8 * k + 3)), B(tmp)))
-        return out
+            cp(B(tmp), X(B(tab), B("LT", 8 * k + 4, 8 * k + 7)))
+            cp(X(B(tab), B("LT", 8 * k, 8 * k + 3)), B(tmp))
 
-    def narrow(o, i):
-        op("G", lambda: g.affine_select(o[0], i[0], [[0, o[3] - o[2]]], A.is_ge, 0.0, 0, 0), [i], [o])
+    def shuffle(bank, n, cc, cg, tm, a=0):
+        mm([(B(bank, 0, 2 * n), Ib, cc, True, False)])
+        for nm, src in (("h", cg), ("b", tm)):
+            if nm == "b":
+                scan(B(tm, a, a + 2 * n), B("KJ", 0, 2 * n), B(cg, a, a + 2 * n), -1.0, A.max, A.min)
+            mm([(B(bank, n * h, n * h + n), B("H%d%s" % (h, nm), 1 - k, 129 - k), B(src, a + n * k, a + n * k + n), False,
+                 nm == "b" and h + k == 2) for h in range(2) for k in range(2)])
 
-    def shuffle(bank, n, nm, src, a=0):
-        if nm == "c":
-            mm([(B(bank, 0, 2 * n), Ib, B(src), True, False)])
-            return
-        mm([(B(bank, n * h, n * h + n), B("H%d%s" % (h, nm), 1 - k, 129 - k), B(src, a + n * k, a + n * k + n), False,
-             nm == "b" and h + k == 2) for h in range(2) for k in range(2)])
-
-    def lists(bank, k, tmp, a, out, between=None):
+    def lists(bank, k, tmp, a, out):
         for s in range(k):
             vtr(B(tmp, a + s, a + 32 * k, k), B(bank, s, 32 * k, k))
-        if between:
-            between()
         ts(B(out, a, a + 32 * k), B(tmp, a, a + 32 * k), WK - 1.0, A.add)
 
-    def scat_a(w, off):
-        act(X(B(w), off), B("ls", 0, 16 * (off[3] - off[2])), AF.Silu)
+    lastw, lastc = {"V": None, "A": None}, {"V": [], "A": []}
 
-    def scat_v(w, off):
-        cp(X(B(w), off), B("lv", 0, 16 * (off[3] - off[2])))
+    def scatter(e, s, off, wins):
+        val = B("ls" if e == "A" else "lv", 224 * s, 224 * s + 16 * size(off))
+
+        def f():
+            w = wins[-1] if lastw[e] == wins[0] else wins[0]
+            lastw[e] = w
+            o = X(B(w), off)
+            return (g.scalar.activation(o[0], val[0], AF.Silu) if e == "A" else v.tensor_copy(o[0], val[0])), o
+        lastc[e] = [call(e, f, [val, off], [B(w) for w in wins], 55 + (SCAT_A if e == "A" else SCAT) * size(val) + HOP * (len(wins) == 1), mark=True, after=lastc[e])]
 
     win = B("XF", D, XW)
-    later = []
-
-    def gap(n=1):
-        for _ in range(n):
-            if later:
-                later.pop(0)()
+    tops = {}
 
     for s in range(3):
         first, last = s == 0, s == 2
+        for b in EB:
+            mm([(B(b), rows("ones", slice(0, 1), 0, 128), rows("JR", slice(0, 1), 0, 512), True, False)])
         scan(B("sc1", 1, 129), B("ones", 0, 128), B("aws"), 0.0, A.mult, A.add)
         mm([(B("pb", 0, 128), B("TRI"), B("aws"), True, False)])
-        for b in range(4):
-            mm([(B(EB[b]), B("sc1", 1, 129), B("BO"), False, True)])
-            if b == 1:
-                mm([(B("pb", 0, 128), BO, B("sc1", 0, 128), False, True)])
-        if first:
-            consts_0()
-        gap()
+        mm([(B("pb", 0, 128), BO, B("sc1", 0, 128), False, True)])
+        act(B("pre"), B("pb", 0, 128), AF.Copy)
+        act(B("sg"), B("pre", 0, 112), AF.Sign, bias=-256.5)
+        for b in EB:
+            mm([(B(b), B("sc1", 1, 129), B("BO"), False, True)])
 
         def count(bank, h, k):
             return [(B(bank, c, c + 1), B("EQ", 1024 * h + 128 * c, 1024 * h + 128 * c + 128),
@@ -452,155 +506,63 @@ def rank_program(g, core, T, topo):
         for h in range(2):
             ts(B("EQ", 1024 * h, 1024 * h + 512), B(EB[2 * h]), 128.0 * h, A.is_le, 0.5, A.subtract)
             act(B("EQ", 1024 * h + 512, 1024 * h + 1024), B(EB[2 * h + 1]), AF.Sign, bias=128.0 * h + 64.5, scale=-1.0)
-            if h == 0:
-                act(B("pre"), B("pb", 0, 128), AF.Copy)
             mm(count(("pf", "pg")[h], h, 0))
-        if first:
-            ts(B("ZS"), x144, col(16), A.is_equal)
-            mark(0, "V")
-            mark(0, "A")
-            mark(1, "A")
         for h in range(2):
+            a, o = 128 * h, B(("pa", "pc")[h], 0, 8)
             ts(B("bw", 8 * h, 8 * h + 8), B(("pf", "pg")[h], 0, 8), 64.0, A.add)
-            o = B(("pa", "pc")[h], 0, 8)
             mm([(o, BO, B("zr", 0, 8), True, False)] + count(("pa", "pc")[h], h, 2))
-            if first:
-                mark(1 + h, "V")
-            gap()
-            tt(B("cmp", 128 * h, 128 * h + 128), X(B("pre"), B("bw", 8 * h, 8 * h + 8)), B("xb", 128 * h, 128 * h + 128), A.is_le)
-            mm([(o, sel("ZS", p), B("cmp", 128 * h + p, 128 * h + 128, 16), False, p == 15) for p in range(16)])
-            if first:
-                enc(h)
-                mark(2 + h, "A")
+            tt(B("cmp", a, a + 128), X(B("pre"), B("bw", 8 * h, 8 * h + 8)), B("xb", a, a + 128), A.is_le)
+            mm([(o, sel("ZS", p), B("cmp", a + p, a + 128, 16), False, p == 15) for p in range(16)])
+            ts(B("eu", 8 * h, 8 * h + 8), o, 1024.0, A.add)
+            cp(B("gve", a, a + 128), X(B("gvi"), B("eu", 8 * h, 8 * h + 8)))
         if first:
-            mark(4, "A")
-            mark(3, "V")
-            enc(2)
-            mark(4, "V")
-            enc(3)
-            consts_a()
-            enc(4)
-        act(B("sg"), B("pre", 0, 112), AF.Sign, bias=-256.5)
-        if s == 1:
-            for d in range(3):
-                lin(PMm(2, d), PMm(1, d), -1.0)
-            lin(B("ZSh"), B("ZS"), 1.0)
-            lin(B("If"), Ib, 1.0)
-            lin(B("ILf"), Ib, LEV[2] / 4)
-        for h in range(2):
-            ts(B("eu", 8 * h, 8 * h + 8), B(("pa", "pc")[h], 0, 8), 1024.0, A.add)
-            gap()
-            if first and h == 0:
-                consts_b()
-            cp(B("gve", 128 * h, 128 * h + 128), X(B("gvi"), B("eu", 8 * h, 8 * h + 8)))
-        if not first:
-            fill(B("ls"), LEV[s])
-            fill(B("lv"), LEV[s])
-        if s == 1:
-            iota(B("F"), [[1, XW]], -D)
-
-        def ga(a, b):
-            act(B("GG", 16 * a, 16 * b), X(win, B("gve", a, b)), AF.Copy)
-
-        def sc(a, b):
-            scan(B("S", 16 * a, 16 * b), B("SM", 0, 16 * (b - a)), B("GG", 16 * a, 16 * b), 0.0, A.mult, A.max)
+            encode()
 
         def four(a, b):
             return B("S", 16 * a + 14, 16 * b, 16), B("S", 16 * a + 15, 16 * b, 16), B("RM", a, b), B("RO", a, b)
 
-        def p_g(a, b, ins=range(15)):
-            mm([(B("ph", a, b), M(0), B("GG", 16 * a + i, 16 * b, 16), False, False) for i in ins])
-
-        def bind(h):
-            a, b = 128 * h, 128 * h + 128
-            mx, go, rm, ro = four(a, b)
-            ts(rm, mx, MAGIC, A.add, MAGIC, A.subtract)
-            ts(ro, go, MAGIC, A.add, MAGIC, A.subtract)
-            mm(grp(B(("pf", "pg")[h], 0, 128), [(M(4), mx), (M(5), rm), (M(7), ro), (M(6), go), (MC, B("ones", 0, 128))]))
-
-        def outs(h, between=None):
-            a, bk = 128 * h, ("pf", "pg")[h]
-            tt(B("ob", a, a + 128), B(bk, 0, 128), B("jr", a, a + 128), A.max)
-            mm(grp(B(bk, 128, 136), [(sel("Z0h", p), B("ob", a + p, a + 128, 16)) for p in range(16)]))
-            if between:
-                between()
-            ts(B("obu", 8 * h, 8 * h + 8), B(bk, 128, 136), SH, A.add)
-
-        def waiters(h):
-            cp(B("cg", 128 * h, 128 * h + 128), X(B("C"), B("obu", 8 * h, 8 * h + 8)))
-            shuffle(("pb", "pc")[h], 64, "c", "CCb")
-            shuffle(("pb", "pc")[h], 64, "h", "cg", 128 * h)
-
-        def marks(h):
-            a = 128 * h
-            scan(B("tm", a, a + 128), B("KJ", 0, 128), B("cg", a, a + 128), -1.0, A.max, A.min)
-            shuffle(("pb", "pc")[h], 64, "b", "tm", a)
-
-        def half(i):
-            return B("wl", 8 * i, 8 * i + 8)
-
-        arows = list(range(BIND_ACT[s]))
-        vrows = list(range(BIND_ACT[s], 32))
-
-        def rows_a(n):
-            for _ in range(n):
-                if arows:
-                    scat_a(("AS", "AS2")[len(arows) % 2], half(arows.pop(0)))
-
-        def rows_v(n):
-            for _ in range(n):
-                if vrows:
-                    scat_v(("AV", "AV2")[len(vrows) % 2], half(vrows.pop(0)))
-
+        for a, b, e in (GATHER0 if first else GATHER):
+            if e == "A":
+                act(B("GG", 16 * a, 16 * b), X(win, B("gve", a, b)), AF.Copy)
+            else:
+                cp(B("GG", 16 * a, 16 * b), X(win, B("gve", a, b)))
+        for a, b in SCANS:
+            scan(B("S", 16 * a, 16 * b), B("SM", 0, 16 * (b - a)), B("GG", 16 * a, 16 * b), 0.0, A.mult, A.max)
         mm([(B("ph", 0, 256), BO, B("zr"), True, False)])
-        ga(0, GA)
-        if first:
-            ga(GA, 128)
-            consts_c()
-            cp(B("C", D, D + 1280), B("ci", 0, 1280))
-            cp(B("C", D + 1280, D + W), B("ci", 1280, W))
-        else:
-            cp(B("GG", 16 * GA, 2048), X(win, B("gve", GA, 128)))
-        sc(0, 128)
-        ga(128, 192)
-        if first:
-            consts_ca()
-        ga(192, 256)
-        p_g(0, 128, range(10))
-        bind(0)
-        if first:
-            ts(col(41), col(1), 0.5, A.add)
-            ts(col(42), col(1), 256.0 + K2 - ZB, A.add)
-            consts_d()
-        outs(0, lambda: sc(128, 192))
-        p_g(0, 128, range(10, 15))
-        waiters(0)
-        marks(0)
-        p_g(128, 256, range(10))
-        sc(192, 256)
-        if first:
-            consts_da()
-        lists("pb", 4, "TT", 0, "wl", lambda: bind(1))
+        for a, b in HALVES:
+            for i in range(0, 15, 3):
+                mm([(B("ph", a, b), M(0), B("GG", 16 * a + j, 16 * b, 16), False, False) for j in range(i, i + 3)], "sum")
+        for h, (a, b) in enumerate(HALVES):
+            bk, bl, n, k = ("pf", "pg")[h], ("pb", "pc")[h], b - a, (b - a) // 16
+            mx, go, rm, ro = four(a, b)
+            ou = B("obu", a // 16, b // 16)
+            ts(rm, mx, MAGIC, A.add, MAGIC, A.subtract)
+            if RO_ACT[h]:
+                act(ro, go, AF.Abs, bias=-14.0625)
+            else:
+                ts(ro, go, 14.0625, A.not_equal)
+            mm(grp(B(bk, 0, n), [(M(4), mx), (M(5), rm), (M(7), ro), (M(8), go), (MC, B("ones", 0, n))]))
+            tt(B("ob", a, b), B(bk, 0, n), B("jr", a, b), A.max)
+            if LATCH[h]:
+                scan(B("lat", a, b), B("LC", 0, n), B("ob", a, b), 0.0, A.add, A.max)
+                ts(ou, B("lat", a + 15, b, 16), col(22), A.subtract)
+            else:
+                mm(grp(B(bk, 256, 256 + k), [(sel("Z0h", p), B("ob", a + p, b, 16)) for p in range(16)]))
+                ts(ou, B(bk, 256, 256 + k), SH, A.add)
+            cp(B("cg", a, b), X(B("C"), ou))
+            shuffle(bl, n // 2, B("CCb", a, b), "cg", "tm", a)
+            lists(bl, k // 2, "TT", a, "wl")
+            for r in range(16):
+                e = "V" if r < BIND_VEC[s][h] else "A"
+                scatter(e, s, B("wl", a + k * r, a + k * r + k), ("AS", "AS2") if e == "A" else ("AV", "AV2"))
         mx, go, rm, ro = four(0, 256)
-        outs(1)
-        mm(grp(B("pa", 0, 256), [(M(8), mx), (M(9), go)]))
-        p_g(128, 256, range(10, 15))
-        rows_a(3)
-        act(B("ab"), B("pa", 0, 256), AF.Abs, scale=0.0625)
-        waiters(1)
         cp(X(B("XF"), B("obu")), mx)
-        old = refresh(range(s - 1, -1, -1))
-        marks(1)
-        o = B("ph", 0, 256)
-        mm([(o, M(1), mx, False, False), (o, M(3), go, False, False), (o, M(7), rm, False, False),
-            (o, M(7), ro, False, False), (o, Ib, B("ab"), False, True)])
-        for k in range(4):
-            if old:
-                old.pop(0)()
-            vtr(B("TT", 128 + k, 256, 4), B("pc", k, 128, 4))
-        snd = B("snd", 224 * s, 224 * s + 224)
-        cp(snd, X(win, B("exu", 0, 14)))
-        deps("G", [snd], [])
+        refresh(range(s - 1, -1, -1))
+        snd, Ln = B("snd", 224 * s, 224 * s + 224), B("land", 224 * s, 224 * s + 224)
+        if SND_ACT:
+            act(snd, X(win, B("exu", 0, 14)), AF.Copy)
+        else:
+            cp(snd, X(win, B("exu", 0, 14)))
         trs = []
         for d in range(1, 8):
             peer = T.cores[rank ^ d]
@@ -613,62 +575,49 @@ def rank_program(g, core, T, topo):
                                          remote_sem=T.sem["arr%d" % s], src=T.snd[:, a:a + 32], dst=T.land[:, a:a + 32]))
             tops["snt"] = tops.get("snt", 0) + n
             tops["arr%d" % s] = tops.get("arr%d" % s, 0) + n
-        g.remote_dma_fused(trs, local_sem=T.sem.snt)
-        Ln = B("land", 224 * s, 224 * s + 224)
-        done(("arr%d" % s, tops["arr%d" % s]), [], [Ln])
-        if first:
-            fill(B("neg1"), -1)
-            fill(B("k4"), 4096)
-            fill(B("XT", 0, D), 0)
-        ts(B("want", 0, 256), o, 2 * K1 + 1.0 / 32, A.is_gt)
-        ts(B("wl", 128, 256), B("TT", 128, 256), WK - 1.0, A.add)
-        mm(grp(B("pd", 0, 256), [(M(8), go), (B("IL"), B("want", 0, 256)), (MC, B("ones", 0, 256))]))
+        call("G", lambda trs=trs: g.remote_dma_fused(trs, local_sem=T.sem.snt), [snd], [Ln], 300, FLY, "arr%d" % s)
+        for a, b in XT_PARTS:
+            cp(X(B("XT", 0, D + V), B("obu", a // 16, b // 16)), four(a, b)[0])
+        mm(grp(B("pa", 0, 256), [(M(8), mx), (M(9), go)]))
+        act(B("ab"), B("pa", 0, 256), AF.Abs, scale=0.0625)
+        o = B("ph", 0, 256)
+        mm([(o, M(1), mx, False, False)], "sum")
+        mm([(o, M(7), rm, False, False), (o, M(7), ro, False, False)], "sum")
+        mm([(o, Ib, B("ab"), False, True)])
+        ts(B("want", 0, 256), o, K1 + 1.0 / 32, A.is_gt)
+        mm([(B("pd", 0, 256), M(8), go, True, False), (B("pd", 0, 256), M(3), B("ones", 0, 256), False, False)])
+        mm([(B("pd", 0, 256), IK, B("want", 0, 256), False, True)])
+        tt(B("SW", 0, 256), B("pd", 0, 256), B("ob"), A.max)
         scan(B("rank"), B("ones"), B("want"), 0.0, A.mult, A.add)
-        rows_a(4)
         for t in range(3):
             act(B("EQ", 304 * t, 304 * t + 304), B("rank"), AF.Sign, bias=B("jh", t, t + 1), scale=-1.0,
                 accum_out=B("ca", t, t + 1))
-        rows_a(3)
-        tt(B("SW", 0, 256), B("pd", 0, 256), B("ob"), A.max)
-        if first:
-            consts_e()
-        if last:
-            cp(X(B("XT", 0, D + V), B("obu")), mx)
-            dma("d_y0", T.yx[:, 0:V], B("XT", D, D + V))
-            turn([lambda t: B("aws", t, 112, 7), lambda t: B("aws", t, 112, 7), lambda t: B("sg", t, 112, 7)], "pb")
-        else:
-            rows_v(2 - first)
         ts(B("lz", 0, 3), B("ca", 0, 3), 8.0, A.mult, 2447.0, A.add)
         ts(B("lz", 4, 7), B("ca", 0, 3), 8.0, A.mult, 2446.0, A.add)
-        rows_v(1)
         cp(B("cs"), X(B("S"), B("lz", 0, 7)))
         dec = [(sel("Zd", p), B("cs", p, 112, 16)) for p in range(16)]
+        mm(grp(B("pe", 0, 7), dec))
         mm([m for t in range(3) for m in grp(B("pa", 48 * t, 48 * t + 48),
                                              [(M(8), B("cs", 64, 112)), (Ib, B("M192", 48 * t, 48 * t + 48))])])
-        mm(grp(B("pe", 0, 7), dec))
         mm([(B("pf", 0, 7), l, x, i == 0, False) for i, (l, x) in enumerate(dec)])
-        lin(B("SW", 256, 400), B("pa", 0, 144), 1.0, ZB - SH)
-        if first:
-            consts_ea()
-        rows_a(32)
-        rows_v(1)
+        if SW_ACT:
+            lin(B("SW", 256, 400), B("pa", 0, 144), 1.0, ZB - SH)
+        else:
+            ts(B("SW", 256, 400), B("pa", 0, 144), ZB - SH, A.add)
         ts(B("LU", 0, 7), B("pe", 0, 7), ZB, A.add)
-        ends = (0, 304, 656, 1056)
-
-        def equal(t):
-            ts(B("E", ends[t], ends[t + 1]), B("SW", 0, 304 + 48 * t), SH - ZB, A.add, B("pe", 4 + t, 5 + t), A.is_equal)
-
-        equal(0)
         cp(B("cc"), X(B("C"), B("LU", 0, 7)))
-        equal(1)
         tt(B("mn"), B("cc", 0, 48), B("cc", 64, 112), A.min)
-        mm([(B("pf", a, a + 3), sel("Z8h", p), B("mn", p, 48, 16), False, False) for a in (0, 4) for p in range(16)])
-        equal(2)
         tt(B("mxc"), B("cc", 0, 48), B("cc", 64, 112), A.max)
+        mm([(B("pf", a, a + 3), sel("Z8h", p), B("mn", p, 48, 16), False, False) for a in (0, 4) for p in range(16)])
+        ends = (0, 304, 656, 1056)
+        for t in range(3):
+            ts(B("E", ends[t], ends[t + 1]), B("SW", 0, 304 + 48 * t), SH - ZB, A.add, B("pe", 4 + t, 5 + t), A.is_equal)
         scan(B("EO"), B("E"), B("E"), 0.0, A.add, A.max)
         mm([(B("pf", a + t, a + t + 1), B("I8h", 128 * k, 128 * k + 128), B("EO", ends[t + 1 - k] - 1, ends[t + 1 - k]),
              False, a + t + k == 7) for a in (0, 4) for t in range(3) for k in range(2) if t >= k])
-        fn = B("fn", 224 * s, 224 * s + 224)
+        for t in range(3):
+            ts(B("LT", 8 * s + t, 8 * s + 8, 4), B("pf", t, 8, 4), B("dd", t, t + 1), A.max, ZB - K2, A.add)
+        cp(X(B("C"), B("LT", 8 * s + 4, 8 * s + 7)), B("mxc"))
 
         def blk(n, d, k=0):
             return B(n, 224 * k + 32 * d - 32, 224 * k + 32 * d)
@@ -679,55 +628,46 @@ def rank_program(g, core, T, topo):
         else:
             lst += [(blk("pg", d), PMm(2, d), blk("fn", d, s - 1), False, False) for d in range(1, 8)]
         mm(lst)
-        if last:
-            vtr(B("remT"), B("pb", 0, 224))
-        shuffle("pb", 112, "c", "CCi")
-        ts(fn, Ln, 14.0625, A.is_equal, -4096.0, A.mult)
+        ts(B("fn", 224 * s, 224 * s + 224), Ln, 14.0625, A.is_equal, -4096.0, A.mult)
         mm([(blk("pg", d), PMm(1, d), blk("fn", d, s), False, d == 7) for d in range(1, 8)])
-        tt(B("sel", 0, 7), B("pf", 0, 7), B("dd", 0, 7), A.max)
-        rows_v(1)
-        ts(B("LT", 8 * s, 8 * s + 7), B("sel", 0, 7), ZB - K2, A.add)
-        rows_v(1)
-        cp(X(B("C"), B("LT", 8 * s + 4, 8 * s + 7)), B("mxc"))
         if last:
-            for a in (0, 1280):
-                narrow(B("C16", a, a + 1280), B("C", D + a, D + a + 1280))
-            dma("d_as", B("asn"), rows("AS2", slice(0, 128, 16), WK, WW))
-        else:
-            narrow(B("ASc"), B("AS2", WK, WW))
-        side = refresh(range(2, -1, -1), "F", "c48") if last else []
-        rows_v(1)
+            turn([lambda t: B("aws", t, 112, 7), lambda t: B("aws", t, 112, 7), lambda t: B("sg", t, 112, 7)], "pb")
+            vtr(B("remT"), B("pb", 0, 224))
         tt(B("Cm"), B("C", D + V, D + W), B("pg", 0, 224), A.min)
-        shuffle("pb", 112, "h", "Cm")
-        rows_v(1)
-        scan(B("ti"), B("KJ"), B("Cm"), -1.0, A.max, A.min)
-        shuffle("pb", 112, "b", "ti")
+        shuffle("pb", 112, B("CCi"), "Cm", "ti")
+        lists("pb", 7, "TI", 0, "wi")
+        if last:
+            dma("d_as", B("asn"), rows("AS2", slice(0, 128, 16), WK, WW), 1200)
+        else:
+            select(B("ASc"), B("AS2", WK, WW), [[0, G]], 0)
+        for r in range(16):
+            e = "A" if r < IMP_ACT[s] else "V"
+            scatter(e, s, B("wi", 14 * r, 14 * r + 14), ("AS",) if e == "A" else ("AV", "AV2")[:1 + (r < 16 - AV_ONLY)])
+        parts = ((0, G - NARROW_G), (G - NARROW_G, G)) if NARROW_G else ((0, 896), (896, G))
+        for a, b in parts:
+            if a and NARROW_G:
+                select(B("ASb", a, b), B("AS", WK + a, WK + b), [[0, b - a]], 0)
+            else:
+                act(B("ASb", a, b), B("AS", WK + a, WK + b), AF.Copy)
         mm([m for d in range(1, 8) for m in grp(blk("pc", d), [(PMm(0, d), blk("land", d, s)), (PMm(1, d), blk("fn", d, s))])])
-        if not last:
+        if last:
+            ts(B("XT", D + V, D + W), B("pc", 0, 224), -1.0, A.max)
+            dma("d_y0", T.yx[:, 0:V], B("XT", D, D + V), 3000)
+            dma("d_y1", T.yx[:, V:W], B("XT", D + V, D + W), 1200)
+            refresh(range(2, -1, -1), "F", "c48")
+            dma("d_yf", T.yf[:], rows("F", slice(0, 128, 16), D, D + W), 1300)
+            for a in (0, 1280):
+                select(B("C16", a, a + 1280), B("C", D + a, D + a + 1280), [[0, 1280]], 0)
+            for a in (0, 8):
+                mm([(B("pe", 0, 160), sel("ZSh", p), B("C16", 160 * p, 160 * p + 160), p == 0, p == 15) for p in range(a, a + 8)])
+            act(B("yc_"), B("pe", 0, 160), AF.Copy)
+            dma("d_yc", T.yc[:], B("yc_"), 1300)
+        else:
             mm([(B("pd", 0, 224), I32x, B("NC", 0, 224), True, False)]
                + [(blk("pd", d), PMm(1, d), blk("fn", d, s), False, d == 7) for d in range(1, 8)])
-        rows_v(1)
-        lists("pb", 7, "TI", 0, "wi", lambda: rows_v(1))
-        if not last:
             lin(B("wS"), B("pd", 0, 224), -1.0, -4097.0)
-            lin(B("ab", 0, 128), Ib, LEV[s] / 4)
-        for r in range(IMP_ACT[s]):
-            scat_a("AS", B("wi", 14 * r, 14 * r + 14))
-        for h in range(2):
-            act(B("ASb", 896 * h, 896 * h + 896), B("AS", WK + 896 * h, WK + 896 * h + 896), AF.Copy)
-        rows_v(32)
-        if last:
-            side.insert(0, lambda: ts(B("XT", D + V, D + W), B("pc", 0, 224), -1.0, A.max))
-            side.insert(1, lambda: dma("d_y1", T.yx[:, V:W], B("XT", D + V, D + W)))
-            side.append(lambda: dma("d_yf", T.yf[:], rows("F", slice(0, 128, 16), D, D + W)))
-        else:
-            side = [lambda: tt(B("XF", D + V, D + W), B("pc", 0, 224), B("wS"), A.max)]
-        for r in range(IMP_ACT[s], 16):
-            scat_v("AV2" if r < 16 - AV_ONLY and r % 2 == AV_ONLY % 2 ^ 1 else "AV", B("wi", 14 * r, 14 * r + 14))
-            if side:
-                side.pop(0)()
-        for f in side:
-            f()
+            tt(B("XF", D + V, D + W), B("pc", 0, 224), B("wS"), A.max)
+            refresh(range(s, -1, -1))
 
         def piece(n, p, a=WK):
             return B(n, a + 112 * p, a + 112 * p + 112) if last else B(n, a + p, a + G, 16)
@@ -735,30 +675,63 @@ def rank_program(g, core, T, topo):
         o = B("ph", 0, 112)
         if last:
             mm([(o, B("If"), B("asn"), True, False)])
-            mm(grp(B("pe", 0, 160), [(sel("ZSh", p), B("C16", 160 * p, 160 * p + 160)) for p in range(16)]))
-            mm([(B("ph", 16 * t, 16 * t + 16), B("ILf"), B("remT", 32 * t, 32 * t + 16), False, False) for t in range(7)])
-            act(B("yc_"), B("pe", 0, 160), AF.Copy)
-            dma("d_yc", T.yc[:], B("yc_"))
+            mm([(B("ph", 16 * t, 16 * t + 16), B("ILf"), B("remT", 32 * t, 32 * t + 16), False, False) for t in range(7)],
+               "sum")
         else:
-            il = B("ab", 0, 128)
+            il = B("IL", 128 * s, 128 * s + 128)
             mm([(o, il, B("aws", 0, 112), True, False), (o, il, B("aws", 0, 112), False, False),
                 (o, il, B("sg"), False, False)])
-            open_counts()
-            mm([(o, sel("Z0", p), piece("ASc", p, 0), False, False) for p in range(16)])
-        mm([(o, sel("Z0", p), piece("AV2", p), False, False) for p in range(16)])
-        for h in range(2):
+            mm([(o, sel("Z0", p), piece("ASc", p, 0), False, False) for p in range(16)], "sum")
+        for n in ("AV2", "AV"):
+            mm([(o, sel("Z0", p), piece(n, p), False, False) for p in range(16)], "sum")
+        for a, b in parts:
             if last:
-                mm([(o, sel("Z0", p), piece("ASb", p, 0), False, False) for p in range(8 * h, 8 * h + 8)])
+                mm([(o, sel("Z0", p), piece("ASb", p, 0), False, False) for p in range(a // 112, b // 112)], "sum")
             else:
-                mm([(B("ph", 56 * h, 56 * h + 56), sel("Z0", p), B("ASb", 896 * h + p, 896 * h + 896, 16), False, False)
-                    for p in range(16)])
-        mm([(o, sel("Z0", p), piece("AV", p), False, p == 15) for p in range(16)])
+                mm([(B("ph", a // 16, b // 16), sel("Z0", p), B("ASb", a + p, b, 16), False, False) for p in range(16)], "sum")
+        mm([(o, BO, B("zr", 0, 112), False, True)])
         if last:
             ts(B("yw_"), o, 0.5 * LEV[s], A.is_gt)
-            dma("d_yw", T.yw[:], B("yw_"))
+            dma("d_yw", T.yw[:], B("yw_"), 1200)
         else:
-            cp(X(B("XT", 0, D + V), B("obu")), mx)
             ts(B("aws", 0, 112), o, 0.5 * LEV[s], A.is_gt)
-            later += refresh(range(s, -1, -1))
-    for k in tops:
-        need("S", (k, tops[k]))
+
+    cnt, seen, uses = {e: 0 for e in eng}, {e: {} for e in eng}, {}
+
+    def need(e, sem, n):
+        if seen[e].get(sem, 0) < n:
+            eng[e].wait_ge(T.sem[sem], n)
+            seen[e][sem] = n
+
+    for c in [calls[i] for i in plan(calls)]:
+        e, w, want = c["e"], c["w"], {}
+        if c["mark"] is True:
+            w = [w[-1] if lastw[e] == w[0][1] else w[0]]
+        for vs, wr in ((c["r"], False), (w, True)):
+            for x in vs:
+                for (sem, w2, sp), n in uses.get(x[1], {}).items():
+                    if not (sem == "sP" and e == "P"):
+                        if (x[1] in PSUMS and sem != "s" + e) or ((wr or w2) and meet(sp, x[2:5])):
+                            want[sem] = max(want.get(sem, 0), n)
+        for sem in want:
+            need(e, sem, want[sem])
+        ins = c["fn"]()
+        if c["sem"] in tops:
+            tok = (c["sem"], tops[c["sem"]])
+            uses.setdefault(c["w"][0][1], {})[(tok[0], True, c["w"][0][2:5])] = tok[1]
+            continue
+        if c["mark"] is True:
+            ins = ins[0]
+        if c["sem"]:
+            tok = (c["sem"], 16)
+            ins.then_inc(T.sem[tok[0]], 16)
+        else:
+            cnt[e] += 1
+            tok = ("s" + e, cnt[e])
+            ins.then_inc(T.sem[tok[0]], 1)
+        seen.setdefault("end", {})[tok[0]] = tok[1]
+        for vs, wr in ((c["r"], False), (w, True)):
+            for x in vs:
+                uses.setdefault(x[1], {})[(tok[0], wr, x[2:5])] = tok[1]
+    for sem, n in list(seen["end"].items()) + list(tops.items()):
+        need("S", sem, n)

@@ -7,27 +7,58 @@ XW = D + W + 64
 WK = 256
 WW = WK + G
 MAGIC = 12582912.0
-K1, K2 = 65536.0, 131072.0
-ZB = float(D - 623925)
+K, K1, K2 = 2.0 ** 24, 2.0 ** 21, 131072.0
+C0 = 15.0 / 128
+ZB = float(D + 2805)
+K_ACT = ()
+CHUNKS = ((V, 2624), (0, 480), (480, 960), (960, 1440), (1440, 1920), (1920, V))
+DIRECT = (0, 0)
 SH = 1024.0
-LEV = (16, 512, 16384)
+LEV = (256, 8192, 262144)
 HALVES = ((0, 128), (128, 256))
 BIND_VEC = ((2, 6), (2, 6), (2, 6))
-LATCH = (False, False)
-RO_ACT = (False, True)
-SW_ACT = False
-XT_PARTS = ((0, 256),)
+SW_ACT = True
+XT_PARTS = ((0, 128), (128, 256))
 ROUNDS = 3
-SCAT_A = 2.8
 SND_ACT = False
-NARROW_G = 672
-IMP_ACT = (5, 6, 6)
+NARROW_G = 560
+IMP_ACT = (5, 5, 6)
 AV_ONLY = 3
-GATHER = ((0, 64, "A"), (64, 128, "V"), (128, 208, "A"), (208, 240, "A"), (240, 256, "V"))
-GATHER0 = GATHER
-SCANS = ((0, 64), (64, 128), (128, 208), (208, 256))
-EM_ACT = ()
-CY, CALL_V, CALL_A, HOP, GATH, SCAT, COL, FLY, OVER = 0.83, 66, 86, 160, 1.3, 2.8, 0.42, 2500, 150
+GATHER = ((0, 64, "A"), (64, 128, "V"), (128, 192, "A"), (192, 256, "A"))
+GATHER0 = ((0, 64, "A"), (64, 128, "V"), (128, 192, "A"), (192, 256, "A"))
+SCANS = ((0, 64), (64, 128), (128, 192), (192, 256))
+CY, INDIRECT = 0.83, {"V": 50, "A": 65}
+OVER = (100, 250, 400)
+STARTS = 8
+CUT = 40
+WORLDS = ((1.1, 1.4, 2.5, 15, 60, 120, 0.36, 2500, 0.6, 160, 1.0, 600, 45, 35),
+          (1.35, 1.3, 1.5, 25, 50, 70, 0.42, 3500, 0.5, 180, 1.2, 1000, 50, 40),
+          (1.15, 1.3, 5.0, 25, 85, 200, 0.36, 3000, 0.8, 100, 1.0, 400, 40, 20))
+POLISH = 14000
+SLACK = 0.0004
+SEED = 1
+LEAN = 0.3
+FILL = 1
+NOTE = []
+Z_G = 448
+NC_G = True
+AS_ONLY = (9, 9, 9)
+NARROW_A = 560
+M14 = ((0, 128, "A"), (128, 256, "A"))
+TESTS = HALVES
+CC_ACT = False
+HB_ACT = True
+BWB = True
+FIRST = 1.5
+LAST_READ = "AV"
+XT_LAST = True
+AW_G = False
+SM_G = True
+AW_OFF = False
+EQ_ACT = 2
+REF_ACT = True
+XF_VEC = ()
+PLANS = []
 
 
 def sb(n, dt):
@@ -38,42 +69,42 @@ F32, BF, F16, I32, U16 = "float32", "bfloat16", "float16", "int32", "uint16"
 SCRATCH = {
     "awi": sb(112, I32), "awb": sb(112, BF), "aws": sb(128, BF), "sc1": sb(136, BF),
     "gvi": sb(2048, I32), "exi": sb(16, I32), "exu": sb(16, U16),
-    "XF": sb(XW, BF), "XT": sb(D + W, BF), "C": sb(XW, I32), "F": sb(XW, F32),
-    "em": sb(V, BF), "et": sb(V, BF),
-    "AV": sb(WW, BF), "AV2": sb(WW, BF), "AS": sb(WW, F32), "AS2": sb(WW, F32), "ASb": sb(G, BF),
+    "XF": sb(XW, BF), "XT": sb(XW, BF), "C": sb(XW, I32), "F": sb(XW, F32),
+    "AV": sb(2640, BF), "AV2": sb(2624, BF), "AS": sb(WW, F32), "AS2": sb(WW, F32), "ASb": sb(G, BF),
     "ASc": sb(G, BF), "C16": sb(W, F16), "asn": sb(112, F32),
     "lv": sb(672, BF), "ls": sb(672, F32),
-    "GG": sb(4096, BF), "S": sb(4864, BF), "SM": sb(16 * max(b - a for a, b in SCANS), BF), "RM": sb(256, BF), "RO": sb(256, BF),
-    "pi": sb(8, I32), "co_": sb(48, F32), "xb": sb(256, BF), "mg": sb(512, BF), "JR": sb(512, BF),
-    "oh": sb(16, F32), "pw": sb(32, F32), "t16": sb(64, F32), "dg": sb(160, F32), "dgi": sb(320, I32),
-    "Bp": sb(512, BF), "An": sb(32, F32), "NC": sb(288, BF),
-    "J": sb(144, BF), "BO": sb(512, BF), "TRI": sb(128, BF), "ZS": sb(144, BF), "Zd": sb(144, BF),
-    "ZSh": sb(144, F16), "Z8h": sb(144, F16), "Z0h": sb(144, F16), "Z0": sb(144, BF),
+    "GG": sb(4096, BF), "S": sb(4864, BF), "SM": sb(16 + 16 * max(b - a for a, b in SCANS), BF),
+    "pi": sb(8, I32), "co_": sb(48, F32), "xb": sb(256, BF), "mg": sb(128, BF), "JR": sb(512, BF),
+    "oh": sb(16, F32), "sK": sb(16, F32), "aK": sb(16, F32), "NC": sb(288, BF),
+    "J": sb(144, BF), "BO": sb(128, BF), "TRI": sb(128, BF), "ZS": sb(144, BF), "Zd": sb(144, BF),
+    "ZSh": sb(144, F16), "Z8h": sb(144, F16), "Z0": sb(144, BF), "Z0f": sb(144, F32),
     "If": sb(128, F32), "IL": sb(384, BF), "ILf": sb(128, F32), "I8h": sb(256, F16),
-    "MM": sb(1408, BF), "PM": sb(1024, BF),
+    "MM": sb(2048, BF), "PM": sb(1024, BF), "OH": sb(128, BF),
     "H0h": sb(144, F16), "H1h": sb(144, F16), "H0b": sb(144, BF), "H1b": sb(144, BF),
-    "ones": sb(304, BF), "hv": sb(4, BF), "zr": sb(256, BF), "neg1": sb(224, BF), "k4": sb(224, BF),
-    "jh": sb(4, F32), "dd": sb(8, F32), "jr": sb(256, F32),
-    "KJ": sb(224, BF), "CCb": sb(256, BF), "LC": sb(256, BF), "lat": sb(256, F32), "CCi": sb(224, BF), "M192": sb(144, BF),
+    "ones": sb(304, BF), "zr": sb(128, BF), "neg1": sb(224, BF),
+    "MAG": sb(256, BF), "t196": sb(256, BF), "cz": sb(4, F32), "bwb": sb(16, BF), "m14": sb(256, BF),
+    "jh": sb(4, F32), "dd": sb(8, F32),
+    "KJ": sb(224, BF), "CCb": sb(256, BF), "LD": sb(256, F32), "lat": sb(256, F32), "CCi": sb(224, BF), "M16": sb(16, BF),
     "EQ": sb(2048, BF), "pre": sb(128, F32), "sg": sb(112, BF), "remT": sb(224, F32),
     "bw": sb(16, U16), "cmp": sb(256, BF), "eu": sb(16, U16), "gve": sb(256, U16),
-    "ob": sb(256, F16), "obu": sb(16, U16), "cg": sb(256, F16), "tm": sb(256, BF),
+    "xu": sb(48, F16), "obu": sb(16, U16), "cg": sb(256, F16), "tm": sb(256, BF),
     "TT": sb(256, F32), "TI": sb(224, F32), "wl": sb(256, U16), "wi": sb(224, U16),
     "ab": sb(256, BF), "want": sb(304, BF), "rank": sb(304, BF), "ca": sb(4, F32),
-    "SW": sb(400, F16), "lz": sb(8, U16), "cs": sb(112, BF), "LU": sb(8, U16),
-    "cc": sb(112, F32), "mn": sb(48, F16), "mxc": sb(48, F32), "E": sb(1056, BF), "EO": sb(1056, F16),
-    "sel": sb(8, F32), "LT": sb(24, U16), "x48": sb(48, BF), "c48": sb(48, F32),
+    "SW": sb(336, F16), "lz": sb(8, U16), "cs": sb(112, BF), "LU": sb(8, U16),
+    "cc": sb(112, F32), "mn": sb(96, F16), "mxc": sb(48, F32), "E": sb(912, BF), "EO": sb(912, F16),
+    "LT": sb(24, U16), "x48": sb(48, BF), "c48": sb(48, F32),
     "snd": sb(672, BF), "land": sb(672, BF), "fn": sb(672, BF), "Cm": sb(224, F16), "ti": sb(224, BF), "wS": sb(224, BF),
     "yw_": sb(112, F32), "yc_": sb(160, F32),
 }
 PART = {}
-for _n in ("oh", "pw", "t16", "An", "jh", "dd", "ca", "sel"):
+for _n in ("oh", "sK", "aK", "jh", "dd", "ca"):
     PART[_n] = (sum(x[1] for x in PART.values()), SCRATCH.pop(_n)[1][1])
 SCRATCH["fs"] = sb(sum(x[1] for x in PART.values()), F32)
 PSUMS = ("pa", "pb", "pc", "pd", "pe", "pf", "pg", "ph")
 for _b in PSUMS:
     SCRATCH[_b] = ("psum", [128, 512], F32)
-DMAS = ["d_aw", "d_x0", "d_gv", "d_ex", "d_co", "d_y0", "d_y1", "d_yf", "d_yw", "d_yc", "d_zS", "d_zV", "d_as"]
+DMAS = ["d_aw", "d_x0", "d_gv", "d_ex", "d_co", "d_y0", "d_y1", "d_yf", "d_yw", "d_yc", "d_as", "d_ci"]
+DMAS += ["d_z%d" % j for j in range(2 * G // Z_G - 1)]
 SEMAPHORES = ["sV", "sA", "sP", "sG", "snt", "arr0", "arr1", "arr2"] + DMAS
 
 
@@ -97,70 +128,157 @@ def plan(calls):
                 if wr and not c["mark"]:
                     old = [u for u in old if not (bank or (x[4] == 1 and x[2] <= u[2][0] and u[2][1] <= x[3]))]
                 uses[x[1]] = old + [(i, wr, x[2:5])]
-    post = [[] for _ in calls]
+    worlds = range(len(WORLDS))
+    queue = [c["e"] for c in calls]
+    ns, late = [[c["ns"][k] for c in calls] for k in worlds], [[c["late"][k] for c in calls] for k in worlds]
+    above = [0] * n
     for i in range(n):
         for j in pre[i]:
-            post[j].append(i)
+            above[i] |= above[j] | 1 << j
+    near = [[j for j in pre[i] if late[0][j] > 100 or not any(above[k] >> j & 1 for k in pre[i])] for i in range(n)]
+    ways = [[[(j, 0 if j in calls[i]["after"] or queue[i] == queue[j] == "P" else
+               WORLDS[k][9 if queue[i] == queue[j] else 5] + late[k][j]) for j in near[i]] for i in range(n)] for k in worlds]
+    post = [[[] for _ in calls] for k in worlds]
+    for k in worlds:
+        for i in range(n):
+            for j, d in ways[k][i]:
+                post[k][j].append((i, d))
 
-    def hop(j, i):
-        if j in calls[i]["after"] or calls[j]["e"] == calls[i]["e"] == "P":
-            return 0
-        return HOP + calls[j]["late"]
-
-    chain = [0] * n
-    for j in range(n - 1, -1, -1):
-        chain[j] = calls[j]["ns"] + max([calls[j]["late"]] + [hop(j, i) + chain[i] for i in post[j]])
-    def place(order, back):
+    def place(order, back, k):
         start, busy = [0] * n, {e: [] for e in "VAPGS"}
         for i in order:
-            ns, line = calls[i]["ns"], busy[calls[i]["e"]]
-            if back:
-                t = max([calls[i]["late"]] + [start[j] + calls[j]["ns"] + hop(i, j) for j in post[i]])
-            else:
-                t = max([0] + [start[j] + calls[j]["ns"] + hop(j, i) for j in pre[i]])
-            k = 0
-            while k < len(line) and line[k][0] < t + ns:
-                t = max(t, line[k][1])
-                k += 1
-            line.insert(k, (t, t + ns))
+            line = busy[queue[i]]
+            t = max([late[k][i] * back] + [start[j] + ns[k][j] + d for j, d in (post if back else ways)[k][i]])
+            a = 0
+            while a < len(line) and line[a][0] < t + ns[k][i]:
+                t = max(t, line[a][1])
+                a += 1
+            line.insert(a, (t, t + ns[k][i]))
             start[i] = t
         return start
 
-    def ends(start, back):
-        return [start[i] + calls[i]["ns"] + (0 if back else calls[i]["late"]) for i in range(n)]
+    def first(k, over):
+        chain = [0] * n
+        for j in range(n - 1, -1, -1):
+            chain[j] = ns[k][j] + max([late[k][j]] + [d + chain[i] for i, d in post[k][j]])
+        left, ready, free = [len(p) for p in near], [0] * n, {e: 0 for e in "VAPGS"}
+        cand = {e: [i for i in range(n) if queue[i] == e and not near[i]] for e in free}
+        order = []
+        while len(order) < n:
+            best = None
+            for e in free:
+                if cand[e]:
+                    pick = top = max(cand[e], key=lambda i: chain[i])
+                    if ready[top] > free[e]:
+                        fit = [i for i in cand[e] if max(free[e], ready[i]) + ns[k][i] <= ready[top] + over and i != top]
+                        pick = max(fit, key=lambda i: chain[i]) if fit else top
+                    t = max(free[e], ready[pick])
+                    if best is None or t < best[0]:
+                        best = (t, e, pick)
+            t, e, j = best
+            order.append(j)
+            cand[e].remove(j)
+            free[e] = t + ns[k][j]
+            for i, d in post[k][j]:
+                ready[i] = max(ready[i], free[e] + d)
+                left[i] -= 1
+                if not left[i]:
+                    cand[queue[i]].append(i)
+        start = place(order, False, k)
+        found = [start]
+        for _ in range(ROUNDS):
+            for back in (True, False):
+                start = place(sorted(range(n), key=lambda i: -start[i] - ns[k][i]), back, k)
+            found.append(start)
+        return [sorted(range(n), key=lambda i: x[i]) for x in found]
 
-    left, ready, free = [len(p) for p in pre], [0] * n, {e: 0 for e in "VAPGS"}
-    cand = {e: [i for i in range(n) if calls[i]["e"] == e and not pre[i]] for e in free}
-    order = []
-    while len(order) < n:
-        best = None
-        for e in free:
-            if cand[e]:
-                pick = top = max(cand[e], key=lambda i: chain[i])
-                if ready[top] > free[e]:
-                    fit = [i for i in cand[e] if max(free[e], ready[i]) + calls[i]["ns"] <= ready[top] + OVER and i != top]
-                    pick = max(fit, key=lambda i: chain[i]) if fit else top
-                t = max(free[e], ready[pick])
-                if best is None or t < best[0]:
-                    best = (t, e, pick)
-        t, e, j = best
-        order.append(j)
-        cand[e].remove(j)
-        free[e] = t + calls[j]["ns"]
-        for i in post[j]:
-            ready[i] = max(ready[i], free[e] + hop(j, i))
-            left[i] -= 1
-            if not left[i]:
-                cand[calls[i]["e"]].append(i)
-    if not ROUNDS:
-        return order
-    best, start = None, place(order, False)
-    for _ in range(ROUNDS):
-        if best is None or max(ends(start, False)) < max(ends(best, False)):
-            best = start
-        for back in (True, False):
-            start = place(sorted(range(n), key=lambda i: -start[i] - calls[i]["ns"]), back)
-    return sorted(range(n), key=lambda i: best[i])
+    tails = [i for i in range(n) if not post[0][i]]
+
+    def run(order, k, a=0, old=None):
+        end, by = (old[3][:], old[2][:]) if old else ([0] * n, [None] * n)
+        last, way, took = {queue[i]: i for i in order[:a]}, ways[k], ns[k]
+        for i in order[a:]:
+            j0 = last.get(queue[i])
+            t = 0 if j0 is None else end[j0]
+            for j, d in way[i]:
+                if end[j] + d > t:
+                    t, j0 = end[j] + d, j
+            end[i], by[i] = t + took[i], j0
+            last[queue[i]] = i
+        top = max(tails, key=lambda i: end[i] + late[k][i])
+        return end[top] + late[k][top] + LEAN * sum(end) / n, top, by, end
+
+    seed = [SEED]
+
+    def draw(m):
+        seed[0] = (seed[0] * 1103515245 + 12345) % 2147483648
+        return (seed[0] >> 8) % m
+
+    def worth(runs):
+        return sum(r[0] / x for r, x in zip(runs, unit))
+
+    def polish(order, steps):
+        runs = [run(order, k) for k in worlds]
+        score = low = worth(runs)
+        keep = order
+        for step in range(steps):
+            _, i, by, _ = runs[draw(len(WORLDS))]
+            pairs, waits = [], []
+            while by[i] is not None:
+                if queue[by[i]] == queue[i] and not above[i] >> by[i] & 1:
+                    pairs.append((by[i], i))
+                elif queue[i] in "VA":
+                    waits.append(i)
+                i = by[i]
+            if waits and draw(4) < FILL:
+                u = waits[draw(len(waits))]
+                a = order.index(u)
+                free = [i for i in order[a + 1:a + 80] if queue[i] == queue[u] and not above[i] >> u & 1]
+                if not free:
+                    continue
+                w = free[draw(len(free))]
+            else:
+                u, w = pairs[draw(len(pairs))]
+            a, b = order.index(u), order.index(w)
+            for _ in range(draw(3)):
+                k = a - 1
+                while k >= 0 and queue[order[k]] != queue[w]:
+                    k -= 1
+                if k >= 0 and not above[w] >> order[k] & 1:
+                    a = k
+            part = order[a:b + 1]
+            if draw(2):
+                move = [i for i in part if i == w or above[w] >> i & 1]
+                part = move + [i for i in part if i not in move]
+            else:
+                move = [i for i in part if i == u or above[i] >> u & 1]
+                part = [i for i in part if i not in move] + move
+            new = order[:a] + part + order[b + 1:]
+            trial = [run(new, k, a, runs[k]) for k in worlds]
+            value = worth(trial)
+            if value <= score + SLACK * draw(1000) / 1000 * (1 - step / steps):
+                ends, at = trial[0][3], {i: k for k, i in enumerate(new)}
+                order, runs, score = sorted(new, key=lambda i: (ends[i] - ns[0][i], at[i])), trial, value
+                if value < low:
+                    low, keep = value, order
+        return low, keep
+
+    found = [x for k in worlds for over in OVER for x in first(k, over)]
+    unit = [run(found[0], k)[0] for k in worlds]
+    found.sort(key=lambda x: worth([run(x, k) for k in worlds]))
+    found = sorted([polish(x, POLISH // 10) for x in found[:STARTS]], key=lambda x: x[0])
+    low, keep = found[0]
+    for _, other in found[1:] * 2:
+        for cut in range(CUT, n, CUT):
+            for x, y in ((keep, other), (other, keep)):
+                front = set(x[:cut])
+                new = x[:cut] + [i for i in y if i not in front]
+                value = worth([run(new, k) for k in worlds])
+                if value < low:
+                    low, keep = value, new
+    keep = polish(keep, POLISH)[1]
+    NOTE.append([round(run(keep, k)[0]) for k in worlds])
+    return keep
 
 
 def rank_program(g, core, T, topo):
@@ -169,6 +287,7 @@ def rank_program(g, core, T, topo):
         return
     eng = {"V": g.vector, "A": g.scalar, "P": g.tensor, "G": g, "S": g.sync}
     calls = []
+    hold = []
 
     def B(n, a=0, b=None, st=1):
         if n in PART:
@@ -185,20 +304,20 @@ def rank_program(g, core, T, topo):
     def size(x):
         return 16 * size(x[5]) if x[5] else len(range(x[2], x[3], x[4]))
 
-    def call(e, fn, r, w, ns, late=0, sem=None, mark=False, after=()):
+    def call(e, fn, r, w, cost, late=lambda x: 0, sem=None, mark=False, after=()):
         r = [x for x in r if isinstance(x, tuple)]
-        calls.append({"e": e, "fn": fn, "r": r + [x[5] for x in r + w if x[5]], "w": w, "ns": ns, "late": late,
-                      "sem": sem, "mark": mark, "after": list(after)})
+        calls.append({"e": e, "fn": fn, "r": r + [x[5] for x in r + w if x[5]], "w": w, "ns": [cost(x) for x in WORLDS],
+                      "late": [late(x) for x in WORLDS], "sem": sem, "mark": mark, "after": list(after)})
         return len(calls) - 1
 
-    def op(e, fn, r, w, cycles=None):
-        o = w[0]
+    def op(e, fn, r, w, cycles=None, more=0):
+        o, k = w[0], 4 if e == "A" else 3
         if o[5] or (r and r[0][5]):
-            ns = 55 + size(o) * (SCAT if o[5] else GATH)
-        else:
-            narrow = all(SCRATCH[x[1]][2] in (BF, F16, U16) for x in [o] + r if isinstance(x, tuple) and size(x) > 1)
-            ns = (CALL_A if e == "A" else CALL_V) + CY * size(o) * (cycles or (0.5 if narrow and e == "V" else 1))
-        return call(e, fn, r, w, ns)
+            return call(e, fn, r, w, lambda x: INDIRECT[e] + CY * x[0] * size(o) * x[2 if o[5] else 1] * (1.5 if cycles else 1))
+        narrow = all(SCRATCH[x[1]][2] in (BF, F16, U16) for x in [o] + r if isinstance(x, tuple) and size(x) > 1)
+        n = size(o) * (cycles or (0.5 if narrow and e == "V" else 1))
+        psum = any(x[1] in PSUMS for x in [o] + r if isinstance(x, tuple))
+        return call(e, fn, r, w, lambda x: more + x[k] + x[13] * psum + CY * x[0] * max(n, x[12]))
 
     def ap(x):
         return x[0] if isinstance(x, tuple) else x
@@ -209,15 +328,15 @@ def rank_program(g, core, T, topo):
             for o, l, x, s0, s1 in lst:
                 ins = g.tensor.matmul(o[0], l[0], x[0], s0, s1)
             return ins
-        ns = sum(max(64, size(m[2])) * COL * (4 if SCRATCH[m[2][1]][2] == F32 else 1) for m in lst)
-        call("P", f, [x for m in lst for x in m[1:3]], [m[0] for m in lst], ns, 60, mark=mark)
+        n = sum(max(64, size(m[2])) * (4 if SCRATCH[m[2][1]][2] == F32 else 1) for m in lst)
+        call("P", f, [x for m in lst for x in m[1:3]], [m[0] for m in lst], lambda x: n * x[0] * x[6], lambda x: 60, mark=mark)
 
     def grp(o, terms):
         return [(o, l, x, i == 0, i == len(terms) - 1) for i, (l, x) in enumerate(terms)]
 
     def dma(sem, o, i, late, after=()):
-        return call("S", lambda: g.sync.dma_start(ap(o), ap(i)), [i], [o] if isinstance(o, tuple) else [], 50, late, sem,
-                    after=after)
+        return call("S", lambda: g.sync.dma_start(ap(o), ap(i)), [i], [o] if isinstance(o, tuple) else [], lambda x: 50,
+                    lambda x: 900 + (late - 900) * x[8], sem, after=after)
 
     v = g.vector
 
@@ -245,23 +364,31 @@ def rank_program(g, core, T, topo):
     def red(o, i):
         op("V", lambda: v.tensor_reduce(o[0], i[0], AxisListType.X, A.add), [i], [o], 16)
 
-    def act(o, i, f, **kw):
+    def act(o, i, f, more=0, **kw):
         acc = [kw["accum_out"]] if "accum_out" in kw else []
         op("A", lambda: g.scalar.activation(o[0], i[0], f, **{k: ap(x) for k, x in kw.items()}),
-           [i] + [kw[k] for k in ("bias", "scale") if k in kw], [o] + acc)
+           [i] + [kw[k] for k in ("bias", "scale") if k in kw], [o] + acc, None, more)
 
     def lin(o, i, scale, bias=0.0):
         act(o, i, AF.Identity, scale=scale, bias=bias)
 
+    def vlin(o, i, scale, bias=0.0):
+        ts(o, i, scale, A.mult, bias, A.add)
+
     def iota(o, pat, base, cm=0):
         kw = {} if SCRATCH[o[1]][2] == I32 else {"allow_small_or_imprecise_dtypes": True}
-        call("G", lambda: g.iota(o[0], pat, base, cm, **kw), [], [o], 130 + 2 * CY * size(o))
+        call("G", lambda: g.iota(o[0], pat, base, cm, **kw), [], [o], lambda x: (130 + 2 * CY * size(o)) * x[10],
+             after=hold)
 
     def fill(o, c):
         iota(o, [[0, size(o)]], c)
 
-    def select(o, i, pat, cm, test=A.is_ge):
-        call("G", lambda: g.affine_select(o[0], i[0], pat, test, 0.0, 0, cm), [i], [o], 170 + 2 * CY * size(o))
+    def select(o, i, pat, cm, test=A.is_ge, other=0.0):
+        return call("G", lambda: g.affine_select(o[0], i[0], pat, test, other, 0, cm), [i], [o],
+                    lambda x: (170 + 2 * CY * size(o)) * x[10], after=hold)
+
+    def ident(o, c):
+        select(o, B("zr"), [[1, 128]], -1, A.not_equal, c)
 
     def col(i):
         return B("co_", i, i + 1)
@@ -274,7 +401,8 @@ def rank_program(g, core, T, topo):
 
     Ib, BO, xb = B("J", 0, 128), B("BO", 0, 128), B("xb", 0, 128)
     x144 = B("xb", 0, 144)
-    I32x, MC, IK = M(2), M(10), B("IL", 256, 384)
+    nKB, KB, I4, KBS, KS, nKS, GM, LM, M8, M9, I20, D2, D1, W2, W1, I16 = [M(i) for i in range(16)]
+    IK = B("IL", 256, 384)
     EB = ("pa", "pc", "pd", "pe")
 
     def PMm(kind, d):
@@ -286,14 +414,14 @@ def rank_program(g, core, T, topo):
 
     k = []
     for sem, o, i, late in (("d_aw", B("awi"), T.aw[:], 1100), ("d_x0", B("XT", D, D + V), T.x0[:], 3100),
-                            ("d_gv", B("gvi", 0, G), T.gv[:], 6200), ("d_ex", B("exi", 0, 14), T.ex[:], 6200),
-                            ("d_co", B("C", D, D + W), T.co[:], 10600)):
+                            ("d_gv", B("gvi", 0, G), T.gv[:], 6200), ("d_ex", B("exi", 0, 14), T.ex[:], 6250),
+                            ("d_co", B("C", D, D + V), T.co[:, 0:V], 10250), ("d_ci", B("C", D + V, D + W), T.co[:, V:W], 10650)):
         k = [dma(sem, o, i, late, k)]
 
     iota(B("pi", 0, 1), [[0, 1]], 0, 1)
     iota(B("xb"), [[1, 256]], 0)
-    iota(B("mg"), [[0, 4], [16, 8], [0, 16]], 0)
-    fill(B("ones"), 1)
+    iota(B("mg"), [[16, 8], [0, 16]], 0)
+    ms(B("ones"), 1.0)
     iota(rows("JR", slice(0, 1), 0, 512), [[-16, 4], [0, 8], [-1, 16]], 0)
     for j, m in enumerate((15, 16, 1, 96)):
         ts(B("pi", j + 1, j + 2), B("pi", 0, 1), m, A.bitwise_and)
@@ -304,127 +432,104 @@ def rank_program(g, core, T, topo):
     ts(col(16), col(15), 15.0, A.add)
     ts(col(17), col(1), 15.0, A.is_equal)
     ts(B("oh"), B("xb", 0, 16), col(1), A.is_equal)
-    for j in range(7):
-        act(B("AS", WK + 256 * j, WK + 256 * j + 256), B("xb"), AF.Silu, scale=0.0)
-        calls[-1]["ns"] += 1300 * (j == 0)
-    dma("d_zS", B("AS2", WK, WW), B("AS", WK, WW), 4000, k)
-    fill(B("AV", WK, WW), 0)
-    dma("d_zV", B("AV2", WK, WW), B("AV", WK, WW), 2500, k)
-    ms(B("t16", 0, 16), 4.0)
-    ms(B("t16", 16, 32), 0.0)
-    ms(B("t16", 32, 48), 0.25)
-    scan(B("pw", 0, 16), B("t16", 0, 16), B("t16", 16, 32), 0.25, A.mult, A.add)
-    scan(B("pw", 16, 32), B("t16", 32, 48), B("t16", 16, 32), 4.0, A.mult, A.add)
-    ts(col(5), col(1), 4.0, A.is_lt)
-    ts(col(6), col(1), 6.5, A.is_lt)
-    tt(col(7), col(6), col(5), A.subtract)
-    tt(B("t16", 48, 64), B("pw", 16, 32), B("oh"), A.mult)
-    red(col(9), B("t16", 48, 64))
-    tt(col(10), col(9), col(5), A.mult)
-    ts(col(11), col(9), 256.0, A.mult, col(7), A.mult)
-    ts(col(33), col(7), -14.0625 / 32, A.mult, -1.0 / 32, A.add)
-    ts(col(34), col(7), -14.0625, A.mult, 15.0625, A.add)
-    ts(B("dgi", 0, 128), xb, col(10), A.mult, -0.4921875, A.add)
-    ts(B("dgi", 128, 160), B("xb", 0, 32), col(11), A.mult, -0.4921875, A.add)
-    ts(B("dgi", 160, 320), B("dgi", 0, 160), 3, A.bitwise_and)
-    ts(B("An"), B("dgi", 288, 320), -0.0625 / 32, A.mult, col(33), A.add)
-    ts(B("Bp", 0, 128), B("dgi", 160, 288), 0.0625, A.mult, col(34), A.add)
-    for n in (128, 256):
-        lin(B("Bp", n, 2 * n), B("Bp", 0, n), 1.0)
-    for a, b, lo, h in ((0, 96, 32, 18), (96, 224, 0, 19), (224, 288, 0, 20)):
-        ts(B("NC", a, b), B("Bp", lo, lo + b - a), B("An", h, h + 1), A.mult)
-    lin(B("XF", D + V, D + W), B("NC", 0, 224), -32.0, -1.0)
+    act(B("ls", 0, 224), B("ones", 0, 224), AF.Silu, 1300, scale=float(LEV[0]))
+    for a in range(WK, WK + Z_G, 448):
+        fill(B("AS", a, a + 448), 0)
+    spots = [("AS", a) for a in range(WK + Z_G, WW, Z_G)] + [("AS2", a) for a in range(WK, WW, Z_G)]
+    for j, (n, a) in enumerate(spots):
+        dma("d_z%d" % j, B(n, a, a + Z_G), B("AS", WK, WK + Z_G), (10650 if Z_G < G else 900) + Z_G * 1.8 * (j + 1), k)
+    ts(col(19), col(1), 10.5, A.is_lt, -8192.0, A.mult)
+    ts(B("sK"), B("oh"), -1.0 / 256, A.mult)
+    ts(col(5), col(17), 225.0 / 256, A.mult)
+    ts(col(6), col(19), -240.0 / 256 / 8192, A.mult, col(5), A.add)
+    ts(B("aK"), B("xb", 0, 16), col(1), A.is_le, col(6), A.mult)
+    ts(B("aK"), B("aK"), -241.0 / 256, A.add)
+    for b in range(11):
+        o, s1, s2 = B("AV", 240 * b, 240 * b + 240), B("sK", b, b + 1), B("aK", b, b + 1)
+        if b in K_ACT:
+            lin(o, B("xb", 0, 240), s1, s2)
+        else:
+            ts(o, B("xb", 0, 240), s1, A.mult, s2, A.add)
+    fill(B("XT", D + V, XW), -1)
     fill(B("S", 4096, 4864), 0)
-    for i in (14, 15):
-        lin(B("S", 4096 + i, 4864, 16), B("NC", 240, 288), -32.0, -1.0)
-    tt(B("t16", 0, 16), B("pw", 0, 16), B("oh"), A.mult)
-    red(col(8), B("t16", 0, 16))
-    ts(col(43), col(7), 8.0, A.mult)
-    ts(col(18), col(5), 16.0, A.mult, col(43), A.add)
-    tt(col(19), col(18), col(8), A.mult)
     select(B("J"), B("ones", 0, 144), [[1, 144]], -1, A.is_equal)
-    ts(B("BO"), B("mg"), col(15), A.is_equal)
+    ts(BO, B("mg"), col(15), A.is_equal)
     select(B("TRI"), BO, [[1, 128]], -1)
     ts(B("ZS"), x144, col(16), A.is_equal)
-    for j, c in enumerate((1, 16)):
-        fill(B("hv", 2 * j, 2 * j + 1), c)
-    lin(B("hv", 1, 4, 2), B("hv", 0, 4, 2), 0.5)
-    lin(I32x, Ib, 32.0)
-    lin(col(38), B("oh", 0, 1), -622592.0)
-    lin(col(39), B("oh", 1, 2), -2048.0, col(38))
-    lin(col(40), B("oh", 2, 3), -5.0, col(39))
-    lin(col(35), col(17), -K1, col(40))
-    lin(col(20), col(17), 16 * K1, 64 * K1)
-    ts(M(0), BO, -64 * K1, A.mult)
-    ts(M(1), BO, col(20), A.mult)
-    lin(M(3), BO, col(35))
-    ts(M(4), BO, -K2, A.mult)
-    ts(M(5), BO, K2, A.mult)
-    ts(M(7), BO, col(17), A.mult, -16 * K1, A.mult)
-    ts(M(8), BO, col(19), A.mult)
-    ts(M(9), BO, col(19), A.mult, -1.0, A.mult)
-    ts(MC, BO, col(40), A.mult)
-    lin(IK, Ib, K1)
-    lin(B("Z0h"), B("ZS"), B("oh", 0, 1))
+    ts(KS, BO, col(17), A.mult, K, A.mult)
+    ts(nKS, BO, col(17), A.mult, -K, A.mult)
+    lin(I20, Ib, 16.0 / K)
+    ts(col(9), col(17), 0.125 - 1.0 / 32, A.mult, 1.0 / 32, A.add)
+    ts(col(10), col(17), 1.0 / 32 - 0.125, A.mult, 1.0 - 1.0 / 32, A.add)
+    lin(D2, Ib, col(9))
+    lin(D1, Ib, col(10))
+    mm(grp(B("pg", 0, 128), [(I20, KS), (D2, Ib)]) + grp(B("pg", 128, 256), [(I20, nKS), (D1, Ib)]))
+    act(B("MM", 128 * 13, 128 * 15), B("pg", 0, 256), AF.Copy)
+    ts(col(11), col(17), K, A.mult, col(19), A.add)
+    ts(nKB, BO, -K, A.mult)
+    ts(KB, BO, K, A.mult)
+    ts(GM, BO, col(11), A.mult)
+    select(LM, nKB, [[1, 128]], -1, A.not_equal, -K * C0)
+    iota(B("OH"), [[0, 8], [1, 16]], 0)
+    ts(B("OH"), B("OH"), col(1), A.is_equal)
+    (lin if HB_ACT else vlin)(M8, BO, col(19))
+    (lin if HB_ACT else vlin)(M9, M8, -1.0)
+    ms(B("zr"), 0.0)
     lin(B("Z0"), B("ZS"), B("oh", 0, 1))
+    if any(DIRECT):
+        lin(B("Z0f"), B("Z0"), 1.0)
     lin(B("Zd"), B("ZS"), col(19))
     lin(B("Z8h"), B("ZS"), -8192.0)
     lin(B("ZSh"), B("ZS"), 1.0)
-    lin(B("If"), Ib, 1.0)
-    lin(B("ILf"), Ib, LEV[2] / 4)
-    for j in range(2):
-        lin(B("IL", 128 * j, 128 * j + 128), Ib, LEV[j] / 4)
-        lin(B("I8h", 128 * j, 128 * j + 128), Ib, 8192.0 * (2 * j - 1))
-    lin(col(23), col(1), 2.0, col(4))
-    lin(col(24), col(23), 1.0, 1.0)
+    ts(col(12), col(17), -K, A.mult, K, A.add)
+    (lin if HB_ACT else vlin)(KBS, BO, col(12))
+    for o, c in ((I16, 16.0), (IK, K1), (B("If"), 1.0), (I4, 4096.0), (B("I8h", 0, 128), -8192.0), (B("I8h", 128, 256), 8192.0),
+                 (B("IL", 0, 128), LEV[0] / 4)):
+        ident(o, c)
+    ts(col(23), col(1), 2.0, A.mult, 1.0, A.add)
+    ts(col(24), col(23), col(4), A.add)
     for n, c in (("H0", 13), ("H1", 14)):
         ts(B(n + "h"), x144, col(24), A.is_equal, col(c), A.mult)
-        lin(B(n + "b"), B(n + "h"), 256.0)
-    lin(col(27), col(15), -1.0, 112.0)
+        (lin if HB_ACT else vlin)(B(n + "b"), B(n + "h"), 256.0)
+    ts(col(27), col(15), -1.0, A.mult, 112.0, A.add)
     ts(col(44), col(15), 0.0, A.is_gt, 128.0, A.mult)
-    lin(col(28), col(27), 1.0, col(1))
-    lin(col(29), col(15), -1.0, col(44))
+    ts(col(28), col(27), col(1), A.add)
+    ts(col(29), col(44), col(15), A.subtract)
     ts(PMm(0, 1), xb, col(28), A.is_equal)
     ts(PMm(0, 2), xb, col(1), A.subtract, col(29), A.is_equal)
     for d, c in ((0, 15), (1, 27), (2, 29)):
         ts(PMm(1, d), B("mg", 0, 128), col(c), A.is_equal, col(17), A.mult)
         lin(PMm(2, d), PMm(1, d), -1.0)
-    lin(B("KJ"), B("xb", 0, 224), 1.0 / 256, 1.0 / 256 - 1.0)
-    for n, c, a, b in [("CCb", 45 + h) + x for h, x in enumerate(HALVES)] + [("CCi", 26, 0, 224)]:
+    (lin if CC_ACT else vlin)(B("KJ"), B("xb", 0, 224), 1.0 / 256, 1.0 / 256 - 1.0)
+    at = {}
+    for a, b in HALVES:
+        at.setdefault(b - a, a)
+    for n, c, a, b in [("CCb", 45 + h, a, a + n) for h, (n, a) in enumerate(at.items())] + [("CCi", 26, 0, 224)]:
         k = (b - a) // 2
-        lin(col(c), col(3), -1.0 * k, 256.0)
+        ts(col(c), col(3), -1.0 * k, A.mult, 256.0, A.add)
         for j in (a, a + k):
-            lin(B(n, j, j + k), B("xb", 0, k), -1.0, col(c))
-    if True in LATCH:
-        ts(col(22), col(1), 15.0, A.is_lt, 4096.0, A.mult)
-        ts(B("lat", 0, 16), B("xb", 0, 16), 1.0, A.subtract, col(1), A.is_equal)
-        ts(B("lat", 16, 32), B("oh"), -2.0, A.mult)
-        tt(B("lat", 32, 48), B("lat", 0, 16), B("lat", 16, 32), A.add)
-        lin(B("LC", 0, 16), B("lat", 32, 48), 4096.0)
-        lin(col(22), col(22), 1.0, -SH)
-        for n in (16, 32, 64, 128):
-            lin(B("LC", n, 2 * n), B("LC", 0, n), 1.0)
-    lin(col(41), col(1), 1.0, 0.5)
-    lin(col(42), col(1), 1.0, 256.0 + K2 - ZB)
-    lin(B("jh", 0, 3), B("xb", 0, 48, 16), 1.0, col(41))
-    lin(B("dd", 0, 3), B("xb", 0, 48, 16), 1.0, col(42))
-    ms(B("aws", 112, 128), 1.0)
-    ms(B("sc1", 0, 1), 0.0)
-    ms(B("SM"), 1.0)
-    ms(B("SM", 0, None, 16), 0.0)
-    ms(B("SM", 15, None, 16), 0.0)
+            (lin if CC_ACT else vlin)(B(n, j, j + k), B("xb", 0, k), -1.0, col(c))
+    fill(B("LD"), 0)
+    ts(col(22), col(1), 240.0 - ZB, A.add)
+    ts(B("LD", 0, 256, 16), B("xb", 0, 256, 16), -1.0, A.mult, col(22), A.add)
+    ts(B("jh", 0, 3), B("xb", 0, 48, 16), col(1), A.add, 0.5, A.add)
+    ts(B("dd", 0, 3), B("xb", 0, 48, 16), col(1), A.add, 256.0, A.add)
+    fill(B("cz"), int(ZB - K2))
+    fill(B("aws", 112, 128), 1)
+    fill(B("sc1", 0, 1), 0)
+    if SM_G:
+        iota(B("SM"), [[0, size(B("SM")) // 16], [20, 16]], -34)
+    else:
+        ms(B("SM"), 20.0)
+        ms(B("SM", 0, None, 16), -20.0)
+        ms(B("SM", 1, None, 16), -20.0)
     ms(B("lz", 3, 4), 4110)
-    iota(B("M192"), [[-16, 3], [1, 48]], 0)
-    ts(B("M192"), B("M192"), col(1), A.is_ge, 8192.0, A.mult)
-    iota(B("jr"), [[1, 256]], -int(SH))
-    for o, c in ((B("zr"), 0), (B("gvi", G, 2048), W), (B("XF", D + W, XW), 0), (B("C", 0, D), -1), (B("C", D + W, XW), -1),
-                 (B("XF", 0, D), 0), (B("want", 256, 304), 1), (B("neg1"), -1), (B("k4"), 4096), (B("XT", 0, D), 0)):
+    ts(B("M16"), B("xb", 0, 16), col(1), A.is_ge, 8192.0, A.mult)
+    for o, c in ((B("gvi", G, 2048), W), (B("XF", D + W, XW), -14), (B("C", 0, D), -1), (B("C", D + W, XW), -1),
+                 (B("XF", 0, D), 0), (B("want", 256, 304), 1), (B("neg1"), -1),
+                 (B("MAG"), int(MAGIC)), (B("t196"), 196)):
         fill(o, c)
-    for s in range(3):
-        fill(B("ls", 224 * s, 224 * s + 224), LEV[s])
-        fill(B("lv", 224 * s, 224 * s + 224), LEV[s])
-    for a in range(0, XW, 488):
-        iota(B("F", a, a + 488), [[1, 488]], a - D)
+    fill(B("lv", 0, 224), LEV[0])
 
     def turn(terms, bank):
         lst = []
@@ -433,30 +538,43 @@ def rank_program(g, core, T, topo):
                 lst += grp(B(bank, 32 * t + a, 32 * t + a + 16), [(B("J", a, a + 128), f(t)) for f in terms])
         mm(lst)
 
-    cp(B("awb"), B("awi"))
+    if AW_G:
+        select(B("awb"), B("awi"), [[0, 112]], 0)
+    else:
+        cp(B("awb"), B("awi"))
     turn([lambda t: B("awb", 16 * t, 16 * t + 16)], "pf")
     for t in range(7):
         vtr(B("TT", t, t + 218, 7), B("pf", 32 * t, 32 * t + 32))
-    cp(B("aws", 0, 112), B("TT", 0, 112))
+    if AW_OFF:
+        act(B("aws", 0, 112), B("TT", 0, 112), AF.Copy)
+    else:
+        cp(B("aws", 0, 112), B("TT", 0, 112))
     cp(B("exu", 0, 14), B("exi", 0, 14))
 
     def encode():
-        for h in range(19):
-            b = min(128 * h + 128, V)
-            if h % 4 in EM_ACT:
-                act(B("em", 128 * h, b), B("XT", D + 128 * h, D + b), AF.Relu, scale=B("An", h, h + 1))
-            else:
-                ts(B("em", 128 * h, b), B("XT", D + 128 * h, D + b), B("An", h, h + 1), A.mult, 0.0, A.max)
-        for k in range(5):
-            a, b = 512 * k, min(512 * k + 512, V)
-            scan(B("et", a, b), B("Bp", 0, b - a), B("em", a, b), 0.0, A.max, A.mult)
+        for k, (a, b) in enumerate(CHUNKS):
+            scan(B("AV2", a, b), B("AV", a, b), B("XT", D + a, D + b), 0.0, A.min, A.max)
             bk = ("ph", "pb")[k % 2]
-            mm(grp(B(bk, 0, b - a), [(Ib, B("XT", D + a, D + b)), (I32x, B("et", a, b))]))
-            act(B("XF", D + a, D + b), B(bk, 0, b - a), AF.Copy)
+            mm(grp(B(bk, 0, b - a), [(W1, B("XT", D + a, D + b)), (W2, B("AV2", a, b))]))
+            if a == V and NC_G:
+                lin(B("NC"), B(bk, 0, b - a), 1.0, -14.0)
+                select(B("XF", D + V, D + W), B("NC", 0, W - V), [[0, W - V]], 0)
+            elif k in XF_VEC:
+                ts(B("XF", D + a, D + min(b, W)), B(bk, 0, min(b, W) - a), -14.0, A.add)
+            else:
+                lin(B("XF", D + a, D + min(b, W)), B(bk, 0, min(b, W) - a), 1.0, -14.0)
+            if a == V:
+                if not NC_G:
+                    lin(B("NC"), B(bk, 0, b - a), 1.0, -14.0)
+                for i in (14, 15):
+                    lin(B("S", 4096 + i, 4864, 16), B("NC", 240, 288), 1.0)
 
-    def refresh(ks, tab="XF", tmp="x48"):
+    def refresh(ks, tab="XF", tmp="x48", e="V"):
         for k in ks:
-            cp(B(tmp), X(B(tab), B("LT", 8 * k + 4, 8 * k + 7)))
+            if e == "A":
+                act(B(tmp), X(B(tab), B("LT", 8 * k + 4, 8 * k + 7)), AF.Copy)
+            else:
+                cp(B(tmp), X(B(tab), B("LT", 8 * k + 4, 8 * k + 7)))
             cp(X(B(tab), B("LT", 8 * k, 8 * k + 3)), B(tmp))
 
     def shuffle(bank, n, cc, cg, tm, a=0):
@@ -480,15 +598,27 @@ def rank_program(g, core, T, topo):
         def f():
             w = wins[-1] if lastw[e] == wins[0] else wins[0]
             lastw[e] = w
-            o = X(B(w), off)
+            o = X(B(w, 0, WW), off)
             return (g.scalar.activation(o[0], val[0], AF.Silu) if e == "A" else v.tensor_copy(o[0], val[0])), o
-        lastc[e] = [call(e, f, [val, off], [B(w) for w in wins], 55 + (SCAT_A if e == "A" else SCAT) * size(val) + HOP * (len(wins) == 1), mark=True, after=lastc[e])]
+        lastc[e] = [call(e, f, [val, off], [B(w, 0, WW) for w in wins],
+                         lambda x: INDIRECT[e] + CY * x[0] * x[2] * size(val) + x[9] * (len(wins) == 1),
+                         mark=True, after=lastc[e])]
 
     win = B("XF", D, XW)
     tops = {}
 
     for s in range(3):
         first, last = s == 0, s == 2
+        if s:
+            for n in ("ls", "lv"):
+                fill(B(n, 224 * s, 224 * s + 224), LEV[s])
+        if s == 1:
+            fill(B("XT", 0, D), 0)
+            ident(B("IL", 128, 256), LEV[1] / 4)
+            for a in range(0, XW, 488):
+                iota(B("F", a, a + 488), [[1, 488]], a - D)
+        if last:
+            ident(B("ILf"), LEV[2] / 4)
         for b in EB:
             mm([(B(b), rows("ones", slice(0, 1), 0, 128), rows("JR", slice(0, 1), 0, 512), True, False)])
         scan(B("sc1", 1, 129), B("ones", 0, 128), B("aws"), 0.0, A.mult, A.add)
@@ -497,20 +627,28 @@ def rank_program(g, core, T, topo):
         act(B("pre"), B("pb", 0, 128), AF.Copy)
         act(B("sg"), B("pre", 0, 112), AF.Sign, bias=-256.5)
         for b in EB:
-            mm([(B(b), B("sc1", 1, 129), B("BO"), False, True)])
+            mm([(B(b, 128 * c, 128 * c + 128), B("sc1", 1, 129), BO, False, c == 3) for c in range(4)])
 
         def count(bank, h, k):
+            wt = [k >> max(c // 4, h * (EQ_ACT - 2)) for c in range(8)]
             return [(B(bank, c, c + 1), B("EQ", 1024 * h + 128 * c, 1024 * h + 128 * c + 128),
-                     B("hv", k + c // 4, k + c // 4 + 1), k == 0, k == 0) for c in range(8)]
+                     B("xb", wt[c], wt[c] + 1), k == 2, k == 2) for c in range(8)]
 
         for h in range(2):
-            ts(B("EQ", 1024 * h, 1024 * h + 512), B(EB[2 * h]), 128.0 * h, A.is_le, 0.5, A.subtract)
+            if h * EQ_ACT < 3:
+                ts(B("EQ", 1024 * h, 1024 * h + 512), B(EB[2 * h]), 128.0 * h, A.is_le, 0.5, A.subtract)
+            else:
+                act(B("EQ", 1024 * h, 1024 * h + 512), B(EB[2 * h]), AF.Sign, bias=128.0 * h + 0.5, scale=-1.0)
             act(B("EQ", 1024 * h + 512, 1024 * h + 1024), B(EB[2 * h + 1]), AF.Sign, bias=128.0 * h + 64.5, scale=-1.0)
-            mm(count(("pf", "pg")[h], h, 0))
+            mm(count(("pf", "pg")[h], h, 2))
         for h in range(2):
             a, o = 128 * h, B(("pa", "pc")[h], 0, 8)
-            ts(B("bw", 8 * h, 8 * h + 8), B(("pf", "pg")[h], 0, 8), 64.0, A.add)
-            mm([(o, BO, B("zr", 0, 8), True, False)] + count(("pa", "pc")[h], h, 2))
+            ts(B("bw", 8 * h, 8 * h + 8), B(("pf", "pg")[h], 0, 8), 0.5, A.mult, 64.0, A.add)
+            if BWB:
+                ts(B("bwb", 8 * h, 8 * h + 8), B(("pf", "pg")[h], 0, 8), 0.5, A.mult)
+                mm([(o, I16, B("bwb", 8 * h, 8 * h + 8), True, False)])
+            else:
+                mm([(o, BO, B("zr", 0, 8), True, False)] + count(("pa", "pc")[h], h, 16))
             tt(B("cmp", a, a + 128), X(B("pre"), B("bw", 8 * h, 8 * h + 8)), B("xb", a, a + 128), A.is_le)
             mm([(o, sel("ZS", p), B("cmp", a + p, a + 128, 16), False, p == 15) for p in range(16)])
             ts(B("eu", 8 * h, 8 * h + 8), o, 1024.0, A.add)
@@ -518,8 +656,13 @@ def rank_program(g, core, T, topo):
         if first:
             encode()
 
-        def four(a, b):
-            return B("S", 16 * a + 14, 16 * b, 16), B("S", 16 * a + 15, 16 * b, 16), B("RM", a, b), B("RO", a, b)
+        def two(a, b):
+            return B("S", 16 * a + 14, 16 * b, 16), B("GG", 16 * a + 15, 16 * b, 16)
+
+        def fraction(o, a, b, m, last):
+            mx, go = two(a, b)
+            mm([(o, m[0], mx, False, False), (o, nKS, B("MAG", 0, b - a), False, False), (o, m[1], mx, False, False)]
+               + [(o, l, x, False, last and i == len(m[2]) - 1) for i, (l, x) in enumerate(m[2])])
 
         for a, b, e in (GATHER0 if first else GATHER):
             if e == "A":
@@ -527,42 +670,47 @@ def rank_program(g, core, T, topo):
             else:
                 cp(B("GG", 16 * a, 16 * b), X(win, B("gve", a, b)))
         for a, b in SCANS:
-            scan(B("S", 16 * a, 16 * b), B("SM", 0, 16 * (b - a)), B("GG", 16 * a, 16 * b), 0.0, A.mult, A.max)
-        mm([(B("ph", 0, 256), BO, B("zr"), True, False)])
+            scan(B("S", 16 * a, 16 * b), B("SM", 1, 1 + 16 * (b - a)), B("GG", 16 * a, 16 * b), 0.0, A.min, A.max)
+        mm([(B("ph", 0, 256), KS, B("MAG"), True, False), (B("ph", 0, 256), nKB, B("t196"), False, False)])
         for a, b in HALVES:
-            for i in range(0, 15, 3):
-                mm([(B("ph", a, b), M(0), B("GG", 16 * a + j, 16 * b, 16), False, False) for j in range(i, i + 3)], "sum")
+            for i in range(0, 16, 4):
+                mm([(B("ph", a, b), nKB if j < 15 else nKS, B("GG", 16 * a + j, 16 * b, 16), False, False)
+                    for j in range(i, i + 4)], "sum")
         for h, (a, b) in enumerate(HALVES):
             bk, bl, n, k = ("pf", "pg")[h], ("pb", "pc")[h], b - a, (b - a) // 16
-            mx, go, rm, ro = four(a, b)
+            mx, go = two(a, b)
             ou = B("obu", a // 16, b // 16)
-            ts(rm, mx, MAGIC, A.add, MAGIC, A.subtract)
-            if RO_ACT[h]:
-                act(ro, go, AF.Abs, bias=-14.0625)
-            else:
-                ts(ro, go, 14.0625, A.not_equal)
-            mm(grp(B(bk, 0, n), [(M(4), mx), (M(5), rm), (M(7), ro), (M(8), go), (MC, B("ones", 0, n))]))
-            tt(B("ob", a, b), B(bk, 0, n), B("jr", a, b), A.max)
-            if LATCH[h]:
-                scan(B("lat", a, b), B("LC", 0, n), B("ob", a, b), 0.0, A.add, A.max)
-                ts(ou, B("lat", a + 15, b, 16), col(22), A.subtract)
-            else:
-                mm(grp(B(bk, 256, 256 + k), [(sel("Z0h", p), B("ob", a + p, b, 16)) for p in range(16)]))
-                ts(ou, B(bk, 256, 256 + k), SH, A.add)
-            cp(B("cg", a, b), X(B("C"), ou))
-            shuffle(bl, n // 2, B("CCb", a, b), "cg", "tm", a)
+            mm([(B(bk, 0, n), KS, B("MAG", 0, n), True, False)])
+            mm([(B(bk, 0, n), nKS, go, False, False)])
+            fraction(B(bk, 0, n), a, b, (KB, nKB, [(GM, go), (LM, B("OH", 0, n))]), True)
+            scan(B("lat", a, b), B("LD", a, b), B(bk, 0, n), 0.0, A.min, A.max)
+            ts(ou, B("lat", a + 15, b, 16), ZB, A.add)
+            cp(B("cg", a, b), X(B("C", 0, D + V), ou))
+            shuffle(bl, n // 2, B("CCb", at[n], at[n] + n), "cg", "tm", a)
             lists(bl, k // 2, "TT", a, "wl")
             for r in range(16):
                 e = "V" if r < BIND_VEC[s][h] else "A"
                 scatter(e, s, B("wl", a + k * r, a + k * r + k), ("AS", "AS2") if e == "A" else ("AV", "AV2"))
-        mx, go, rm, ro = four(0, 256)
-        cp(X(B("XF"), B("obu")), mx)
-        refresh(range(s - 1, -1, -1))
+        mx, go = two(0, 256)
+        for a, b, e in M14:
+            if e == "A":
+                lin(B("m14", a, b), two(a, b)[0], 1.0, 14.0)
+            else:
+                ts(B("m14", a, b), two(a, b)[0], 14.0, A.add)
+        tab, free = ("XT", -1.0) if last and XT_LAST else ("XF", C0)
+        if tab == "XF":
+            cp(X(B("XF"), B("obu")), mx)
+        for a, b in XT_PARTS if tab == "XF" else ((0, 256),):
+            cp(X(B("XT", 0, D + V), B("obu", a // 16, b // 16)), B("m14", a, b))
+        refresh(range(s - 1, -1, -1), tab)
         snd, Ln = B("snd", 224 * s, 224 * s + 224), B("land", 224 * s, 224 * s + 224)
         if SND_ACT:
-            act(snd, X(win, B("exu", 0, 14)), AF.Copy)
+            act(snd, X(B(tab, D, XW), B("exu", 0, 14)), AF.Copy)
         else:
-            cp(snd, X(win, B("exu", 0, 14)))
+            cp(snd, X(B(tab, D, XW), B("exu", 0, 14)))
+        if tab == "XT":
+            for k in range(s):
+                cp(X(B("XT"), B("LT", 8 * k, 8 * k + 3)), B("neg1", 0, 48))
         trs = []
         for d in range(1, 8):
             peer = T.cores[rank ^ d]
@@ -575,19 +723,19 @@ def rank_program(g, core, T, topo):
                                          remote_sem=T.sem["arr%d" % s], src=T.snd[:, a:a + 32], dst=T.land[:, a:a + 32]))
             tops["snt"] = tops.get("snt", 0) + n
             tops["arr%d" % s] = tops.get("arr%d" % s, 0) + n
-        call("G", lambda trs=trs: g.remote_dma_fused(trs, local_sem=T.sem.snt), [snd], [Ln], 300, FLY, "arr%d" % s)
-        for a, b in XT_PARTS:
-            cp(X(B("XT", 0, D + V), B("obu", a // 16, b // 16)), four(a, b)[0])
-        mm(grp(B("pa", 0, 256), [(M(8), mx), (M(9), go)]))
-        act(B("ab"), B("pa", 0, 256), AF.Abs, scale=0.0625)
+        call("G", lambda trs=trs: g.remote_dma_fused(trs, local_sem=T.sem.snt), [snd], [Ln], lambda x: x[11],
+             lambda x: x[7] * (FIRST if first else 1), "arr%d" % s)
+        for a, b in TESTS:
+            mm(grp(B("pa", a, b), list(zip((M8, M9), two(a, b)))))
+            act(B("ab", a, b), B("pa", a, b), AF.Abs)
         o = B("ph", 0, 256)
-        mm([(o, M(1), mx, False, False)], "sum")
-        mm([(o, M(7), rm, False, False), (o, M(7), ro, False, False)], "sum")
+        fraction(o, 0, 256, (KBS, KS, [(KS, go)]), False)
         mm([(o, Ib, B("ab"), False, True)])
-        ts(B("want", 0, 256), o, K1 + 1.0 / 32, A.is_gt)
-        mm([(B("pd", 0, 256), M(8), go, True, False), (B("pd", 0, 256), M(3), B("ones", 0, 256), False, False)])
-        mm([(B("pd", 0, 256), IK, B("want", 0, 256), False, True)])
-        tt(B("SW", 0, 256), B("pd", 0, 256), B("ob"), A.max)
+        ts(B("want", 0, 256), o, 2 * K * C0 + 0.5, A.is_gt)
+        o = B("pd", 0, 256)
+        mm([(o, M8, go, True, False)])
+        mm([(o, IK, B("want", 0, 256), False, True)])
+        ts(B("SW", 0, 256), o, ZB - SH - K1, A.add, -2000.0, A.max)
         scan(B("rank"), B("ones"), B("want"), 0.0, A.mult, A.add)
         for t in range(3):
             act(B("EQ", 304 * t, 304 * t + 304), B("rank"), AF.Sign, bias=B("jh", t, t + 1), scale=-1.0,
@@ -597,26 +745,28 @@ def rank_program(g, core, T, topo):
         cp(B("cs"), X(B("S"), B("lz", 0, 7)))
         dec = [(sel("Zd", p), B("cs", p, 112, 16)) for p in range(16)]
         mm(grp(B("pe", 0, 7), dec))
-        mm([m for t in range(3) for m in grp(B("pa", 48 * t, 48 * t + 48),
-                                             [(M(8), B("cs", 64, 112)), (Ib, B("M192", 48 * t, 48 * t + 48))])])
-        mm([(B("pf", 0, 7), l, x, i == 0, False) for i, (l, x) in enumerate(dec)])
+        mm([m for j in range(5) for m in grp(B("pa", 16 * j, 16 * j + 16), [(M8, B("cs", 64 + 16 * (j // 2), 80 + 16 * (j // 2)))]
+                                             + [(Ib, B("M16"))] * (1 - j % 2))])
+        mm([(B("pf", 0, 3), B("If"), B("cz", 0, 3), True, False)])
         if SW_ACT:
-            lin(B("SW", 256, 400), B("pa", 0, 144), 1.0, ZB - SH)
+            lin(B("SW", 256, 336), B("pa", 0, 80), 1.0, ZB - SH)
         else:
-            ts(B("SW", 256, 400), B("pa", 0, 144), ZB - SH, A.add)
+            ts(B("SW", 256, 336), B("pa", 0, 80), ZB - SH, A.add)
         ts(B("LU", 0, 7), B("pe", 0, 7), ZB, A.add)
         cp(B("cc"), X(B("C"), B("LU", 0, 7)))
-        tt(B("mn"), B("cc", 0, 48), B("cc", 64, 112), A.min)
+        ts(B("xu"), X(B(tab), B("LU", 4, 7)), free, A.not_equal, col(17), A.mult)
+        tt(B("mn", 48, 96), B("cc", 0, 48), B("cc", 64, 112), A.min)
+        tt(B("mn", 0, 48), B("mn", 48, 96), B("xu"), A.add)
         tt(B("mxc"), B("cc", 0, 48), B("cc", 64, 112), A.max)
-        mm([(B("pf", a, a + 3), sel("Z8h", p), B("mn", p, 48, 16), False, False) for a in (0, 4) for p in range(16)])
-        ends = (0, 304, 656, 1056)
+        mm([(B("pf", 0, 3), sel("Z8h", p), B("mn", p, 48, 16), False, False) for p in range(16)])
+        ends = (0, 272, 576, 912)
         for t in range(3):
-            ts(B("E", ends[t], ends[t + 1]), B("SW", 0, 304 + 48 * t), SH - ZB, A.add, B("pe", 4 + t, 5 + t), A.is_equal)
+            ts(B("E", ends[t], ends[t + 1]), B("SW", 0, 272 + 32 * t), SH - ZB, A.add, B("pe", 4 + t, 5 + t), A.is_equal)
         scan(B("EO"), B("E"), B("E"), 0.0, A.add, A.max)
-        mm([(B("pf", a + t, a + t + 1), B("I8h", 128 * k, 128 * k + 128), B("EO", ends[t + 1 - k] - 1, ends[t + 1 - k]),
-             False, a + t + k == 7) for a in (0, 4) for t in range(3) for k in range(2) if t >= k])
+        mm([(B("pf", t, t + 1), B("I8h", 128 * k, 128 * k + 128), B("EO", ends[t + 1 - k] - 1, ends[t + 1 - k]),
+             False, t + k == 3) for t in range(3) for k in range(2) if t >= k])
         for t in range(3):
-            ts(B("LT", 8 * s + t, 8 * s + 8, 4), B("pf", t, 8, 4), B("dd", t, t + 1), A.max, ZB - K2, A.add)
+            ts(B("LT", 8 * s + t, 8 * s + 8, 4), B("pe", t, 8, 4), B("pf", t, t + 1), A.add, B("dd", t, t + 1), A.max)
         cp(X(B("C"), B("LT", 8 * s + 4, 8 * s + 7)), B("mxc"))
 
         def blk(n, d, k=0):
@@ -624,11 +774,11 @@ def rank_program(g, core, T, topo):
 
         lst = [(B("pg", 0, 224), Ib, B("neg1"), True, False)]
         if first:
-            lst.append((B("pg", 0, 224), Ib, B("k4"), False, False))
+            lst.append((B("pg", 0, 224), I4, B("ones", 0, 224), False, False))
         else:
             lst += [(blk("pg", d), PMm(2, d), blk("fn", d, s - 1), False, False) for d in range(1, 8)]
         mm(lst)
-        ts(B("fn", 224 * s, 224 * s + 224), Ln, 14.0625, A.is_equal, -4096.0, A.mult)
+        ts(B("fn", 224 * s, 224 * s + 224), Ln, free, A.is_equal, -4096.0, A.mult)
         mm([(blk("pg", d), PMm(1, d), blk("fn", d, s), False, d == 7) for d in range(1, 8)])
         if last:
             turn([lambda t: B("aws", t, 112, 7), lambda t: B("aws", t, 112, 7), lambda t: B("sg", t, 112, 7)], "pb")
@@ -636,23 +786,29 @@ def rank_program(g, core, T, topo):
         tt(B("Cm"), B("C", D + V, D + W), B("pg", 0, 224), A.min)
         shuffle("pb", 112, B("CCi"), "Cm", "ti")
         lists("pb", 7, "TI", 0, "wi")
-        if last:
-            dma("d_as", B("asn"), rows("AS2", slice(0, 128, 16), WK, WW), 1200)
-        else:
-            select(B("ASc"), B("AS2", WK, WW), [[0, G]], 0)
         for r in range(16):
+            if r == max(0, IMP_ACT[s] - AS_ONLY[s]) and last:
+                dma("d_as", B("asn"), rows("AS2", slice(0, 128, 16), WK, WW), 1600)
+            elif r == max(0, IMP_ACT[s] - AS_ONLY[s]):
+                hold[:] = [select(B("ASc", 0, G - DIRECT[1]), B("AS2", WK, WW - DIRECT[1]), [[0, G - DIRECT[1]]], 0)]
             e = "A" if r < IMP_ACT[s] else "V"
-            scatter(e, s, B("wi", 14 * r, 14 * r + 14), ("AS",) if e == "A" else ("AV", "AV2")[:1 + (r < 16 - AV_ONLY)])
-        parts = ((0, G - NARROW_G), (G - NARROW_G, G)) if NARROW_G else ((0, 896), (896, G))
+            both = r < (IMP_ACT[s] - AS_ONLY[s] if e == "A" else 16 - AV_ONLY)
+            scatter(e, s, B("wi", 14 * r, 14 * r + 14), (("AS", "AS2") if e == "A" else ("AV", "AV2"))[:1 + both])
+        cut = G - DIRECT[0]
+        parts = [x for x in ((0, cut - NARROW_G - NARROW_A), (cut - NARROW_G - NARROW_A, cut - NARROW_G), (cut - NARROW_G, cut))
+                 if x[0] < x[1]]
         for a, b in parts:
-            if a and NARROW_G:
-                select(B("ASb", a, b), B("AS", WK + a, WK + b), [[0, b - a]], 0)
+            if b == cut and NARROW_G:
+                hold[:] = [select(B("ASb", a, b), B("AS", WK + a, WK + b), [[0, b - a]], 0)][:1 - last]
             else:
                 act(B("ASb", a, b), B("AS", WK + a, WK + b), AF.Copy)
-        mm([m for d in range(1, 8) for m in grp(blk("pc", d), [(PMm(0, d), blk("land", d, s)), (PMm(1, d), blk("fn", d, s))])])
+        mm([m for d in range(1, 8) for m in grp(blk("pc", d), [(PMm(0, d), blk("land", d, s)), (PMm(1, d), blk("fn", d, s))][:1 + (tab == "XF")])])
+        if tab == "XT":
+            act(B("XT", D + V, D + W), B("pc", 0, 224), AF.Copy)
+        elif s == 2 - XT_LAST:
+            ts(B("XT", D + V, D + W), B("pc", 0, 224), 14.0, A.add, -1.0, A.max)
         if last:
-            ts(B("XT", D + V, D + W), B("pc", 0, 224), -1.0, A.max)
-            dma("d_y0", T.yx[:, 0:V], B("XT", D, D + V), 3000)
+            dma("d_y0", T.yx[:, 0:V], B("XT", D, D + V), 6000)
             dma("d_y1", T.yx[:, V:W], B("XT", D + V, D + W), 1200)
             refresh(range(2, -1, -1), "F", "c48")
             dma("d_yf", T.yf[:], rows("F", slice(0, 128, 16), D, D + W), 1300)
@@ -663,11 +819,12 @@ def rank_program(g, core, T, topo):
             act(B("yc_"), B("pe", 0, 160), AF.Copy)
             dma("d_yc", T.yc[:], B("yc_"), 1300)
         else:
-            mm([(B("pd", 0, 224), I32x, B("NC", 0, 224), True, False)]
-               + [(blk("pd", d), PMm(1, d), blk("fn", d, s), False, d == 7) for d in range(1, 8)])
-            lin(B("wS"), B("pd", 0, 224), -1.0, -4097.0)
+            mm([(B("pd", 0, 224), I4, B("neg1"), True, False)]
+               + [(blk("pd", d), PMm(2, d), blk("fn", d, s), False, False) for d in range(1, 8)]
+               + [(B("pd", 0, 224), Ib, B("NC", 0, 224), False, True)])
+            act(B("wS"), B("pd", 0, 224), AF.Copy)
             tt(B("XF", D + V, D + W), B("pc", 0, 224), B("wS"), A.max)
-            refresh(range(s, -1, -1))
+            refresh(range(s, -1, -1), e="VA"[REF_ACT])
 
         def piece(n, p, a=WK):
             return B(n, a + 112 * p, a + 112 * p + 112) if last else B(n, a + p, a + G, 16)
@@ -681,15 +838,20 @@ def rank_program(g, core, T, topo):
             il = B("IL", 128 * s, 128 * s + 128)
             mm([(o, il, B("aws", 0, 112), True, False), (o, il, B("aws", 0, 112), False, False),
                 (o, il, B("sg"), False, False)])
-            mm([(o, sel("Z0", p), piece("ASc", p, 0), False, False) for p in range(16)], "sum")
-        for n in ("AV2", "AV"):
-            mm([(o, sel("Z0", p), piece(n, p), False, False) for p in range(16)], "sum")
-        for a, b in parts:
+        reads = [("Z0", n, WK, 0, G) for n in ("AV2", "AV")] + [("Z0", "ASb", 0, a, b) for a, b in parts]
+        reads += [("Z0f", "AS", WK, cut, G)]
+        if not last:
+            reads += [("Z0", "ASc", 0, 0, G - DIRECT[1]), ("Z0f", "AS2", WK, G - DIRECT[1], G)]
+        for z, n, at0, a, b in sorted([x for x in reads if x[3] < x[4]], key=lambda x: x[1] == LAST_READ):
+            end = n == LAST_READ
             if last:
-                mm([(o, sel("Z0", p), piece("ASb", p, 0), False, False) for p in range(a // 112, b // 112)], "sum")
+                mm([(o, sel(z, p), piece(n, p, at0), False, end and p == b // 112 - 1) for p in range(a // 112, b // 112)],
+                   not end and "sum")
             else:
-                mm([(B("ph", a // 16, b // 16), sel("Z0", p), B("ASb", a + p, b, 16), False, False) for p in range(16)], "sum")
-        mm([(o, BO, B("zr", 0, 112), False, True)])
+                mm([(B("ph", a // 16, b // 16), sel(z, p), B(n, at0 + a + p, at0 + b, 16), False, end and p == 15)
+                    for p in range(16)], not end and "sum")
+        if not LAST_READ:
+            mm([(o, BO, B("zr", 0, 112), False, True)])
         if last:
             ts(B("yw_"), o, 0.5 * LEV[s], A.is_gt)
             dma("d_yw", T.yw[:], B("yw_"), 1200)
@@ -698,12 +860,18 @@ def rank_program(g, core, T, topo):
 
     cnt, seen, uses = {e: 0 for e in eng}, {e: {} for e in eng}, {}
 
+    known = {}
+
     def need(e, sem, n):
         if seen[e].get(sem, 0) < n:
             eng[e].wait_ge(T.sem[sem], n)
             seen[e][sem] = n
+            for k, m in known.get((sem, n), (0, {}))[1].items():
+                seen[e][k] = max(seen[e].get(k, 0), m)
 
-    for c in [calls[i] for i in plan(calls)]:
+    if not PLANS:
+        PLANS.append(plan(calls))
+    for c in [calls[i] for i in PLANS[0]]:
         e, w, want = c["e"], c["w"], {}
         if c["mark"] is True:
             w = [w[-1] if lastw[e] == w[0][1] else w[0]]
@@ -713,7 +881,7 @@ def rank_program(g, core, T, topo):
                     if not (sem == "sP" and e == "P"):
                         if (x[1] in PSUMS and sem != "s" + e) or ((wr or w2) and meet(sp, x[2:5])):
                             want[sem] = max(want.get(sem, 0), n)
-        for sem in want:
+        for sem in sorted(want, key=lambda k: -known.get((k, want[k]), (0,))[0]):
             need(e, sem, want[sem])
         ins = c["fn"]()
         if c["sem"] in tops:
@@ -729,6 +897,7 @@ def rank_program(g, core, T, topo):
             cnt[e] += 1
             tok = ("s" + e, cnt[e])
             ins.then_inc(T.sem[tok[0]], 1)
+        known[tok] = (len(known), dict(seen[e]))
         seen.setdefault("end", {})[tok[0]] = tok[1]
         for vs, wr in ((c["r"], False), (w, True)):
             for x in vs:

@@ -10,20 +10,36 @@ MAGIC = 12582912.0
 K, K1, K2 = 2.0 ** 24, 2.0 ** 21, 131072.0
 C0 = 15.0 / 128
 ZB = float(D + 2805)
-K_ACT = ()
-CHUNKS = ((V, 2624), (0, 480), (480, 960), (960, 1440), (1440, 1920), (1920, V))
-DIRECT = (0, 0)
+K_ACT = (6, 7, 8, 9, 10)
+CHUNKS = ((0, 480), (480, 960), (960, 1440), (1440, 1920), (1920, V), (V, W))
+SO = 4112
+IDLE = 22.0 / 8192
+EQ_A = ((1, 1), (1, 1), (1, 1))
+READS = 4
+XI_ACT = (True, True, True)
+NARROW = (8, 8, 8)
+COUNT_ACT = False
+SUMS, TERMS = ((0, 128), (128, 192), (192, 256)), 4
+PAIRS = 3
+F_ACT = True
+PAIR_H = 1
+TURN_LAST = ("AV2",)
+HALVED = ((0, 0), (0, 0), (0, 0))
+EARLY = ("pi", "xb", "J", "mg", "RS", "TRI", "jp", "XT", "gvi", "XF", "AS", "SM", "I4")
+KS_ACT, D_ACT = True, False
+WANT = "ph"
+AW_F32 = False
 SH = 1024.0
 LEV = (256, 8192, 262144)
 HALVES = ((0, 128), (128, 256))
-BIND_VEC = ((2, 6), (2, 6), (2, 6))
-SW_ACT = True
-XT_PARTS = ((0, 128), (128, 256))
+BIND_VEC = ((1, 5), (1, 5), (1, 5))
+SW_ACT = False
+XT_PARTS = ((0, 256),)
+XF_PARTS = ((0, 128), (128, 256))
 ROUNDS = 3
 SND_ACT = False
-NARROW_G = 560
-IMP_ACT = (5, 5, 6)
-AV_ONLY = 3
+IMP_ACT = (5, 5, 5)
+AV_ONLY = 1
 GATHER = ((0, 64, "A"), (64, 128, "V"), (128, 192, "A"), (192, 256, "A"))
 GATHER0 = ((0, 64, "A"), (64, 128, "V"), (128, 192, "A"), (192, 256, "A"))
 SCANS = ((0, 64), (64, 128), (128, 192), (192, 256))
@@ -33,29 +49,21 @@ STARTS = 8
 CUT = 40
 WORLDS = ((1.1, 1.4, 2.5, 15, 60, 120, 0.36, 2500, 0.6, 160, 1.0, 600, 45, 35),
           (1.35, 1.3, 1.5, 25, 50, 70, 0.42, 3500, 0.5, 180, 1.2, 1000, 50, 40),
-          (1.15, 1.3, 5.0, 25, 85, 200, 0.36, 3000, 0.8, 100, 1.0, 400, 40, 20))
-POLISH = 14000
+          (1.15, 1.3, 5.0, 25, 85, 200, 0.36, 3000, 0.8, 100, 1.0, 400, 40, 20),
+          (1.4, 1.9, 5.6, 20, 60, 120, 0.4, 3000, 0.7, 140, 1.1, 700, 45, 30))
+POLISH = 12000
+PASSES, STRETCH, BEYOND = 1, 400, 30
 SLACK = 0.0004
 SEED = 1
 LEAN = 0.3
 FILL = 1
 NOTE = []
 Z_G = 448
-NC_G = True
-AS_ONLY = (9, 9, 9)
-NARROW_A = 560
-M14 = ((0, 128, "A"), (128, 256, "A"))
-TESTS = HALVES
+AS_ONLY = (2, 2, 2)
 CC_ACT = False
 HB_ACT = True
-BWB = True
 FIRST = 1.5
-LAST_READ = "AV"
-XT_LAST = True
 AW_G = False
-SM_G = True
-AW_OFF = False
-EQ_ACT = 2
 REF_ACT = True
 XF_VEC = ()
 PLANS = []
@@ -67,33 +75,33 @@ def sb(n, dt):
 
 F32, BF, F16, I32, U16 = "float32", "bfloat16", "float16", "int32", "uint16"
 SCRATCH = {
-    "awi": sb(112, I32), "awb": sb(112, BF), "aws": sb(128, BF), "sc1": sb(136, BF),
-    "gvi": sb(2048, I32), "exi": sb(16, I32), "exu": sb(16, U16),
+    "awi": sb(112, I32), "awb": sb(112, BF), "aws": sb(112, BF), "awT": sb(128, BF), "wT": sb(128, BF),
+    "RS": sb(128, BF), "nB": sb(8, BF), "jp": sb(256, BF), "jn": sb(256, F16), "Yb": sb(112, BF), "At": sb(128, BF), "ASb": sb(896, BF),
+    "gvi": sb(G + 16, I32), "exi": sb(16, I32), "exu": sb(16, U16),
     "XF": sb(XW, BF), "XT": sb(XW, BF), "C": sb(XW, I32), "F": sb(XW, F32),
-    "AV": sb(2640, BF), "AV2": sb(2624, BF), "AS": sb(WW, F32), "AS2": sb(WW, F32), "ASb": sb(G, BF),
-    "ASc": sb(G, BF), "C16": sb(W, F16), "asn": sb(112, F32),
-    "lv": sb(672, BF), "ls": sb(672, F32),
-    "GG": sb(4096, BF), "S": sb(4864, BF), "SM": sb(16 + 16 * max(b - a for a, b in SCANS), BF),
-    "pi": sb(8, I32), "co_": sb(48, F32), "xb": sb(256, BF), "mg": sb(128, BF), "JR": sb(512, BF),
-    "oh": sb(16, F32), "sK": sb(16, F32), "aK": sb(16, F32), "NC": sb(288, BF),
+    "AV": sb(2640, BF), "AV2": sb(W, BF), "AS": sb(2 * WW, F32), "AS2": sb(2 * WW, F32), "C16": sb(W, F16),
+    "lv": sb(768, BF), "ls": sb(768, F32), "RO": sb(640, BF),
+    "GS": sb(2 * SO, BF), "SM": sb(16 * max(b - a for a, b in SCANS), BF),
+    "pi": sb(8, I32), "co_": sb(48, F32), "xb": sb(256, BF), "mg": sb(128, BF),
+    "oh": sb(16, F32), "sK": sb(16, F32), "aK": sb(16, F32),
     "J": sb(144, BF), "BO": sb(128, BF), "TRI": sb(128, BF), "ZS": sb(144, BF), "Zd": sb(144, BF),
-    "ZSh": sb(144, F16), "Z8h": sb(144, F16), "Z0": sb(144, BF), "Z0f": sb(144, F32),
+    "ZSh": sb(144, F16), "Z8h": sb(144, F16), "Z0": sb(144, BF),
     "If": sb(128, F32), "IL": sb(384, BF), "ILf": sb(128, F32), "I8h": sb(256, F16),
-    "MM": sb(2048, BF), "PM": sb(1024, BF), "OH": sb(128, BF),
+    "MM": sb(2176, BF), "PM": sb(512, BF), "OH": sb(128, BF),
     "H0h": sb(144, F16), "H1h": sb(144, F16), "H0b": sb(144, BF), "H1b": sb(144, BF),
-    "ones": sb(304, BF), "zr": sb(128, BF), "neg1": sb(224, BF),
-    "MAG": sb(256, BF), "t196": sb(256, BF), "cz": sb(4, F32), "bwb": sb(16, BF), "m14": sb(256, BF),
+    "ones": sb(256, BF), "zr": sb(256, BF), "PL": sb(768, BF), "neg1": sb(224, BF),
+    "MAG": sb(256, BF), "t196": sb(256, BF), "cz": sb(4, F32), "c14": sb(256, BF),
     "jh": sb(4, F32), "dd": sb(8, F32),
     "KJ": sb(224, BF), "CCb": sb(256, BF), "LD": sb(256, F32), "lat": sb(256, F32), "CCi": sb(224, BF), "M16": sb(16, BF),
     "EQ": sb(2048, BF), "pre": sb(128, F32), "sg": sb(112, BF), "remT": sb(224, F32),
     "bw": sb(16, U16), "cmp": sb(256, BF), "eu": sb(16, U16), "gve": sb(256, U16),
-    "xu": sb(48, F16), "obu": sb(16, U16), "cg": sb(256, F16), "tm": sb(256, BF),
+    "obu": sb(16, U16), "cg": sb(256, F16), "tm": sb(256, BF),
     "TT": sb(256, F32), "TI": sb(224, F32), "wl": sb(256, U16), "wi": sb(224, U16),
-    "ab": sb(256, BF), "want": sb(304, BF), "rank": sb(304, BF), "ca": sb(4, F32),
+    "want": sb(256, BF), "rank": sb(256, BF), "ca": sb(4, F32),
     "SW": sb(336, F16), "lz": sb(8, U16), "cs": sb(112, BF), "LU": sb(8, U16),
     "cc": sb(112, F32), "mn": sb(96, F16), "mxc": sb(48, F32), "E": sb(912, BF), "EO": sb(912, F16),
     "LT": sb(24, U16), "x48": sb(48, BF), "c48": sb(48, F32),
-    "snd": sb(672, BF), "land": sb(672, BF), "fn": sb(672, BF), "Cm": sb(224, F16), "ti": sb(224, BF), "wS": sb(224, BF),
+    "snd": sb(672, BF), "land": sb(672, BF), "Cm": sb(224, F16), "ti": sb(224, BF),
     "yw_": sb(112, F32), "yc_": sb(160, F32),
 }
 PART = {}
@@ -103,7 +111,7 @@ SCRATCH["fs"] = sb(sum(x[1] for x in PART.values()), F32)
 PSUMS = ("pa", "pb", "pc", "pd", "pe", "pf", "pg", "ph")
 for _b in PSUMS:
     SCRATCH[_b] = ("psum", [128, 512], F32)
-DMAS = ["d_aw", "d_x0", "d_gv", "d_ex", "d_co", "d_y0", "d_y1", "d_yf", "d_yw", "d_yc", "d_as", "d_ci"]
+DMAS = ["d_aw", "d_x0", "d_gv", "d_ex", "d_co", "d_y0", "d_y1", "d_yf", "d_yw", "d_yc", "d_ci"]
 DMAS += ["d_z%d" % j for j in range(2 * G // Z_G - 1)]
 SEMAPHORES = ["sV", "sA", "sP", "sG", "snt", "arr0", "arr1", "arr2"] + DMAS
 
@@ -194,10 +202,14 @@ def plan(calls):
 
     tails = [i for i in range(n) if not post[0][i]]
 
-    def run(order, k, a=0, old=None):
+    def run(order, k, a=0, old=None, goal=None, z=n):
         end, by = (old[3][:], old[2][:]) if old else ([0] * n, [None] * n)
-        last, way, took = {queue[i]: i for i in order[:a]}, ways[k], ns[k]
-        for i in order[a:]:
+        last, way, took = {}, ways[k], ns[k]
+        for i in range(a - 1, -1, -1):
+            last.setdefault(queue[order[i]], order[i])
+            if len(last) == 5:
+                break
+        for i in order[a:z]:
             j0 = last.get(queue[i])
             t = 0 if j0 is None else end[j0]
             for j, d in way[i]:
@@ -205,8 +217,8 @@ def plan(calls):
                     t, j0 = end[j] + d, j
             end[i], by[i] = t + took[i], j0
             last[queue[i]] = i
-        top = max(tails, key=lambda i: end[i] + late[k][i])
-        return end[top] + late[k][top] + LEAN * sum(end) / n, top, by, end
+        top = goal or max(tails, key=lambda i: end[i] + late[k][i])
+        return end[top] + late[k][top] + LEAN * sum(end) / (n if goal is None else STRETCH), top, by, end
 
     seed = [SEED]
 
@@ -217,14 +229,14 @@ def plan(calls):
     def worth(runs):
         return sum(r[0] / x for r, x in zip(runs, unit))
 
-    def polish(order, steps):
-        runs = [run(order, k) for k in worlds]
+    def polish(order, steps, goal=None, since=None):
+        runs = [run(order, k, goal=goal) for k in worlds]
         score = low = worth(runs)
-        keep = order
+        keep, z = order, order.index(goal) + BEYOND if goal else n
         for step in range(steps):
-            _, i, by, _ = runs[draw(len(WORLDS))]
+            _, i, by, end = runs[draw(len(WORLDS))]
             pairs, waits = [], []
-            while by[i] is not None:
+            while by[i] is not None and (since is None or end[i] > end[since]):
                 if queue[by[i]] == queue[i] and not above[i] >> by[i] & 1:
                     pairs.append((by[i], i))
                 elif queue[i] in "VA":
@@ -233,12 +245,14 @@ def plan(calls):
             if waits and draw(4) < FILL:
                 u = waits[draw(len(waits))]
                 a = order.index(u)
-                free = [i for i in order[a + 1:a + 80] if queue[i] == queue[u] and not above[i] >> u & 1]
+                free = [i for i in order[a + 1:min(z, a + 80)] if queue[i] == queue[u] and not above[i] >> u & 1]
                 if not free:
                     continue
                 w = free[draw(len(free))]
-            else:
+            elif pairs:
                 u, w = pairs[draw(len(pairs))]
+            else:
+                continue
             a, b = order.index(u), order.index(w)
             for _ in range(draw(3)):
                 k = a - 1
@@ -254,14 +268,20 @@ def plan(calls):
                 move = [i for i in part if i == u or above[i] >> u & 1]
                 part = [i for i in part if i not in move] + move
             new = order[:a] + part + order[b + 1:]
-            trial = [run(new, k, a, runs[k]) for k in worlds]
+            trial = [run(new, k, a, runs[k], goal, z) for k in worlds]
             value = worth(trial)
             if value <= score + SLACK * draw(1000) / 1000 * (1 - step / steps):
-                ends, at = trial[0][3], {i: k for k, i in enumerate(new)}
-                order, runs, score = sorted(new, key=lambda i: (ends[i] - ns[0][i], at[i])), trial, value
+                ends = trial[0][3]
+                order, runs, score = new[:a] + sorted(new[a:z], key=lambda i: ends[i] - ns[0][i]) + new[z:], trial, value
                 if value < low:
                     low, keep = value, order
         return low, keep
+
+    def stretches(order, steps):
+        marks = sorted([i for i in range(n) if calls[i]["goal"]], key=order.index) + [None]
+        for since, goal in zip([None] + marks, marks):
+            order = polish(order, steps, goal, since)[1]
+        return worth([run(order, k) for k in worlds]), order
 
     found = [x for k in worlds for over in OVER for x in first(k, over)]
     unit = [run(found[0], k)[0] for k in worlds]
@@ -276,6 +296,8 @@ def plan(calls):
                 value = worth([run(new, k) for k in worlds])
                 if value < low:
                     low, keep = value, new
+    for _ in range(PASSES):
+        low, keep = min((low, keep), stretches(keep, POLISH), key=lambda x: x[0])
     keep = polish(keep, POLISH)[1]
     NOTE.append([round(run(keep, k)[0]) for k in worlds])
     return keep
@@ -298,6 +320,9 @@ def rank_program(g, core, T, topo):
     def rows(n, part, a, b):
         return (T[n][part, a:b], n, a, b, 1, None)
 
+    def R(n, a, b, st=1):
+        return (T[n][0:112, a:b:st] if st > 1 else T[n][0:112, a:b], n, a, b, st, None)
+
     def X(win, off):
         return (win[0].indirect(off[0]),) + win[1:5] + (off,)
 
@@ -307,13 +332,13 @@ def rank_program(g, core, T, topo):
     def call(e, fn, r, w, cost, late=lambda x: 0, sem=None, mark=False, after=()):
         r = [x for x in r if isinstance(x, tuple)]
         calls.append({"e": e, "fn": fn, "r": r + [x[5] for x in r + w if x[5]], "w": w, "ns": [cost(x) for x in WORLDS],
-                      "late": [late(x) for x in WORLDS], "sem": sem, "mark": mark, "after": list(after)})
+                      "late": [late(x) for x in WORLDS], "sem": sem, "mark": mark, "after": list(after), "goal": False})
         return len(calls) - 1
 
     def op(e, fn, r, w, cycles=None, more=0):
         o, k = w[0], 4 if e == "A" else 3
         if o[5] or (r and r[0][5]):
-            return call(e, fn, r, w, lambda x: INDIRECT[e] + CY * x[0] * size(o) * x[2 if o[5] else 1] * (1.5 if cycles else 1))
+            return call(e, fn, r, w, lambda x: INDIRECT[e] + CY * x[0] * size(o) * x[2 if o[5] else 1] * (1.3 if cycles and not o[5] else 1))
         narrow = all(SCRATCH[x[1]][2] in (BF, F16, U16) for x in [o] + r if isinstance(x, tuple) and size(x) > 1)
         n = size(o) * (cycles or (0.5 if narrow and e == "V" else 1))
         psum = any(x[1] in PSUMS for x in [o] + r if isinstance(x, tuple))
@@ -328,8 +353,12 @@ def rank_program(g, core, T, topo):
             for o, l, x, s0, s1 in lst:
                 ins = g.tensor.matmul(o[0], l[0], x[0], s0, s1)
             return ins
-        n = sum(max(64, size(m[2])) * (4 if SCRATCH[m[2][1]][2] == F32 else 1) for m in lst)
-        call("P", f, [x for m in lst for x in m[1:3]], [m[0] for m in lst], lambda x: n * x[0] * x[6], lambda x: 60, mark=mark)
+        n = sum(max(min(64, size(m[1])), size(m[2])) * (4 if SCRATCH[m[2][1]][2] == F32 else 1) for m in lst)
+        after = []
+        if mark and mark[0] == "then":
+            after = [i for i in range(len(calls) - 16, len(calls)) if calls[i]["mark"] == ("sum",) + mark[1:]]
+        call("P", f, [x for m in lst for x in m[1:3]], [m[0] for m in lst], lambda x: n * x[0] * x[6], lambda x: 60,
+             mark=mark, after=after)
 
     def grp(o, terms):
         return [(o, l, x, i == 0, i == len(terms) - 1) for i, (l, x) in enumerate(terms)]
@@ -356,7 +385,7 @@ def rank_program(g, core, T, topo):
         op("V", lambda: v.memset(o[0], c), [], [o])
 
     def scan(o, a, b, init, o0, o1):
-        op("V", lambda: v.tensor_tensor_scan(o[0], a[0], b[0], init, o0, o1), [a, b], [o])
+        op("V", lambda: v.tensor_tensor_scan(o[0], a[0], b[0], ap(init), o0, o1), [a, b, init], [o])
 
     def vtr(o, i):
         op("V", lambda: v.transpose(o[0], i[0]), [i], [o])
@@ -377,18 +406,18 @@ def rank_program(g, core, T, topo):
 
     def iota(o, pat, base, cm=0):
         kw = {} if SCRATCH[o[1]][2] == I32 else {"allow_small_or_imprecise_dtypes": True}
-        call("G", lambda: g.iota(o[0], pat, base, cm, **kw), [], [o], lambda x: (130 + 2 * CY * size(o)) * x[10],
-             after=hold)
+        return call("G", lambda: g.iota(o[0], pat, base, cm, **kw), [], [o], lambda x: (130 + 2 * CY * size(o)) * x[10],
+                    after=hold)
 
     def fill(o, c):
-        iota(o, [[0, size(o)]], c)
+        return iota(o, [[0, size(o)]], c)
 
-    def select(o, i, pat, cm, test=A.is_ge, other=0.0):
-        return call("G", lambda: g.affine_select(o[0], i[0], pat, test, other, 0, cm), [i], [o],
+    def select(o, i, pat, cm, test=A.is_ge, other=0.0, base=0):
+        return call("G", lambda: g.affine_select(o[0], i[0], pat, test, other, base, cm), [i], [o],
                     lambda x: (170 + 2 * CY * size(o)) * x[10], after=hold)
 
     def ident(o, c):
-        select(o, B("zr"), [[1, 128]], -1, A.not_equal, c)
+        return select(o, B("zr", 0, 128), [[1, 128]], -1, A.not_equal, c)
 
     def col(i):
         return B("co_", i, i + 1)
@@ -401,16 +430,21 @@ def rank_program(g, core, T, topo):
 
     Ib, BO, xb = B("J", 0, 128), B("BO", 0, 128), B("xb", 0, 128)
     x144 = B("xb", 0, 144)
-    nKB, KB, I4, KBS, KS, nKS, GM, LM, M8, M9, I20, D2, D1, W2, W1, I16 = [M(i) for i in range(16)]
+    nKB, KB, I4, KBS, KS, nKS, GM, LM, M8, M9, I20, D2, D1, W2, W1, nI4, S15 = [M(i) for i in range(17)]
     IK = B("IL", 256, 384)
-    EB = ("pa", "pc", "pd", "pe")
 
     def PMm(kind, d):
         k = d % 3
-        if (kind, k) == (0, 0):
-            return Ib
-        a = 128 * (3 * kind + k - 1)
+        if k == 0:
+            return (Ib, I4)[kind]
+        a = 128 * (2 * kind + k - 1)
         return B("PM", a, a + 128)
+
+    def GG(a, b, st=1):
+        return B("GS", a, b, st)
+
+    def S(a, b, st=1):
+        return B("GS", SO + a, SO + b, st)
 
     k = []
     for sem, o, i, late in (("d_aw", B("awi"), T.aw[:], 1100), ("d_x0", B("XT", D, D + V), T.x0[:], 3100),
@@ -418,11 +452,29 @@ def rank_program(g, core, T, topo):
                             ("d_co", B("C", D, D + V), T.co[:, 0:V], 10250), ("d_ci", B("C", D + V, D + W), T.co[:, V:W], 10650)):
         k = [dma(sem, o, i, late, k)]
 
-    iota(B("pi", 0, 1), [[0, 1]], 0, 1)
-    iota(B("xb"), [[1, 256]], 0)
-    iota(B("mg"), [[16, 8], [0, 16]], 0)
     ms(B("ones"), 1.0)
-    iota(rows("JR", slice(0, 1), 0, 512), [[-16, 4], [0, 8], [-1, 16]], 0)
+    ms(B("zr"), 0.0)
+    early = {
+        "pi": lambda: iota(B("pi", 0, 1), [[0, 1]], 0, 1),
+        "xb": lambda: iota(B("xb"), [[1, 256]], 0),
+        "J": lambda: select(B("J"), B("ones", 0, 144), [[1, 144]], -1, A.is_equal),
+        "mg": lambda: iota(B("mg"), [[16, 8], [0, 16]], 0),
+        "RS": lambda: iota(B("RS"), [[0, 8], [16, 16]], 0),
+        "TRI": lambda: select(B("TRI"), B("ones", 0, 128), [[1, 128]], -1, A.is_gt),
+        "jp": lambda: iota(B("jp"), [[128, 2], [1, 16], [16, 8]], 0),
+        "If": lambda: ident(B("If"), 1.0),
+        "I4": lambda: ident(I4, 4096.0),
+        "XT": lambda: fill(B("XT", D + V, D + W), -1),
+        "gvi": lambda: fill(B("gvi", G, G + 16), W),
+        "XF": lambda: fill(B("XF", D + W, XW), -14),
+        "AS": lambda: fill(B("AS", WK, WK + Z_G), 0),
+        "SM": lambda: iota(B("SM"), [[0, size(B("SM")) // 16], [20, 16]], -14),
+    }
+    for n in EARLY:
+        hold[:] = [early.pop(n)()]
+    for n in early:
+        early[n]()
+    ts(B("jn"), B("jp"), -2.0, A.mult, -1.0, A.add)
     for j, m in enumerate((15, 16, 1, 96)):
         ts(B("pi", j + 1, j + 2), B("pi", 0, 1), m, A.bitwise_and)
     cp(B("co_", 0, 5), B("pi", 0, 5))
@@ -432,9 +484,8 @@ def rank_program(g, core, T, topo):
     ts(col(16), col(15), 15.0, A.add)
     ts(col(17), col(1), 15.0, A.is_equal)
     ts(B("oh"), B("xb", 0, 16), col(1), A.is_equal)
-    act(B("ls", 0, 224), B("ones", 0, 224), AF.Silu, 1300, scale=float(LEV[0]))
-    for a in range(WK, WK + Z_G, 448):
-        fill(B("AS", a, a + 448), 0)
+    act(B("ls", 0, 256), B("ones", 0, 256), AF.Silu, 1300, scale=float(LEV[0]))
+    warm = len(calls) - 1
     spots = [("AS", a) for a in range(WK + Z_G, WW, Z_G)] + [("AS2", a) for a in range(WK, WW, Z_G)]
     for j, (n, a) in enumerate(spots):
         dma("d_z%d" % j, B(n, a, a + Z_G), B("AS", WK, WK + Z_G), (10650 if Z_G < G else 900) + Z_G * 1.8 * (j + 1), k)
@@ -450,20 +501,26 @@ def rank_program(g, core, T, topo):
             lin(o, B("xb", 0, 240), s1, s2)
         else:
             ts(o, B("xb", 0, 240), s1, A.mult, s2, A.add)
-    fill(B("XT", D + V, XW), -1)
-    fill(B("S", 4096, 4864), 0)
-    select(B("J"), B("ones", 0, 144), [[1, 144]], -1, A.is_equal)
+    fill(B("XT", D + W, XW), 0)
+    for o in (GG(4096, SO), S(4096, SO)):
+        select(o, B("ones", 0, 16), [[0, 16]], 0, A.is_gt, IDLE)
     ts(BO, B("mg"), col(15), A.is_equal)
-    select(B("TRI"), BO, [[1, 128]], -1)
+    ts(S15, BO, col(17), A.mult, 16.0, A.mult)
+    lift = {0: (0.0, 0.0), 8: (56.0, 896.0)}
+    for j, n in enumerate(sorted(set(sum(EQ_A, ())) - {0, 8})):
+        lift[n] = (col(30 + 2 * j), col(31 + 2 * j))
+        ts(lift[n][0], col(0), 127.5 - 16 * n, A.is_gt, 56.0, A.mult)
+        ts(lift[n][1], col(0), 127.5 - 16 * n, A.is_gt, 896.0, A.mult)
+    ms(B("pre", 112, 128), 4096.0)
     ts(B("ZS"), x144, col(16), A.is_equal)
-    ts(KS, BO, col(17), A.mult, K, A.mult)
-    ts(nKS, BO, col(17), A.mult, -K, A.mult)
-    lin(I20, Ib, 16.0 / K)
+    (lin if KS_ACT else vlin)(KS, S15, K / 16)
+    (lin if KS_ACT else vlin)(nKS, S15, -K / 16)
     ts(col(9), col(17), 0.125 - 1.0 / 32, A.mult, 1.0 / 32, A.add)
     ts(col(10), col(17), 1.0 / 32 - 0.125, A.mult, 1.0 - 1.0 / 32, A.add)
-    lin(D2, Ib, col(9))
-    lin(D1, Ib, col(10))
-    mm(grp(B("pg", 0, 128), [(I20, KS), (D2, Ib)]) + grp(B("pg", 128, 256), [(I20, nKS), (D1, Ib)]))
+    ts(I20, BO, col(17), A.mult, -16.0, A.mult)
+    (lin if D_ACT else vlin)(D2, Ib, col(9))
+    (lin if D_ACT else vlin)(D1, Ib, col(10))
+    mm(grp(B("pg", 0, 128), [(Ib, S15), (D2, Ib)]) + grp(B("pg", 128, 256), [(Ib, I20), (D1, Ib)]))
     act(B("MM", 128 * 13, 128 * 15), B("pg", 0, 256), AF.Copy)
     ts(col(11), col(17), K, A.mult, col(19), A.add)
     ts(nKB, BO, -K, A.mult)
@@ -473,18 +530,14 @@ def rank_program(g, core, T, topo):
     iota(B("OH"), [[0, 8], [1, 16]], 0)
     ts(B("OH"), B("OH"), col(1), A.is_equal)
     (lin if HB_ACT else vlin)(M8, BO, col(19))
-    (lin if HB_ACT else vlin)(M9, M8, -1.0)
-    ms(B("zr"), 0.0)
-    lin(B("Z0"), B("ZS"), B("oh", 0, 1))
-    if any(DIRECT):
-        lin(B("Z0f"), B("Z0"), 1.0)
+    (lin if HB_ACT else vlin)(M9, M8, -2.0)
     lin(B("Zd"), B("ZS"), col(19))
     lin(B("Z8h"), B("ZS"), -8192.0)
     lin(B("ZSh"), B("ZS"), 1.0)
     ts(col(12), col(17), -K, A.mult, K, A.add)
     (lin if HB_ACT else vlin)(KBS, BO, col(12))
-    for o, c in ((I16, 16.0), (IK, K1), (B("If"), 1.0), (I4, 4096.0), (B("I8h", 0, 128), -8192.0), (B("I8h", 128, 256), 8192.0),
-                 (B("IL", 0, 128), LEV[0] / 4)):
+    for o, c in ((nI4, -4096.0), (IK, -K1), (B("I8h", 0, 128), -8192.0),
+                 (B("I8h", 128, 256), 8192.0), (B("IL", 0, 128), LEV[0] / 2)):
         ident(o, c)
     ts(col(23), col(1), 2.0, A.mult, 1.0, A.add)
     ts(col(24), col(23), col(4), A.add)
@@ -497,9 +550,7 @@ def rank_program(g, core, T, topo):
     ts(col(29), col(44), col(15), A.subtract)
     ts(PMm(0, 1), xb, col(28), A.is_equal)
     ts(PMm(0, 2), xb, col(1), A.subtract, col(29), A.is_equal)
-    for d, c in ((0, 15), (1, 27), (2, 29)):
-        ts(PMm(1, d), B("mg", 0, 128), col(c), A.is_equal, col(17), A.mult)
-        lin(PMm(2, d), PMm(1, d), -1.0)
+    (lin if HB_ACT else vlin)(B("PM", 256, 512), B("PM", 0, 256), 4096.0)
     (lin if CC_ACT else vlin)(B("KJ"), B("xb", 0, 224), 1.0 / 256, 1.0 / 256 - 1.0)
     at = {}
     for a, b in HALVES:
@@ -512,21 +563,14 @@ def rank_program(g, core, T, topo):
     fill(B("LD"), 0)
     ts(col(22), col(1), 240.0 - ZB, A.add)
     ts(B("LD", 0, 256, 16), B("xb", 0, 256, 16), -1.0, A.mult, col(22), A.add)
-    ts(B("jh", 0, 3), B("xb", 0, 48, 16), col(1), A.add, 0.5, A.add)
+    ts(B("jh", 0, 3), B("xb", 0, 48, 16), col(1), A.add, 1.0, A.add)
+    iota(B("PL"), [[0, 3], [1, 256]], 1)
     ts(B("dd", 0, 3), B("xb", 0, 48, 16), col(1), A.add, 256.0, A.add)
-    fill(B("cz"), int(ZB - K2))
-    fill(B("aws", 112, 128), 1)
-    fill(B("sc1", 0, 1), 0)
-    if SM_G:
-        iota(B("SM"), [[0, size(B("SM")) // 16], [20, 16]], -34)
-    else:
-        ms(B("SM"), 20.0)
-        ms(B("SM", 0, None, 16), -20.0)
-        ms(B("SM", 1, None, 16), -20.0)
+    fill(B("cz"), int(ZB - 2 * K2))
     ms(B("lz", 3, 4), 4110)
     ts(B("M16"), B("xb", 0, 16), col(1), A.is_ge, 8192.0, A.mult)
-    for o, c in ((B("gvi", G, 2048), W), (B("XF", D + W, XW), -14), (B("C", 0, D), -1), (B("C", D + W, XW), -1),
-                 (B("XF", 0, D), 0), (B("want", 256, 304), 1), (B("neg1"), -1),
+    for o, c in ((B("C", 0, D), -1), (B("C", D + W, XW), -1),
+                 (B("XF", 0, D), 0), (B("XT", 0, D), 0), (B("neg1"), -1), (B("c14"), 14),
                  (B("MAG"), int(MAGIC)), (B("t196"), 196)):
         fill(o, c)
     fill(B("lv", 0, 224), LEV[0])
@@ -545,29 +589,20 @@ def rank_program(g, core, T, topo):
     turn([lambda t: B("awb", 16 * t, 16 * t + 16)], "pf")
     for t in range(7):
         vtr(B("TT", t, t + 218, 7), B("pf", 32 * t, 32 * t + 32))
-    if AW_OFF:
-        act(B("aws", 0, 112), B("TT", 0, 112), AF.Copy)
+    if AW_F32:
+        mm(grp(R("ph", 0, 128), [(B("TT", 0, 112), B("If"))]))
     else:
-        cp(B("aws", 0, 112), B("TT", 0, 112))
+        cp(B("aws"), B("TT", 0, 112))
+        mm(grp(R("ph", 0, 128), [(B("aws"), Ib)]))
     cp(B("exu", 0, 14), B("exi", 0, 14))
 
-    def encode():
-        for k, (a, b) in enumerate(CHUNKS):
-            scan(B("AV2", a, b), B("AV", a, b), B("XT", D + a, D + b), 0.0, A.min, A.max)
-            bk = ("ph", "pb")[k % 2]
-            mm(grp(B(bk, 0, b - a), [(W1, B("XT", D + a, D + b)), (W2, B("AV2", a, b))]))
-            if a == V and NC_G:
-                lin(B("NC"), B(bk, 0, b - a), 1.0, -14.0)
-                select(B("XF", D + V, D + W), B("NC", 0, W - V), [[0, W - V]], 0)
-            elif k in XF_VEC:
-                ts(B("XF", D + a, D + min(b, W)), B(bk, 0, min(b, W) - a), -14.0, A.add)
-            else:
-                lin(B("XF", D + a, D + min(b, W)), B(bk, 0, min(b, W) - a), 1.0, -14.0)
-            if a == V:
-                if not NC_G:
-                    lin(B("NC"), B(bk, 0, b - a), 1.0, -14.0)
-                for i in (14, 15):
-                    lin(B("S", 4096 + i, 4864, 16), B("NC", 240, 288), 1.0)
+    def encode(a, b, bk, e="A"):
+        scan(B("AV2", a, b), B("AV", a, b), B("XT", D + a, D + b), 0.0, A.min, A.max)
+        mm(grp(B(bk, 0, b - a), [(W1, B("XT", D + a, D + b)), (W2, B("AV2", a, b))]))
+        if e == "V":
+            ts(B("XF", D + a, D + b), B(bk, 0, b - a), -14.0, A.add)
+        else:
+            lin(B("XF", D + a, D + b), B(bk, 0, b - a), 1.0, -14.0)
 
     def refresh(ks, tab="XF", tmp="x48", e="V"):
         for k in ks:
@@ -577,8 +612,9 @@ def rank_program(g, core, T, topo):
                 cp(B(tmp), X(B(tab), B("LT", 8 * k + 4, 8 * k + 7)))
             cp(X(B(tab), B("LT", 8 * k, 8 * k + 3)), B(tmp))
 
-    def shuffle(bank, n, cc, cg, tm, a=0):
-        mm([(B(bank, 0, 2 * n), Ib, cc, True, False)])
+    def shuffle(bank, n, cc, cg, tm, a=0, up=None):
+        mm([(B(bank, 0, 2 * n), Ib, cc, True, False)]
+           + ([(B(bank, 0, 2 * n), up, rows("ones", slice(0, 1), 0, 2 * n), False, False)] if up else []))
         for nm, src in (("h", cg), ("b", tm)):
             if nm == "b":
                 scan(B(tm, a, a + 2 * n), B("KJ", 0, 2 * n), B(cg, a, a + 2 * n), -1.0, A.max, A.min)
@@ -592,90 +628,102 @@ def rank_program(g, core, T, topo):
 
     lastw, lastc = {"V": None, "A": None}, {"V": [], "A": []}
 
-    def scatter(e, s, off, wins):
-        val = B("ls" if e == "A" else "lv", 224 * s, 224 * s + 16 * size(off))
+    def scatter(e, s, off, wins, wide=1):
+        val = B("ls" if e == "A" else "lv", 256 * s, 256 * s + 16 * size(off))
 
         def f():
             w = wins[-1] if lastw[e] == wins[0] else wins[0]
             lastw[e] = w
-            o = X(B(w, 0, WW), off)
+            o = X(B(w, 0, wide * WW), off)
             return (g.scalar.activation(o[0], val[0], AF.Silu) if e == "A" else v.tensor_copy(o[0], val[0])), o
-        lastc[e] = [call(e, f, [val, off], [B(w, 0, WW) for w in wins],
+        lastc[e] = [call(e, f, [val, off], [B(w, 0, wide * WW) for w in wins],
                          lambda x: INDIRECT[e] + CY * x[0] * x[2] * size(val) + x[9] * (len(wins) == 1),
                          mark=True, after=lastc[e])]
 
     win = B("XF", D, XW)
-    tops = {}
+    tops, odd = {}, {}
 
     for s in range(3):
         first, last = s == 0, s == 2
         if s:
-            for n in ("ls", "lv"):
-                fill(B(n, 224 * s, 224 * s + 224), LEV[s])
+            for n, k in (("ls", 256), ("lv", 224)):
+                fill(B(n, 256 * s, 256 * s + k), LEV[s])
+        if s == PAIRS:
+            for n in ("AS", "AS2"):
+                for a in range(WW + WK, 2 * WW, 448):
+                    fill(B(n, a, a + 448), 0)
+            iota(B("RO", 0, 128), [[0, 32], [WW, 2], [0, 2]], 0)
+            for j, r in enumerate(sorted({x + x % 2 for y in BIND_VEC[s:] for x in y})):
+                odd[r] = rows("RO", slice(0, 1), 128 * j + 128, 128 * j + 256)
+                select(B("RO", 128 * j + 128, 128 * j + 256), B("RO", 0, 128), [[0, 4], [1, 32]], 0, base=-2 * r)
         if s == 1:
-            fill(B("XT", 0, D), 0)
-            ident(B("IL", 128, 256), LEV[1] / 4)
+            ident(B("IL", 128, 256), LEV[1] / 2)
             for a in range(0, XW, 488):
                 iota(B("F", a, a + 488), [[1, 488]], a - D)
         if last:
-            ident(B("ILf"), LEV[2] / 4)
-        for b in EB:
-            mm([(B(b), rows("ones", slice(0, 1), 0, 128), rows("JR", slice(0, 1), 0, 512), True, False)])
-        scan(B("sc1", 1, 129), B("ones", 0, 128), B("aws"), 0.0, A.mult, A.add)
-        mm([(B("pb", 0, 128), B("TRI"), B("aws"), True, False)])
-        mm([(B("pb", 0, 128), BO, B("sc1", 0, 128), False, True)])
-        act(B("pre"), B("pb", 0, 128), AF.Copy)
-        act(B("sg"), B("pre", 0, 112), AF.Sign, bias=-256.5)
-        for b in EB:
-            mm([(B(b, 128 * c, 128 * c + 128), B("sc1", 1, 129), BO, False, c == 3) for c in range(4)])
+            ident(B("ILf"), LEV[2] / 2)
+            lin(B("Z0"), B("ZS"), B("oh", 0, 1))
+        ts(R("awT", 0, 128), R("ph", 0, 128), 0.0, A.is_gt)
+        calls[-1]["goal"] = not first
+        if first:
+            for k, (a, b) in enumerate(CHUNKS):
+                encode(a, b, ("pe", "ph")[k % 2], "AV"[k in XF_VEC])
+        scan(R("wT", 0, 128), R("RS", 0, 128), R("awT", 0, 128), 0.0, A.min, A.add)
+        mm(grp(R("pd", 0, 8), [(R("TRI", 1, 113), R("wT", 15, 128, 16))]))
+        ts(R("nB", 0, 8), R("pd", 0, 8), -2.0, A.mult, -512.0, A.max)
+        mm(grp(B("pb", 0, 112), [(R("wT", 0, 128), R("TRI", 0, 112))]))
+        lin(B("Yb"), B("pb", 0, 112), 1.0 / 16)
+        place = [(R("wT", 0, 128), R("J", 0, 112)), (S15, B("Yb"))]
+        mm(grp(B("pb", 128, 240), place))
+        act(B("pre", 0, 112), B("pb", 128, 240), AF.Copy)
+        mm(grp(B("pb", 256, 368), place + [(R("awT", 0, 128), R("MM", 256, 368))]))
+        act(B("sg"), B("pb", 256, 368), AF.Sign, bias=-4352.5)
 
         def count(bank, h, k):
-            wt = [k >> max(c // 4, h * (EQ_ACT - 2)) for c in range(8)]
-            return [(B(bank, c, c + 1), B("EQ", 1024 * h + 128 * c, 1024 * h + 128 * c + 128),
-                     B("xb", wt[c], wt[c] + 1), k == 2, k == 2) for c in range(8)]
+            return [(B(bank, c, c + 1), R("EQ", 1024 * h + c, 1024 * h + 1024, 8), R("xb", k, k + 1), k == 1, k == 1)
+                    for c in range(8)]
 
         for h in range(2):
-            if h * EQ_ACT < 3:
-                ts(B("EQ", 1024 * h, 1024 * h + 512), B(EB[2 * h]), 128.0 * h, A.is_le, 0.5, A.subtract)
-            else:
-                act(B("EQ", 1024 * h, 1024 * h + 512), B(EB[2 * h]), AF.Sign, bias=128.0 * h + 0.5, scale=-1.0)
-            act(B("EQ", 1024 * h + 512, 1024 * h + 1024), B(EB[2 * h + 1]), AF.Sign, bias=128.0 * h + 64.5, scale=-1.0)
-            mm(count(("pf", "pg")[h], h, 2))
+            for j in range(8):
+                o, i = R("EQ", 1024 * h + 128 * j, 1024 * h + 128 * j + 128), R("jn", 128 * h, 128 * h + 128)
+                if j < 8 - EQ_A[s][h]:
+                    ts(o, i, R("nB", j, j + 1), A.is_le, 2.0, A.mult)
+                else:
+                    act(o, i, AF.Sign, bias=R("nB", j, j + 1), scale=-1.0)
+            mm(count(("pf", "pg")[h], h, 1))
         for h in range(2):
             a, o = 128 * h, B(("pa", "pc")[h], 0, 8)
-            ts(B("bw", 8 * h, 8 * h + 8), B(("pf", "pg")[h], 0, 8), 0.5, A.mult, 64.0, A.add)
-            if BWB:
-                ts(B("bwb", 8 * h, 8 * h + 8), B(("pf", "pg")[h], 0, 8), 0.5, A.mult)
-                mm([(o, I16, B("bwb", 8 * h, 8 * h + 8), True, False)])
-            else:
-                mm([(o, BO, B("zr", 0, 8), True, False)] + count(("pa", "pc")[h], h, 16))
+            ts(B("bw", 8 * h, 8 * h + 8), B(("pf", "pg")[h], 0, 8), 0.5, A.mult, lift[EQ_A[s][h]][0], A.add)
+            mm([(o, BO, B("zr", 0, 8), True, False)] + count(("pa", "pc")[h], h, 8))
             tt(B("cmp", a, a + 128), X(B("pre"), B("bw", 8 * h, 8 * h + 8)), B("xb", a, a + 128), A.is_le)
             mm([(o, sel("ZS", p), B("cmp", a + p, a + 128, 16), False, p == 15) for p in range(16)])
-            ts(B("eu", 8 * h, 8 * h + 8), o, 1024.0, A.add)
+            ts(B("eu", 8 * h, 8 * h + 8), o, lift[EQ_A[s][h]][1], A.add)
             cp(B("gve", a, a + 128), X(B("gvi"), B("eu", 8 * h, 8 * h + 8)))
-        if first:
-            encode()
 
         def two(a, b):
-            return B("S", 16 * a + 14, 16 * b, 16), B("GG", 16 * a + 15, 16 * b, 16)
+            return S(16 * a + 14, 16 * b, 16), GG(16 * a + 15, 16 * b, 16)
 
-        def fraction(o, a, b, m, last):
+        def fraction(o, a, b, m, last, mark=False):
             mx, go = two(a, b)
             mm([(o, m[0], mx, False, False), (o, nKS, B("MAG", 0, b - a), False, False), (o, m[1], mx, False, False)]
-               + [(o, l, x, False, last and i == len(m[2]) - 1) for i, (l, x) in enumerate(m[2])])
+               + [(o, l, x, False, last and i == len(m[2]) - 1) for i, (l, x) in enumerate(m[2])], mark)
 
         for a, b, e in (GATHER0 if first else GATHER):
             if e == "A":
-                act(B("GG", 16 * a, 16 * b), X(win, B("gve", a, b)), AF.Copy)
+                act(GG(16 * a, 16 * b), X(win, B("gve", a, b)), AF.Copy)
             else:
-                cp(B("GG", 16 * a, 16 * b), X(win, B("gve", a, b)))
+                cp(GG(16 * a, 16 * b), X(win, B("gve", a, b)))
         for a, b in SCANS:
-            scan(B("S", 16 * a, 16 * b), B("SM", 1, 1 + 16 * (b - a)), B("GG", 16 * a, 16 * b), 0.0, A.min, A.max)
-        mm([(B("ph", 0, 256), KS, B("MAG"), True, False), (B("ph", 0, 256), nKB, B("t196"), False, False)])
-        for a, b in HALVES:
-            for i in range(0, 16, 4):
-                mm([(B("ph", a, b), nKB if j < 15 else nKS, B("GG", 16 * a + j, 16 * b, 16), False, False)
-                    for j in range(i, i + 4)], "sum")
+            scan(S(16 * a, 16 * b), B("SM", 0, 16 * (b - a)), GG(16 * a, 16 * b), 0.0, A.min, A.max)
+        mm([(B(WANT, 0, 256), KS, B("MAG"), True, False), (B(WANT, 0, 256), nKB, B("t196"), False, False)])
+        for a, b in SUMS:
+            for i in range(0, 16, TERMS):
+                mm([(B(WANT, a, b), nKB if j < 15 else nKS, GG(16 * a + j, 16 * b, 16), False, False)
+                    for j in range(i, i + TERMS)], ("sum", a, b))
+            mx, go = two(a, b)
+            fraction(B(WANT, a, b), a, b, (KBS, KS, [(KS, go), (M8, mx), (M8, go), (M9, S(16 * a + 15, 16 * b, 16))]), False,
+                     ("then", a, b))
+        mm([(B(WANT, 0, 1), BO, B("zr", 0, 1), False, True)])
         for h, (a, b) in enumerate(HALVES):
             bk, bl, n, k = ("pf", "pg")[h], ("pb", "pc")[h], b - a, (b - a) // 16
             mx, go = two(a, b)
@@ -686,31 +734,34 @@ def rank_program(g, core, T, topo):
             scan(B("lat", a, b), B("LD", a, b), B(bk, 0, n), 0.0, A.min, A.max)
             ts(ou, B("lat", a + 15, b, 16), ZB, A.add)
             cp(B("cg", a, b), X(B("C", 0, D + V), ou))
-            shuffle(bl, n // 2, B("CCb", at[n], at[n] + n), "cg", "tm", a)
+            two_from = BIND_VEC[s][h] + BIND_VEC[s][h] % 2 if s >= PAIRS and h < PAIR_H else 16
+            shuffle(bl, n // 2, B("CCb", at[n], at[n] + n), "cg", "tm", a, odd.get(two_from))
             lists(bl, k // 2, "TT", a, "wl")
+            calls[-1]["goal"] = h == 0
             for r in range(16):
                 e = "V" if r < BIND_VEC[s][h] else "A"
-                scatter(e, s, B("wl", a + k * r, a + k * r + k), ("AS", "AS2") if e == "A" else ("AV", "AV2"))
+                if r >= two_from:
+                    if r % 2 == 0:
+                        scatter(e, s, B("wl", a + k * r, a + k * r + 2 * k), ("AS", "AS2"), 2)
+                    continue
+                m = k // 2 if e == "V" and r < HALVED[s][h] else k
+                for j in range(a + k * r, a + k * r + k, m):
+                    scatter(e, s, B("wl", j, j + m), ("AS", "AS2") if e == "A" else ("AV", "AV2"))
         mx, go = two(0, 256)
-        for a, b, e in M14:
-            if e == "A":
-                lin(B("m14", a, b), two(a, b)[0], 1.0, 14.0)
-            else:
-                ts(B("m14", a, b), two(a, b)[0], 14.0, A.add)
-        tab, free = ("XT", -1.0) if last and XT_LAST else ("XF", C0)
-        if tab == "XF":
-            cp(X(B("XF"), B("obu")), mx)
-        for a, b in XT_PARTS if tab == "XF" else ((0, 256),):
-            cp(X(B("XT", 0, D + V), B("obu", a // 16, b // 16)), B("m14", a, b))
-        refresh(range(s - 1, -1, -1), tab)
+        for a, b in XT_PARTS:
+            tt(X(B("XT", 0, D + V), B("obu", a // 16, b // 16)), two(a, b)[0], B("c14", a, b), A.add)
+        refresh(range(s - 1, -1, -1), "XT")
         snd, Ln = B("snd", 224 * s, 224 * s + 224), B("land", 224 * s, 224 * s + 224)
         if SND_ACT:
-            act(snd, X(B(tab, D, XW), B("exu", 0, 14)), AF.Copy)
+            act(snd, X(B("XT", D, XW), B("exu", 0, 14)), AF.Copy)
         else:
-            cp(snd, X(B(tab, D, XW), B("exu", 0, 14)))
-        if tab == "XT":
+            cp(snd, X(B("XT", D, XW), B("exu", 0, 14)))
+        if last:
             for k in range(s):
                 cp(X(B("XT"), B("LT", 8 * k, 8 * k + 3)), B("neg1", 0, 48))
+        else:
+            for a, b in XF_PARTS:
+                cp(X(B("XF", 0, D + V), B("obu", a // 16, b // 16)), two(a, b)[0])
         trs = []
         for d in range(1, 8):
             peer = T.cores[rank ^ d]
@@ -723,26 +774,27 @@ def rank_program(g, core, T, topo):
                                          remote_sem=T.sem["arr%d" % s], src=T.snd[:, a:a + 32], dst=T.land[:, a:a + 32]))
             tops["snt"] = tops.get("snt", 0) + n
             tops["arr%d" % s] = tops.get("arr%d" % s, 0) + n
-        call("G", lambda trs=trs: g.remote_dma_fused(trs, local_sem=T.sem.snt), [snd], [Ln], lambda x: x[11],
-             lambda x: x[7] * (FIRST if first else 1), "arr%d" % s)
-        for a, b in TESTS:
-            mm(grp(B("pa", a, b), list(zip((M8, M9), two(a, b)))))
-            act(B("ab", a, b), B("pa", a, b), AF.Abs)
-        o = B("ph", 0, 256)
-        fraction(o, 0, 256, (KBS, KS, [(KS, go)]), False)
-        mm([(o, Ib, B("ab"), False, True)])
-        ts(B("want", 0, 256), o, 2 * K * C0 + 0.5, A.is_gt)
+        hold[:] = [call("G", lambda trs=trs: g.remote_dma_fused(trs, local_sem=T.sem.snt), [snd], [Ln], lambda x: x[11],
+                        lambda x: x[7] * (FIRST if first else 1), "arr%d" % s)]
+        o = B(WANT, 0, 256)
+        ts(B("want", 0, 256), o, 2 * K * C0 + 0.5, A.is_gt, -1.0, A.mult)
         o = B("pd", 0, 256)
         mm([(o, M8, go, True, False)])
         mm([(o, IK, B("want", 0, 256), False, True)])
         ts(B("SW", 0, 256), o, ZB - SH - K1, A.add, -2000.0, A.max)
-        scan(B("rank"), B("ones"), B("want"), 0.0, A.mult, A.add)
-        for t in range(3):
-            act(B("EQ", 304 * t, 304 * t + 304), B("rank"), AF.Sign, bias=B("jh", t, t + 1), scale=-1.0,
-                accum_out=B("ca", t, t + 1))
-        ts(B("lz", 0, 3), B("ca", 0, 3), 8.0, A.mult, 2447.0, A.add)
-        ts(B("lz", 4, 7), B("ca", 0, 3), 8.0, A.mult, 2446.0, A.add)
-        cp(B("cs"), X(B("S"), B("lz", 0, 7)))
+        if COUNT_ACT:
+            scan(B("rank"), B("ones"), B("want"), -0.5, A.mult, A.add)
+            for t in range(3):
+                act(B("EQ", 256 * t, 256 * t + 256), B("rank"), AF.Sign, bias=B("jh", t, t + 1), accum_out=B("ca", t, t + 1))
+            ts(B("lz", 0, 3), B("ca", 0, 3), 8.0, A.mult, 2063.0, A.add)
+            ts(B("lz", 4, 7), B("ca", 0, 3), 8.0, A.mult, SO + 2062.0, A.add)
+        else:
+            for t in range(3):
+                scan(B("EQ", 256 * t, 256 * t + 256), B("want"), B("zr"), B("jh", t, t + 1), A.add, A.max)
+            scan(B("EQ", 1024, 1792), B("EQ", 0, 768), B("PL"), 0.0, A.add, A.min)
+            ts(B("lz", 0, 3), B("EQ", 1279, 1792, 256), 16.0, A.mult, 15.0, A.add)
+            ts(B("lz", 4, 7), B("EQ", 1279, 1792, 256), 16.0, A.mult, SO + 14.0, A.add)
+        cp(B("cs"), X(B("GS"), B("lz", 0, 7)))
         dec = [(sel("Zd", p), B("cs", p, 112, 16)) for p in range(16)]
         mm(grp(B("pe", 0, 7), dec))
         mm([m for j in range(5) for m in grp(B("pa", 16 * j, 16 * j + 16), [(M8, B("cs", 64 + 16 * (j // 2), 80 + 16 * (j // 2)))]
@@ -754,9 +806,8 @@ def rank_program(g, core, T, topo):
             ts(B("SW", 256, 336), B("pa", 0, 80), ZB - SH, A.add)
         ts(B("LU", 0, 7), B("pe", 0, 7), ZB, A.add)
         cp(B("cc"), X(B("C"), B("LU", 0, 7)))
-        ts(B("xu"), X(B(tab), B("LU", 4, 7)), free, A.not_equal, col(17), A.mult)
         tt(B("mn", 48, 96), B("cc", 0, 48), B("cc", 64, 112), A.min)
-        tt(B("mn", 0, 48), B("mn", 48, 96), B("xu"), A.add)
+        tt(B("mn", 0, 48), X(B("XT"), B("LU", 4, 7)), B("mn", 48, 96), A.add)
         tt(B("mxc"), B("cc", 0, 48), B("cc", 64, 112), A.max)
         mm([(B("pf", 0, 3), sel("Z8h", p), B("mn", p, 48, 16), False, False) for p in range(16)])
         ends = (0, 272, 576, 912)
@@ -772,45 +823,28 @@ def rank_program(g, core, T, topo):
         def blk(n, d, k=0):
             return B(n, 224 * k + 32 * d - 32, 224 * k + 32 * d)
 
-        lst = [(B("pg", 0, 224), Ib, B("neg1"), True, False)]
-        if first:
-            lst.append((B("pg", 0, 224), I4, B("ones", 0, 224), False, False))
-        else:
-            lst += [(blk("pg", d), PMm(2, d), blk("fn", d, s - 1), False, False) for d in range(1, 8)]
-        mm(lst)
-        ts(B("fn", 224 * s, 224 * s + 224), Ln, free, A.is_equal, -4096.0, A.mult)
-        mm([(blk("pg", d), PMm(1, d), blk("fn", d, s), False, d == 7) for d in range(1, 8)])
+        xi = B("XT", D + V, D + W)
+        mm([(B("pg", 0, 224), Ib, B("neg1"), True, False), (B("pg", 0, 224), nI4, xi, False, False)])
+        mm([(blk("pg", d), PMm(1, d), blk("land", d, s), False, d == 7) for d in range(1, 8)])
         if last:
-            turn([lambda t: B("aws", t, 112, 7), lambda t: B("aws", t, 112, 7), lambda t: B("sg", t, 112, 7)], "pb")
+            turn([lambda t: B("sg", t, 112, 7)], "pb")
             vtr(B("remT"), B("pb", 0, 224))
         tt(B("Cm"), B("C", D + V, D + W), B("pg", 0, 224), A.min)
         shuffle("pb", 112, B("CCi"), "Cm", "ti")
         lists("pb", 7, "TI", 0, "wi")
         for r in range(16):
-            if r == max(0, IMP_ACT[s] - AS_ONLY[s]) and last:
-                dma("d_as", B("asn"), rows("AS2", slice(0, 128, 16), WK, WW), 1600)
-            elif r == max(0, IMP_ACT[s] - AS_ONLY[s]):
-                hold[:] = [select(B("ASc", 0, G - DIRECT[1]), B("AS2", WK, WW - DIRECT[1]), [[0, G - DIRECT[1]]], 0)]
             e = "A" if r < IMP_ACT[s] else "V"
             both = r < (IMP_ACT[s] - AS_ONLY[s] if e == "A" else 16 - AV_ONLY)
             scatter(e, s, B("wi", 14 * r, 14 * r + 14), (("AS", "AS2") if e == "A" else ("AV", "AV2"))[:1 + both])
-        cut = G - DIRECT[0]
-        parts = [x for x in ((0, cut - NARROW_G - NARROW_A), (cut - NARROW_G - NARROW_A, cut - NARROW_G), (cut - NARROW_G, cut))
-                 if x[0] < x[1]]
-        for a, b in parts:
-            if b == cut and NARROW_G:
-                hold[:] = [select(B("ASb", a, b), B("AS", WK + a, WK + b), [[0, b - a]], 0)][:1 - last]
-            else:
-                act(B("ASb", a, b), B("AS", WK + a, WK + b), AF.Copy)
-        mm([m for d in range(1, 8) for m in grp(blk("pc", d), [(PMm(0, d), blk("land", d, s)), (PMm(1, d), blk("fn", d, s))][:1 + (tab == "XF")])])
-        if tab == "XT":
-            act(B("XT", D + V, D + W), B("pc", 0, 224), AF.Copy)
-        elif s == 2 - XT_LAST:
-            ts(B("XT", D + V, D + W), B("pc", 0, 224), 14.0, A.add, -1.0, A.max)
+        mm([m for d in range(1, 8) for m in grp(blk("pc", d), [(PMm(0, d), blk("land", d, s))])])
+        if XI_ACT[s]:
+            act(xi, B("pc", 0, 224), AF.Copy)
+        else:
+            cp(xi, B("pc", 0, 224))
         if last:
             dma("d_y0", T.yx[:, 0:V], B("XT", D, D + V), 6000)
             dma("d_y1", T.yx[:, V:W], B("XT", D + V, D + W), 1200)
-            refresh(range(2, -1, -1), "F", "c48")
+            refresh(range(2, -1, -1), "F", "c48", "VA"[F_ACT])
             dma("d_yf", T.yf[:], rows("F", slice(0, 128, 16), D, D + W), 1300)
             for a in (0, 1280):
                 select(B("C16", a, a + 1280), B("C", D + a, D + a + 1280), [[0, 1280]], 0)
@@ -819,44 +853,50 @@ def rank_program(g, core, T, topo):
             act(B("yc_"), B("pe", 0, 160), AF.Copy)
             dma("d_yc", T.yc[:], B("yc_"), 1300)
         else:
-            mm([(B("pd", 0, 224), I4, B("neg1"), True, False)]
-               + [(blk("pd", d), PMm(2, d), blk("fn", d, s), False, False) for d in range(1, 8)]
-               + [(B("pd", 0, 224), Ib, B("NC", 0, 224), False, True)])
-            act(B("wS"), B("pd", 0, 224), AF.Copy)
-            tt(B("XF", D + V, D + W), B("pc", 0, 224), B("wS"), A.max)
+            encode(V, W, "pd")
             refresh(range(s, -1, -1), e="VA"[REF_ACT])
 
-        def piece(n, p, a=WK):
-            return B(n, a + 112 * p, a + 112 * p + 112) if last else B(n, a + p, a + G, 16)
+        def turned(bank, n, k, end, WK=WK, WW=WW):
+            one = B("If" if SCRATCH[n][2] == F32 else "J", 0, 128, 16)
+            ps = list(range(16))
+            if n == "AS" and NARROW[s] and WK < G:
+                m = NARROW[s]
+                ps = ps[:16 - m] if last else [p for p in ps if p % (16 // m)]
+                act(B("ASb", 0, 112 * m), B(n, WW - 112 * m, WW) if last else B(n, WK, WW, 16 // m), AF.Copy)
+            for a in range(0, len(ps), k):
+                mm([(R(bank, p, 128, 16), B(n, WK + 112 * p, WK + 112 * p + 112) if last else B(n, WK + p, WW, 16), one,
+                     False, end and p == 15) for p in ps[a:a + k]], not (end and 15 in ps[a:a + k]) and "sum")
+            if len(ps) < 16:
+                mm([(R(bank, 16 - m + j if last else 16 // m * j, 128, 16),
+                     B("ASb", 112 * j, 112 * j + 112) if last else B("ASb", j, 112 * m, m), B("J", 0, 128, 16),
+                     False, end and j == m - 1) for j in range(m)], not end and "sum")
 
-        o = B("ph", 0, 112)
         if last:
-            mm([(o, B("If"), B("asn"), True, False)])
+            o = B("ph", 0, 112)
+            mm([(o, BO, B("zr", 0, 112), True, False)])
             mm([(B("ph", 16 * t, 16 * t + 16), B("ILf"), B("remT", 32 * t, 32 * t + 16), False, False) for t in range(7)],
                "sum")
-        else:
-            il = B("IL", 128 * s, 128 * s + 128)
-            mm([(o, il, B("aws", 0, 112), True, False), (o, il, B("aws", 0, 112), False, False),
-                (o, il, B("sg"), False, False)])
-        reads = [("Z0", n, WK, 0, G) for n in ("AV2", "AV")] + [("Z0", "ASb", 0, a, b) for a, b in parts]
-        reads += [("Z0f", "AS", WK, cut, G)]
-        if not last:
-            reads += [("Z0", "ASc", 0, 0, G - DIRECT[1]), ("Z0f", "AS2", WK, G - DIRECT[1], G)]
-        for z, n, at0, a, b in sorted([x for x in reads if x[3] < x[4]], key=lambda x: x[1] == LAST_READ):
-            end = n == LAST_READ
-            if last:
-                mm([(o, sel(z, p), piece(n, p, at0), False, end and p == b // 112 - 1) for p in range(a // 112, b // 112)],
-                   not end and "sum")
-            else:
-                mm([(B("ph", a // 16, b // 16), sel(z, p), B(n, at0 + a + p, at0 + b, 16), False, end and p == 15)
-                    for p in range(16)], not end and "sum")
-        if not LAST_READ:
-            mm([(o, BO, B("zr", 0, 112), False, True)])
-        if last:
-            ts(B("yw_"), o, 0.5 * LEV[s], A.is_gt)
+            mm([(R("pa", 0, 128), B("zr", 0, 112), BO, True, False)])
+            for n in ("AS", "AS2") * (s >= PAIRS):
+                turned("pa", n, READS, False, WW + WK, 2 * WW)
+            for n in TURN_LAST:
+                turned("pa", n, 16, False)
+            turned("pa", "AS2", READS, False)
+            turned("pa", "AS", READS, True)
+            act(R("At", 0, 128), R("pa", 0, 128), AF.Copy)
+            mm([(o, R("At", 0, 128), R("J", 0, 112), False, False)], "sum")
+            for n in ("AV2", "AV")[len(TURN_LAST):]:
+                mm([(o, sel("Z0", p), B(n, WK + 112 * p, WK + 112 * p + 112), False, False) for p in range(16)], "sum")
+            mm([(B("ph", 0, 1), BO, B("zr", 0, 1), False, True)])
+            ts(B("yw_"), o, 0.0, A.is_gt)
             dma("d_yw", T.yw[:], B("yw_"), 1200)
         else:
-            ts(B("aws", 0, 112), o, 0.5 * LEV[s], A.is_gt)
+            mm([(R("ph", 0, 128), B("sg"), B("IL", 128 * s, 128 * s + 128), True, False)])
+            for n in ("AS", "AS2") * (s >= PAIRS):
+                turned("ph", n, READS, False, WW + WK, 2 * WW)
+            for n in ("AS2", "AS", "AV2"):
+                turned("ph", n, READS if n[1] == "S" else 16, False)
+            turned("ph", "AV", 16, True)
 
     cnt, seen, uses = {e: 0 for e in eng}, {e: {} for e in eng}, {}
 
@@ -869,6 +909,9 @@ def rank_program(g, core, T, topo):
             for k, m in known.get((sem, n), (0, {}))[1].items():
                 seen[e][k] = max(seen[e].get(k, 0), m)
 
+    for c in calls[warm + 1:]:
+        if c["e"] == "A" and not c["after"]:
+            c["after"] = [warm]
     if not PLANS:
         PLANS.append(plan(calls))
     for c in [calls[i] for i in PLANS[0]]:

from concourse.bass import DstId, RemoteDMATransfer
from concourse.mybir import AluOpType as A, AxisListType, ActivationFunctionType as AF

V, W, G = 2336, 2560, 1792
D = 304
XW = D + W + 64
WK = 256
WW = WK + G
MAGIC = 12582912.0
K, K1, K2 = 2.0 ** 24, 2.0 ** 21, 131072.0
C0 = 15.0 / 128
ZB = float(D + 2805)
K_ACT = (6, 7, 8, 9, 10)
CHUNKS = ((0, 480), (480, 960), (960, 1440), (1440, 1920), (1920, V), (V, W))
SO = 4112
IDLE = 22.0 / 8192
EQ_A = ((1, 1), (1, 1), (1, 1))
READS = 4
XI_ACT = (True, True, True)
NARROW = (8, 8, 8)
COUNT_ACT = False
SUMS, TERMS = ((0, 128), (128, 192), (192, 256)), 4
PAIRS = 3
F_ACT = True
PAIR_H = 1
TURN_LAST = ("AV2",)
HALVED = ((0, 0), (0, 0), (0, 0))
EARLY = ("pi", "xb", "J", "mg", "RS", "TRI", "jp", "XT", "gvi", "XF", "AS", "SM", "I4")
KS_ACT, D_ACT = True, False
WANT = "ph"
AW_F32 = False
SH = 1024.0
LEV = (256, 8192, 262144)
HALVES = ((0, 128), (128, 256))
BIND_VEC = ((1, 5), (1, 5), (1, 5))
SW_ACT = False
XT_PARTS = ((0, 256),)
XF_PARTS = ((0, 128), (128, 256))
ROUNDS = 3
SND_ACT = False
IMP_ACT = (5, 5, 5)
AV_ONLY = 1
GATHER = ((0, 64, "A"), (64, 128, "V"), (128, 192, "A"), (192, 256, "A"))
GATHER0 = ((0, 64, "A"), (64, 128, "V"), (128, 192, "A"), (192, 256, "A"))
SCANS = ((0, 64), (64, 128), (128, 192), (192, 256))
CY, INDIRECT = 0.83, {"V": 50, "A": 65}
OVER = (100, 250, 400)
STARTS = 8
CUT = 40
WORLDS = ((1.1, 1.4, 2.5, 15, 60, 120, 0.36, 2500, 0.6, 160, 1.0, 600, 45, 35),
          (1.35, 1.3, 1.5, 25, 50, 70, 0.42, 3500, 0.5, 180, 1.2, 1000, 50, 40),
          (1.15, 1.3, 5.0, 25, 85, 200, 0.36, 3000, 0.8, 100, 1.0, 400, 40, 20),
          (1.4, 1.9, 5.6, 20, 60, 120, 0.4, 3000, 0.7, 140, 1.1, 700, 45, 30))
POLISH = 12000
PASSES, STRETCH, BEYOND = 1, 400, 30
SLACK = 0.0004
SEED = 1
LEAN = 0.3
FILL = 1
NOTE = []
Z_G = 448
AS_ONLY = (2, 2, 2)
CC_ACT = False
HB_ACT = True
FIRST = 1.5
AW_G = False
REF_ACT = True
XF_VEC = ()
PLANS = []


def sb(n, dt):
    return ("sbuf", [128, n], dt)


F32, BF, F16, I32, U16 = "float32", "bfloat16", "float16", "int32", "uint16"
SCRATCH = {
    "awi": sb(112, I32), "awb": sb(112, BF), "aws": sb(112, BF), "awT": sb(128, BF), "wT": sb(128, BF),
    "RS": sb(128, BF), "nB": sb(8, BF), "jp": sb(256, BF), "jn": sb(256, F16), "Yb": sb(112, BF), "At": sb(128, BF), "ASb": sb(896, BF),
    "gvi": sb(G + 16, I32), "exi": sb(16, I32), "exu": sb(16, U16),
    "XF": sb(XW, BF), "XT": sb(XW, BF), "C": sb(XW, I32), "F": sb(XW, F32),
    "AV": sb(2640, BF), "AV2": sb(W, BF), "AS": sb(2 * WW, F32), "AS2": sb(2 * WW, F32), "C16": sb(W, F16),
    "lv": sb(768, BF), "ls": sb(768, F32), "RO": sb(640, BF),
    "GS": sb(2 * SO, BF), "SM": sb(16 * max(b - a for a, b in SCANS), BF),
    "pi": sb(8, I32), "co_": sb(48, F32), "xb": sb(256, BF), "mg": sb(128, BF),
    "oh": sb(16, F32), "sK": sb(16, F32), "aK": sb(16, F32),
    "J": sb(144, BF), "BO": sb(128, BF), "TRI": sb(128, BF), "ZS": sb(144, BF), "Zd": sb(144, BF),
    "ZSh": sb(144, F16), "Z8h": sb(144, F16), "Z0": sb(144, BF),
    "If": sb(128, F32), "IL": sb(384, BF), "ILf": sb(128, F32), "I8h": sb(256, F16),
    "MM": sb(2176, BF), "PM": sb(512, BF), "OH": sb(128, BF),
    "H0h": sb(144, F16), "H1h": sb(144, F16), "H0b": sb(144, BF), "H1b": sb(144, BF),
    "ones": sb(256, BF), "zr": sb(256, BF), "PL": sb(768, BF), "neg1": sb(224, BF),
    "MAG": sb(256, BF), "t196": sb(256, BF), "cz": sb(4, F32), "c14": sb(256, BF),
    "jh": sb(4, F32), "dd": sb(8, F32),
    "KJ": sb(224, BF), "CCb": sb(256, BF), "LD": sb(256, F32), "lat": sb(256, F32), "CCi": sb(224, BF), "M16": sb(16, BF),
    "EQ": sb(2048, BF), "pre": sb(128, F32), "sg": sb(112, BF), "remT": sb(224, F32),
    "bw": sb(16, U16), "cmp": sb(256, BF), "eu": sb(16, U16), "gve": sb(256, U16),
    "obu": sb(16, U16), "cg": sb(256, F16), "tm": sb(256, BF),
    "TT": sb(256, F32), "TI": sb(224, F32), "wl": sb(256, U16), "wi": sb(224, U16),
    "want": sb(256, BF), "rank": sb(256, BF), "ca": sb(4, F32),
    "SW": sb(336, F16), "lz": sb(8, U16), "cs": sb(112, BF), "LU": sb(8, U16),
    "cc": sb(112, F32), "mn": sb(96, F16), "mxc": sb(48, F32), "E": sb(912, BF), "EO": sb(912, F16),
    "LT": sb(24, U16), "x48": sb(48, BF), "c48": sb(48, F32),
    "snd": sb(672, BF), "land": sb(672, BF), "Cm": sb(224, F16), "ti": sb(224, BF),
    "yw_": sb(112, F32), "yc_": sb(160, F32),
}
PART = {}
for _n in ("oh", "sK", "aK", "jh", "dd", "ca"):
    PART[_n] = (sum(x[1] for x in PART.values()), SCRATCH.pop(_n)[1][1])
SCRATCH["fs"] = sb(sum(x[1] for x in PART.values()), F32)
PSUMS = ("pa", "pb", "pc", "pd", "pe", "pf", "pg", "ph")
for _b in PSUMS:
    SCRATCH[_b] = ("psum", [128, 512], F32)
DMAS = ["d_aw", "d_x0", "d_gv", "d_ex", "d_co", "d_y0", "d_y1", "d_yf", "d_yw", "d_yc", "d_ci"]
DMAS += ["d_z%d" % j for j in range(2 * G // Z_G - 1)]
SEMAPHORES = ["sV", "sA", "sP", "sG", "snt", "arr0", "arr1", "arr2"] + DMAS


def meet(p, q):
    if p[0] >= q[1] or q[0] >= p[1]:
        return False
    return p[2] != q[2] or (p[0] - q[0]) % p[2] == 0


def plan(calls):
    n, uses = len(calls), {}
    pre = [set(c["after"]) for c in calls]
    for i, c in enumerate(calls):
        for vs, wr in ((c["r"], False), (c["w"], True)):
            for x in vs:
                old, bank = uses.get(x[1], []), x[1] in PSUMS
                for j, w2, sp in old:
                    if j != i and not (c["mark"] and wr and w2 and calls[j]["mark"]):
                        if (bank and (wr or w2 or calls[j]["e"] != c["e"])) or ((wr or w2) and meet(sp, x[2:5])):
                            pre[i].add(j)
                if wr and not c["mark"]:
                    old = [u for u in old if not (bank or (x[4] == 1 and x[2] <= u[2][0] and u[2][1] <= x[3]))]
                uses[x[1]] = old + [(i, wr, x[2:5])]
    worlds = range(len(WORLDS))
    queue = [c["e"] for c in calls]
    ns, late = [[c["ns"][k] for c in calls] for k in worlds], [[c["late"][k] for c in calls] for k in worlds]
    above = [0] * n
    for i in range(n):
        for j in pre[i]:
            above[i] |= above[j] | 1 << j
    near = [[j for j in pre[i] if late[0][j] > 100 or not any(above[k] >> j & 1 for k in pre[i])] for i in range(n)]
    ways = [[[(j, 0 if j in calls[i]["after"] or queue[i] == queue[j] == "P" else
               WORLDS[k][9 if queue[i] == queue[j] else 5] + late[k][j]) for j in near[i]] for i in range(n)] for k in worlds]
    post = [[[] for _ in calls] for k in worlds]
    for k in worlds:
        for i in range(n):
            for j, d in ways[k][i]:
                post[k][j].append((i, d))

    def place(order, back, k):
        start, busy = [0] * n, {e: [] for e in "VAPGS"}
        for i in order:
            line = busy[queue[i]]
            t = max([late[k][i] * back] + [start[j] + ns[k][j] + d for j, d in (post if back else ways)[k][i]])
            a = 0
            while a < len(line) and line[a][0] < t + ns[k][i]:
                t = max(t, line[a][1])
                a += 1
            line.insert(a, (t, t + ns[k][i]))
            start[i] = t
        return start

    def first(k, over):
        chain = [0] * n
        for j in range(n - 1, -1, -1):
            chain[j] = ns[k][j] + max([late[k][j]] + [d + chain[i] for i, d in post[k][j]])
        left, ready, free = [len(p) for p in near], [0] * n, {e: 0 for e in "VAPGS"}
        cand = {e: [i for i in range(n) if queue[i] == e and not near[i]] for e in free}
        order = []
        while len(order) < n:
            best = None
            for e in free:
                if cand[e]:
                    pick = top = max(cand[e], key=lambda i: chain[i])
                    if ready[top] > free[e]:
                        fit = [i for i in cand[e] if max(free[e], ready[i]) + ns[k][i] <= ready[top] + over and i != top]
                        pick = max(fit, key=lambda i: chain[i]) if fit else top
                    t = max(free[e], ready[pick])
                    if best is None or t < best[0]:
                        best = (t, e, pick)
            t, e, j = best
            order.append(j)
            cand[e].remove(j)
            free[e] = t + ns[k][j]
            for i, d in post[k][j]:
                ready[i] = max(ready[i], free[e] + d)
                left[i] -= 1
                if not left[i]:
                    cand[queue[i]].append(i)
        start = place(order, False, k)
        found = [start]
        for _ in range(ROUNDS):
            for back in (True, False):
                start = place(sorted(range(n), key=lambda i: -start[i] - ns[k][i]), back, k)
            found.append(start)
        return [sorted(range(n), key=lambda i: x[i]) for x in found]

    tails = [i for i in range(n) if not post[0][i]]

    def run(order, k, a=0, old=None, goal=None, z=n):
        end, by = (old[3][:], old[2][:]) if old else ([0] * n, [None] * n)
        last, way, took = {}, ways[k], ns[k]
        for i in range(a - 1, -1, -1):
            last.setdefault(queue[order[i]], order[i])
            if len(last) == 5:
                break
        for i in order[a:z]:
            j0 = last.get(queue[i])
            t = 0 if j0 is None else end[j0]
            for j, d in way[i]:
                if end[j] + d > t:
                    t, j0 = end[j] + d, j
            end[i], by[i] = t + took[i], j0
            last[queue[i]] = i
        top = goal or max(tails, key=lambda i: end[i] + late[k][i])
        return end[top] + late[k][top] + LEAN * sum(end) / (n if goal is None else STRETCH), top, by, end

    seed = [SEED]

    def draw(m):
        seed[0] = (seed[0] * 1103515245 + 12345) % 2147483648
        return (seed[0] >> 8) % m

    def worth(runs):
        return sum(r[0] / x for r, x in zip(runs, unit))

    def polish(order, steps, goal=None, since=None):
        runs = [run(order, k, goal=goal) for k in worlds]
        score = low = worth(runs)
        keep, z = order, order.index(goal) + BEYOND if goal else n
        for step in range(steps):
            _, i, by, end = runs[draw(len(WORLDS))]
            pairs, waits = [], []
            while by[i] is not None and (since is None or end[i] > end[since]):
                if queue[by[i]] == queue[i] and not above[i] >> by[i] & 1:
                    pairs.append((by[i], i))
                elif queue[i] in "VA":
                    waits.append(i)
                i = by[i]
            if waits and draw(4) < FILL:
                u = waits[draw(len(waits))]
                a = order.index(u)
                free = [i for i in order[a + 1:min(z, a + 80)] if queue[i] == queue[u] and not above[i] >> u & 1]
                if not free:
                    continue
                w = free[draw(len(free))]
            elif pairs:
                u, w = pairs[draw(len(pairs))]
            else:
                continue
            a, b = order.index(u), order.index(w)
            for _ in range(draw(3)):
                k = a - 1
                while k >= 0 and queue[order[k]] != queue[w]:
                    k -= 1
                if k >= 0 and not above[w] >> order[k] & 1:
                    a = k
            part = order[a:b + 1]
            if draw(2):
                move = [i for i in part if i == w or above[w] >> i & 1]
                part = move + [i for i in part if i not in move]
            else:
                move = [i for i in part if i == u or above[i] >> u & 1]
                part = [i for i in part if i not in move] + move
            new = order[:a] + part + order[b + 1:]
            trial = [run(new, k, a, runs[k], goal, z) for k in worlds]
            value = worth(trial)
            if value <= score + SLACK * draw(1000) / 1000 * (1 - step / steps):
                ends = trial[0][3]
                order, runs, score = new[:a] + sorted(new[a:z], key=lambda i: ends[i] - ns[0][i]) + new[z:], trial, value
                if value < low:
                    low, keep = value, order
        return low, keep

    def stretches(order, steps):
        marks = sorted([i for i in range(n) if calls[i]["goal"]], key=order.index) + [None]
        for since, goal in zip([None] + marks, marks):
            order = polish(order, steps, goal, since)[1]
        return worth([run(order, k) for k in worlds]), order

    found = [x for k in worlds for over in OVER for x in first(k, over)]
    unit = [run(found[0], k)[0] for k in worlds]
    found.sort(key=lambda x: worth([run(x, k) for k in worlds]))
    found = sorted([polish(x, POLISH // 10) for x in found[:STARTS]], key=lambda x: x[0])
    low, keep = found[0]
    for _, other in found[1:] * 2:
        for cut in range(CUT, n, CUT):
            for x, y in ((keep, other), (other, keep)):
                front = set(x[:cut])
                new = x[:cut] + [i for i in y if i not in front]
                value = worth([run(new, k) for k in worlds])
                if value < low:
                    low, keep = value, new
    for _ in range(PASSES):
        low, keep = min((low, keep), stretches(keep, POLISH), key=lambda x: x[0])
    keep = polish(keep, POLISH)[1]
    NOTE.append([round(run(keep, k)[0]) for k in worlds])
    return keep


def rank_program(g, core, T, topo):
    rank = T.rank_of(core)
    if rank is None:
        return
    eng = {"V": g.vector, "A": g.scalar, "P": g.tensor, "G": g, "S": g.sync}
    calls = []
    hold = []

    def B(n, a=0, b=None, st=1):
        if n in PART:
            return B("fs", PART[n][0] + a, PART[n][0] + (PART[n][1] if b is None else b), st)
        b = SCRATCH[n][1][1] if b is None else b
        return (T[n][:, a:b:st] if st > 1 else T[n][:, a:b], n, a, b, st, None)

    def rows(n, part, a, b):
        return (T[n][part, a:b], n, a, b, 1, None)

    def R(n, a, b, st=1):
        return (T[n][0:112, a:b:st] if st > 1 else T[n][0:112, a:b], n, a, b, st, None)

    def X(win, off):
        return (win[0].indirect(off[0]),) + win[1:5] + (off,)

    def size(x):
        return 16 * size(x[5]) if x[5] else len(range(x[2], x[3], x[4]))

    def call(e, fn, r, w, cost, late=lambda x: 0, sem=None, mark=False, after=()):
        r = [x for x in r if isinstance(x, tuple)]
        calls.append({"e": e, "fn": fn, "r": r + [x[5] for x in r + w if x[5]], "w": w, "ns": [cost(x) for x in WORLDS],
                      "late": [late(x) for x in WORLDS], "sem": sem, "mark": mark, "after": list(after), "goal": False})
        return len(calls) - 1

    def op(e, fn, r, w, cycles=None, more=0):
        o, k = w[0], 4 if e == "A" else 3
        if o[5] or (r and r[0][5]):
            return call(e, fn, r, w, lambda x: INDIRECT[e] + CY * x[0] * size(o) * x[2 if o[5] else 1] * (1.3 if cycles and not o[5] else 1))
        narrow = all(SCRATCH[x[1]][2] in (BF, F16, U16) for x in [o] + r if isinstance(x, tuple) and size(x) > 1)
        n = size(o) * (cycles or (0.5 if narrow and e == "V" else 1))
        psum = any(x[1] in PSUMS for x in [o] + r if isinstance(x, tuple))
        return call(e, fn, r, w, lambda x: more + x[k] + x[13] * psum + CY * x[0] * max(n, x[12]))

    def ap(x):
        return x[0] if isinstance(x, tuple) else x

    def mm(lst, mark=False):
        def f():
            ins = None
            for o, l, x, s0, s1 in lst:
                ins = g.tensor.matmul(o[0], l[0], x[0], s0, s1)
            return ins
        n = sum(max(min(64, size(m[1])), size(m[2])) * (4 if SCRATCH[m[2][1]][2] == F32 else 1) for m in lst)
        after = []
        if mark and mark[0] == "then":
            after = [i for i in range(len(calls) - 16, len(calls)) if calls[i]["mark"] == ("sum",) + mark[1:]]
        call("P", f, [x for m in lst for x in m[1:3]], [m[0] for m in lst], lambda x: n * x[0] * x[6], lambda x: 60,
             mark=mark, after=after)

    def grp(o, terms):
        return [(o, l, x, i == 0, i == len(terms) - 1) for i, (l, x) in enumerate(terms)]

    def dma(sem, o, i, late, after=()):
        return call("S", lambda: g.sync.dma_start(ap(o), ap(i)), [i], [o] if isinstance(o, tuple) else [], lambda x: 50,
                    lambda x: 900 + (late - 900) * x[8], sem, after=after)

    v = g.vector

    def ts(o, i, s1, o0, s2=None, o1=None):
        if o1 is None:
            op("V", lambda: v.tensor_scalar(o[0], i[0], ap(s1), None, o0), [i, s1], [o])
        else:
            op("V", lambda: v.tensor_scalar(o[0], i[0], ap(s1), ap(s2), o0, o1), [i, s1, s2], [o])

    def tt(o, a, b, o0):
        op("V", lambda: v.tensor_tensor(o[0], a[0], b[0], o0), [a, b], [o], 1 if a[1] in PSUMS or b[1] in PSUMS else 2)

    def cp(o, i):
        op("V", lambda: v.tensor_copy(o[0], i[0]), [i], [o])

    def ms(o, c):
        op("V", lambda: v.memset(o[0], c), [], [o])

    def scan(o, a, b, init, o0, o1):
        op("V", lambda: v.tensor_tensor_scan(o[0], a[0], b[0], ap(init), o0, o1), [a, b, init], [o])

    def vtr(o, i):
        op("V", lambda: v.transpose(o[0], i[0]), [i], [o])

    def red(o, i):
        op("V", lambda: v.tensor_reduce(o[0], i[0], AxisListType.X, A.add), [i], [o], 16)

    def act(o, i, f, more=0, **kw):
        acc = [kw["accum_out"]] if "accum_out" in kw else []
        op("A", lambda: g.scalar.activation(o[0], i[0], f, **{k: ap(x) for k, x in kw.items()}),
           [i] + [kw[k] for k in ("bias", "scale") if k in kw], [o] + acc, None, more)

    def lin(o, i, scale, bias=0.0):
        act(o, i, AF.Identity, scale=scale, bias=bias)

    def vlin(o, i, scale, bias=0.0):
        ts(o, i, scale, A.mult, bias, A.add)

    def iota(o, pat, base, cm=0):
        kw = {} if SCRATCH[o[1]][2] == I32 else {"allow_small_or_imprecise_dtypes": True}
        return call("G", lambda: g.iota(o[0], pat, base, cm, **kw), [], [o], lambda x: (130 + 2 * CY * size(o)) * x[10],
                    after=hold)

    def fill(o, c):
        return iota(o, [[0, size(o)]], c)

    def select(o, i, pat, cm, test=A.is_ge, other=0.0, base=0):
        return call("G", lambda: g.affine_select(o[0], i[0], pat, test, other, base, cm), [i], [o],
                    lambda x: (170 + 2 * CY * size(o)) * x[10], after=hold)

    def ident(o, c):
        return select(o, B("zr", 0, 128), [[1, 128]], -1, A.not_equal, c)

    def col(i):
        return B("co_", i, i + 1)

    def M(i):
        return B("MM", 128 * i, 128 * i + 128)

    def sel(n, p):
        return B(n, 15 - p, 143 - p)

    Ib, BO, xb = B("J", 0, 128), B("BO", 0, 128), B("xb", 0, 128)
    x144 = B("xb", 0, 144)
    nKB, KB, I4, KBS, KS, nKS, GM, LM, M8, M9, I20, D2, D1, W2, W1, nI4, S15 = [M(i) for i in range(17)]
    IK = B("IL", 256, 384)

    def PMm(kind, d):
        k = d % 3
        if k == 0:
            return (Ib, I4)[kind]
        a = 128 * (2 * kind + k - 1)
        return B("PM", a, a + 128)

    def GG(a, b, st=1):
        return B("GS", a, b, st)

    def S(a, b, st=1):
        return B("GS", SO + a, SO + b, st)

    k = []
    for sem, o, i, late in (("d_aw", B("awi"), T.aw[:], 1100), ("d_x0", B("XT", D, D + V), T.x0[:], 3100),
                            ("d_gv", B("gvi", 0, G), T.gv[:], 6200), ("d_ex", B("exi", 0, 14), T.ex[:], 6250),
                            ("d_co", B("C", D, D + V), T.co[:, 0:V], 10250), ("d_ci", B("C", D + V, D + W), T.co[:, V:W], 10650)):
        k = [dma(sem, o, i, late, k)]

    ms(B("ones"), 1.0)
    ms(B("zr"), 0.0)
    early = {
        "pi": lambda: iota(B("pi", 0, 1), [[0, 1]], 0, 1),
        "xb": lambda: iota(B("xb"), [[1, 256]], 0),
        "J": lambda: select(B("J"), B("ones", 0, 144), [[1, 144]], -1, A.is_equal),
        "mg": lambda: iota(B("mg"), [[16, 8], [0, 16]], 0),
        "RS": lambda: iota(B("RS"), [[0, 8], [16, 16]], 0),
        "TRI": lambda: select(B("TRI"), B("ones", 0, 128), [[1, 128]], -1, A.is_gt),
        "jp": lambda: iota(B("jp"), [[128, 2], [1, 16], [16, 8]], 0),
        "If": lambda: ident(B("If"), 1.0),
        "I4": lambda: ident(I4, 4096.0),
        "XT": lambda: fill(B("XT", D + V, D + W), -1),
        "gvi": lambda: fill(B("gvi", G, G + 16), W),
        "XF": lambda: fill(B("XF", D + W, XW), -14),
        "AS": lambda: fill(B("AS", WK, WK + Z_G), 0),
        "SM": lambda: iota(B("SM"), [[0, size(B("SM")) // 16], [20, 16]], -14),
    }
    for n in EARLY:
        hold[:] = [early.pop(n)()]
    for n in early:
        early[n]()
    ts(B("jn"), B("jp"), -2.0, A.mult, -1.0, A.add)
    for j, m in enumerate((15, 16, 1, 96)):
        ts(B("pi", j + 1, j + 2), B("pi", 0, 1), m, A.bitwise_and)
    cp(B("co_", 0, 5), B("pi", 0, 5))
    ts(col(13), col(2), 0.0, A.is_equal)
    ts(col(14), col(2), 0.0, A.is_gt)
    tt(col(15), col(0), col(1), A.subtract)
    ts(col(16), col(15), 15.0, A.add)
    ts(col(17), col(1), 15.0, A.is_equal)
    ts(B("oh"), B("xb", 0, 16), col(1), A.is_equal)
    act(B("ls", 0, 256), B("ones", 0, 256), AF.Silu, 1300, scale=float(LEV[0]))
    warm = len(calls) - 1
    spots = [("AS", a) for a in range(WK + Z_G, WW, Z_G)] + [("AS2", a) for a in range(WK, WW, Z_G)]
    for j, (n, a) in enumerate(spots):
        dma("d_z%d" % j, B(n, a, a + Z_G), B("AS", WK, WK + Z_G), (10650 if Z_G < G else 900) + Z_G * 1.8 * (j + 1), k)
    ts(col(19), col(1), 10.5, A.is_lt, -8192.0, A.mult)
    ts(B("sK"), B("oh"), -1.0 / 256, A.mult)
    ts(col(5), col(17), 225.0 / 256, A.mult)
    ts(col(6), col(19), -240.0 / 256 / 8192, A.mult, col(5), A.add)
    ts(B("aK"), B("xb", 0, 16), col(1), A.is_le, col(6), A.mult)
    ts(B("aK"), B("aK"), -241.0 / 256, A.add)
    for b in range(11):
        o, s1, s2 = B("AV", 240 * b, 240 * b + 240), B("sK", b, b + 1), B("aK", b, b + 1)
        if b in K_ACT:
            lin(o, B("xb", 0, 240), s1, s2)
        else:
            ts(o, B("xb", 0, 240), s1, A.mult, s2, A.add)
    fill(B("XT", D + W, XW), 0)
    for o in (GG(4096, SO), S(4096, SO)):
        select(o, B("ones", 0, 16), [[0, 16]], 0, A.is_gt, IDLE)
    ts(BO, B("mg"), col(15), A.is_equal)
    ts(S15, BO, col(17), A.mult, 16.0, A.mult)
    lift = {0: (0.0, 0.0), 8: (56.0, 896.0)}
    for j, n in enumerate(sorted(set(sum(EQ_A, ())) - {0, 8})):
        lift[n] = (col(30 + 2 * j), col(31 + 2 * j))
        ts(lift[n][0], col(0), 127.5 - 16 * n, A.is_gt, 56.0, A.mult)
        ts(lift[n][1], col(0), 127.5 - 16 * n, A.is_gt, 896.0, A.mult)
    ms(B("pre", 112, 128), 4096.0)
    ts(B("ZS"), x144, col(16), A.is_equal)
    (lin if KS_ACT else vlin)(KS, S15, K / 16)
    (lin if KS_ACT else vlin)(nKS, S15, -K / 16)
    ts(col(9), col(17), 0.125 - 1.0 / 32, A.mult, 1.0 / 32, A.add)
    ts(col(10), col(17), 1.0 / 32 - 0.125, A.mult, 1.0 - 1.0 / 32, A.add)
    ts(I20, BO, col(17), A.mult, -16.0, A.mult)
    (lin if D_ACT else vlin)(D2, Ib, col(9))
    (lin if D_ACT else vlin)(D1, Ib, col(10))
    mm(grp(B("pg", 0, 128), [(Ib, S15), (D2, Ib)]) + grp(B("pg", 128, 256), [(Ib, I20), (D1, Ib)]))
    act(B("MM", 128 * 13, 128 * 15), B("pg", 0, 256), AF.Copy)
    ts(col(11), col(17), K, A.mult, col(19), A.add)
    ts(nKB, BO, -K, A.mult)
    ts(KB, BO, K, A.mult)
    ts(GM, BO, col(11), A.mult)
    select(LM, nKB, [[1, 128]], -1, A.not_equal, -K * C0)
    iota(B("OH"), [[0, 8], [1, 16]], 0)
    ts(B("OH"), B("OH"), col(1), A.is_equal)
    (lin if HB_ACT else vlin)(M8, BO, col(19))
    (lin if HB_ACT else vlin)(M9, M8, -2.0)
    lin(B("Zd"), B("ZS"), col(19))
    lin(B("Z8h"), B("ZS"), -8192.0)
    lin(B("ZSh"), B("ZS"), 1.0)
    ts(col(12), col(17), -K, A.mult, K, A.add)
    (lin if HB_ACT else vlin)(KBS, BO, col(12))
    for o, c in ((nI4, -4096.0), (IK, -K1), (B("I8h", 0, 128), -8192.0),
                 (B("I8h", 128, 256), 8192.0), (B("IL", 0, 128), LEV[0] / 2)):
        ident(o, c)
    ts(col(23), col(1), 2.0, A.mult, 1.0, A.add)
    ts(col(24), col(23), col(4), A.add)
    for n, c in (("H0", 13), ("H1", 14)):
        ts(B(n + "h"), x144, col(24), A.is_equal, col(c), A.mult)
        (lin if HB_ACT else vlin)(B(n + "b"), B(n + "h"), 256.0)
    ts(col(27), col(15), -1.0, A.mult, 112.0, A.add)
    ts(col(44), col(15), 0.0, A.is_gt, 128.0, A.mult)
    ts(col(28), col(27), col(1), A.add)
    ts(col(29), col(44), col(15), A.subtract)
    ts(PMm(0, 1), xb, col(28), A.is_equal)
    ts(PMm(0, 2), xb, col(1), A.subtract, col(29), A.is_equal)
    (lin if HB_ACT else vlin)(B("PM", 256, 512), B("PM", 0, 256), 4096.0)
    (lin if CC_ACT else vlin)(B("KJ"), B("xb", 0, 224), 1.0 / 256, 1.0 / 256 - 1.0)
    at = {}
    for a, b in HALVES:
        at.setdefault(b - a, a)
    for n, c, a, b in [("CCb", 45 + h, a, a + n) for h, (n, a) in enumerate(at.items())] + [("CCi", 26, 0, 224)]:
        k = (b - a) // 2
        ts(col(c), col(3), -1.0 * k, A.mult, 256.0, A.add)
        for j in (a, a + k):
            (lin if CC_ACT else vlin)(B(n, j, j + k), B("xb", 0, k), -1.0, col(c))
    fill(B("LD"), 0)
    ts(col(22), col(1), 240.0 - ZB, A.add)
    ts(B("LD", 0, 256, 16), B("xb", 0, 256, 16), -1.0, A.mult, col(22), A.add)
    ts(B("jh", 0, 3), B("xb", 0, 48, 16), col(1), A.add, 1.0, A.add)
    iota(B("PL"), [[0, 3], [1, 256]], 1)
    ts(B("dd", 0, 3), B("xb", 0, 48, 16), col(1), A.add, 256.0, A.add)
    fill(B("cz"), int(ZB - 2 * K2))
    ms(B("lz", 3, 4), 4110)
    ts(B("M16"), B("xb", 0, 16), col(1), A.is_ge, 8192.0, A.mult)
    for o, c in ((B("C", 0, D), -1), (B("C", D + W, XW), -1),
                 (B("XF", 0, D), 0), (B("XT", 0, D), 0), (B("neg1"), -1), (B("c14"), 14),
                 (B("MAG"), int(MAGIC)), (B("t196"), 196)):
        fill(o, c)
    fill(B("lv", 0, 224), LEV[0])

    def turn(terms, bank):
        lst = []
        for t in range(7):
            for a in (0, 16):
                lst += grp(B(bank, 32 * t + a, 32 * t + a + 16), [(B("J", a, a + 128), f(t)) for f in terms])
        mm(lst)

    if AW_G:
        select(B("awb"), B("awi"), [[0, 112]], 0)
    else:
        cp(B("awb"), B("awi"))
    turn([lambda t: B("awb", 16 * t, 16 * t + 16)], "pf")
    for t in range(7):
        vtr(B("TT", t, t + 218, 7), B("pf", 32 * t, 32 * t + 32))
    if AW_F32:
        mm(grp(R("ph", 0, 128), [(B("TT", 0, 112), B("If"))]))
    else:
        cp(B("aws"), B("TT", 0, 112))
        mm(grp(R("ph", 0, 128), [(B("aws"), Ib)]))
    cp(B("exu", 0, 14), B("exi", 0, 14))

    def encode(a, b, bk, e="A"):
        scan(B("AV2", a, b), B("AV", a, b), B("XT", D + a, D + b), 0.0, A.min, A.max)
        mm(grp(B(bk, 0, b - a), [(W1, B("XT", D + a, D + b)), (W2, B("AV2", a, b))]))
        if e == "V":
            ts(B("XF", D + a, D + b), B(bk, 0, b - a), -14.0, A.add)
        else:
            lin(B("XF", D + a, D + b), B(bk, 0, b - a), 1.0, -14.0)

    def refresh(ks, tab="XF", tmp="x48", e="V"):
        for k in ks:
            if e == "A":
                act(B(tmp), X(B(tab), B("LT", 8 * k + 4, 8 * k + 7)), AF.Copy)
            else:
                cp(B(tmp), X(B(tab), B("LT", 8 * k + 4, 8 * k + 7)))
            cp(X(B(tab), B("LT", 8 * k, 8 * k + 3)), B(tmp))

    def shuffle(bank, n, cc, cg, tm, a=0, up=None):
        mm([(B(bank, 0, 2 * n), Ib, cc, True, False)]
           + ([(B(bank, 0, 2 * n), up, rows("ones", slice(0, 1), 0, 2 * n), False, False)] if up else []))
        for nm, src in (("h", cg), ("b", tm)):
            if nm == "b":
                scan(B(tm, a, a + 2 * n), B("KJ", 0, 2 * n), B(cg, a, a + 2 * n), -1.0, A.max, A.min)
            mm([(B(bank, n * h, n * h + n), B("H%d%s" % (h, nm), 1 - k, 129 - k), B(src, a + n * k, a + n * k + n), False,
                 nm == "b" and h + k == 2) for h in range(2) for k in range(2)])

    def lists(bank, k, tmp, a, out):
        for s in range(k):
            vtr(B(tmp, a + s, a + 32 * k, k), B(bank, s, 32 * k, k))
        ts(B(out, a, a + 32 * k), B(tmp, a, a + 32 * k), WK - 1.0, A.add)

    lastw, lastc = {"V": None, "A": None}, {"V": [], "A": []}

    def scatter(e, s, off, wins, wide=1):
        val = B("ls" if e == "A" else "lv", 256 * s, 256 * s + 16 * size(off))

        def f():
            w = wins[-1] if lastw[e] == wins[0] else wins[0]
            lastw[e] = w
            o = X(B(w, 0, wide * WW), off)
            return (g.scalar.activation(o[0], val[0], AF.Silu) if e == "A" else v.tensor_copy(o[0], val[0])), o
        lastc[e] = [call(e, f, [val, off], [B(w, 0, wide * WW) for w in wins],
                         lambda x: INDIRECT[e] + CY * x[0] * x[2] * size(val) + x[9] * (len(wins) == 1),
                         mark=True, after=lastc[e])]

    win = B("XF", D, XW)
    tops, odd = {}, {}

    for s in range(3):
        first, last = s == 0, s == 2
        if s:
            for n, k in (("ls", 256), ("lv", 224)):
                fill(B(n, 256 * s, 256 * s + k), LEV[s])
        if s == PAIRS:
            for n in ("AS", "AS2"):
                for a in range(WW + WK, 2 * WW, 448):
                    fill(B(n, a, a + 448), 0)
            iota(B("RO", 0, 128), [[0, 32], [WW, 2], [0, 2]], 0)
            for j, r in enumerate(sorted({x + x % 2 for y in BIND_VEC[s:] for x in y})):
                odd[r] = rows("RO", slice(0, 1), 128 * j + 128, 128 * j + 256)
                select(B("RO", 128 * j + 128, 128 * j + 256), B("RO", 0, 128), [[0, 4], [1, 32]], 0, base=-2 * r)
        if s == 1:
            ident(B("IL", 128, 256), LEV[1] / 2)
            for a in range(0, XW, 488):
                iota(B("F", a, a + 488), [[1, 488]], a - D)
        if last:
            ident(B("ILf"), LEV[2] / 2)
            lin(B("Z0"), B("ZS"), B("oh", 0, 1))
        ts(R("awT", 0, 128), R("ph", 0, 128), 0.0, A.is_gt)
        calls[-1]["goal"] = not first
        if first:
            for k, (a, b) in enumerate(CHUNKS):
                encode(a, b, ("pe", "ph")[k % 2], "AV"[k in XF_VEC])
        scan(R("wT", 0, 128), R("RS", 0, 128), R("awT", 0, 128), 0.0, A.min, A.add)
        mm(grp(R("pd", 0, 8), [(R("TRI", 1, 113), R("wT", 15, 128, 16))]))
        ts(R("nB", 0, 8), R("pd", 0, 8), -2.0, A.mult, -512.0, A.max)
        mm(grp(B("pb", 0, 112), [(R("wT", 0, 128), R("TRI", 0, 112))]))
        lin(B("Yb"), B("pb", 0, 112), 1.0 / 16)
        place = [(R("wT", 0, 128), R("J", 0, 112)), (S15, B("Yb"))]
        mm(grp(B("pb", 128, 240), place))
        act(B("pre", 0, 112), B("pb", 128, 240), AF.Copy)
        mm(grp(B("pb", 256, 368), place + [(R("awT", 0, 128), R("MM", 256, 368))]))
        act(B("sg"), B("pb", 256, 368), AF.Sign, bias=-4352.5)

        def count(bank, h, k):
            return [(B(bank, c, c + 1), R("EQ", 1024 * h + c, 1024 * h + 1024, 8), R("xb", k, k + 1), k == 1, k == 1)
                    for c in range(8)]

        for h in range(2):
            for j in range(8):
                o, i = R("EQ", 1024 * h + 128 * j, 1024 * h + 128 * j + 128), R("jn", 128 * h, 128 * h + 128)
                if j < 8 - EQ_A[s][h]:
                    ts(o, i, R("nB", j, j + 1), A.is_le, 2.0, A.mult)
                else:
                    act(o, i, AF.Sign, bias=R("nB", j, j + 1), scale=-1.0)
            mm(count(("pf", "pg")[h], h, 1))
        for h in range(2):
            a, o = 128 * h, B(("pa", "pc")[h], 0, 8)
            ts(B("bw", 8 * h, 8 * h + 8), B(("pf", "pg")[h], 0, 8), 0.5, A.mult, lift[EQ_A[s][h]][0], A.add)
            mm([(o, BO, B("zr", 0, 8), True, False)] + count(("pa", "pc")[h], h, 8))
            tt(B("cmp", a, a + 128), X(B("pre"), B("bw", 8 * h, 8 * h + 8)), B("xb", a, a + 128), A.is_le)
            mm([(o, sel("ZS", p), B("cmp", a + p, a + 128, 16), False, p == 15) for p in range(16)])
            ts(B("eu", 8 * h, 8 * h + 8), o, lift[EQ_A[s][h]][1], A.add)
            cp(B("gve", a, a + 128), X(B("gvi"), B("eu", 8 * h, 8 * h + 8)))

        def two(a, b):
            return S(16 * a + 14, 16 * b, 16), GG(16 * a + 15, 16 * b, 16)

        def fraction(o, a, b, m, last, mark=False):
            mx, go = two(a, b)
            mm([(o, m[0], mx, False, False), (o, nKS, B("MAG", 0, b - a), False, False), (o, m[1], mx, False, False)]
               + [(o, l, x, False, last and i == len(m[2]) - 1) for i, (l, x) in enumerate(m[2])], mark)

        for a, b, e in (GATHER0 if first else GATHER):
            if e == "A":
                act(GG(16 * a, 16 * b), X(win, B("gve", a, b)), AF.Copy)
            else:
                cp(GG(16 * a, 16 * b), X(win, B("gve", a, b)))
        for a, b in SCANS:
            scan(S(16 * a, 16 * b), B("SM", 0, 16 * (b - a)), GG(16 * a, 16 * b), 0.0, A.min, A.max)
        mm([(B(WANT, 0, 256), KS, B("MAG"), True, False), (B(WANT, 0, 256), nKB, B("t196"), False, False)])
        for a, b in SUMS:
            for i in range(0, 16, TERMS):
                mm([(B(WANT, a, b), nKB if j < 15 else nKS, GG(16 * a + j, 16 * b, 16), False, False)
                    for j in range(i, i + TERMS)], ("sum", a, b))
            mx, go = two(a, b)
            fraction(B(WANT, a, b), a, b, (KBS, KS, [(KS, go), (M8, mx), (M8, go), (M9, S(16 * a + 15, 16 * b, 16))]), False,
                     ("then", a, b))
        mm([(B(WANT, 0, 1), BO, B("zr", 0, 1), False, True)])
        for h, (a, b) in enumerate(HALVES):
            bk, bl, n, k = ("pf", "pg")[h], ("pb", "pc")[h], b - a, (b - a) // 16
            mx, go = two(a, b)
            ou = B("obu", a // 16, b // 16)
            mm([(B(bk, 0, n), KS, B("MAG", 0, n), True, False)])
            mm([(B(bk, 0, n), nKS, go, False, False)])
            fraction(B(bk, 0, n), a, b, (KB, nKB, [(GM, go), (LM, B("OH", 0, n))]), True)
            scan(B("lat", a, b), B("LD", a, b), B(bk, 0, n), 0.0, A.min, A.max)
            ts(ou, B("lat", a + 15, b, 16), ZB, A.add)
            cp(B("cg", a, b), X(B("C", 0, D + V), ou))
            two_from = BIND_VEC[s][h] + BIND_VEC[s][h] % 2 if s >= PAIRS and h < PAIR_H else 16
            shuffle(bl, n // 2, B("CCb", at[n], at[n] + n), "cg", "tm", a, odd.get(two_from))
            lists(bl, k // 2, "TT", a, "wl")
            calls[-1]["goal"] = h == 0
            for r in range(16):
                e = "V" if r < BIND_VEC[s][h] else "A"
                if r >= two_from:
                    if r % 2 == 0:
                        scatter(e, s, B("wl", a + k * r, a + k * r + 2 * k), ("AS", "AS2"), 2)
                    continue
                m = k // 2 if e == "V" and r < HALVED[s][h] else k
                for j in range(a + k * r, a + k * r + k, m):
                    scatter(e, s, B("wl", j, j + m), ("AS", "AS2") if e == "A" else ("AV", "AV2"))
        mx, go = two(0, 256)
        for a, b in XT_PARTS:
            tt(X(B("XT", 0, D + V), B("obu", a // 16, b // 16)), two(a, b)[0], B("c14", a, b), A.add)
        refresh(range(s - 1, -1, -1), "XT")
        snd, Ln = B("snd", 224 * s, 224 * s + 224), B("land", 224 * s, 224 * s + 224)
        if SND_ACT:
            act(snd, X(B("XT", D, XW), B("exu", 0, 14)), AF.Copy)
        else:
            cp(snd, X(B("XT", D, XW), B("exu", 0, 14)))
        if last:
            for k in range(s):
                cp(X(B("XT"), B("LT", 8 * k, 8 * k + 3)), B("neg1", 0, 48))
        else:
            for a, b in XF_PARTS:
                cp(X(B("XF", 0, D + V), B("obu", a // 16, b // 16)), two(a, b)[0])
        trs = []
        for d in range(1, 8):
            peer = T.cores[rank ^ d]
            en = topo.engines(core, peer)
            n = len(en) // 8
            mask = sum(1 << e for e in en[n * (d - 1):n * d])
            rid, pid, _ = topo.addr(peer)
            a = 224 * s + 32 * (d - 1)
            trs.append(RemoteDMATransfer(dst_ids=[DstId(rid=rid, pnc=pid)], dma_engine_mask=mask,
                                         remote_sem=T.sem["arr%d" % s], src=T.snd[:, a:a + 32], dst=T.land[:, a:a + 32]))
            tops["snt"] = tops.get("snt", 0) + n
            tops["arr%d" % s] = tops.get("arr%d" % s, 0) + n
        hold[:] = [call("G", lambda trs=trs: g.remote_dma_fused(trs, local_sem=T.sem.snt), [snd], [Ln], lambda x: x[11],
                        lambda x: x[7] * (FIRST if first else 1), "arr%d" % s)]
        o = B(WANT, 0, 256)
        ts(B("want", 0, 256), o, 2 * K * C0 + 0.5, A.is_gt, -1.0, A.mult)
        o = B("pd", 0, 256)
        mm([(o, M8, go, True, False)])
        mm([(o, IK, B("want", 0, 256), False, True)])
        ts(B("SW", 0, 256), o, ZB - SH - K1, A.add, -2000.0, A.max)
        if COUNT_ACT:
            scan(B("rank"), B("ones"), B("want"), -0.5, A.mult, A.add)
            for t in range(3):
                act(B("EQ", 256 * t, 256 * t + 256), B("rank"), AF.Sign, bias=B("jh", t, t + 1), accum_out=B("ca", t, t + 1))
            ts(B("lz", 0, 3), B("ca", 0, 3), 8.0, A.mult, 2063.0, A.add)
            ts(B("lz", 4, 7), B("ca", 0, 3), 8.0, A.mult, SO + 2062.0, A.add)
        else:
            for t in range(3):
                scan(B("EQ", 256 * t, 256 * t + 256), B("want"), B("zr"), B("jh", t, t + 1), A.add, A.max)
            scan(B("EQ", 1024, 1792), B("EQ", 0, 768), B("PL"), 0.0, A.add, A.min)
            ts(B("lz", 0, 3), B("EQ", 1279, 1792, 256), 16.0, A.mult, 15.0, A.add)
            ts(B("lz", 4, 7), B("EQ", 1279, 1792, 256), 16.0, A.mult, SO + 14.0, A.add)
        cp(B("cs"), X(B("GS"), B("lz", 0, 7)))
        dec = [(sel("Zd", p), B("cs", p, 112, 16)) for p in range(16)]
        mm(grp(B("pe", 0, 7), dec))
        mm([m for j in range(5) for m in grp(B("pa", 16 * j, 16 * j + 16), [(M8, B("cs", 64 + 16 * (j // 2), 80 + 16 * (j // 2)))]
                                             + [(Ib, B("M16"))] * (1 - j % 2))])
        mm([(B("pf", 0, 3), B("If"), B("cz", 0, 3), True, False)])
        if SW_ACT:
            lin(B("SW", 256, 336), B("pa", 0, 80), 1.0, ZB - SH)
        else:
            ts(B("SW", 256, 336), B("pa", 0, 80), ZB - SH, A.add)
        ts(B("LU", 0, 7), B("pe", 0, 7), ZB, A.add)
        cp(B("cc"), X(B("C"), B("LU", 0, 7)))
        tt(B("mn", 48, 96), B("cc", 0, 48), B("cc", 64, 112), A.min)
        tt(B("mn", 0, 48), X(B("XT"), B("LU", 4, 7)), B("mn", 48, 96), A.add)
        tt(B("mxc"), B("cc", 0, 48), B("cc", 64, 112), A.max)
        mm([(B("pf", 0, 3), sel("Z8h", p), B("mn", p, 48, 16), False, False) for p in range(16)])
        ends = (0, 272, 576, 912)
        for t in range(3):
            ts(B("E", ends[t], ends[t + 1]), B("SW", 0, 272 + 32 * t), SH - ZB, A.add, B("pe", 4 + t, 5 + t), A.is_equal)
        scan(B("EO"), B("E"), B("E"), 0.0, A.add, A.max)
        mm([(B("pf", t, t + 1), B("I8h", 128 * k, 128 * k + 128), B("EO", ends[t + 1 - k] - 1, ends[t + 1 - k]),
             False, t + k == 3) for t in range(3) for k in range(2) if t >= k])
        for t in range(3):
            ts(B("LT", 8 * s + t, 8 * s + 8, 4), B("pe", t, 8, 4), B("pf", t, t + 1), A.add, B("dd", t, t + 1), A.max)
        cp(X(B("C"), B("LT", 8 * s + 4, 8 * s + 7)), B("mxc"))

        def blk(n, d, k=0):
            return B(n, 224 * k + 32 * d - 32, 224 * k + 32 * d)

        xi = B("XT", D + V, D + W)
        mm([(B("pg", 0, 224), Ib, B("neg1"), True, False), (B("pg", 0, 224), nI4, xi, False, False)])
        mm([(blk("pg", d), PMm(1, d), blk("land", d, s), False, d == 7) for d in range(1, 8)])
        if last:
            turn([lambda t: B("sg", t, 112, 7)], "pb")
            vtr(B("remT"), B("pb", 0, 224))
        tt(B("Cm"), B("C", D + V, D + W), B("pg", 0, 224), A.min)
        shuffle("pb", 112, B("CCi"), "Cm", "ti")
        lists("pb", 7, "TI", 0, "wi")
        for r in range(16):
            e = "A" if r < IMP_ACT[s] else "V"
            both = r < (IMP_ACT[s] - AS_ONLY[s] if e == "A" else 16 - AV_ONLY)
            scatter(e, s, B("wi", 14 * r, 14 * r + 14), (("AS", "AS2") if e == "A" else ("AV", "AV2"))[:1 + both])
        mm([m for d in range(1, 8) for m in grp(blk("pc", d), [(PMm(0, d), blk("land", d, s))])])
        if XI_ACT[s]:
            act(xi, B("pc", 0, 224), AF.Copy)
        else:
            cp(xi, B("pc", 0, 224))
        if last:
            dma("d_y0", T.yx[:, 0:V], B("XT", D, D + V), 6000)
            dma("d_y1", T.yx[:, V:W], B("XT", D + V, D + W), 1200)
            refresh(range(2, -1, -1), "F", "c48", "VA"[F_ACT])
            dma("d_yf", T.yf[:], rows("F", slice(0, 128, 16), D, D + W), 1300)
            for a in (0, 1280):
                select(B("C16", a, a + 1280), B("C", D + a, D + a + 1280), [[0, 1280]], 0)
            for a in (0, 8):
                mm([(B("pe", 0, 160), sel("ZSh", p), B("C16", 160 * p, 160 * p + 160), p == 0, p == 15) for p in range(a, a + 8)])
            act(B("yc_"), B("pe", 0, 160), AF.Copy)
            dma("d_yc", T.yc[:], B("yc_"), 1300)
        else:
            encode(V, W, "pd")
            refresh(range(s, -1, -1), e="VA"[REF_ACT])

        def turned(bank, n, k, end, WK=WK, WW=WW):
            one = B("If" if SCRATCH[n][2] == F32 else "J", 0, 128, 16)
            ps = list(range(16))
            if n == "AS" and NARROW[s] and WK < G:
                m = NARROW[s]
                ps = ps[:16 - m] if last else [p for p in ps if p % (16 // m)]
                act(B("ASb", 0, 112 * m), B(n, WW - 112 * m, WW) if last else B(n, WK, WW, 16 // m), AF.Copy)
            for a in range(0, len(ps), k):
                mm([(R(bank, p, 128, 16), B(n, WK + 112 * p, WK + 112 * p + 112) if last else B(n, WK + p, WW, 16), one,
                     False, end and p == 15) for p in ps[a:a + k]], not (end and 15 in ps[a:a + k]) and "sum")
            if len(ps) < 16:
                mm([(R(bank, 16 - m + j if last else 16 // m * j, 128, 16),
                     B("ASb", 112 * j, 112 * j + 112) if last else B("ASb", j, 112 * m, m), B("J", 0, 128, 16),
                     False, end and j == m - 1) for j in range(m)], not end and "sum")

        if last:
            o = B("ph", 0, 112)
            mm([(o, BO, B("zr", 0, 112), True, False)])
            mm([(B("ph", 16 * t, 16 * t + 16), B("ILf"), B("remT", 32 * t, 32 * t + 16), False, False) for t in range(7)],
               "sum")
            mm([(R("pa", 0, 128), B("zr", 0, 112), BO, True, False)])
            for n in ("AS", "AS2") * (s >= PAIRS):
                turned("pa", n, READS, False, WW + WK, 2 * WW)
            for n in TURN_LAST:
                turned("pa", n, 16, False)
            turned("pa", "AS2", READS, False)
            turned("pa", "AS", READS, True)
            act(R("At", 0, 128), R("pa", 0, 128), AF.Copy)
            mm([(o, R("At", 0, 128), R("J", 0, 112), False, False)], "sum")
            for n in ("AV2", "AV")[len(TURN_LAST):]:
                mm([(o, sel("Z0", p), B(n, WK + 112 * p, WK + 112 * p + 112), False, False) for p in range(16)], "sum")
            mm([(B("ph", 0, 1), BO, B("zr", 0, 1), False, True)])
            ts(B("yw_"), o, 0.0, A.is_gt)
            dma("d_yw", T.yw[:], B("yw_"), 1200)
        else:
            mm([(R("ph", 0, 128), B("sg"), B("IL", 128 * s, 128 * s + 128), True, False)])
            for n in ("AS", "AS2") * (s >= PAIRS):
                turned("ph", n, READS, False, WW + WK, 2 * WW)
            for n in ("AS2", "AS", "AV2"):
                turned("ph", n, READS if n[1] == "S" else 16, False)
            turned("ph", "AV", 16, True)

    cnt, seen, uses = {e: 0 for e in eng}, {e: {} for e in eng}, {}

    known = {}

    def need(e, sem, n):
        if seen[e].get(sem, 0) < n:
            eng[e].wait_ge(T.sem[sem], n)
            seen[e][sem] = n
            for k, m in known.get((sem, n), (0, {}))[1].items():
                seen[e][k] = max(seen[e].get(k, 0), m)

    for c in calls[warm + 1:]:
        if c["e"] == "A" and not c["after"]:
            c["after"] = [warm]
    if not PLANS:
        PLANS.append(plan(calls))
    for c in [calls[i] for i in PLANS[0]]:
        e, w, want = c["e"], c["w"], {}
        if c["mark"] is True:
            w = [w[-1] if lastw[e] == w[0][1] else w[0]]
        for vs, wr in ((c["r"], False), (w, True)):
            for x in vs:
                for (sem, w2, sp), n in uses.get(x[1], {}).items():
                    if not (sem == "sP" and e == "P"):
                        if (x[1] in PSUMS and sem != "s" + e) or ((wr or w2) and meet(sp, x[2:5])):
                            want[sem] = max(want.get(sem, 0), n)
        for sem in sorted(want, key=lambda k: -known.get((k, want[k]), (0,))[0]):
            need(e, sem, want[sem])
        ins = c["fn"]()
        if c["sem"] in tops:
            tok = (c["sem"], tops[c["sem"]])
            uses.setdefault(c["w"][0][1], {})[(tok[0], True, c["w"][0][2:5])] = tok[1]
            continue
        if c["mark"] is True:
            ins = ins[0]
        if c["sem"]:
            tok = (c["sem"], 16)
            ins.then_inc(T.sem[tok[0]], 16)
        else:
            cnt[e] += 1
            tok = ("s" + e, cnt[e])
            ins.then_inc(T.sem[tok[0]], 1)
        known[tok] = (len(known), dict(seen[e]))
        seen.setdefault("end", {})[tok[0]] = tok[1]
        for vs, wr in ((c["r"], False), (w, True)):
            for x in vs:
                uses.setdefault(x[1], {})[(tok[0], wr, x[2:5])] = tok[1]
    for sem, n in list(seen["end"].items()) + list(tops.items()):
        need("S", sem, n)
